import numpy as np, ml_dtypes
CORES = [5,29,101,125,133,157,229,253]
N = 8
BF = ml_dtypes.bfloat16
def gentries(a):
    return np.ascontiguousarray(a.reshape(8, 16, -1).transpose(0, 2, 1)).reshape(8, -1)
def gtable(e):
    e = np.asarray(e); return np.ascontiguousarray(e.reshape(8, -1, 16).transpose(0, 2, 1)).reshape(128, -1).astype(np.int32)
TT, P, R, S, CAP = 1024, 384, 2, 3, 16
def walk(planes, nbr, x, c):
    A = planes.astype(np.int64).reshape(N, 4, 4, TT).transpose(0, 3, 1, 2).reshape(N * TT, 4, 4); B = nbr.astype(np.int64).transpose(0, 2, 1).reshape(N * TT, 4)
    h = np.concatenate([x.astype(np.int64), np.ones((len(x), 1), np.int64)], 1); c = c.astype(np.int64); w = [c]
    for k in range(R):
        q = c // TT
        for s in range(S):
            v = np.einsum("mfc,mc->mf", A[c], h); face = np.argmin(v, 1)
            c = np.where((c // TT == q) & (np.min(v, 1) < 0), B[c, face], c)
        w.append(c)
    return np.stack(w)
def codes(rng, shape, own):
    r = np.arange(N).reshape(N, 1, 1); q = np.where(rng.random(shape) < own, r, (r + rng.integers(1, N, shape)) % N)
    return q * TT + rng.integers(0, TT, shape)
def mesh(rng, big, lo, hi):
    p = rng.integers(-big, big + 1, (N, 4, 4, TT)); p[:, :, 3] = rng.integers(lo, hi + 1, (N, 4, TT)); return p
def roomy(rng, p):
    h = np.stack([1 + rng.permutation(TT - 2)[:TT // 16] for r in range(N)]); k = h.shape[1]
    for r in range(N):
        u = p[r]; u[:, :3, h[r]] = rng.integers(-255, 256, (4, 3, k)); u[:, 3, h[r]] = rng.integers(3 * 255 * 1023, 2 ** 20 + 1, (4, k))
    return h
def choose(rng, p, h, b, x, c):
    big = int(np.abs(x).max()); r = np.arange(N).reshape(N, 1, 1)
    x = np.concatenate([x, rng.integers(-big, big + 1, (N, 8, P, 3))], 2); c = np.concatenate([c, r * TT + h[r, rng.integers(0, h.shape[1], (N, 8, P))]], 2)
    planes = p.reshape(N, 16, TT).astype(np.int32); m = c.shape[2]
    w = walk(planes, b, x.reshape(-1, 3), c.reshape(-1))[:R].reshape(R, N, 8, m) // TT
    cap = np.where(np.eye(N, dtype=bool), P, CAP); cnt = np.zeros((R, N, 8, N), np.int64); n = np.zeros((N, 8), np.int64); keep = np.zeros((N, 8, m), bool)
    k, i, g = np.ogrid[:R, :N, :8]
    for j in range(m):
        q = w[:, :, :, j]; ok = np.all(cnt[k, i, g, q] < cap[i, q], axis=0) & (n < P)
        cnt[k, i, g, q] += ok; n += ok; keep[:, :, j] = ok
    e = rng.permuted(np.nonzero(keep.reshape(N * 8, m))[1].reshape(N, 8, P), axis=2)
    x = np.take_along_axis(x, e[:, :, :, None], 2); c = np.take_along_axis(c, e, 2)
    return {"planes": planes, "nbr": b.astype(np.int32), "pts": np.ascontiguousarray(x.transpose(0, 1, 3, 2)).reshape(N, 24, P).astype(np.int32), "tet0": np.stack([gtable(u) for u in c])}
def setup_inputs(rng):
    p = mesh(rng, 127, -20000, 60000); h = roomy(rng, p)
    return choose(rng, p, h, codes(rng, (N, 4, TT), 0.6), rng.integers(-255, 256, (N, 8, 3 * P, 3)), codes(rng, (N, 8, 3 * P), 0.5))
def setup_inputs_full(rng):
    p = mesh(rng, 127, -20000, 60000); h = roomy(rng, p); r = np.arange(N).reshape(N, 1, 1); m = (N - 1) * CAP
    q = np.broadcast_to((r + 1 + np.arange(m) // CAP) % N, (N, 8, m)); c = q * TT + h[q, rng.integers(0, h.shape[1], (N, 8, m))]
    c = np.where(np.arange(8).reshape(1, 8, 1) % 2 == 0, c, codes(rng, (N, 8, m), 0.0)); c = np.concatenate([c, codes(rng, (N, 8, 2 * P), 0.8)], 2)
    return choose(rng, p, h, codes(rng, (N, 4, TT), 0.6), rng.integers(-255, 256, (N, 8, m + 2 * P, 3)), c)
def setup_inputs_ties(rng):
    p = mesh(rng, 1, -1, 2)
    p[:, 3] = np.where(rng.random((N, 1, TT)) < 0.5, p[:, 1], p[:, 3]); p[:, 2] = np.where(rng.random((N, 1, TT)) < 0.5, p[:, 0], p[:, 2]); h = roomy(rng, p)
    return choose(rng, p, h, codes(rng, (N, 4, TT), 0.6), rng.integers(-2, 3, (N, 8, 3 * P, 3)), codes(rng, (N, 8, 3 * P), 0.5))
def setup_inputs_few(rng):
    p = mesh(rng, 127, -20000, 60000); h = roomy(rng, p); b = codes(rng, (N, 4, TT), 1.0); q = rng.integers(0, N); b[q] = codes(rng, (N, 4, TT), 0.3)[q]
    c = codes(rng, (N, 8, 3 * P), 1.0); out = []
    for v in (b, c):
        u = rng.random(v.shape); out.append(np.where(u < 0.2, v // TT * TT, np.where(u < 0.4, v // TT * TT + TT - 1, v)))
    b, c = out; x = rng.integers(-255, 256, (N, 8, 3 * P, 3)); one = rng.random((N, 8, 3 * P)) < 0.4
    c = np.where(one, c[:, :, :1], c); x = np.where(one[:, :, :, None], x[:, :, :1], x)
    return choose(rng, p, h, b, x, c)
def setup_inputs_spread(rng):
    def some(bits, top, shape, plus):
        v = np.minimum(np.floor(np.exp2(bits * rng.random(shape))).astype(np.int64), top); v = np.where(rng.random(shape) < 0.125, top, v)
        return np.where(rng.random(shape) < plus, v, -v)
    p = some(10, 1023, (N, 4, 4, TT), 0.5); p[:, :, 3] = some(20, 2 ** 20, (N, 4, TT), 0.75); h = roomy(rng, p)
    return choose(rng, p, h, codes(rng, (N, 4, TT), 0.6), some(10, 1023, (N, 8, 3 * P, 3), 0.5), codes(rng, (N, 8, 3 * P), 0.5))
def points(pts, tet0):
    return pts.reshape(N, 8, 3, P).transpose(0, 1, 3, 2).reshape(-1, 3), np.stack([gentries(a) for a in tet0]).reshape(-1)
def check_inputs(d):
    bad = []; p = d["planes"].astype(np.int64).reshape(N, 4, 4, TT)
    if np.abs(p[:, :, :3]).max() > 1023 or np.abs(p[:, :, 3]).max() > 2 ** 20: bad.append("planes out of range")
    if np.abs(d["pts"].astype(np.int64)).max() > 1023: bad.append("pts out of range")
    for a in ("nbr", "tet0"):
        if d[a].min() < 0 or d[a].max() >= N * TT: bad.append(a + " out of range")
    if bad: return bad
    x, c = points(d["pts"], d["tet0"]); w = walk(d["planes"], d["nbr"], x, c)[:R].reshape(R, N, 8, P) // TT
    for q in range(N):
        n = np.count_nonzero(w == q, axis=3); n[:, q] = 0
        if n.max() > CAP: bad.append("more than CAP points of a group on rank " + str(q))
    return bad
def reference(planes, nbr, pts, tet0):
    x, c = points(pts, tet0); e = walk(planes, nbr, x, c)[R].reshape(N, 8, P)
    return {"y": np.stack([gtable(u) for u in e]).astype(np.float32)}

@@ -1,0 +1,618 @@
+from concourse.bass import DstId, RemoteDMATransfer
+from concourse.mybir import AluOpType as A, ActivationFunctionType as F
+
+NT, NP, NK = 1024, 384, 24
+LO, HI, PWID = 8, 1032, 1040
+DEAD = 7.375
+MSG = 17
+WIN = 640
+BIG, MID = 8388608, 4194304
+NONE = (1 << 21) + 1024
+N_REL, ENG_HOP, ENG_OUT, ENG_DIR = 2, 4, 4, 2
+PER = 4 // N_REL
+
+_sb = {
+    "X": ([128, NP], "int32"), "L0": ([128, NK], "int32"), "PW": ([128, PWID], "int32"), "NB": ([128, PWID], "int32"),
+    "ND": ([128, PWID], "float32"), "Xv": ([128, 112], "float32"), "xB": ([128, 112], "float32"),
+    "pi": ([128, 4], "int32"), "pj": ([128, 8], "int32"), "pf": ([128, 8], "float32"), "jm": ([128, 128], "bfloat16"), "x1": ([128, NK], "int32"),
+    "mk": ([128, 128], "float32"), "md16": ([128, 128], "float32"), "m16": ([128, NP], "bfloat16"), "Rd": ([128, NP], "float32"),
+    "G16": ([128, 128], "float16"), "G2k": ([128, 128], "float16"), "Gf": ([128, 128], "float32"),
+    "U16": ([128, 128], "float16"), "I16": ([128, 128], "float16"), "If": ([128, 128], "float32"),
+    "S1": ([128, 48], "float32"), "S2": ([128, 48], "float32"), "sA": ([128, 48], "float32"), "sC": ([128, 49], "float32"), "Ms": ([128, 8], "float32"),
+    "R1c": ([128, 144], "float32"), "scC": ([128, 192], "float32"), "scD": ([128, 112], "float32"), "I1k": ([128, 128], "float16"),
+    "oKi": ([128, NK], "int32"), "oRi": ([128, 12], "float32"), "oT": ([128, 72], "uint16"),
+    "Rs": ([128, 224], "float32"), "cQ": ([128, 256], "float32"), "cD": ([128, 8], "bfloat16"), "bc": ([128, 128], "bfloat16"),
+    "cOw": ([128, NK], "float32"), "cO16": ([128, NK], "float16"), "cS": ([128, 8], "float32"),
+    "rk": ([128, 32], "int32"), "ci": ([128, NK], "int32"), "ti": ([128, NK], "int32"), "tf": ([128, NK], "float32"), "rkB": ([128, 8], "int32"),
+    "oh1": ([128, 192], "float16"), "ohA": ([128, 192], "float16"), "ex": ([128, NP], "float16"),
+    "scn": ([128, 64], "float32"), "zz": ([128, 64], "float32"), "mx": ([128, 56], "float32"),
+    "z1": ([128, 168], "float16"), "z2": ([128, 192], "float16"), "cnt": ([128, 8], "float16"), "PK": ([128, NP], "int32"),
+    "su1": ([128, NK], "uint16"), "suA": ([128, NK], "uint16"), "suB": ([128, 8], "uint16"),
+    "W1": ([128, WIN], "int32"), "W2": ([128, WIN], "int32"),
+    "sd": ([128, 112], "int32"), "yi1": ([128, 7, MSG], "int32"), "yi2": ([128, 7, MSG], "int32"), "yB": ([128, 112], "int32"),
+    "msg1": ([128, 7, MSG], "float16"), "msg2": ([128, 7, MSG], "float16"),
+    "land1": ([128, 7, MSG], "float16"), "land2": ([128, 7, MSG], "float16"),
+    "sBv": ([128, 8], "float32"), "sBg": ([128, 8], "float32"),
+    "out1": ([128, 8], "float32"), "out2": ([128, 8], "float32"), "rep1": ([128, 8], "float32"), "rep2": ([128, 8], "float32"),
+    "Lo": ([128, NK], "float32"), "wO": ([128, NK], "uint16"), "Lv": ([128, 8], "float32"), "Lv0": ([128, 8], "float32"),
+    "Ld": ([128, 8], "float32"), "wv": ([128, 8], "uint16"), "Lb": ([128, 8], "float32"), "wr": ([128, 8], "uint16"),
+    "smA": ([128, NK], "float32"), "smB": ([128, 8], "float32"), "vB": ([128, 8], "float32"), "exv": ([128, 112], "float32"),
+    "vW": ([128, 120], "float32"), "s1c": ([128, NK], "uint16"), "gv": ([128, NP], "float32"), "sv": ([128, NP], "float32"),
+    "vO": ([128, NK], "float32"), "vt": ([128, NK], "int32"), "tau": ([128, NK], "uint16"),
+    "Yb": ([128, NK], "float32"), "dW": ([128, 136], "float32"),
+    "hq1": ([128, PER, MSG], "float16"), "hq2": ([128, PER, MSG], "float16"), "hp1": ([128, PER], "float32"), "hp2": ([128, PER], "float32"),
+}
+for _t, _n in (("O", 384), ("V", 128), ("R", 128)):
+    _m = _n // 128 * 48
+    for _b, _w in (("pr", _n), ("pa", _n), ("u", _m + 8), ("k", _m), ("re", _m), ("e", _n)):
+        _sb[_b + _t] = ([128, _w], "float32")
+SCRATCH = {_k: ("sbuf", _v[0], _v[1]) for _k, _v in _sb.items()}
+PSUM = ("oK", "oP", "vK", "vP", "vL", "rA", "rB", "rC")
+for _k in PSUM:
+    SCRATCH[_k] = ("psum", [128, 512], "float32")
+SEMAPHORES = ["sV", "sS", "sT", "sG", "ldA", "ldP", "ldB", "ldC", "st", "rq1", "rq2", "rp1", "rp2", "hq1", "hq2", "hp1", "hp2", "loc"]
+
+FLY = (9, 6.5, 6, 5)
+WAKE, SLACK, SLACK2 = 0.1, 0.1, 0.1
+P_O1, P_O2, P_A, P_O3, P_R, P_C = 2, 2, 1, 5, 4, 4
+
+
+def wiring(T, topo, core):
+    others = [c for c in T.cores if c != core]
+    cross = [c for c in others if not topo.may_write(core, c)]
+    direct = [c for c in others if topo.may_write(core, c)]
+    rel = [c for c in topo.cores_of(core) if c not in T.cores and all(topo.may_write(c, d) for d in cross)]
+    rel.sort(key=lambda c: (topo.die(c) != topo.die(core), c))
+    return cross, direct, rel[:N_REL]
+
+
+def emask(engs):
+    return sum(1 << e for e in engs)
+
+
+def place_of(T, topo, owner, dst):
+    cross, direct, rel = wiring(T, topo, dst)
+    return (cross + direct).index(owner)
+
+
+def relay_program(g, core, T, topo, owner):
+    cross, direct, rel = wiring(T, topo, owner)
+    k = rel.index(core)
+    dsts = cross[PER * k:PER * k + PER]
+    n = 0
+    for src, dname, sem_out, req in (("hq1", "land1", "rq1", True), ("hp1", "rep1", "rp1", False),
+                                     ("hq2", "land2", "rq2", True), ("hp2", "rep2", "rp2", False)):
+        g.wait_ge(T.sem[src], ENG_HOP)
+        trs = []
+        for i, d in enumerate(dsts):
+            rid, pid = topo.addr(d, core)
+            es = topo.engines(core, d)[ENG_OUT * i:ENG_OUT * i + ENG_OUT]
+            at = place_of(T, topo, owner, d)
+            if req:
+                s_ap, d_ap = T[src][:, i, :], T[dname][:, at, :]
+            else:
+                s_ap, d_ap = T[src][:, i:i + 1], T[dname][:, at:at + 1]
+            trs.append(RemoteDMATransfer(dst_ids=[DstId(rid=rid, pnc=pid)], dma_engine_mask=emask(es), remote_sem=T.sem[sem_out],
+                                         src=s_ap, dst=d_ap))
+            n += len(es)
+        g.remote_dma_fused(trs, local_sem=T.sem.loc)
+    g.wait_ge(T.sem.loc, n)
+
+
+def plan(tasks):
+    n = len(tasks)
+    fin, free, order, ready = {}, {}, {}, {}
+    pre = [t["deps"] | t["odeps"] | ({t["aft"][0]} if t["aft"] else set()) for t in tasks]
+    pend = [len(x) for x in pre]
+    succ = [[] for _ in tasks]
+    for i, x in enumerate(pre):
+        for d in x:
+            succ[d].append(i)
+    tail = [0.0] * n
+    for i in range(n - 1, -1, -1):
+        tail[i] = tasks[i]["cost"] + WAKE + max([0.0] + [tail[x] for x in succ[i] if tasks[x]["prio"] <= tasks[i]["prio"]])
+
+    def enter(i):
+        t = tasks[i]
+        e = max([0.0] + [fin[d] + WAKE for d in t["deps"]] + [fin[d] for d in t["odeps"]])
+        if t["aft"]:
+            e = max(e, fin[t["aft"][0]] + t["aft"][1])
+        ready.setdefault(t["q"], {})[i] = e
+    for i in range(n):
+        if pend[i] == 0:
+            enter(i)
+    while len(fin) < n:
+        m, q = min((max(free.get(q, 0.0), min(l.values())), q) for q, l in ready.items() if l)
+        l, fr = ready[q], free.get(q, 0.0)
+        st = {i: max(fr, e) for i, e in l.items()}
+        pick = min(l, key=lambda i: (tasks[i]["prio"], max(st[i] - m - SLACK, 0.0), -tail[i], i))
+        if st[pick] > m + SLACK:
+            fits = [i for i in l if st[i] + tasks[i]["cost"] <= st[pick] + SLACK2]
+            now = [i for i in fits if st[i] <= m + SLACK]
+            if now:
+                pick = min(now, key=lambda i: (tasks[i]["prio"], -tail[i], i))
+            elif fits:
+                pick = min(fits, key=lambda i: (st[i], tasks[i]["prio"], i))
+        fin[pick] = st[pick] + tasks[pick]["cost"]
+        free[q] = fin[pick]
+        fin[pick] += tasks[pick]["lat"]
+        order.setdefault(q, []).append(pick)
+        del l[pick]
+        for x in succ[pick]:
+            pend[x] -= 1
+            if pend[x] == 0:
+                enter(x)
+    return order
+
+
+def runs(v):
+    out, i = [], 0
+    while i < len(v):
+        j, st = i + 1, (v[i + 1] - v[i] if i + 1 < len(v) else 0)
+        while j < len(v) and v[j] - v[j - 1] == st:
+            j += 1
+        out.append((i, j - i, v[i], st if j - i > 1 else 0))
+        i = j
+    return out
+
+
+def rank_program(g, core, T, topo):
+    rank = T.rank_of(core)
+    if rank is None:
+        for c in T.cores:
+            if c in topo.cores_of(core) and core in wiring(T, topo, c)[2]:
+                relay_program(g, core, T, topo, c)
+        return
+    cross, direct, rel = wiring(T, topo, core)
+    prank = [T.cores.index(c) for c in cross + direct]
+    base = NT * rank
+    SH = base - LO
+    tasks, wr, rd = [], {}, {}
+    V, S, E = g.vector, g.scalar, g.tensor
+    cy = 0.00083
+
+    def add(q, fn, reads, writes, cost, prio=1, ext=(), aft=None):
+        i = len(tasks)
+        deps, odeps = set(), set()
+        for b in reads:
+            if b in wr:
+                deps.add(wr[b])
+            if b in PSUM:
+                deps.update(x for x in rd.get(b, ()) if tasks[x]["q"] != q)
+        for b in writes:
+            if b in wr:
+                (odeps if q == "T" and tasks[wr[b]]["q"] == "T" else deps).add(wr[b])
+            deps.update(rd.get(b, ()))
+        tasks.append(dict(q=q, fn=fn, deps=deps, odeps=odeps, cost=cost, prio=prio, ext=tuple(ext), aft=aft, dma=None, lat=0.0))
+        for b in reads:
+            rd.setdefault(b, []).append(i)
+        for b in writes:
+            wr[b] = i
+            rd[b] = []
+        return i
+
+    def vop(fn, reads, writes, n, prio=1, ext=(), aft=None, f=1.0):
+        return add("V", lambda: [fn()], reads, writes, (0.02 if f == int(f) else 0.07) + 1.2 * cy * max(64, n * f), prio, ext, aft)
+
+    def ts(out, on, in0, inn, s1, s2, op0, op1=None, n=24, prio=1, ext=(), aft=None, extra=()):
+        if op1 is None:
+            return vop(lambda: V.tensor_scalar(out, in0, s1, None, op0), [inn] + list(extra), [on], n, prio, ext, aft)
+        return vop(lambda: V.tensor_scalar(out, in0, s1, s2, op0, op1), [inn] + list(extra), [on], n, prio, ext, aft)
+
+    def tt(out, on, in0, n0, in1, n1, op, n=24, prio=1, ext=(), aft=None, extra=(), f=1.0):
+        return vop(lambda: V.tensor_tensor(out, in0, in1, op), [n0, n1] + list(extra), [on], n, prio, ext, aft, f)
+
+    def cp(out, on, in_, inn, n=24, prio=1, extra=(), f=1.0):
+        return vop(lambda: V.tensor_copy(out, in_), [inn] + list(extra), [on], n, prio, f=f)
+
+    def fill(ap, on, v, n, prio=1):
+        return vop(lambda: V.memset(ap, v), [], [on], n, prio)
+
+    def act(out, on, in_, inn, n, prio=1, **kw):
+        return add("S", lambda: [S.activation(out, in_, F.Copy, **kw)], inn, [on], 0.03 + 1.2 * cy * max(64, n), prio)
+
+    def iota(ap, on, pat, b, ch, n, prio=1, fl=True):
+        if fl:
+            return add("G", lambda: [g.iota(ap, pat, b, ch, allow_small_or_imprecise_dtypes=True)], [], [on], 0.15 + 2.2 * cy * n, prio)
+        return add("G", lambda: [g.iota(ap, pat, b, ch)], [], [on], 0.15 + 2.2 * cy * n, prio)
+
+    def gfill(ap, on, v, n, prio=1):
+        return iota(ap, on, [[0, n]], v, 0, n, prio)
+
+    def mm(lst, reads, bank, prio=1):
+        c = sum((0.03 + 0.0008 * max(64, n) * (4 if f4 else 1)) for (_, n, f4) in lst)
+        return add("T", lambda: [E.matmul(*a) for (a, n, f4) in lst], reads, [bank], c, prio)
+
+    loads = {}
+
+    def load(q, sem, fn, cnt, deps, writes, cost, lat, prio=0):
+        i = add(q, fn, deps, writes, cost, prio)
+        tasks[i]["dma"] = sem
+        tasks[i]["lat"] = lat
+        loads[sem] = loads.get(sem, 0) + 16 * cnt
+        return i
+
+    def ld_pts(q, fs):
+        return [q.dma_start(T.X[4 * f + i:128:16, :], T.pts[i:24:3, :]) for f in fs for i in range(3)]
+
+    fill(T.bc[:, 0:128], "one", 1.0, 64, -10)
+    fill(T.x1[:], "x1", 1, NK, -9)
+    load("Y", "ldA", lambda: [g.sync.dma_start(T.L0[:], T.tet0[:])], 1, [], ["L0"], 0.1, 2.0, -9)
+    load("Y", "ldP", lambda: ld_pts(g.sync, (0, 1)) + [g.sync.dma_start(T.X[4 * f + 3:128:16, :], T.x1[:]) for f in range(4)],
+         10, ["x1"], ["Xa"], 1.0, 2.0)
+    load("S", "ldP", lambda: ld_pts(g.scalar, (2, 3)), 6, [], ["X"], 0.6, 2.5)
+    load("Y", "ldB", lambda: [g.sync.dma_start(T.PW[16 * k:16 * k + 16, LO:HI], T.planes[:]) for k in range(8)], 8, [], ["PW"], 0.8, 4.0)
+
+    iota(T.pi[:], "pi", [[0, 4]], 0, 1, 4, -9, False)
+    iota(T.md16[:], "md16", [[1, 8], [0, 16]], 0, 0, 128, -9)
+    iota(T.oRi[:], "oRi", [[0, 4], [-8, 3]], 16, 0, 12, -8)
+    iota(T.mk[:], "mk", [[1, 128]], 0, -1, 128, -7)
+    iota(T.oKi[:], "oKi", [[1, 24]], 0, 0, 24, -4, False)
+    iota(T.jm[:, 0:128], "jm", [[0, 8], [1, 16]], 0, 0, 128, -5)
+    iota(T.cOw[:], "cOw", [[16, 24]], 128, 1, 24, -3)
+    iota(T.cD[:, 0:7], "cD", [[16, 7]], -1, 0, 7, -2)
+    gfill(T.Rs[:, 0:168], "Rs", 1, 168, -1)
+    gfill(T.Rs[:, 0:168:24], "Rs", 0, 7, -1)
+    CQ, CQB, CS = [], [], []
+    for k, v in enumerate(prank + [rank]):
+        act(T.cQ[:, 24 * k:24 * k + 24], "cQ%d" % k, T.bc[:, 0:24], ["one"], 24, -8, scale=0.0, bias=float(v))
+        CQ.append("cQ%d" % k)
+    iota(T.NB[:], "NB", [[1, PWID]], SH, 0, PWID, 1, False)
+    load("S", "ldC", lambda: [g.scalar.dma_start(T.NB[16 * k:16 * k + 16:4, LO:HI], T.nbr[:]) for k in range(8)], 8, [], ["NB"], 0.8, 3.5)
+    iota(T.S1[:], "S1", [[8, 8], [1, 6]], -1, 0, 48, 1)
+    iota(T.sA[:], "sA", [[32, 8], [4, 6]], -4, 0, 48, 1)
+    iota(T.sC[:, 1:49], "sC", [[32, 8], [0, 6]], 1, 0, 48, 1)
+    gfill(T.sC[:, 0:1], "sC0", 0, 1, 1)
+    iota(T.Ms[:], "Ms", [[1, 8]], 0, 0, 8, 1)
+    gfill(T.R1c[:], "R1c", -BIG, 144, 1)
+    gfill(T.R1c[:, 5:144:6], "R1c", BIG, 24, 1)
+    for s, n, a, st in runs(prank + [rank]):
+        iota(T.cQ[:, 192 + 8 * s:192 + 8 * (s + n)], "cQB%d" % s, [[st, n], [0, 8]], a, 0, 8 * n, 4)
+        CQB.append("cQB%d" % s)
+    for s, n, a, st in runs(prank):
+        iota(T.cS[:, s:s + n], "cS%d" % s, [[NT * st, n]], NT * a - SH, 0, n, 4)
+        CS.append("cS%d" % s)
+
+    ones = T.bc[0:1, 0:128]
+    iota(T.W1[:, 0:112], "W1", [[0, 112]], NONE, 0, 112, 0, False)
+    gfill(T.PW[:, 0:LO], "PW0", 0, 8, 2)
+    gfill(T.PW[:, HI:PWID], "PW1", 0, 8, 2)
+    ts(T.pj[:, 0:1], "pj0", T.pi[:, 0:1], "pi", 15, None, A.bitwise_and, n=1, prio=-7)
+    ts(T.pj[:, 1:2], "pj1", T.pi[:, 0:1], "pi", 4, None, A.arith_shift_right, n=1, prio=-7)
+    ts(T.pj[:, 2:3], "pj2", T.pi[:, 0:1], "pi", 2, None, A.arith_shift_right, n=1, prio=-7)
+    vop(lambda: V.tensor_copy(T.pf[:, 0:3], T.pj[:, 0:3]), ["pj0", "pj1", "pj2"], ["pf"], 3, -7)
+    p16, pg, p4, p8, p32, pK = [T.pf[:, k:k + 1] for k in range(6)]
+    oK, oE, oR, oB8 = T.oT[:, 0:24], T.oT[:, 24:48], T.oT[:, 48:60], T.oT[:, 64:68]
+    ts(oR, "oR", T.oRi[:], "oRi", p16, None, A.add, n=12, prio=-6, extra=["pf"])
+    ts(T.G16[:], "G16", T.md16[:], "md16", pg, None, A.is_equal, n=128, prio=-3, extra=["pf"])
+    ts(T.I16[:], "I16", T.mk[:], "mk", 0.0, None, A.is_equal, n=128, prio=-1)
+    cp(T.If[:], "If", T.I16[:], "I16", 128, 2)
+    ts(T.mk[:], "mk", T.mk[:], "mk", 0.0, -1.0, A.is_lt, A.mult, n=128, prio=0)
+    tt(T.U16[:], "U16", T.mk[:], "mk", T.G16[:], "G16", A.mult, n=128, prio=0, f=2)
+    cp(T.cO16[:], "cO16", T.cOw[:], "cOw", 24, -1)
+    cp(oK, "oK", T.oKi[:], "oKi", 24, -1)
+    ts(T.m16[:, 0:128], "m16", T.jm[:], "jm", p16, None, A.is_equal, n=64, prio=-1, extra=["pf"])
+    act(T.m16[:, 128:256], "m16b", T.m16[:, 0:128], ["m16"], 128, -1)
+    act(T.m16[:, 256:384], "m16c", T.m16[:, 0:128], ["m16"], 128, -1)
+    M16 = ["m16", "m16b", "m16c"]
+    ts(T.G2k[:], "G2k", T.md16[:], "md16", pg, 2048.0, A.is_equal, A.mult, n=128, prio=-1, extra=["pf"])
+    gfill(T.scD[:, 0:1], "scD0", 0, 1, 0)
+    act(T.scC[:, 0:112], "scC", T.m16[:, 0:112], ["m16"], 112, 0, scale=-float(BIG))
+    act(T.scD[:, 1:112], "scD", T.m16[:, 0:111], ["m16"], 112, 0, scale=float(MID))
+    tt(T.scC[:, 0:112], "scC", T.scC[:, 0:112], "scC", T.scD[:], "scD", A.add, n=112, prio=0, f=2, extra=["scD0"])
+    act(T.scC[:, 112:192], "scCb", T.scC[:, 0:80], ["scC"], 80, 5)
+
+    def slots(oh, ohn, M, co, cqn, rkw, rkn, offs, offn, rs, rsn, su, sun, prio, cnt=None):
+        n7, n8 = 7 * M, 8 * M
+        cq = T.cQ[:, co:co + n8]
+        z1, z2 = T.z1, T.z2
+        if cnt is None:
+            mm([((T.rB[:, n7:n8], T.I16[:], T.cO16[:, 0:M], True, True), M, 0)], ["I16", "cO16"], "rB", prio)
+        vop(lambda: V.tensor_tensor(oh[:, 0:n8], rkw.indirect(offs), cq, A.is_equal), rkn + offn + cqn, [ohn], n8, prio, f=1.5)
+        if cnt is not None:
+            mm([((T.rA[:, 0:n7], T.G16[:], oh[:, 0:n7], True, False), n7, 0), ((T.rA[:, 0:n7:M], T.I16[:], cnt, False, True), 7, 0)],
+               ["G16", ohn, "I16", "cnt"], "rA", prio)
+            mm([((T.rB[:, 0:n8], T.I1k[:], oh[:, 0:n8], True, False), n8, 0), ((T.rB[:, 0:n7], T.U16[:], oh[:, 0:n7], False, False), n7, 0),
+                ((T.rB[:, n7:n8], T.I16[:], T.cO16[:, 0:M], False, True), M, 0)], ["I1k", "U16", "I16", "cO16", ohn], "rB", prio)
+            vop(lambda: V.tensor_tensor_scan(T.scn[:, 0:n7], rs, T.rA[:, 0:n7], 0.0, A.mult, A.add), [rsn, "rA"], ["scn"], n7, prio)
+            vop(lambda: V.tensor_tensor(T.zz[:, 0:n8], T.scn[:, 0:n8], T.rB[:, 0:n8], A.add), ["scn", "scnz", "rB"], ["zz"], n8, prio)
+            h = n8 // 2
+            tt(T.mx[:, 0:h], "mx0", T.zz[:, 0:h], "zz", T.zz[:, h:n8], "zz", A.max, n=h, prio=prio)
+            tt(T.mx[:, 32:32 + h // 2], "mx1", T.mx[:, 0:h // 2], "mx0", T.mx[:, h // 2:h], "mx0", A.max, n=h // 2, prio=prio)
+            tt(T.mx[:, 48:48 + M], "mx2", T.mx[:, 32:32 + M], "mx1", T.mx[:, 32 + M:32 + 2 * M], "mx1", A.max, n=M, prio=prio)
+            return ts(su[:, 0:M], sun, T.mx[:, 48:48 + M], "mx2", -1024.0, None, A.add, n=M, prio=prio)
+        mm([((T.rA[:, 0:n7], T.G16[:], oh[:, 0:n7], True, False), n7, 0), ((T.rA[:, 0:n7:M], ones, T.cD[0:1, 0:7], False, True), 7, 0)],
+           ["G16", ohn, "one", "cD"], "rA", prio)
+        mm([((T.rB[:, 0:n7], T.U16[:], oh[:, 0:n7], True, True), n7, 0)], ["U16", ohn], "rB", prio)
+        sc = T.rA[:, 256:256 + n7]
+        vop(lambda: V.tensor_tensor_scan(sc, rs, T.rA[:, 0:n7], 0.0, A.mult, A.add), [rsn, "rA"], ["sc"], n7, prio)
+        vop(lambda: V.tensor_tensor(z2[:, 0:n8], T.rB[:, 0:n8], oh[:, 0:n8], A.mult), ["rB", ohn], ["z2"], n8, prio)
+        vop(lambda: V.tensor_tensor(z1[:, 0:n7], sc, oh[:, 0:n7], A.mult), ["sc", "rA", ohn], ["z1"], n7, prio)
+        mm([((T.rB[:, 0:M], T.I16[:], z2[:, M * b:M * b + M], b == 0, False), M, 0) for b in range(8)], ["I16", "z2"], "rB", prio)
+        mm([((T.rB[:, 0:M], T.I16[:], z1[:, M * b:M * b + M], False, b == 6), M, 0) for b in range(7)], ["I16", "z1"], "rB", prio)
+        cp(su[:, 0:M], sun, T.rB[:, 0:M], "rB", M, prio)
+
+    def pack(xap, xn, tib, tin, k, prio):
+        n = 16 * k
+        vop(lambda: V.tensor_tensor(T.ex[:, 0:n], tib.indirect(T.oT[:, 0:k]), T.m16[:, 0:n], A.mult), [tin, "oK"] + M16, ["ex"], n, prio, f=1.6)
+        mm([((T.rC[:, 0:n], T.G2k[:], T.ex[:, 0:n], True, True), n, 0)], ["G2k", "ex"], "rC", prio)
+        tt(T.PK[:, 0:n], "PK", T.rC[:, 0:n], "rC", xap, xn, A.add, n=n, prio=prio)
+
+    def decode(W, wn, yi, yin, msg, msgn, prio):
+        vop(lambda: V.tensor_tensor_scan(T.sd[:], T.scC[:, 0:112], W[:, 0:112], 0.0, A.add, A.max), ["scC", wn], ["sd"], 112, prio)
+        ts(yi[:, :, 0:16], yin, W[:, 0:112], wn, 2047, None, A.bitwise_and, n=112, prio=prio)
+        ts(yi[:, :, 16], yin + "t", T.sd[:, 15:112:16], "sd", 11, 2047, A.arith_shift_right, A.bitwise_and, n=7, prio=prio)
+        cp(msg[:], msgn, yi[:], yin, 119, prio, extra=[yin + "t"])
+
+    nloc = [0]
+
+    def send(src, srcn, hname, dname, sem, req, prio):
+        def fn():
+            own8 = topo.engines(core, direct[0])
+            alle = topo.engines(core, rel[0])
+            hop = [e for e in alle if e not in own8]
+            if len(hop) < ENG_HOP * N_REL:
+                hop = hop + [e for e in alle if e in own8]
+            trs = []
+            for k, r in enumerate(rel):
+                rid, pid = topo.addr(r, core)
+                s_ap = src[:, PER * k:PER * k + PER, :] if req else src[:, PER * k:PER * k + PER]
+                es = hop[ENG_HOP * k:ENG_HOP * k + ENG_HOP]
+                trs.append(RemoteDMATransfer(dst_ids=[DstId(rid=rid, pnc=pid)], dma_engine_mask=emask(es), remote_sem=T.sem[hname],
+                                             src=s_ap, dst=T[hname][:]))
+                nloc[0] += len(es)
+            g.remote_dma_fused(trs, local_sem=T.sem.loc)
+            trs = []
+            for k, d in enumerate(direct):
+                rid, pid = topo.addr(d, core)
+                es = topo.engines(core, d)[ENG_DIR * k:ENG_DIR * k + ENG_DIR]
+                b, at = len(cross) + k, place_of(T, topo, core, d)
+                if req:
+                    s_ap, d_ap = src[:, b, :], T[dname][:, at, :]
+                else:
+                    s_ap, d_ap = src[:, b:b + 1], T[dname][:, at:at + 1]
+                trs.append(RemoteDMATransfer(dst_ids=[DstId(rid=rid, pnc=pid)], dma_engine_mask=emask(es), remote_sem=T.sem[sem],
+                                             src=s_ap, dst=d_ap))
+                nloc[0] += len(es)
+            g.remote_dma_fused(trs, local_sem=T.sem.loc)
+            return []
+        return add("G", fn, [srcn], [], 1.0, prio)
+    ARR = ENG_OUT * len(cross) + ENG_DIR * len(direct)
+
+    def step(t, k, X, xn, w, wn, L, Ln, bK, bP, bL, prio, last=None, Lacc=None, Laccn=None):
+        B = 3 if k == 24 else 1
+        m, kc = 48 * B, 8 * B
+        pr, pa, u, kp, re, e = [T[x + t] for x in ("pr", "pa", "u", "k", "re", "e")]
+        nm = lambda x: x + t
+        part = lambda x, q: x + t + ("" if B == 1 else "_%d" % q)
+        lo = 256 if bK == bL else 0
+        for q, (a, z) in enumerate(((0, 16), (16, 24)) if B == 3 else ((0, k),)):
+            vop(lambda a=a, z=z: V.tensor_tensor(pr[:, 16 * a:16 * z], T.PW[:].indirect(w[:, a:z]), X[:, 16 * a:16 * z], A.mult),
+                ["PW", "PW0", "PW1", wn, xn], [part("pr", q)], 16 * (z - a), prio, f=1.6)
+            add("S", lambda a=a, z=z: [S.activation(pa[:, 16 * a:16 * z], T.ND[:].indirect(w[:, a:z]), F.Copy)], ["ND", wn], [part("pa", q)],
+                0.1 + 1.8 * cy * 16 * (z - a), prio)
+        for b in range(B):
+            first = mm([((T[bK][:, 48 * b:48 * b + 48], pr[:, 128 * b:128 * b + 128], T.S1[:], True, True), 48, 1)],
+                       [part("pr", b // 2), "S1"], bK, prio)
+        for b in range(B):
+            second = mm([((T[bP][:, 48 * b:48 * b + 48], pa[:, 128 * b:128 * b + 128], T.S2[:], True, True), 48, 1)],
+                        [part("pa", b // 2), "S2"], bP, prio)
+        if B == 1:
+            tasks[second]["odeps"].add(first)
+        Li, Lin = (L, Ln) if Lacc is None else (Lacc, Laccn)
+        il = lambda: mm([((T[bL][:, lo:lo + kc], T.If[:], Li[:, 0:kc], True, False), kc, 1)], ["If", Lin], bL, prio)
+        if bL != bK:
+            il()
+        vop(lambda: V.tensor_tensor_scan(u[:, 1:m + 1], T[bK][:, 0:m], T.R1c[:, 0:m], 0.0, A.min, A.max), ["R1c", bK], [nm("u")], m, prio)
+        vop(lambda: V.tensor_tensor(kp[:, 0:m], T[bK][:, 0:m], u[:, 0:m], A.is_ge), [bK, nm("u"), nm("u0")], [nm("k")], m, prio)
+        if bL == bK:
+            il()
+        vop(lambda: V.tensor_tensor_scan(re[:, 0:m], T[bP][:, 0:m], kp[:, 0:m], 0.0, A.add, A.mult), [nm("k"), bP], [nm("re")], m, prio)
+        for q, (a, z) in enumerate(((0, 16), (16, 24)) if B == 3 else ((0, 8),)):
+            vop(lambda a=a, z=z: V.tensor_tensor(e[:, 16 * a:16 * z], re[:, 0:m].indirect(T.oT[:, 24 + a:24 + z]), T.m16[:, 16 * a:16 * z], A.mult),
+                [nm("re"), "oE"] + M16, [part("e", q)], 16 * (z - a), prio, f=1.6)
+        for b in range(B):
+            mm([((T[bL][:, lo + 8 * b:lo + 8 * b + 8], e[:, 128 * b:128 * b + 128], T.Ms[:], False, b == B - 1), 8, 1)],
+               [part("e", b // 2), "Ms"], bL, prio)
+        if last is not None:
+            cp(last[0][:, 0:k], last[1], T[bL][:, lo:lo + k], bL, k, prio)
+        else:
+            ts(w[:, 0:k], wn, T[bL][:, lo:lo + k], bL, 0.0, float(HI), A.max, A.min, n=k, prio=prio)
+            act(L[:, 0:kc], Ln, T[bL][:, lo:lo + kc], [bL], kc, prio)
+
+    ts(T.rk[:, 16:32], "rka", T.L0[:, 0:16], "L0", 10, None, A.arith_shift_right, prio=-4)
+    ts(T.rk[:, 0:16], "rkb", T.L0[:, 8:24], "L0", 10, None, A.arith_shift_right, prio=-4)
+    RK = ["rka", "rkb"]
+    slots(T.oh1, "oh1", 24, 0, CQ, T.rk[:, 0:32], RK, oR, ["oR"], T.Rs[:, 0:168], "Rs", T.su1, "su1", 0)
+    ts(T.ti[:], "ti", T.L0[:], "L0", 1023, None, A.bitwise_and, prio=0)
+    ts(T.tf[:], "tf", T.ti[:], "ti", 0.5, None, A.add, prio=0)
+    pack(T.X[:], "X", T.tf[:], "tf", 24, 0)
+    cp(T.W1[:].indirect(T.su1[:]), "W1", T.PK[:], "PK", NP, 0, extra=["su1"], f=3.5)
+    decode(T.W1, "W1", T.yi1, "yi1", T.msg1, "msg1", 0)
+    s1 = send(T.msg1, "msg1", "hq1", "land1", "rq1", True, 0)
+
+    ts(p8, "p8", pg, "pf", 4.0, p4, A.mult, A.add, n=1, prio=2)
+    ts(p32, "p32", pg, "pf", 32.0, p16, A.mult, A.add, n=1, prio=2)
+    ts(T.S1[:], "S1", T.S1[:], "S1", p8, None, A.is_equal, n=48, prio=2, extra=["p8"])
+    ts(T.sA[:], "sA", T.sA[:], "sA", p32, None, A.is_equal, n=48, prio=2, extra=["p32"])
+    ts(T.sC[:, 1:49], "sC", T.sC[:, 1:49], "sC", p32, None, A.is_equal, n=48, prio=2, extra=["p32"])
+    fill(T.sC[:, 1:49:6], "sC", 0.0, 8, 2)
+    fill(T.sC[:, 6:49:6], "sC", 0.0, 8, 2)
+    tt(T.sC[:, 1:49], "sC", T.sA[:], "sA", T.sC[:, 1:49], "sC", A.subtract, n=48, prio=2)
+    tt(T.S2[:], "S2", T.sC[:, 0:48], "sC", T.sC[:, 1:49], "sC", A.subtract, n=48, prio=2, extra=["sC0"])
+    ts(T.Ms[:], "Ms", T.Ms[:], "Ms", pg, None, A.is_equal, n=8, prio=2, extra=["pf"])
+    ts(oE, "oE", T.oKi[:], "oKi", 6.0, 5.0, A.mult, A.add, n=24, prio=2)
+    act(T.Rd[:, 0:128], "Rd", T.jm[:], ["jm"], 128, 5)
+    ts(T.Rd[:, 0:128], "Rd", T.Rd[:, 0:128], "Rd", 1.0, None, A.min, n=128, prio=5)
+    act(T.Rd[:, 128:256], "Rdb", T.Rd[:, 0:128], ["Rd"], 128, 5)
+    act(T.Rd[:, 256:384], "Rdc", T.Rd[:, 0:128], ["Rd"], 128, 5)
+    ts(T.I1k[:], "I1k", T.I16[:], "I16", 1024.0, None, A.mult, n=64, prio=4)
+    gfill(T.scn[:, 56:64], "scnz", 0, 8, 4)
+    for t in ("O", "V", "R"):
+        gfill(T["u" + t][:, 0:1], "u0" + t, BIG, 1, 2)
+    for t in ("V", "R"):
+        gfill(T["pr" + t][:, 112:128], "pr" + t, 0, 16, 2)
+        gfill(T["pa" + t][:, 112:128], "pa" + t, 0, 16, 2)
+    gfill(T.Lv[:, 7:8], "Lv", 0, 1, 2)
+    gfill(T.Lv0[:, 7:8], "Lv0", 0, 1, 2)
+    cp(T.ND[:], "ND", T.NB[:], "NB", PWID, 2)
+    ts(T.Lo[:], "Lo", T.L0[:], "L0", float(-SH) - DEAD, None, A.add, prio=2)
+    tt(T.Lo[:], "Lo", T.Lo[:], "Lo", T.oh1[:, 168:192], "oh1", A.mult, prio=2)
+    ts(T.Lo[:], "Lo", T.Lo[:], "Lo", DEAD, None, A.add, prio=2)
+    ts(T.wO[:], "wO", T.Lo[:], "Lo", 0.0, float(HI), A.max, A.min, prio=2)
+    own = lambda pr: step("O", 24, T.X, "X", T.wO, "wO", T.Lo, "Lo", "oK", "oP", "oK", pr)
+    own(P_O1)
+
+    def visitors(land, ln, out, outn, sem, sent, fly):
+        add("V", lambda: [V.tensor_scalar(T.wv[:, 0:7], land[:, :, 16], 8.0, None, A.add)], [], ["wv", ln], 0.08, 0, [(sem, ARR)], (sent, fly))
+        ts(T.Xv[:], "Xv", land[:, :, 0:16], ln, -1024.0, None, A.add, n=112, prio=0)
+        add("V", lambda: [V.tensor_scalar(T.Lv0[:, 0:7], land[:, :, 16], 8.0, None, A.add)], [ln], ["Lv0"], 0.08, 1)
+        act(T.Lv[:, 0:7], "Lv", T.Lv0[:, 0:7], ["Lv0"], 7, 1)
+        a = (7, T.Xv, "Xv", T.wv, "wv", T.Lv, "Lv", "vK", "vP", "vL", 0)
+        step("V", *a)
+        step("V", *a)
+        tt(T.Ld[:], "Ld", T.Lv[:], "Lv", T.Lv0[:], "Lv0", A.subtract, n=8, prio=0)
+        step("V", *a, last=(out, outn), Lacc=T.Ld, Laccn="Ld")
+
+    visitors(T.land1, "land1", T.out1, "out1", "rq1", s1, FLY[0])
+    s2 = send(T.out1, "out1", "hp1", "rep1", "rp1", False, 0)
+
+    ts(T.sBv[:, 0:7], "sBv", T.yi1[:, :, 16], "yi1t", -DEAD, None, A.add, n=7, prio=4)
+    tt(T.sBv[:, 0:7], "sBv", T.sBv[:, 0:7], "sBv", T.cS[:, 0:7], CS[0], A.add, n=7, prio=4, extra=CS[1:])
+    ts(T.sBg[:, 0:7], "sBg", T.yi1[:, :, 16], "yi1t", float(NT), None, A.is_lt, n=7, prio=4)
+    tt(T.sBv[:, 0:7], "sBv", T.sBv[:, 0:7], "sBv", T.sBg[:, 0:7], "sBg", A.mult, n=7, prio=4)
+    ts(T.sBv[:, 0:7], "sBv", T.sBv[:, 0:7], "sBv", DEAD, None, A.add, n=7, prio=4)
+    cp(T.yB[:], "yB", T.yi1[:, :, 0:16], "yi1", 112, 4)
+    ts(T.xB[:], "xB", T.yi1[:, :, 0:16], "yi1", -1024.0, None, A.add, n=112, prio=5)
+    gfill(T.W2[:, 0:112], "W2", NONE, 112, 3)
+    gfill(T.Rs[:, 168:224], "RsB", 1, 56, 4)
+    gfill(T.Rs[:, 168:224:8], "RsB", 0, 7, 4)
+    gfill(T.rkB[:, 7:8], "rkB", rank, 1, 4)
+    fill(T.Lb[:, 7:8], "Lb", DEAD, 1, 4)
+    ts(T.pj[:, 4:8], "pj4", T.pi[:], "pi", 7, None, A.bitwise_and, n=4, prio=4)
+    cp(oB8, "oB8", T.pj[:, 4:8], "pj4", 4, 4)
+    own(P_O2)
+    own(P_O2)
+
+    RKC = (SH - 511.1875) / 1024.0
+    ts(T.rk[:, 16:32], "rka", T.Lo[:, 0:16], "Lo", 1.0 / 1024, RKC, A.mult, A.add, prio=P_A)
+    ts(T.rk[:, 0:16], "rkb", T.Lo[:, 8:24], "Lo", 1.0 / 1024, RKC, A.mult, A.add, prio=P_A)
+    ts(T.ci[:], "ci", T.Lo[:], "Lo", float(SH), None, A.add, prio=P_A)
+    ts(T.ti[:], "ti", T.ci[:], "ci", 1023, None, A.bitwise_and, prio=P_A)
+    ts(T.tf[:], "tf", T.ti[:], "ti", 0.5, None, A.add, prio=P_A)
+    slots(T.ohA, "ohA", 24, 0, CQ, T.rk[:, 0:32], RK, oR, ["oR"], T.Rs[:, 0:168], "Rs", T.suA, "suA", P_A)
+    cp(T.cnt[:, 0:7], "cnt", T.rA[:, 279:424:24], "rA", 7, P_A, extra=["sc"])
+    pack(T.X[:], "X", T.tf[:], "tf", 24, P_A)
+    cp(T.W2[:].indirect(T.suA[:]), "W2", T.PK[:], "PK", NP, P_A, extra=["suA"], f=3.5)
+
+    vop(lambda: V.tensor_tensor(T.Lb[:, 0:7], T.sBv[:, 0:7], T.rep1[:, 0:7], A.add), ["sBv"], ["Lb"], 7, 0, [("rp1", ARR)], (s2, FLY[1]))
+    ts(T.rkB[:, 0:7], "rkB", T.Lb[:, 0:7], "Lb", 1.0 / 1024, RKC, A.mult, A.add, n=7, prio=0)
+    ts(T.ci[:, 0:7], "ci", T.Lb[:, 0:7], "Lb", float(SH), None, A.add, n=7, prio=0)
+    ts(T.ti[:, 0:7], "ti", T.ci[:, 0:7], "ci", 1023, None, A.bitwise_and, n=7, prio=0)
+    slots(T.ohA, "ohA", 8, 192, CQB, T.rkB[:], ["rkB"], oB8, ["oB8"], T.Rs[:, 168:224], "RsB", T.suB, "suB", 0, cnt=T.cnt[:, 0:7])
+    pack(T.yB[:], "yB", T.ti[:, 0:8], "ti", 7, 0)
+    cp(T.W2[:].indirect(T.suB[:, 0:7]), "W2", T.PK[:, 0:112], "PK", 112, 0, extra=["suB"], f=3.5)
+    decode(T.W2, "W2", T.yi2, "yi2", T.msg2, "msg2", 0)
+    s3 = send(T.msg2, "msg2", "hq2", "land2", "rq2", True, 0)
+
+    ts(T.wr[:, 0:7], "wr", T.Lb[:, 0:7], "Lb", 0.0, float(HI), A.max, A.min, n=7, prio=P_C)
+    cp(T.Gf[:], "Gf", T.G16[:], "G16", 128, P_C)
+    gfill(T.vW[:, 112:120], "vW", 0, 8, 4)
+    gfill(T.dW[:, 112:136], "dW0", 8192, 24, 4)
+    ts(pK, "pK", p16, "pf", 14.5, -float(MID), A.is_lt, A.mult, n=1, prio=5)
+    for _ in range(3):
+        step("R", 7, T.xB, "xB", T.wr, "wr", T.Lb, "Lb", "rA", "rB", "rC", P_R)
+        own(P_O3)
+    visitors(T.land2, "land2", T.out2, "out2", "rq2", s3, FLY[2])
+    s4 = send(T.out2, "out2", "hp2", "rep2", "rp2", False, 0)
+
+    ts(T.s1c[:], "s1c", T.su1[:], "su1", 112.0, None, A.min, prio=P_C)
+    ts(T.smA[:], "smA", T.suA[:], "suA", 128.0, None, A.min, prio=P_C)
+    ts(T.smB[:, 0:7], "smB", T.suB[:, 0:7], "suB", 128.0, None, A.min, n=7, prio=P_C)
+    ts(T.vB[:, 0:7], "vB", T.Lb[:, 0:7], "Lb", 8192.0, 256.0, A.add, A.mult, n=7, prio=P_C)
+    tt(T.vB[:, 0:7], "vB", T.vB[:, 0:7], "vB", T.smB[:, 0:7], "smB", A.add, n=7, prio=P_C)
+    vop(lambda: V.tensor_tensor(T.exv[:], T.vB[:, 0:7].indirect(T.oT[:, 0:7]), T.m16[:, 0:112], A.mult), ["vB", "oK"] + M16, ["exv"], 112, P_C, f=1.6)
+    mm([((T.rC[:, 0:112], T.Gf[:], T.exv[:], True, True), 112, 1)], ["Gf", "exv"], "rC", P_C)
+    cp(T.vW[:, 0:112], "vW", T.rC[:, 0:112], "rC", 112, P_C)
+    vop(lambda: V.tensor_tensor(T.gv[:], T.vW[:].indirect(T.s1c[:]), T.m16[:], A.mult), ["vW", "s1c"] + M16, ["gv", "gvb"], NP, P_C, f=1.6)
+    vop(lambda: V.tensor_tensor_scan(T.sv[:], T.Rd[:], T.gv[:], 0.0, A.mult, A.add), ["Rd", "Rdb", "Rdc", "gv", "gvb"], ["sv", "svb"], NP, P_C)
+    ts(T.vO[:], "vO", T.Lo[:], "Lo", 8192.0, 256.0, A.add, A.mult, prio=P_C)
+    tt(T.vO[:], "vO", T.vO[:], "vO", T.smA[:], "smA", A.add, prio=P_C)
+    tt(T.vO[:], "vO", T.vO[:], "vO", T.oh1[:, 168:192], "oh1", A.mult, prio=P_C)
+    tt(T.vt[:], "vt", T.vO[:], "vO", T.sv[:, 15:NP:16], "sv", A.add, prio=P_C, extra=["svb"])
+    ts(T.ci[:], "ci", T.vt[:], "vt", 255, None, A.bitwise_and, prio=P_C)
+    cp(T.tau[:], "tau", T.ci[:], "ci", 24, P_C)
+    ts(T.vt[:], "vt", T.vt[:], "vt", 8, None, A.arith_shift_right, prio=P_C)
+    ts(T.Yb[:], "Yb", T.vt[:], "vt", float(SH - 16384), pK, A.add, A.add, prio=P_C, extra=["pK"])
+
+    vop(lambda: V.tensor_tensor(T.exv[:], T.rep2[:, 0:7].indirect(T.oT[:, 0:7]), T.m16[:, 0:112], A.mult), ["oK"] + M16, ["exv"], 112, 0,
+        [("rp2", ARR)], (s4, FLY[3]), f=1.6)
+    mm([((T.rC[:, 0:112], T.Gf[:], T.exv[:], True, True), 112, 1)], ["Gf", "exv"], "rC", 0)
+    ts(T.dW[:, 0:112], "dW", T.rC[:, 0:112], "rC", 8192.0, None, A.add, n=112, prio=0)
+    add("S", lambda: [S.activation(T.gv[:, 192:NP], T.dW[:].indirect(T.tau[:, 12:24]), F.Copy)], ["dW", "dW0", "tau"], ["gvb"], 0.4, 0)
+    vop(lambda: V.tensor_copy(T.gv[:, 0:192], T.dW[:].indirect(T.tau[:, 0:12])), ["dW", "dW0", "tau"], ["gv"], 192, 0, f=1.6)
+    for h, n in ((0, ""), (192, "b")):
+        vop(lambda h=h: V.tensor_tensor_scan(T.sv[:, h:h + 192], T.scC[:], T.gv[:, h:h + 192], 0.0, A.add, A.max), ["scC", "scCb", "gv" + n], ["sv" + n], 192, 0)
+    tt(T.vO[:], "vO", T.sv[:, 15:NP:16], "sv", T.Yb[:], "Yb", A.add, prio=0, extra=["svb"])
+    load("Y", "st", lambda: [g.sync.dma_start(T.y[:], T.vO[:])], 1, ["vO"], [], 0.1, 0.0)
+
+    order = plan(tasks)
+    queue = {"V": V, "S": S, "T": E, "G": g, "Y": g.sync}
+    semof = {"V": "sV", "S": "sS", "T": "sT", "G": "sG"}
+    done, know, total = {}, {}, {}
+    ptr = {q: 0 for q in order}
+    known = {q: {} for q in order}
+    left = len(tasks)
+    while left:
+        before = left
+        for q in order:
+            while ptr[q] < len(order[q]):
+                i = order[q][ptr[q]]
+                t = tasks[i]
+                if any(d not in done for d in t["deps"]):
+                    break
+                kq = known[q]
+                for d in sorted(t["deps"], key=lambda d: (-len(know[d]), -done[d][1])):
+                    s, v = done[d]
+                    if s is None or kq.get(s, 0) >= v:
+                        continue
+                    v = max(done[x][1] for x in t["deps"] if done[x][0] == s)
+                    if any(done[x][0] not in (s, None) and know[x].get(s, 0) >= v and kq.get(done[x][0], 0) < done[x][1] for x in t["deps"]):
+                        continue
+                    queue[q].wait_ge(T.sem[s], v)
+                    for x in t["deps"]:
+                        if done[x][0] == s:
+                            for s2, v2 in know[x].items():
+                                kq[s2] = max(kq.get(s2, 0), v2)
+                    kq[s] = max(kq.get(s, 0), v)
+                for s, v in t["ext"]:
+                    if kq.get(s, 0) < v:
+                        queue[q].wait_ge(T.sem[s], v)
+                        kq[s] = v
+                ins = t["fn"]()
+                if t["dma"]:
+                    for x in ins:
+                        x.then_inc(T.sem[t["dma"]], 16)
+                    done[i] = (t["dma"], loads[t["dma"]])
+                elif not ins:
+                    done[i] = (None, 0)
+                else:
+                    s = semof[q]
+                    for x in ins:
+                        x.then_inc(T.sem[s], 1)
+                    total[s] = total.get(s, 0) + len(ins)
+                    done[i] = (s, total[s])
+                know[i] = dict(kq)
+                if done[i][0] is not None:
+                    know[i][done[i][0]] = done[i][1]
+                ptr[q] += 1
+                left -= 1
+        if left == before:
+            raise ValueError("the order can't be emitted")
+    for s, v in sorted(total.items()):
+        g.wait_ge(T.sem[s], v)
+    for s, v in loads.items():
+        g.wait_ge(T.sem[s], v)
+    for s in ("rq1", "rp1", "rq2", "rp2"):
+        g.wait_ge(T.sem[s], ARR)
+    g.wait_ge(T.sem.loc, nloc[0])

@@ -4,99 +4,95 @@ from concourse.mybir import AluOpType as A, ActivationFunctionType as F
 NT, NP, NK = 1024, 384, 24
 LO, HI, PWID = 8, 1032, 1040
 DEAD = 7.375
-MSG = 17
 WIN = 640
-BIG, MID = 8388608, 4194304
-NONE = (1 << 21) + 1024
-N_REL, ENG_HOP, ENG_OUT, ENG_DIR = 2, 4, 4, 2
-PER = 4 // N_REL
+BIG, K16, K4 = 8388608, 32768, 8192
+NONE = 4096
+HOLD = 2.0 ** 60
+GW, QW = 7, 896
 
 _sb = {
-    "X": ([128, NP], "int32"), "L0": ([128, NK], "int32"), "PW": ([128, PWID], "int32"), "NB": ([128, PWID], "int32"),
-    "ND": ([128, PWID], "float32"), "Xv": ([128, 112], "float32"), "xB": ([128, 112], "float32"),
-    "pi": ([128, 4], "int32"), "pj": ([128, 8], "int32"), "pf": ([128, 8], "float32"), "jm": ([128, 128], "bfloat16"), "x1": ([128, NK], "int32"),
-    "mk": ([128, 128], "float32"), "md16": ([128, 128], "float32"), "m16": ([128, NP], "bfloat16"), "Rd": ([128, NP], "float32"),
-    "G16": ([128, 128], "float16"), "G2k": ([128, 128], "float16"), "Gf": ([128, 128], "float32"),
-    "U16": ([128, 128], "float16"), "I16": ([128, 128], "float16"), "If": ([128, 128], "float32"),
-    "S1": ([128, 48], "float32"), "S2": ([128, 48], "float32"), "sA": ([128, 48], "float32"), "sC": ([128, 49], "float32"), "Ms": ([128, 8], "float32"),
-    "R1c": ([128, 144], "float32"), "scC": ([128, 192], "float32"), "scD": ([128, 112], "float32"), "I1k": ([128, 128], "float16"),
-    "oKi": ([128, NK], "int32"), "oRi": ([128, 12], "float32"), "oT": ([128, 72], "uint16"),
-    "Rs": ([128, 224], "float32"), "cQ": ([128, 256], "float32"), "cD": ([128, 8], "bfloat16"), "bc": ([128, 128], "bfloat16"),
-    "cOw": ([128, NK], "float32"), "cO16": ([128, NK], "float16"), "cS": ([128, 8], "float32"),
-    "rk": ([128, 32], "int32"), "ci": ([128, NK], "int32"), "ti": ([128, NK], "int32"), "tf": ([128, NK], "float32"), "rkB": ([128, 8], "int32"),
-    "oh1": ([128, 192], "float16"), "ohA": ([128, 192], "float16"), "ex": ([128, NP], "float16"),
-    "scn": ([128, 64], "float32"), "zz": ([128, 64], "float32"), "mx": ([128, 56], "float32"),
-    "z1": ([128, 168], "float16"), "z2": ([128, 192], "float16"), "cnt": ([128, 8], "float16"), "PK": ([128, NP], "int32"),
-    "su1": ([128, NK], "uint16"), "suA": ([128, NK], "uint16"), "suB": ([128, 8], "uint16"),
-    "W1": ([128, WIN], "int32"), "W2": ([128, WIN], "int32"),
-    "sd": ([128, 112], "int32"), "yi1": ([128, 7, MSG], "int32"), "yi2": ([128, 7, MSG], "int32"), "yB": ([128, 112], "int32"),
-    "msg1": ([128, 7, MSG], "float16"), "msg2": ([128, 7, MSG], "float16"),
-    "land1": ([128, 7, MSG], "float16"), "land2": ([128, 7, MSG], "float16"),
-    "sBv": ([128, 8], "float32"), "sBg": ([128, 8], "float32"),
-    "out1": ([128, 8], "float32"), "out2": ([128, 8], "float32"), "rep1": ([128, 8], "float32"), "rep2": ([128, 8], "float32"),
-    "Lo": ([128, NK], "float32"), "wO": ([128, NK], "uint16"), "Lv": ([128, 8], "float32"), "Lv0": ([128, 8], "float32"),
-    "Ld": ([128, 8], "float32"), "wv": ([128, 8], "uint16"), "Lb": ([128, 8], "float32"), "wr": ([128, 8], "uint16"),
-    "smA": ([128, NK], "float32"), "smB": ([128, 8], "float32"), "vB": ([128, 8], "float32"), "exv": ([128, 112], "float32"),
-    "vW": ([128, 120], "float32"), "s1c": ([128, NK], "uint16"), "gv": ([128, NP], "float32"), "sv": ([128, NP], "float32"),
-    "vO": ([128, NK], "float32"), "vt": ([128, NK], "int32"), "tau": ([128, NK], "uint16"),
-    "Yb": ([128, NK], "float32"), "dW": ([128, 136], "float32"),
-    "hq1": ([128, PER, MSG], "float16"), "hq2": ([128, PER, MSG], "float16"), "hp1": ([128, PER], "float32"), "hp2": ([128, PER], "float32"),
+    "X": ([128, NP], "int32"), "L0": ([128, NK], "int32"), "PW": ([128, 2 * PWID], "float32"), "ND": ([128, 2 * PWID], "bfloat16"),
+    "Xv": ([128, 128], "float32"), "xB": ([128, 128], "float32"),
+    "Zp": ([128, 128], "int32"), "Zd": ([128, 32], "int32"), "Zn": ([128, 32], "int32"), "H1": ([128, 128], "float16"),
+    "Ld": ([128, 64], "float16"), "NU": ([128, 32], "uint16"),
+    "NP": ([128, 32], "uint16"), "st": ([128, 128], "float32"), "HL0": ([128, 64], "bfloat16"),
+    "HL1": ([128, 64], "bfloat16"), "R0": ([128, NT], "float16"), "R1": ([128, NT], "float16"), "N0": ([128, NT], "bfloat16"),
+    "N1": ([128, NT], "bfloat16"), "LP": ([128, 128], "float16"),
+    "pi": ([128, 4], "int32"), "pj": ([128, 12], "int32"), "pf": ([128, 28], "float32"), "jm": ([128, 128], "bfloat16"),
+    "mk": ([128, 128], "float32"), "md16": ([128, 128], "bfloat16"), "m16": ([128, NP], "bfloat16"), "Rd": ([128, NP], "float32"),
+    "G2": ([128, 128], "float16"), "G3": ([128, 128], "float16"), "Gf": ([128, 128], "float32"), "cE": ([128, 128], "bfloat16"),
+    "U2": ([128, 128], "float16"), "I16": ([128, 128], "float16"), "If": ([128, 128], "float32"), "I1k": ([128, 128], "float16"),
+    "EX": ([128, 512], "float16"), "cL": ([128, 144], "bfloat16"), "LI": ([128, 144], "float16"), "j4": ([128, 128], "bfloat16"),
+    "S1": ([128, 56], "float32"), "hk": ([128, 128], "float32"), "sA": ([128, 120], "bfloat16"), "Ms": ([128, 8], "float32"),
+    "R1c": ([128, 168], "float32"), "scC": ([128, 192], "float32"), "sc4": ([128, 128], "float32"),
+    "oKi": ([128, 32], "int32"), "oRi": ([128, 12], "float32"), "oT": ([128, 48], "uint16"),
+    "Rs": ([128, 168], "float32"), "cQ": ([128, 192], "float32"), "cD": ([128, 72], "bfloat16"), "bc": ([128, 128], "bfloat16"),
+    "cOw": ([128, NK], "float32"), "cO16": ([128, 40], "float16"), "cS": ([128, 8], "float32"),
+    "rk": ([128, 32], "int32"), "ci": ([128, 32], "int32"), "ti": ([128, 32], "int32"), "rkB": ([128, 8], "int32"),
+    "oh1": ([128, 192], "float16"), "ohA": ([128, 192], "float16"), "ohB": ([128, 64], "float16"), "ex": ([128, NP], "float16"),
+    "exB": ([128, 128], "float16"), "scn": ([128, 64], "float32"), "zz": ([128, 64], "float32"), "mx": ([128, 56], "float32"),
+    "z1": ([128, 168], "float16"), "z2": ([128, 192], "float16"), "PK": ([128, NP], "int32"), "PKB": ([128, 128], "int32"),
+    "su": ([128, 96], "uint16"), "W1": ([128, WIN], "int32"), "W2": ([128, WIN], "int32"), "sd": ([128, 128], "float32"),
+    "MB1": ([128, 56], "float16"), "MB2": ([128, 56], "float16"), "RP1": ([128, 16], "float32"), "RP2": ([128, 16], "float32"),
+    "sB": ([128, 16], "float32"),
+    "Lo": ([128, NK], "float32"), "wO": ([128, NK], "uint16"), "Lv0": ([128, 8], "float32"), "Lv": ([128, 8], "float32"), "wv": ([128, 8], "uint16"),
+    "Lb": ([128, 8], "float32"), "wr": ([128, 8], "uint16"),
+    "sm": ([128, 64], "float32"), "exv": ([128, 128], "float32"), "vW": ([128, 136], "float32"), "gv": ([128, NP], "float32"),
+    "sv": ([128, NP], "float32"), "vO": ([128, NK], "float32"), "vt": ([128, NK], "int32"), "tau": ([128, NK], "uint16"),
+    "dW": ([128, 136], "float32"),
 }
-for _t, _n in (("O", 384), ("V", 128), ("R", 128)):
-    _m = _n // 128 * 48
-    for _b, _w in (("pr", _n), ("pa", _n), ("u", _m + 8), ("k", _m), ("re", _m), ("e", _n)):
-        _sb[_b + _t] = ([128, _w], "float32")
+for _t, _n in (("O", 3), ("V", 1), ("R", 1)):
+    _sb["pr" + _t] = ([128, 128 * _n], "float32")
+    _sb["pa" + _t] = ([128, 128 * _n], "bfloat16")
+    _sb["u" + _t] = ([128, 56 * _n + 8], "float32")
+    _sb["k" + _t] = ([128, 56 * _n], "float32")
+    _sb["q" + _t] = ([128, QW * _n + 80], "float32")
+    _sb["e" + _t] = ([128, 128 * _n], "float32")
 SCRATCH = {_k: ("sbuf", _v[0], _v[1]) for _k, _v in _sb.items()}
-PSUM = ("oK", "oP", "vK", "vP", "vL", "rA", "rB", "rC")
+SCRATCH["A1"] = ("dram", [128, 128], "float16")
+SCRATCH["A2"] = ("dram", [128, 32], "float16")
+SCRATCH["A3"] = ("dram", [128, 32], "uint16")
+PSUM = ("oK", "oP", "oL", "vK", "vP", "vL", "rA", "rB")
 for _k in PSUM:
     SCRATCH[_k] = ("psum", [128, 512], "float32")
-SEMAPHORES = ["sV", "sS", "sT", "sG", "ldA", "ldP", "ldB", "ldC", "st", "rq1", "rq2", "rp1", "rp2", "hq1", "hq2", "hp1", "hp2", "loc"]
+SEMAPHORES = ["sV", "sS", "sT", "sG", "ldA", "ldP", "ldZ", "ldD", "ldN", "lr0", "ln0", "lr1", "ln1", "st", "rq1", "rq2", "rp1", "rp2",
+              "hA", "hB", "hC", "tA", "tB", "tC", "loc"]
 
-FLY = (9, 6.5, 6, 5)
+FLY = (3.0, 3.0, 3.0, 3.0)
+FLY_T = (10.0, 10.0, 9.5)
 WAKE, SLACK, SLACK2 = 0.1, 0.1, 0.1
-P_O1, P_O2, P_A, P_O3, P_R, P_C = 2, 2, 1, 5, 4, 4
+P_T, P_TO, P_O1, P_O2, P_A, P_O3, P_R, P_C = -8, 1, 2, 2, 1, 5, 4, 4
 
 
 def wiring(T, topo, core):
-    others = [c for c in T.cores if c != core]
-    cross = [c for c in others if not topo.may_write(core, c)]
-    direct = [c for c in others if topo.may_write(core, c)]
-    rel = [c for c in topo.cores_of(core) if c not in T.cores and all(topo.may_write(c, d) for d in cross)]
+    mine = [c for c in T.cores if c == core or topo.may_write(core, c)]
+    other = [c for c in T.cores if c not in mine]
+    i = mine.index(core)
+    peers = [mine[i ^ k] for k in range(1, len(mine))]
+    partner = dict(zip(mine, other))
+    rel = [c for c in topo.cores_of(core) if c not in T.cores and topo.may_write(c, partner[core])]
     rel.sort(key=lambda c: (topo.die(c) != topo.die(core), c))
-    return cross, direct, rel[:N_REL]
+    return peers, partner, rel[:2]
 
 
 def emask(engs):
     return sum(1 << e for e in engs)
 
 
-def place_of(T, topo, owner, dst):
-    cross, direct, rel = wiring(T, topo, dst)
-    return (cross + direct).index(owner)
+def transfer(topo, src_core, dst_core, es, sem, s_ap, d_ap):
+    rid, pid = topo.addr(dst_core, src_core)
+    return RemoteDMATransfer(dst_ids=[DstId(rid=rid, pnc=pid)], dma_engine_mask=emask(es), remote_sem=sem, src=s_ap, dst=d_ap)
 
 
 def relay_program(g, core, T, topo, owner):
-    cross, direct, rel = wiring(T, topo, owner)
-    k = rel.index(core)
-    dsts = cross[PER * k:PER * k + PER]
-    n = 0
-    for src, dname, sem_out, req in (("hq1", "land1", "rq1", True), ("hp1", "rep1", "rp1", False),
-                                     ("hq2", "land2", "rq2", True), ("hp2", "rep2", "rp2", False)):
-        g.wait_ge(T.sem[src], ENG_HOP)
-        trs = []
-        for i, d in enumerate(dsts):
-            rid, pid = topo.addr(d, core)
-            es = topo.engines(core, d)[ENG_OUT * i:ENG_OUT * i + ENG_OUT]
-            at = place_of(T, topo, owner, d)
-            if req:
-                s_ap, d_ap = T[src][:, i, :], T[dname][:, at, :]
-            else:
-                s_ap, d_ap = T[src][:, i:i + 1], T[dname][:, at:at + 1]
-            trs.append(RemoteDMATransfer(dst_ids=[DstId(rid=rid, pnc=pid)], dma_engine_mask=emask(es), remote_sem=T.sem[sem_out],
-                                         src=s_ap, dst=d_ap))
-            n += len(es)
-        g.remote_dma_fused(trs, local_sem=T.sem.loc)
-    g.wait_ge(T.sem.loc, n)
+    peers, partner, rel = wiring(T, topo, owner)
+    d = partner[owner]
+    es = topo.engines(core, d)
+    pieces = ((("A", T.A1, T.A1),), (("C", T.A3, T.NP), ("B", T.A2, T.A2)))[rel.index(core)]
+    for s, src, dst in pieces:
+        g.wait_ge(T.sem["h" + s], len(es))
+        g.remote_dma_fused([transfer(topo, core, d, es, T.sem["t" + s], src[:], dst[:])], local_sem=T.sem.loc)
+    g.wait_ge(T.sem.loc, len(es) * len(pieces))
 
 
 def plan(tasks):
@@ -145,17 +141,6 @@ def plan(tasks):
     return order
 
 
-def runs(v):
-    out, i = [], 0
-    while i < len(v):
-        j, st = i + 1, (v[i + 1] - v[i] if i + 1 < len(v) else 0)
-        while j < len(v) and v[j] - v[j - 1] == st:
-            j += 1
-        out.append((i, j - i, v[i], st if j - i > 1 else 0))
-        i = j
-    return out
-
-
 def rank_program(g, core, T, topo):
     rank = T.rank_of(core)
     if rank is None:
@@ -163,8 +148,8 @@ def rank_program(g, core, T, topo):
             if c in topo.cores_of(core) and core in wiring(T, topo, c)[2]:
                 relay_program(g, core, T, topo, c)
         return
-    cross, direct, rel = wiring(T, topo, core)
-    prank = [T.cores.index(c) for c in cross + direct]
+    peers, partner, rel = wiring(T, topo, core)
+    owners = [T.cores.index(c) for s in peers + [core] for c in (partner[s], s)]
     base = NT * rank
     SH = base - LO
     tasks, wr, rd = [], {}, {}
@@ -192,7 +177,7 @@ def rank_program(g, core, T, topo):
         return i
 
     def vop(fn, reads, writes, n, prio=1, ext=(), aft=None, f=1.0):
-        return add("V", lambda: [fn()], reads, writes, (0.02 if f == int(f) else 0.07) + 1.2 * cy * max(64, n * f), prio, ext, aft)
+        return add("V", lambda: [fn()], reads, writes, (0.02 if f == int(f) else 0.07) + 1.15 * cy * max(64, n * f), prio, ext, aft)
 
     def ts(out, on, in0, inn, s1, s2, op0, op1=None, n=24, prio=1, ext=(), aft=None, extra=()):
         if op1 is None:
@@ -208,8 +193,8 @@ def rank_program(g, core, T, topo):
     def fill(ap, on, v, n, prio=1):
         return vop(lambda: V.memset(ap, v), [], [on], n, prio)
 
-    def act(out, on, in_, inn, n, prio=1, **kw):
-        return add("S", lambda: [S.activation(out, in_, F.Copy, **kw)], inn, [on], 0.03 + 1.2 * cy * max(64, n), prio)
+    def act(out, on, in_, inn, n, prio=1, fn=F.Copy, **kw):
+        return add("S", lambda: [S.activation(out, in_, fn, **kw)], inn, [on], 0.03 + 1.15 * cy * max(64, n), prio)
 
     def iota(ap, on, pat, b, ch, n, prio=1, fl=True):
         if fl:
@@ -219,14 +204,14 @@ def rank_program(g, core, T, topo):
     def gfill(ap, on, v, n, prio=1):
         return iota(ap, on, [[0, n]], v, 0, n, prio)
 
-    def mm(lst, reads, bank, prio=1):
-        c = sum((0.03 + 0.0008 * max(64, n) * (4 if f4 else 1)) for (_, n, f4) in lst)
-        return add("T", lambda: [E.matmul(*a) for (a, n, f4) in lst], reads, [bank], c, prio)
+    def mm(lst, reads, bank, prio=1, ext=(), aft=None):
+        c = sum((0.01 + 1.15 * cy * max(64, n) * (4 if f4 else 1)) for (_, n, f4) in lst)
+        return add("T", lambda: [E.matmul(*a) for (a, n, f4) in lst], reads, [bank], c, prio, ext, aft)
 
     loads = {}
 
-    def load(q, sem, fn, cnt, deps, writes, cost, lat, prio=0):
-        i = add(q, fn, deps, writes, cost, prio)
+    def load(q, sem, fn, cnt, deps, writes, cost, lat, prio=0, ext=(), aft=None):
+        i = add(q, fn, deps, writes, cost, prio, ext, aft)
         tasks[i]["dma"] = sem
         tasks[i]["lat"] = lat
         loads[sem] = loads.get(sem, 0) + 16 * cnt
@@ -235,325 +220,356 @@ def rank_program(g, core, T, topo):
     def ld_pts(q, fs):
         return [q.dma_start(T.X[4 * f + i:128:16, :], T.pts[i:24:3, :]) for f in fs for i in range(3)]
 
+    nloc = [0]
+
+    def remote(calls, reads, prio):
+        def fn():
+            for c in calls:
+                g.remote_dma_fused([transfer(topo, core, d, es, T.sem[s], a, b) for d, es, s, a, b in c], local_sem=T.sem.loc)
+                nloc[0] += sum(len(x[1]) for x in c)
+            return []
+        return add("G", fn, reads, [], 0.5 * len(calls), prio)
+    E8 = topo.engines(core, peers[0])
+
+    fill(T.X[:], "X", 1, NP, -10)
     fill(T.bc[:, 0:128], "one", 1.0, 64, -10)
-    fill(T.x1[:], "x1", 1, NK, -9)
-    load("Y", "ldA", lambda: [g.sync.dma_start(T.L0[:], T.tet0[:])], 1, [], ["L0"], 0.1, 2.0, -9)
-    load("Y", "ldP", lambda: ld_pts(g.sync, (0, 1)) + [g.sync.dma_start(T.X[4 * f + 3:128:16, :], T.x1[:]) for f in range(4)],
-         10, ["x1"], ["Xa"], 1.0, 2.0)
-    load("S", "ldP", lambda: ld_pts(g.scalar, (2, 3)), 6, [], ["X"], 0.6, 2.5)
-    load("Y", "ldB", lambda: [g.sync.dma_start(T.PW[16 * k:16 * k + 16, LO:HI], T.planes[:]) for k in range(8)], 8, [], ["PW"], 0.8, 4.0)
+    load("Y", "ldN", lambda: [g.sync.dma_start(T.Zn[:], T.nbr[:])], 1, [], ["Zn"], 0.1, 2.0, -11)
+    load("S", "ldZ", lambda: [g.scalar.dma_start(T.Zp[:], T.planes[:])], 1, [], ["Zp"], 0.1, 2.3, -11)
+    load("Y", "ldA", lambda: [g.sync.dma_start(T.L0[:], T.tet0[:])], 1, [], ["L0"], 0.1, 2.5, -10)
+    load("S", "ldD", lambda: [g.scalar.dma_start(T.Zd[:], T.planes[3:16:4, :])], 1, [], ["Zd"], 0.1, 2.7, -10)
+    load("Y", "ldP", lambda: ld_pts(g.sync, range(4)), 12, [], ["X"], 1.2, 2.0)
+
+    cp(T.NU[:], "NU", T.Zn[:], "Zn", 32, P_T - 1)
+    sC = remote([[(rel[1], E8, "hC", T.NU[:], T.A3[:])]], ["NU"], P_T - 1)
+    ts(T.H1[:], "H1", T.Zp[:], "Zp", 1.0 / 64, None, A.mult, n=128, prio=P_T)
+    sA = remote([[(rel[0], E8, "hA", T.H1[:], T.A1[:])]], ["H1"], P_T)
+    tasks[sA]["odeps"].add(sC)
+    xd, tI, Ld, Hd = T.st[:, 64:96], T.st[:, 96:128], T.Ld[:, 0:32], T.Ld[:, 32:64]
+    ts(xd, "xd", T.Zd[:], "Zd", 1.0 / 64, None, A.mult, n=32, prio=P_T)
+    ts(Hd, "Hd", T.Zd[:], "Zd", 1.0 / 64, None, A.mult, n=32, prio=P_T)
+    tt(Ld, "Ld", xd, "xd", Hd, "Hd", A.subtract, n=32, prio=P_T, f=2)
+    sB = remote([[(rel[1], E8, "hB", Ld, T.A2[:])]], ["Ld"], P_T)
+    tasks[sB]["odeps"].add(sA)
 
     iota(T.pi[:], "pi", [[0, 4]], 0, 1, 4, -9, False)
-    iota(T.md16[:], "md16", [[1, 8], [0, 16]], 0, 0, 128, -9)
+    iota(T.jm[:, 0:128], "jm", [[0, 8], [1, 16]], 0, 0, 128, -8)
     iota(T.oRi[:], "oRi", [[0, 4], [-8, 3]], 16, 0, 12, -8)
+    iota(T.md16[:], "md16", [[1, 8], [0, 16]], 0, 0, 128, -7)
     iota(T.mk[:], "mk", [[1, 128]], 0, -1, 128, -7)
-    iota(T.oKi[:], "oKi", [[1, 24]], 0, 0, 24, -4, False)
-    iota(T.jm[:, 0:128], "jm", [[0, 8], [1, 16]], 0, 0, 128, -5)
+    iota(T.oKi[:], "oKi", [[1, 32]], 0, 0, 32, -6, False)
     iota(T.cOw[:], "cOw", [[16, 24]], 128, 1, 24, -3)
-    iota(T.cD[:, 0:7], "cD", [[16, 7]], -1, 0, 7, -2)
-    gfill(T.Rs[:, 0:168], "Rs", 1, 168, -1)
-    gfill(T.Rs[:, 0:168:24], "Rs", 0, 7, -1)
-    CQ, CQB, CS = [], [], []
-    for k, v in enumerate(prank + [rank]):
+    iota(T.cD[:, 0:8], "cD", [[32, 4], [1, 2]], -2, 0, 8, -3)
+    iota(T.cE[:], "cE", [[4, 8], [0, 4], [1, 4]], 0, 0, 128, -2)
+    gfill(T.Rs[:, 0:168], "Rs", 1, 168, -2)
+    gfill(T.Rs[:, 0:168:24], "Rs", 0, 7, -2)
+    iota(tI, "tI", [[1, 32]], 0, 32, 32, -1)
+    iota(T.j4[:], "j4", [[0, 32], [1, 4]], 0, 0, 128, 0)
+    iota(T.W1[:, 0:128], "W1", [[0, 128]], NONE, 0, 128, 0, False)
+    CQ = []
+    for k, v in enumerate(owners):
         act(T.cQ[:, 24 * k:24 * k + 24], "cQ%d" % k, T.bc[:, 0:24], ["one"], 24, -8, scale=0.0, bias=float(v))
         CQ.append("cQ%d" % k)
-    iota(T.NB[:], "NB", [[1, PWID]], SH, 0, PWID, 1, False)
-    load("S", "ldC", lambda: [g.scalar.dma_start(T.NB[16 * k:16 * k + 16:4, LO:HI], T.nbr[:]) for k in range(8)], 8, [], ["NB"], 0.8, 3.5)
-    iota(T.S1[:], "S1", [[8, 8], [1, 6]], -1, 0, 48, 1)
-    iota(T.sA[:], "sA", [[32, 8], [4, 6]], -4, 0, 48, 1)
-    iota(T.sC[:, 1:49], "sC", [[32, 8], [0, 6]], 1, 0, 48, 1)
-    gfill(T.sC[:, 0:1], "sC0", 0, 1, 1)
-    iota(T.Ms[:], "Ms", [[1, 8]], 0, 0, 8, 1)
-    gfill(T.R1c[:], "R1c", -BIG, 144, 1)
-    gfill(T.R1c[:, 5:144:6], "R1c", BIG, 24, 1)
-    for s, n, a, st in runs(prank + [rank]):
-        iota(T.cQ[:, 192 + 8 * s:192 + 8 * (s + n)], "cQB%d" % s, [[st, n], [0, 8]], a, 0, 8 * n, 4)
-        CQB.append("cQB%d" % s)
-    for s, n, a, st in runs(prank):
-        iota(T.cS[:, s:s + n], "cS%d" % s, [[NT * st, n]], NT * a - SH, 0, n, 4)
-        CS.append("cS%d" % s)
-
     ones = T.bc[0:1, 0:128]
-    iota(T.W1[:, 0:112], "W1", [[0, 112]], NONE, 0, 112, 0, False)
-    gfill(T.PW[:, 0:LO], "PW0", 0, 8, 2)
-    gfill(T.PW[:, HI:PWID], "PW1", 0, 8, 2)
-    ts(T.pj[:, 0:1], "pj0", T.pi[:, 0:1], "pi", 15, None, A.bitwise_and, n=1, prio=-7)
-    ts(T.pj[:, 1:2], "pj1", T.pi[:, 0:1], "pi", 4, None, A.arith_shift_right, n=1, prio=-7)
-    ts(T.pj[:, 2:3], "pj2", T.pi[:, 0:1], "pi", 2, None, A.arith_shift_right, n=1, prio=-7)
-    vop(lambda: V.tensor_copy(T.pf[:, 0:3], T.pj[:, 0:3]), ["pj0", "pj1", "pj2"], ["pf"], 3, -7)
-    p16, pg, p4, p8, p32, pK = [T.pf[:, k:k + 1] for k in range(6)]
-    oK, oE, oR, oB8 = T.oT[:, 0:24], T.oT[:, 24:48], T.oT[:, 48:60], T.oT[:, 64:68]
+    for k, (w, a, o1, b, o2) in enumerate(((1, 15, A.bitwise_and, None, None), (1, 4, A.arith_shift_right, None, None),
+                                           (1, 2, A.arith_shift_right, None, None), (1, 3, A.bitwise_and, None, None),
+                                           (1, 2, A.arith_shift_right, 3, A.bitwise_and), (1, 5, A.arith_shift_right, None, None),
+                                           (2, 1, A.bitwise_and, None, None))):
+        ts(T.pj[:, k:k + w], "pj%d" % k, T.pi[:, 0:w], "pi", a, b, o1, o2, n=1, prio=-9)
+    vop(lambda: V.tensor_copy(T.pf[:, 0:8], T.pj[:, 0:8]), ["pj%d" % k for k in range(7)], ["pf"], 8, -9)
+    col = lambda k: T.pf[:, k:k + 1]
+    p16, pg, p4, pi_, pf_, p5, par = [col(k) for k in range(7)]
+    cf, s3, hL, ck, cl, c3, c1, lo, hi, pK, pK4, m3, xm, c2 = [col(k) for k in range(8, 22)]
+    for ap, nm, src, sc, bi, pr in ((c3, "c3", pg, 4.0, 3.0, -4), (cf, "cf", p5, 1024.0, 0.0, -2), (s3, "s3", pg, 3.0, 1.0, -2),
+                                    (pK4, "pK4", pf_, float(K4), -3.0 * K4, -1), (lo, "lo", par, float(PWID), 0.0, 2),
+                                    (hi, "hi", par, float(PWID), float(HI), 2), (pK, "pK", p16, float(K16), -15.0 * K16, 5)):
+        act(ap, nm, src, ["pf"], 1, pr, scale=sc, bias=bi)
+    act(hL, "hL", p16, ["pf", "s3"], 1, -2, F.Identity, scale=s3, bias=s3)
+    for ap, nm, sc, bi in ((ck, "ck", 4.0, pi_), (cl, "cl", 16.0, pf_), (c1, "c1", float(GW), pi_), (c2, "c2", float(GW), pf_)):
+        act(ap, nm, pg, ["pf"], 1, 2, F.Identity, scale=sc, bias=bi)
+    oK, oR, oB8 = T.oT[:, 0:24], T.oT[:, 24:36], T.oT[:, 40:44]
     ts(oR, "oR", T.oRi[:], "oRi", p16, None, A.add, n=12, prio=-6, extra=["pf"])
-    ts(T.G16[:], "G16", T.md16[:], "md16", pg, None, A.is_equal, n=128, prio=-3, extra=["pf"])
+    ts(T.G2[:], "G2", T.md16[:], "md16", pg, 2.0, A.is_equal, A.mult, n=64, prio=-3, extra=["pf"])
     ts(T.I16[:], "I16", T.mk[:], "mk", 0.0, None, A.is_equal, n=128, prio=-1)
-    cp(T.If[:], "If", T.I16[:], "I16", 128, 2)
     ts(T.mk[:], "mk", T.mk[:], "mk", 0.0, -1.0, A.is_lt, A.mult, n=128, prio=0)
-    tt(T.U16[:], "U16", T.mk[:], "mk", T.G16[:], "G16", A.mult, n=128, prio=0, f=2)
-    cp(T.cO16[:], "cO16", T.cOw[:], "cOw", 24, -1)
-    cp(oK, "oK", T.oKi[:], "oKi", 24, -1)
+    tt(T.U2[:], "U2", T.mk[:], "mk", T.G2[:], "G2", A.mult, n=128, prio=0, f=2)
+    cp(T.cO16[:, 0:24], "cO16", T.cOw[:], "cOw", 24, -1)
+    cp(oK, "oK", T.oKi[:, 0:24], "oKi", 24, -1)
     ts(T.m16[:, 0:128], "m16", T.jm[:], "jm", p16, None, A.is_equal, n=64, prio=-1, extra=["pf"])
     act(T.m16[:, 128:256], "m16b", T.m16[:, 0:128], ["m16"], 128, -1)
     act(T.m16[:, 256:384], "m16c", T.m16[:, 0:128], ["m16"], 128, -1)
     M16 = ["m16", "m16b", "m16c"]
-    ts(T.G2k[:], "G2k", T.md16[:], "md16", pg, 2048.0, A.is_equal, A.mult, n=128, prio=-1, extra=["pf"])
-    gfill(T.scD[:, 0:1], "scD0", 0, 1, 0)
-    act(T.scC[:, 0:112], "scC", T.m16[:, 0:112], ["m16"], 112, 0, scale=-float(BIG))
-    act(T.scD[:, 1:112], "scD", T.m16[:, 0:111], ["m16"], 112, 0, scale=float(MID))
-    tt(T.scC[:, 0:112], "scC", T.scC[:, 0:112], "scC", T.scD[:], "scD", A.add, n=112, prio=0, f=2, extra=["scD0"])
-    act(T.scC[:, 112:192], "scCb", T.scC[:, 0:80], ["scC"], 80, 5)
+    ts(T.G3[:], "G3", T.cE[:], "cE", c3, None, A.is_equal, n=64, prio=-1, extra=["c3"])
+    ts(T.j4[:], "j4", T.j4[:], "j4", pf_, None, A.is_equal, n=64, prio=0, extra=["pf"])
+    act(T.sc4[:], "sc4", T.j4[:], ["j4"], 128, 0, scale=-float(BIG + K4), bias=float(K4))
+    ts(T.LP[0:20, :], "LP", T.jm[0:20, :], "jm", 1.0, T.pf[0:20, 10:11], A.add, A.is_equal, n=64, prio=P_TO, extra=["hL"])
 
-    def slots(oh, ohn, M, co, cqn, rkw, rkn, offs, offn, rs, rsn, su, sun, prio, cnt=None):
-        n7, n8 = 7 * M, 8 * M
-        cq = T.cQ[:, co:co + n8]
+    def steps_rows(src, srcn, b, c, HL, N, sem, prio, ext=(), aft=None):
+        st = T.st[:, c:c + 32]
+        ts(st, "st%d" % c, src, srcn, cf, float(-b), A.add, A.add, n=32, prio=prio, extra=["cf"], ext=ext, aft=aft)
+        tt(st, "st%d" % c, st, "st%d" % c, tI, "tI", A.subtract, n=32, prio=prio, f=2)
+        cp(T[HL][:, 0:32], HL, st, "st%d" % c, 32, prio)
+        tt(T[HL][:, 32:64], HL + "b", st, "st%d" % c, T[HL][:, 0:32], HL, A.subtract, n=32, prio=prio, f=2)
+        load("Y", sem, lambda: [g.sync.dma_start(T[N][4 * h:4 * h + 4, :], T[HL][:, 32 * h:32 * h + 32]) for h in range(2)], 2,
+             [HL, HL + "b"], [N], 0.2, 2.0, prio)
+
+    def windows(t, R, Rn, N, banks, on, prio):
+        c = PWID * t + LO
+        for h in range(2):
+            mm([((T[banks[2 + h]][:], T.m16[0:8, 0:128], T[N][0:8, 512 * h:512 * h + 512], True, True), 512, 0)], ["m16", N], banks[2 + h], prio)
+            o, nm = T.ND[:, c + 512 * h:c + 512 * h + 512], "ND%d%d" % (t, h)
+            if on[2 + h] == "S":
+                act(o, nm, T[banks[2 + h]][:], [banks[2 + h]], 512, prio)
+            else:
+                cp(o, nm, T[banks[2 + h]][:], banks[2 + h], 512, prio)
+        for h in range(2):
+            mm([((T[banks[h]][:], T.LP[0:20, :], T[R][0:20, 512 * h:512 * h + 512], True, True), 512, 0)], ["LP"] + Rn, banks[h], prio)
+            o, nm = T.PW[:, c + 512 * h:c + 512 * h + 512], "PW%d%d" % (t, h)
+            if on[h] == "S":
+                act(o, nm, T[banks[h]][:], [banks[h]], 512, prio, scale=64.0)
+            else:
+                ts(o, nm, T[banks[h]][:], banks[h], 64.0, None, A.mult, n=512, prio=prio)
+
+    load("Y", "lr0", lambda: [g.sync.dma_start(T.R0[0:16, :], T.H1[:]), g.sync.dma_start(T.R0[16:20, :], Ld)], 2, ["H1", "Ld"], ["R0"],
+         0.2, 2.0, P_TO)
+    steps_rows(T.Zn[:], "Zn", base, 0, "HL0", "N0", "ln0", P_TO)
+    windows(1, "R0", ["R0"], "N0", ("oK", "oP", "vK", "vP"), "SSSS", P_TO)
+    PZ = []
+    for w in ("PW", "ND"):
+        for a, z in ((0, LO), (HI, PWID + LO), (PWID + HI, 2 * PWID)):
+            gfill(T[w][:, a:z], "z%s%d" % (w, a), 0, z - a, 2)
+            PZ.append("z%s%d" % (w, a))
+
+    su1, suA, suB, s1c = T.su[:, 0:24], T.su[:, 24:48], T.su[:, 48:56], T.su[:, 64:88]
+
+    def slots(oh, ohn, su, sun, prio):
+        M, n7, n8 = 24, 168, 192
         z1, z2 = T.z1, T.z2
-        if cnt is None:
-            mm([((T.rB[:, n7:n8], T.I16[:], T.cO16[:, 0:M], True, True), M, 0)], ["I16", "cO16"], "rB", prio)
-        vop(lambda: V.tensor_tensor(oh[:, 0:n8], rkw.indirect(offs), cq, A.is_equal), rkn + offn + cqn, [ohn], n8, prio, f=1.5)
-        if cnt is not None:
-            mm([((T.rA[:, 0:n7], T.G16[:], oh[:, 0:n7], True, False), n7, 0), ((T.rA[:, 0:n7:M], T.I16[:], cnt, False, True), 7, 0)],
-               ["G16", ohn, "I16", "cnt"], "rA", prio)
-            mm([((T.rB[:, 0:n8], T.I1k[:], oh[:, 0:n8], True, False), n8, 0), ((T.rB[:, 0:n7], T.U16[:], oh[:, 0:n7], False, False), n7, 0),
-                ((T.rB[:, n7:n8], T.I16[:], T.cO16[:, 0:M], False, True), M, 0)], ["I1k", "U16", "I16", "cO16", ohn], "rB", prio)
-            vop(lambda: V.tensor_tensor_scan(T.scn[:, 0:n7], rs, T.rA[:, 0:n7], 0.0, A.mult, A.add), [rsn, "rA"], ["scn"], n7, prio)
-            vop(lambda: V.tensor_tensor(T.zz[:, 0:n8], T.scn[:, 0:n8], T.rB[:, 0:n8], A.add), ["scn", "scnz", "rB"], ["zz"], n8, prio)
-            h = n8 // 2
-            tt(T.mx[:, 0:h], "mx0", T.zz[:, 0:h], "zz", T.zz[:, h:n8], "zz", A.max, n=h, prio=prio)
-            tt(T.mx[:, 32:32 + h // 2], "mx1", T.mx[:, 0:h // 2], "mx0", T.mx[:, h // 2:h], "mx0", A.max, n=h // 2, prio=prio)
-            tt(T.mx[:, 48:48 + M], "mx2", T.mx[:, 32:32 + M], "mx1", T.mx[:, 32 + M:32 + 2 * M], "mx1", A.max, n=M, prio=prio)
-            return ts(su[:, 0:M], sun, T.mx[:, 48:48 + M], "mx2", -1024.0, None, A.add, n=M, prio=prio)
-        mm([((T.rA[:, 0:n7], T.G16[:], oh[:, 0:n7], True, False), n7, 0), ((T.rA[:, 0:n7:M], ones, T.cD[0:1, 0:7], False, True), 7, 0)],
-           ["G16", ohn, "one", "cD"], "rA", prio)
-        mm([((T.rB[:, 0:n7], T.U16[:], oh[:, 0:n7], True, True), n7, 0)], ["U16", ohn], "rB", prio)
+        mm([((T.rB[:, n7:n8], T.I16[:], T.cO16[:, 0:M], True, True), M, 0)], ["I16", "cO16"], "rB", prio)
+        vop(lambda: V.tensor_tensor(oh[:], T.rk[:, 0:32].indirect(oR), T.cQ[:], A.is_equal), ["rka", "rkb", "oR"] + CQ, [ohn], n8, prio, f=1.6)
+        mm([((T.rA[:, 0:n7], T.G2[:], oh[:, 0:n7], True, False), n7, 0), ((T.rA[:, 0:n7:M], ones, T.cD[0:1, 0:7], False, True), 7, 0)],
+           ["G2", ohn, "one", "cD"], "rA", prio)
+        mm([((T.rB[:, 0:n7], T.U2[:], oh[:, 0:n7], True, True), n7, 0)], ["U2", ohn], "rB", prio)
         sc = T.rA[:, 256:256 + n7]
-        vop(lambda: V.tensor_tensor_scan(sc, rs, T.rA[:, 0:n7], 0.0, A.mult, A.add), [rsn, "rA"], ["sc"], n7, prio)
+        vop(lambda: V.tensor_tensor_scan(sc, T.Rs[:], T.rA[:, 0:n7], 0.0, A.mult, A.add), ["Rs", "rA"], ["sc"], n7, prio)
         vop(lambda: V.tensor_tensor(z2[:, 0:n8], T.rB[:, 0:n8], oh[:, 0:n8], A.mult), ["rB", ohn], ["z2"], n8, prio)
         vop(lambda: V.tensor_tensor(z1[:, 0:n7], sc, oh[:, 0:n7], A.mult), ["sc", "rA", ohn], ["z1"], n7, prio)
         mm([((T.rB[:, 0:M], T.I16[:], z2[:, M * b:M * b + M], b == 0, False), M, 0) for b in range(8)], ["I16", "z2"], "rB", prio)
         mm([((T.rB[:, 0:M], T.I16[:], z1[:, M * b:M * b + M], False, b == 6), M, 0) for b in range(7)], ["I16", "z1"], "rB", prio)
-        cp(su[:, 0:M], sun, T.rB[:, 0:M], "rB", M, prio)
+        cp(su, sun, T.rB[:, 0:M], "rB", M, prio)
 
-    def pack(xap, xn, tib, tin, k, prio):
+    def pack(ex, exn, PK, PKn, xap, xn, tib, tin, k, bank, prio):
         n = 16 * k
-        vop(lambda: V.tensor_tensor(T.ex[:, 0:n], tib.indirect(T.oT[:, 0:k]), T.m16[:, 0:n], A.mult), [tin, "oK"] + M16, ["ex"], n, prio, f=1.6)
-        mm([((T.rC[:, 0:n], T.G2k[:], T.ex[:, 0:n], True, True), n, 0)], ["G2k", "ex"], "rC", prio)
-        tt(T.PK[:, 0:n], "PK", T.rC[:, 0:n], "rC", xap, xn, A.add, n=n, prio=prio)
+        vop(lambda: V.tensor_tensor(ex, tib.indirect(T.oT[:, 0:k]), T.m16[:, 0:n], A.mult), [tin, "oK"] + M16, [exn], n, prio, f=1.6)
+        mm([((T[bank][:, 0:n], T.G3[:], ex, True, True), n, 0)], ["G3", exn], bank, prio)
+        tt(PK, PKn, T[bank][:, 0:n], bank, xap, xn, A.add, n=n, prio=prio)
 
-    def decode(W, wn, yi, yin, msg, msgn, prio):
-        vop(lambda: V.tensor_tensor_scan(T.sd[:], T.scC[:, 0:112], W[:, 0:112], 0.0, A.add, A.max), ["scC", wn], ["sd"], 112, prio)
-        ts(yi[:, :, 0:16], yin, W[:, 0:112], wn, 2047, None, A.bitwise_and, n=112, prio=prio)
-        ts(yi[:, :, 16], yin + "t", T.sd[:, 15:112:16], "sd", 11, 2047, A.arith_shift_right, A.bitwise_and, n=7, prio=prio)
-        cp(msg[:], msgn, yi[:], yin, 119, prio, extra=[yin + "t"])
+    def message(W, wn, MB, mn, prio):
+        vop(lambda: V.tensor_tensor_scan(T.sd[:], T.sc4[:], W[:, 0:128], 0.0, A.add, A.max), ["sc4", wn], ["sd"], 128, prio)
+        ts(MB[:, 0:32], mn, T.sd[:, 3:128:4], "sd", pK4, None, A.add, n=32, prio=prio, extra=["pK4"])
 
-    nloc = [0]
+    def send(buf, reads, sem, w, src, dst, prio):
+        x = [(d, sem, buf[:, src + w * k:src + w * k + w], buf[:, dst + w * k:dst + w * k + w]) for k, d in enumerate(peers)]
+        return remote([[(x[0][0], E8[:4]) + x[0][1:], (x[1][0], E8[4:]) + x[1][1:]], [(x[2][0], E8) + x[2][1:]]], reads, prio)
+    ARR = 2 * len(E8)
 
-    def send(src, srcn, hname, dname, sem, req, prio):
-        def fn():
-            own8 = topo.engines(core, direct[0])
-            alle = topo.engines(core, rel[0])
-            hop = [e for e in alle if e not in own8]
-            if len(hop) < ENG_HOP * N_REL:
-                hop = hop + [e for e in alle if e in own8]
-            trs = []
-            for k, r in enumerate(rel):
-                rid, pid = topo.addr(r, core)
-                s_ap = src[:, PER * k:PER * k + PER, :] if req else src[:, PER * k:PER * k + PER]
-                es = hop[ENG_HOP * k:ENG_HOP * k + ENG_HOP]
-                trs.append(RemoteDMATransfer(dst_ids=[DstId(rid=rid, pnc=pid)], dma_engine_mask=emask(es), remote_sem=T.sem[hname],
-                                             src=s_ap, dst=T[hname][:]))
-                nloc[0] += len(es)
-            g.remote_dma_fused(trs, local_sem=T.sem.loc)
-            trs = []
-            for k, d in enumerate(direct):
-                rid, pid = topo.addr(d, core)
-                es = topo.engines(core, d)[ENG_DIR * k:ENG_DIR * k + ENG_DIR]
-                b, at = len(cross) + k, place_of(T, topo, core, d)
-                if req:
-                    s_ap, d_ap = src[:, b, :], T[dname][:, at, :]
-                else:
-                    s_ap, d_ap = src[:, b:b + 1], T[dname][:, at:at + 1]
-                trs.append(RemoteDMATransfer(dst_ids=[DstId(rid=rid, pnc=pid)], dma_engine_mask=emask(es), remote_sem=T.sem[sem],
-                                             src=s_ap, dst=d_ap))
-                nloc[0] += len(es)
-            g.remote_dma_fused(trs, local_sem=T.sem.loc)
-            return []
-        return add("G", fn, [srcn], [], 1.0, prio)
-    ARR = ENG_OUT * len(cross) + ENG_DIR * len(direct)
-
-    def step(t, k, X, xn, w, wn, L, Ln, bK, bP, bL, prio, last=None, Lacc=None, Laccn=None):
-        B = 3 if k == 24 else 1
-        m, kc = 48 * B, 8 * B
-        pr, pa, u, kp, re, e = [T[x + t] for x in ("pr", "pa", "u", "k", "re", "e")]
+    def step(t, X, xn, w, wn, c0, bK, bP, bL, Lr, Lwn, clo, chi, prio, last=False):
+        B = 3 if t == "O" else 1
+        Lw = T[Lwn]
+        m, k = 56 * B, 8 * B
+        pr, pa, u, kk, re, e = [T[x + t] for x in ("pr", "pa", "u", "k", "q", "e")]
         nm = lambda x: x + t
         part = lambda x, q: x + t + ("" if B == 1 else "_%d" % q)
-        lo = 256 if bK == bL else 0
+        pc = 256 if bK == bP else 0
+        tabs = ("1",) if c0 else ("0", "1")
+        PWn, NDn = [[x + a + h for a in tabs for h in "01"] + PZ for x in ("PW", "ND")]
         for q, (a, z) in enumerate(((0, 16), (16, 24)) if B == 3 else ((0, k),)):
-            vop(lambda a=a, z=z: V.tensor_tensor(pr[:, 16 * a:16 * z], T.PW[:].indirect(w[:, a:z]), X[:, 16 * a:16 * z], A.mult),
-                ["PW", "PW0", "PW1", wn, xn], [part("pr", q)], 16 * (z - a), prio, f=1.6)
-            add("S", lambda a=a, z=z: [S.activation(pa[:, 16 * a:16 * z], T.ND[:].indirect(w[:, a:z]), F.Copy)], ["ND", wn], [part("pa", q)],
-                0.1 + 1.8 * cy * 16 * (z - a), prio)
+            vop(lambda a=a, z=z: V.tensor_tensor(pr[:, 16 * a:16 * z], T.PW[:, c0:].indirect(w[:, a:z]), X[:, 16 * a:16 * z], A.mult),
+                PWn + [wn, xn], [part("pr", q)], 16 * (z - a), prio, f=1.6)
+            add("S", lambda a=a, z=z: [S.activation(pa[:, 16 * a:16 * z], T.ND[:, c0:].indirect(w[:, a:z]), F.Copy)], NDn + [wn], [part("pa", q)],
+                0.07 + 1.8 * cy * 16 * (z - a), prio)
         for b in range(B):
-            first = mm([((T[bK][:, 48 * b:48 * b + 48], pr[:, 128 * b:128 * b + 128], T.S1[:], True, True), 48, 1)],
+            first = mm([((T[bK][:, 56 * b:56 * b + 56], pr[:, 128 * b:128 * b + 128], T.S1[:], True, True), 56, 1)],
                        [part("pr", b // 2), "S1"], bK, prio)
         for b in range(B):
-            second = mm([((T[bP][:, 48 * b:48 * b + 48], pa[:, 128 * b:128 * b + 128], T.S2[:], True, True), 48, 1)],
+            second = mm([((T[bP][:, pc + 56 * b:pc + 56 * b + 56], pa[:, 128 * b:128 * b + 128], T.sA[:, 64:120], True, True), 56, 0)],
                         [part("pa", b // 2), "S2"], bP, prio)
         if B == 1:
             tasks[second]["odeps"].add(first)
-        Li, Lin = (L, Ln) if Lacc is None else (Lacc, Laccn)
-        il = lambda: mm([((T[bL][:, lo:lo + kc], T.If[:], Li[:, 0:kc], True, False), kc, 1)], ["If", Lin], bL, prio)
-        if bL != bK:
-            il()
+        third = mm([((T[bL][:, 0:k], T.If[:], T[Lr][:], True, False), k, 1)], ["If", Lr], bL, prio)
+        tasks[third]["odeps"].add(second)
         vop(lambda: V.tensor_tensor_scan(u[:, 1:m + 1], T[bK][:, 0:m], T.R1c[:, 0:m], 0.0, A.min, A.max), ["R1c", bK], [nm("u")], m, prio)
-        vop(lambda: V.tensor_tensor(kp[:, 0:m], T[bK][:, 0:m], u[:, 0:m], A.is_ge), [bK, nm("u"), nm("u0")], [nm("k")], m, prio)
-        if bL == bK:
-            il()
-        vop(lambda: V.tensor_tensor_scan(re[:, 0:m], T[bP][:, 0:m], kp[:, 0:m], 0.0, A.add, A.mult), [nm("k"), bP], [nm("re")], m, prio)
-        for q, (a, z) in enumerate(((0, 16), (16, 24)) if B == 3 else ((0, 8),)):
-            vop(lambda a=a, z=z: V.tensor_tensor(e[:, 16 * a:16 * z], re[:, 0:m].indirect(T.oT[:, 24 + a:24 + z]), T.m16[:, 16 * a:16 * z], A.mult),
-                [nm("re"), "oE"] + M16, [part("e", q)], 16 * (z - a), prio, f=1.6)
+        vop(lambda: V.tensor_tensor(kk[:], T[bK][:, 0:m], u[:, 0:m], A.is_ge), [bK, nm("u"), nm("u0")], [nm("k")], m, prio)
+        vop(lambda: V.tensor_tensor_scan(re[:, 0:16 * m:16], T[bP][:, pc:pc + m], kk[:], 0.0, A.add, A.mult), [nm("k"), bP], [nm("re")], m, prio)
         for b in range(B):
-            mm([((T[bL][:, lo + 8 * b:lo + 8 * b + 8], e[:, 128 * b:128 * b + 128], T.Ms[:], False, b == B - 1), 8, 1)],
-               [part("e", b // 2), "Ms"], bL, prio)
-        if last is not None:
-            cp(last[0][:, 0:k], last[1], T[bL][:, lo:lo + k], bL, k, prio)
-        else:
-            ts(w[:, 0:k], wn, T[bL][:, lo:lo + k], bL, 0.0, float(HI), A.max, A.min, n=k, prio=prio)
-            act(L[:, 0:kc], Ln, T[bL][:, lo:lo + kc], [bL], kc, prio)
+            vop(lambda b=b: V.tensor_tensor_scan(e[:, 128 * b:128 * b + 128], T.hk[:], re[:, QW * b + 80:QW * b + 80 + QW:GW], 0.0, A.mult, A.add),
+                ["hk", nm("re"), nm("rz")], [nm("e%d" % b)], 128, prio)
+            mm([((T[bL][:, 8 * b:8 * b + 8], e[:, 128 * b:128 * b + 128], T.Ms[:], False, b == B - 1), 8, 1)], [nm("e%d" % b), "Ms"], bL, prio)
+        if not last:
+            ts(w[:, 0:k], wn, T[bL][:, 0:k], bL, clo, chi, A.max, A.min, n=k, prio=prio, extra=["lo", "hi"])
+            act(Lw[:], Lwn, T[bL][:, 0:k], [bL], k, prio)
 
     ts(T.rk[:, 16:32], "rka", T.L0[:, 0:16], "L0", 10, None, A.arith_shift_right, prio=-4)
     ts(T.rk[:, 0:16], "rkb", T.L0[:, 8:24], "L0", 10, None, A.arith_shift_right, prio=-4)
-    RK = ["rka", "rkb"]
-    slots(T.oh1, "oh1", 24, 0, CQ, T.rk[:, 0:32], RK, oR, ["oR"], T.Rs[:, 0:168], "Rs", T.su1, "su1", 0)
-    ts(T.ti[:], "ti", T.L0[:], "L0", 1023, None, A.bitwise_and, prio=0)
-    ts(T.tf[:], "tf", T.ti[:], "ti", 0.5, None, A.add, prio=0)
-    pack(T.X[:], "X", T.tf[:], "tf", 24, 0)
-    cp(T.W1[:].indirect(T.su1[:]), "W1", T.PK[:], "PK", NP, 0, extra=["su1"], f=3.5)
-    decode(T.W1, "W1", T.yi1, "yi1", T.msg1, "msg1", 0)
-    s1 = send(T.msg1, "msg1", "hq1", "land1", "rq1", True, 0)
+    slots(T.oh1, "oh1", su1, "su1", 0)
+    ts(T.ti[:, 0:24], "ti", T.L0[:], "L0", 1023, None, A.bitwise_and, prio=0)
+    pack(T.ex[:], "ex", T.PK[:], "PK", T.X[:], "X", T.ti[:, 0:24], "ti", 24, "vL", 0)
+    cp(T.W1[:].indirect(su1), "W1", T.PK[:], "PK", NP, 0, extra=["su1"], f=3.8)
+    message(T.W1, "W1", T.MB1, "msg1", 0)
+    s1 = send(T.MB1, ["msg1"], "rq1", 8, 0, 32, 0)
 
-    ts(p8, "p8", pg, "pf", 4.0, p4, A.mult, A.add, n=1, prio=2)
-    ts(p32, "p32", pg, "pf", 32.0, p16, A.mult, A.add, n=1, prio=2)
-    ts(T.S1[:], "S1", T.S1[:], "S1", p8, None, A.is_equal, n=48, prio=2, extra=["p8"])
-    ts(T.sA[:], "sA", T.sA[:], "sA", p32, None, A.is_equal, n=48, prio=2, extra=["p32"])
-    ts(T.sC[:, 1:49], "sC", T.sC[:, 1:49], "sC", p32, None, A.is_equal, n=48, prio=2, extra=["p32"])
-    fill(T.sC[:, 1:49:6], "sC", 0.0, 8, 2)
-    fill(T.sC[:, 6:49:6], "sC", 0.0, 8, 2)
-    tt(T.sC[:, 1:49], "sC", T.sA[:], "sA", T.sC[:, 1:49], "sC", A.subtract, n=48, prio=2)
-    tt(T.S2[:], "S2", T.sC[:, 0:48], "sC", T.sC[:, 1:49], "sC", A.subtract, n=48, prio=2, extra=["sC0"])
-    ts(T.Ms[:], "Ms", T.Ms[:], "Ms", pg, None, A.is_equal, n=8, prio=2, extra=["pf"])
-    ts(oE, "oE", T.oKi[:], "oKi", 6.0, 5.0, A.mult, A.add, n=24, prio=2)
-    act(T.Rd[:, 0:128], "Rd", T.jm[:], ["jm"], 128, 5)
-    ts(T.Rd[:, 0:128], "Rd", T.Rd[:, 0:128], "Rd", 1.0, None, A.min, n=128, prio=5)
-    act(T.Rd[:, 128:256], "Rdb", T.Rd[:, 0:128], ["Rd"], 128, 5)
-    act(T.Rd[:, 256:384], "Rdc", T.Rd[:, 0:128], ["Rd"], 128, 5)
-    ts(T.I1k[:], "I1k", T.I16[:], "I16", 1024.0, None, A.mult, n=64, prio=4)
-    gfill(T.scn[:, 56:64], "scnz", 0, 8, 4)
-    for t in ("O", "V", "R"):
-        gfill(T["u" + t][:, 0:1], "u0" + t, BIG, 1, 2)
-    for t in ("V", "R"):
-        gfill(T["pr" + t][:, 112:128], "pr" + t, 0, 16, 2)
-        gfill(T["pa" + t][:, 112:128], "pa" + t, 0, 16, 2)
-    gfill(T.Lv[:, 7:8], "Lv", 0, 1, 2)
-    gfill(T.Lv0[:, 7:8], "Lv0", 0, 1, 2)
-    cp(T.ND[:], "ND", T.NB[:], "NB", PWID, 2)
+    iota(T.sA[:, 0:57], "sA", [[1, 57]], -2, 0, 57, 1)
+    act(T.R1c[:], "R1c", T.cQ[:, 0:168], CQ, 168, 1, scale=0.0, bias=-float(BIG))
+    act(T.R1c[:, 6:168:GW], "R1c", T.bc[:, 0:24], ["one"], 24, 1, scale=float(BIG))
+    iota(T.cL[:, 0:140], "cL", [[1, 140]], -12, 0, 140, 2)
+    ts(T.S1[:], "S1", T.sA[:, 1:57], "sA", c2, None, A.is_equal, n=56, prio=2, extra=["c2"])
+    ts(T.sA[:, 0:57], "sA", T.sA[:, 0:57], "sA", c1, 1.0 / HOLD, A.is_equal, A.mult, n=57, prio=2, extra=["c1"])
+    tt(T.sA[:, 64:120], "S2", T.sA[:, 0:56], "sA", T.sA[:, 1:57], "sA", A.subtract, n=56, prio=2, f=2)
+    act(T.If[:], "If", T.I16[:], ["I16"], 128, 2)
+    ts(T.xB[:], "xB", T.jm[:], "jm", p16, None, A.is_lt, n=128, prio=2, extra=["pf"])
+    act(T.exv[:], "exv", T.m16[:, 0:128], ["m16"], 128, 2, scale=HOLD)
+    tt(T.hk[:], "hk", T.xB[:], "xB", T.exv[:], "exv", A.add, n=128, prio=2, f=2)
+    ts(T.Ms[:], "Ms", T.oKi[:, 0:8], "oKi", pg, T.hk[:, 0:1], A.is_equal, A.mult, n=8, prio=2, extra=["pf", "hk"])
+    act(T.hk[:, 0:128:16], "hk", T.bc[:, 0:8], ["one"], 8, 2, scale=0.0)
+    for t, n, pr in (("O", 3, 2), ("V", 1, 2), ("R", 1, 4)):
+        for b in range(n):
+            act(T["q" + t][:, QW * b + 80:QW * b + 80 + QW:GW], "re" + t, T.bc[:], ["one"], 128, pr, scale=0.0)
+        gfill(T["u" + t][:, 0:1], "u0" + t, BIG, 1, pr)
+    ts(m3, "m3", pi_, "pf", 3.0, None, A.is_equal, n=1, prio=2)
+    ts(xm, "xm", pi_, "pf", 3.0, None, A.is_lt, n=1, prio=2)
+    ts(T.pf[:, 24:28], "mf", T.oKi[:, 0:4], "oKi", pf_, None, A.is_equal, n=4, prio=2, extra=["pf"])
+    for f in range(4):
+        ts(T.EX[:, 128 * f:128 * f + 128], "EX%d" % f, T.cE[:], "cE", ck, col(24 + f), A.is_equal, A.mult, n=64, prio=2, extra=["ck", "mf"])
+    ts(T.LI[:, 0:140], "LI", T.cL[:, 0:140], "cL", cl, m3, A.is_equal, A.mult, n=70, prio=2, extra=["cl", "m3"])
+    ts(T.cO16[:, 32:40], "off", T.bc[:, 0:8], "one", lo, float(LO - 1), A.mult, A.add, n=8, prio=2, extra=["lo"])
     ts(T.Lo[:], "Lo", T.L0[:], "L0", float(-SH) - DEAD, None, A.add, prio=2)
     tt(T.Lo[:], "Lo", T.Lo[:], "Lo", T.oh1[:, 168:192], "oh1", A.mult, prio=2)
     ts(T.Lo[:], "Lo", T.Lo[:], "Lo", DEAD, None, A.add, prio=2)
     ts(T.wO[:], "wO", T.Lo[:], "Lo", 0.0, float(HI), A.max, A.min, prio=2)
-    own = lambda pr: step("O", 24, T.X, "X", T.wO, "wO", T.Lo, "Lo", "oK", "oP", "oK", pr)
+    own = lambda pr, last=False: step("O", T.X, "X", T.wO, "wO", PWID, "oK", "oP", "oL", "Lo", "Lo", 0.0, float(HI), pr, last)
     own(P_O1)
 
-    def visitors(land, ln, out, outn, sem, sent, fly):
-        add("V", lambda: [V.tensor_scalar(T.wv[:, 0:7], land[:, :, 16], 8.0, None, A.add)], [], ["wv", ln], 0.08, 0, [(sem, ARR)], (sent, fly))
-        ts(T.Xv[:], "Xv", land[:, :, 0:16], ln, -1024.0, None, A.add, n=112, prio=0)
-        add("V", lambda: [V.tensor_scalar(T.Lv0[:, 0:7], land[:, :, 16], 8.0, None, A.add)], [ln], ["Lv0"], 0.08, 1)
-        act(T.Lv[:, 0:7], "Lv", T.Lv0[:, 0:7], ["Lv0"], 7, 1)
-        a = (7, T.Xv, "Xv", T.wv, "wv", T.Lv, "Lv", "vK", "vP", "vL", 0)
-        step("V", *a)
-        step("V", *a)
-        tt(T.Ld[:], "Ld", T.Lv[:], "Lv", T.Lv0[:], "Lv0", A.subtract, n=8, prio=0)
-        step("V", *a, last=(out, outn), Lacc=T.Ld, Laccn="Ld")
+    def to_list(out, MB, c0, reads, bank, start, prio, ext=(), aft=None):
+        return mm([((out, T.LI[:, 12 - 4 * c:140 - 4 * c], MB[:, c0 + c:c0 + 32:4], start and c == 0, c == 3), 8, 0) for c in range(4)],
+                  ["LI"] + reads, bank, prio, ext, aft)
 
-    visitors(T.land1, "land1", T.out1, "out1", "rq1", s1, FLY[0])
-    s2 = send(T.out1, "out1", "hp1", "rep1", "rp1", False, 0)
+    def arrive(MB, mn, sem, sent, fly):
+        mm([((T.vL[:, 0:8], T.I16[:], T.cO16[:, 32:40], True, False), 8, 0)], ["I16", "off"], "vL", 0)
+        a = mm([((T.vP[:, f:128:4], T.EX[:, 128 * f:128 * f + 128], MB[:, 24:56], True, True), 32, 0) for f in range(4)],
+               ["EX%d" % f for f in range(4)] + [mn], "vP", 0, [(sem, ARR)], (sent, fly))
+        b = to_list(T.vL[:, 0:8], MB, 24, [mn], "vL", False, 0, [(sem, ARR)], (sent, fly))
+        tasks[b]["odeps"].add(a)
+        ts(T.Xv[:], "Xv", T.vP[:, 0:128], "vP", xm, m3, A.mult, A.add, n=128, prio=0, extra=["xm", "m3"])
+        ts(T.wv[:], "wv", T.vL[:, 0:8], "vL", lo, hi, A.max, A.min, n=8, prio=0, extra=["lo", "hi"])
+        act(T.Lv0[:], "Lv0", T.vL[:, 0:8], ["vL"], 8, 0)
 
-    ts(T.sBv[:, 0:7], "sBv", T.yi1[:, :, 16], "yi1t", -DEAD, None, A.add, n=7, prio=4)
-    tt(T.sBv[:, 0:7], "sBv", T.sBv[:, 0:7], "sBv", T.cS[:, 0:7], CS[0], A.add, n=7, prio=4, extra=CS[1:])
-    ts(T.sBg[:, 0:7], "sBg", T.yi1[:, :, 16], "yi1t", float(NT), None, A.is_lt, n=7, prio=4)
-    tt(T.sBv[:, 0:7], "sBv", T.sBv[:, 0:7], "sBv", T.sBg[:, 0:7], "sBg", A.mult, n=7, prio=4)
-    ts(T.sBv[:, 0:7], "sBv", T.sBv[:, 0:7], "sBv", DEAD, None, A.add, n=7, prio=4)
-    cp(T.yB[:], "yB", T.yi1[:, :, 0:16], "yi1", 112, 4)
-    ts(T.xB[:], "xB", T.yi1[:, :, 0:16], "yi1", -1024.0, None, A.add, n=112, prio=5)
-    gfill(T.W2[:, 0:112], "W2", NONE, 112, 3)
-    gfill(T.Rs[:, 168:224], "RsB", 1, 56, 4)
-    gfill(T.Rs[:, 168:224:8], "RsB", 0, 7, 4)
-    gfill(T.rkB[:, 7:8], "rkB", rank, 1, 4)
-    fill(T.Lb[:, 7:8], "Lb", DEAD, 1, 4)
-    ts(T.pj[:, 4:8], "pj4", T.pi[:], "pi", 7, None, A.bitwise_and, n=4, prio=4)
-    cp(oB8, "oB8", T.pj[:, 4:8], "pj4", 4, 4)
+    def visitors(RP, outn):
+        for s in range(3):
+            step("V", T.Xv, "Xv", T.wv, "wv", 0, "vK", "vP", "vL", "Lv" if s else "Lv0", "Lv", lo, hi, 0, s == 2)
+        tt(RP[:, 8:16], outn, T.vL[:, 0:8], "vL", T.Lv0[:], "Lv0", A.subtract, n=8, prio=0)
+
+    arrive(T.MB1, "msg1", "rq1", s1, FLY[0])
+    steps_rows(T.NP[:], "NP", NT * owners[6], 32, "HL1", "N1", "ln1", 0, [("tC", len(E8))], (sC, FLY_T[0]))
+    load("Y", "lr1", lambda: [g.sync.dma_start(T.R1[0:16, :], T.A1[:])], 1, [], ["R1"], 0.1, 2.0, 0, [("tA", len(E8))], (sA, FLY_T[1]))
+    load("Y", "lr1", lambda: [g.sync.dma_start(T.R1[16:20, :], T.A2[:])], 1, [], ["R1b"], 0.1, 2.0, 0, [("tB", len(E8))], (sB, FLY_T[2]))
+    windows(0, "R1", ["R1", "R1b"], "N1", ("rA", "rB", "vK", "vP"), "VSSV", 0)
+    visitors(T.RP1, "out1")
+    s2 = send(T.RP1, ["out1"], "rp1", 2, 10, 2, 0)
+
+    for k in range(4):
+        a, b = owners[2 * k], owners[2 * k + 1]
+        act(T.cS[:, 2 * k:2 * k + 2], "cS%d" % k, T.pf[:, 6:8], ["pf"], 2, 4, scale=float(NT * (b - a)), bias=float(NT * a - SH - 1) - DEAD)
+    sBv, sBg = T.sB[:, 0:8], T.sB[:, 8:16]
+    to_list(T.rA[:, 0:8], T.MB1, 0, ["msg1"], "rA", True, 3)
+    tt(sBv, "sBv", T.rA[:, 0:8], "rA", T.cS[:], "cS0", A.add, n=8, prio=3, extra=["cS1", "cS2", "cS3"])
+    ts(sBg, "sBg", T.rA[:, 0:8], "rA", 2000.0, None, A.is_lt, n=8, prio=3)
+    tt(sBv, "sBv", sBv, "sBv", sBg, "sBg", A.mult, n=8, prio=3)
+    ts(sBv, "sBv", sBv, "sBv", DEAD, None, A.add, n=8, prio=3)
+    ts(T.xB[:], "xB", T.W1[:, 0:128], "W1", xm, m3, A.mult, A.add, n=128, prio=3, extra=["xm", "m3"])
+    iota(T.W2[:, 0:128], "W2", [[0, 128]], NONE, 0, 128, 3, False)
+    iota(T.cD[:, 8:72], "cB", [[-32, 4], [-1, 2], [0, 8]], 0, 0, 64, 3)
+    gfill(T.scn[:, 56:64], "scnz", 0, 8, 4)
+    gfill(T.RP2[:, 0:2], "RP2p", 0, 2, 3)
+    ts(T.cO16[:, 24:32], "cOn", T.cOw[:, 0:8], "cOw", -1.0, 129.0, A.mult, A.add, n=8, prio=3)
+    ts(T.I1k[:], "I1k", T.I16[:], "I16", 1024.0, None, A.mult, n=64, prio=3)
+    ts(T.pj[:, 8:12], "pj8", T.pi[:], "pi", 7, None, A.bitwise_and, n=4, prio=3)
+    cp(oB8, "oB8", T.pj[:, 8:12], "pj8", 4, 3)
     own(P_O2)
     own(P_O2)
 
     RKC = (SH - 511.1875) / 1024.0
     ts(T.rk[:, 16:32], "rka", T.Lo[:, 0:16], "Lo", 1.0 / 1024, RKC, A.mult, A.add, prio=P_A)
     ts(T.rk[:, 0:16], "rkb", T.Lo[:, 8:24], "Lo", 1.0 / 1024, RKC, A.mult, A.add, prio=P_A)
-    ts(T.ci[:], "ci", T.Lo[:], "Lo", float(SH), None, A.add, prio=P_A)
-    ts(T.ti[:], "ti", T.ci[:], "ci", 1023, None, A.bitwise_and, prio=P_A)
-    ts(T.tf[:], "tf", T.ti[:], "ti", 0.5, None, A.add, prio=P_A)
-    slots(T.ohA, "ohA", 24, 0, CQ, T.rk[:, 0:32], RK, oR, ["oR"], T.Rs[:, 0:168], "Rs", T.suA, "suA", P_A)
-    cp(T.cnt[:, 0:7], "cnt", T.rA[:, 279:424:24], "rA", 7, P_A, extra=["sc"])
-    pack(T.X[:], "X", T.tf[:], "tf", 24, P_A)
-    cp(T.W2[:].indirect(T.suA[:]), "W2", T.PK[:], "PK", NP, P_A, extra=["suA"], f=3.5)
+    ts(T.ci[:, 0:24], "ci", T.Lo[:], "Lo", float(SH), None, A.add, prio=P_A)
+    ts(T.ti[:, 0:24], "ti", T.ci[:, 0:24], "ci", 1023, None, A.bitwise_and, prio=P_A)
+    slots(T.ohA, "ohA", suA, "suA", P_A)
+    pack(T.ex[:], "ex", T.PK[:], "PK", T.X[:], "X", T.ti[:, 0:24], "ti", 24, "oP", P_A)
+    cp(T.W2[:].indirect(suA), "W2", T.PK[:], "PK", NP, P_A, extra=["suA"], f=3.8)
 
-    vop(lambda: V.tensor_tensor(T.Lb[:, 0:7], T.sBv[:, 0:7], T.rep1[:, 0:7], A.add), ["sBv"], ["Lb"], 7, 0, [("rp1", ARR)], (s2, FLY[1]))
-    ts(T.rkB[:, 0:7], "rkB", T.Lb[:, 0:7], "Lb", 1.0 / 1024, RKC, A.mult, A.add, n=7, prio=0)
-    ts(T.ci[:, 0:7], "ci", T.Lb[:, 0:7], "Lb", float(SH), None, A.add, n=7, prio=0)
-    ts(T.ti[:, 0:7], "ti", T.ci[:, 0:7], "ci", 1023, None, A.bitwise_and, n=7, prio=0)
-    slots(T.ohA, "ohA", 8, 192, CQB, T.rkB[:], ["rkB"], oB8, ["oB8"], T.Rs[:, 168:224], "RsB", T.suB, "suB", 0, cnt=T.cnt[:, 0:7])
-    pack(T.yB[:], "yB", T.ti[:, 0:8], "ti", 7, 0)
-    cp(T.W2[:].indirect(T.suB[:, 0:7]), "W2", T.PK[:, 0:112], "PK", 112, 0, extra=["suB"], f=3.5)
-    decode(T.W2, "W2", T.yi2, "yi2", T.msg2, "msg2", 0)
-    s3 = send(T.msg2, "msg2", "hq2", "land2", "rq2", True, 0)
+    mm([((T.vP[:, 0:64], ones, T.cD[0:1, 8:72], True, False), 64, 0), ((T.vP[:, 56:64], T.I16[:], T.cO16[:, 24:32], False, False), 8, 0)],
+       ["one", "cB", "I16", "cOn"], "vP", 1)
+    vop(lambda: V.tensor_tensor(T.Lb[:], sBv, T.RP1[:, 2:10], A.add), ["sBv", "out1"], ["Lb"], 8, 0, [("rp1", ARR)], (s2, FLY[1]))
+    ts(T.rkB[:], "rkB", T.Lb[:], "Lb", 1.0 / 1024, RKC, A.mult, A.add, n=8, prio=0)
+    ts(T.ci[:, 24:32], "ciB", T.Lb[:], "Lb", float(SH), None, A.add, n=8, prio=0)
+    ts(T.ti[:, 24:32], "tiB", T.ci[:, 24:32], "ciB", 1023, None, A.bitwise_and, n=8, prio=0)
+    vop(lambda: V.tensor_tensor(T.ohB[:], T.rkB[:].indirect(oB8), T.cQ[:, 0:192:3], A.is_equal), ["rkB", "oB8"] + CQ, ["ohB"], 64, 0, f=1.6)
+    mm([((T.vK[:, 0:56], T.G2[:], T.ohB[:, 0:56], True, True), 56, 0)], ["G2", "ohB"], "vK", 0)
+    mm([((T.vP[:, 0:64], T.I1k[:], T.ohB[:], False, False), 64, 0), ((T.vP[:, 0:56], T.U2[:], T.ohB[:, 0:56], False, True), 56, 0)],
+       ["I1k", "U2", "ohB"], "vP", 0)
+    vop(lambda: V.tensor_tensor_scan(T.scn[:, 0:56], T.Rs[:, 0:168:3], T.vK[:, 0:56], 0.0, A.mult, A.add), ["Rs", "vK"], ["scn"], 56, 0)
+    vop(lambda: V.tensor_tensor(T.zz[:], T.scn[:], T.vP[:, 0:64], A.add), ["scn", "scnz", "vP"], ["zz"], 64, 0)
+    tt(T.mx[:, 0:32], "mx0", T.zz[:, 0:32], "zz", T.zz[:, 32:64], "zz", A.max, n=32, prio=0)
+    tt(T.mx[:, 32:48], "mx1", T.mx[:, 0:16], "mx0", T.mx[:, 16:32], "mx0", A.max, n=16, prio=0)
+    tt(T.mx[:, 48:56], "mx2", T.mx[:, 32:40], "mx1", T.mx[:, 40:48], "mx1", A.max, n=8, prio=0)
+    ts(suB, "suB", T.mx[:, 48:56], "mx2", -1.0, 1056.0, A.mult, A.add, n=8, prio=0)
+    pack(T.exB[:], "exB", T.PKB[:], "PKB", T.xB[:], "xB", T.ti[:, 24:32], "tiB", 8, "vL", 0)
+    cp(T.W2[:].indirect(suB), "W2", T.PKB[:], "PKB", 128, 0, extra=["suB"], f=3.8)
+    message(T.W2, "W2", T.MB2, "msg2", 0)
+    s3 = send(T.MB2, ["msg2", "RP2p"], "rq2", 8, 0, 32, 0)
 
-    ts(T.wr[:, 0:7], "wr", T.Lb[:, 0:7], "Lb", 0.0, float(HI), A.max, A.min, n=7, prio=P_C)
-    cp(T.Gf[:], "Gf", T.G16[:], "G16", 128, P_C)
-    gfill(T.vW[:, 112:120], "vW", 0, 8, 4)
-    gfill(T.dW[:, 112:136], "dW0", 8192, 24, 4)
-    ts(pK, "pK", p16, "pf", 14.5, -float(MID), A.is_lt, A.mult, n=1, prio=5)
-    for _ in range(3):
-        step("R", 7, T.xB, "xB", T.wr, "wr", T.Lb, "Lb", "rA", "rB", "rC", P_R)
-        own(P_O3)
-    visitors(T.land2, "land2", T.out2, "out2", "rq2", s3, FLY[2])
-    s4 = send(T.out2, "out2", "hp2", "rep2", "rp2", False, 0)
+    ts(T.wr[:], "wr", T.Lb[:], "Lb", 0.0, float(HI), A.max, A.min, n=8, prio=P_C)
+    act(T.Gf[:], "Gf", T.G2[:], ["G2"], 128, P_C, scale=0.5)
+    gfill(T.vW[:, 128:136], "vW0", 0, 8, 4)
+    gfill(T.dW[:, 128:136], "dW0", 8192, 8, 4)
+    act(T.scC[:], "scC", T.m16[:, 0:192], M16, 192, 5, scale=-float(BIG + K16), bias=float(K16))
+    ts(T.Rd[:, 0:128], "Rd", T.jm[:], "jm", 1.0, None, A.min, n=128, prio=5)
+    act(T.Rd[:, 128:256], "Rdb", T.Rd[:, 0:128], ["Rd"], 128, 5)
+    act(T.Rd[:, 256:384], "Rdc", T.Rd[:, 0:128], ["Rd"], 128, 5)
+    for s in range(3):
+        step("R", T.xB, "xB", T.wr, "wr", PWID, "rA", "rA", "rB", "Lb", "Lb", 0.0, float(HI), P_R, s == 2)
+        own(P_O3, s == 2)
+    arrive(T.MB2, "msg2", "rq2", s3, FLY[2])
+    visitors(T.RP2, "out2")
+    s4 = send(T.RP2, ["out2"], "rp2", 2, 10, 2, 0)
 
-    ts(T.s1c[:], "s1c", T.su1[:], "su1", 112.0, None, A.min, prio=P_C)
-    ts(T.smA[:], "smA", T.suA[:], "suA", 128.0, None, A.min, prio=P_C)
-    ts(T.smB[:, 0:7], "smB", T.suB[:, 0:7], "suB", 128.0, None, A.min, n=7, prio=P_C)
-    ts(T.vB[:, 0:7], "vB", T.Lb[:, 0:7], "Lb", 8192.0, 256.0, A.add, A.mult, n=7, prio=P_C)
-    tt(T.vB[:, 0:7], "vB", T.vB[:, 0:7], "vB", T.smB[:, 0:7], "smB", A.add, n=7, prio=P_C)
-    vop(lambda: V.tensor_tensor(T.exv[:], T.vB[:, 0:7].indirect(T.oT[:, 0:7]), T.m16[:, 0:112], A.mult), ["vB", "oK"] + M16, ["exv"], 112, P_C, f=1.6)
-    mm([((T.rC[:, 0:112], T.Gf[:], T.exv[:], True, True), 112, 1)], ["Gf", "exv"], "rC", P_C)
-    cp(T.vW[:, 0:112], "vW", T.rC[:, 0:112], "rC", 112, P_C)
-    vop(lambda: V.tensor_tensor(T.gv[:], T.vW[:].indirect(T.s1c[:]), T.m16[:], A.mult), ["vW", "s1c"] + M16, ["gv", "gvb"], NP, P_C, f=1.6)
+    smA, smB, vB = T.sm[:, 0:24], T.sm[:, 24:32], T.sm[:, 32:40]
+    ts(s1c, "s1c", su1, "su1", 128.0, None, A.min, prio=P_C)
+    ts(smA, "smA", suA, "suA", 128.0, None, A.min, prio=P_C)
+    ts(smB, "smB", suB, "suB", 128.0, None, A.min, n=8, prio=P_C)
+    ts(vB, "vB", T.rB[:, 0:8], "rB", 8192.0, 256.0, A.add, A.mult, n=8, prio=P_C)
+    tt(vB, "vB", vB, "vB", smB, "smB", A.add, n=8, prio=P_C)
+    vop(lambda: V.tensor_tensor(T.exv[:], vB.indirect(T.oT[:, 0:8]), T.m16[:, 0:128], A.mult), ["vB", "oK"] + M16, ["exv"], 128, P_C, f=1.6)
+    mm([((T.rA[:, 0:128], T.Gf[:], T.exv[:], True, True), 128, 1)], ["Gf", "exv"], "rA", P_C)
+    act(T.vW[:, 0:128], "vW", T.rA[:, 0:128], ["rA"], 128, P_C)
+    vop(lambda: V.tensor_tensor(T.gv[:], T.vW[:].indirect(s1c), T.m16[:], A.mult), ["vW", "vW0", "s1c"] + M16, ["gv", "gvb"], NP, P_C, f=1.6)
     vop(lambda: V.tensor_tensor_scan(T.sv[:], T.Rd[:], T.gv[:], 0.0, A.mult, A.add), ["Rd", "Rdb", "Rdc", "gv", "gvb"], ["sv", "svb"], NP, P_C)
-    ts(T.vO[:], "vO", T.Lo[:], "Lo", 8192.0, 256.0, A.add, A.mult, prio=P_C)
-    tt(T.vO[:], "vO", T.vO[:], "vO", T.smA[:], "smA", A.add, prio=P_C)
+    ts(T.vO[:], "vO", T.oL[:, 0:24], "oL", 8192.0, 256.0, A.add, A.mult, prio=P_C)
+    tt(T.vO[:], "vO", T.vO[:], "vO", smA, "smA", A.add, prio=P_C)
     tt(T.vO[:], "vO", T.vO[:], "vO", T.oh1[:, 168:192], "oh1", A.mult, prio=P_C)
     tt(T.vt[:], "vt", T.vO[:], "vO", T.sv[:, 15:NP:16], "sv", A.add, prio=P_C, extra=["svb"])
-    ts(T.ci[:], "ci", T.vt[:], "vt", 255, None, A.bitwise_and, prio=P_C)
-    cp(T.tau[:], "tau", T.ci[:], "ci", 24, P_C)
+    ts(T.ci[:, 0:24], "ci", T.vt[:], "vt", 255, None, A.bitwise_and, prio=P_C)
+    cp(T.tau[:], "tau", T.ci[:, 0:24], "ci", 24, P_C)
     ts(T.vt[:], "vt", T.vt[:], "vt", 8, None, A.arith_shift_right, prio=P_C)
-    ts(T.Yb[:], "Yb", T.vt[:], "vt", float(SH - 16384), pK, A.add, A.add, prio=P_C, extra=["pK"])
+    ts(T.sm[:, 40:64], "Yb", T.vt[:], "vt", float(SH - 16384), pK, A.add, A.add, prio=P_C, extra=["pK"])
 
-    vop(lambda: V.tensor_tensor(T.exv[:], T.rep2[:, 0:7].indirect(T.oT[:, 0:7]), T.m16[:, 0:112], A.mult), ["oK"] + M16, ["exv"], 112, 0,
-        [("rp2", ARR)], (s4, FLY[3]), f=1.6)
-    mm([((T.rC[:, 0:112], T.Gf[:], T.exv[:], True, True), 112, 1)], ["Gf", "exv"], "rC", 0)
-    ts(T.dW[:, 0:112], "dW", T.rC[:, 0:112], "rC", 8192.0, None, A.add, n=112, prio=0)
+    vop(lambda: V.tensor_tensor(T.exv[:], T.RP2[:, 0:10].indirect(T.oT[:, 2:10]), T.m16[:, 0:128], A.mult), ["oK", "out2", "RP2p"] + M16,
+        ["exv"], 128, 0, [("rp2", ARR)], (s4, FLY[3]), f=1.6)
+    mm([((T.rA[:, 0:128], T.Gf[:], T.exv[:], True, True), 128, 1)], ["Gf", "exv"], "rA", 0)
+    ts(T.dW[:, 0:128], "dW", T.rA[:, 0:128], "rA", 8192.0, None, A.add, n=128, prio=0)
     add("S", lambda: [S.activation(T.gv[:, 192:NP], T.dW[:].indirect(T.tau[:, 12:24]), F.Copy)], ["dW", "dW0", "tau"], ["gvb"], 0.4, 0)
     vop(lambda: V.tensor_copy(T.gv[:, 0:192], T.dW[:].indirect(T.tau[:, 0:12])), ["dW", "dW0", "tau"], ["gv"], 192, 0, f=1.6)
     for h, n in ((0, ""), (192, "b")):
-        vop(lambda h=h: V.tensor_tensor_scan(T.sv[:, h:h + 192], T.scC[:], T.gv[:, h:h + 192], 0.0, A.add, A.max), ["scC", "scCb", "gv" + n], ["sv" + n], 192, 0)
-    tt(T.vO[:], "vO", T.sv[:, 15:NP:16], "sv", T.Yb[:], "Yb", A.add, prio=0, extra=["svb"])
+        vop(lambda h=h: V.tensor_tensor_scan(T.sv[:, h:h + 192], T.scC[:], T.gv[:, h:h + 192], 0.0, A.add, A.max), ["scC", "gv" + n], ["sv" + n], 192, 0)
+    tt(T.vO[:], "vO", T.sv[:, 15:NP:16], "sv", T.sm[:, 40:64], "Yb", A.add, prio=0, extra=["svb"])
     load("Y", "st", lambda: [g.sync.dma_start(T.y[:], T.vO[:])], 1, ["vO"], [], 0.1, 0.0)
 
     order = plan(tasks)
@@ -615,4 +631,6 @@ def rank_program(g, core, T, topo):
         g.wait_ge(T.sem[s], v)
     for s in ("rq1", "rp1", "rq2", "rp2"):
         g.wait_ge(T.sem[s], ARR)
+    for s in ("tA", "tB", "tC"):
+        g.wait_ge(T.sem[s], len(E8))
     g.wait_ge(T.sem.loc, nloc[0])

@@ -5,7 +5,7 @@ NT, NP, NK = 1024, 384, 24
 LO, HI, PWID = 8, 1032, 1040
 DEAD = 7.375
 WIN = 640
-BIG, K16, K4 = 8388608, 32768, 8192
+BIG, MID, K4 = 8388608, 4194304, 8192
 NONE = 4096
 HOLD = 2.0 ** 60
 GW, QW = 7, 896
@@ -14,29 +14,28 @@ _sb = {
     "X": ([128, NP], "int32"), "L0": ([128, NK], "int32"), "PW": ([128, 2 * PWID], "float32"), "ND": ([128, 2 * PWID], "bfloat16"),
     "Xv": ([128, 128], "float32"), "xB": ([128, 128], "float32"),
     "Zp": ([128, 128], "int32"), "Zd": ([128, 32], "int32"), "Zn": ([128, 32], "int32"), "H1": ([128, 128], "float16"),
-    "Ld": ([128, 64], "float16"), "NU": ([128, 32], "uint16"),
-    "NP": ([128, 32], "uint16"), "st": ([128, 128], "float32"), "HL0": ([128, 64], "bfloat16"),
-    "HL1": ([128, 64], "bfloat16"), "R0": ([128, NT], "float16"), "R1": ([128, NT], "float16"), "N0": ([128, NT], "bfloat16"),
-    "N1": ([128, NT], "bfloat16"), "LP": ([128, 128], "float16"),
-    "pi": ([128, 4], "int32"), "pj": ([128, 12], "int32"), "pf": ([128, 28], "float32"), "jm": ([128, 128], "bfloat16"),
-    "mk": ([128, 128], "float32"), "md16": ([128, 128], "bfloat16"), "m16": ([128, NP], "bfloat16"), "Rd": ([128, NP], "float32"),
+    "Ld": ([128, 64], "float16"), "NU": ([128, 32], "uint16"), "NP": ([128, 32], "uint16"), "st": ([128, 128], "float32"),
+    "HL0": ([128, 64], "bfloat16"), "HL1": ([128, 64], "bfloat16"), "R0": ([128, NT], "float16"), "R1": ([128, NT], "float16"),
+    "N0": ([128, NT], "bfloat16"), "N1": ([128, NT], "bfloat16"), "LP": ([128, 128], "float16"),
+    "pi": ([128, 4], "int32"), "pj": ([128, 12], "int32"), "pf": ([128, 32], "float32"), "jm": ([128, 128], "bfloat16"),
+    "mk": ([128, 128], "float32"), "md16": ([128, 128], "bfloat16"), "m16": ([128, 192], "bfloat16"),
     "G2": ([128, 128], "float16"), "G3": ([128, 128], "float16"), "Gf": ([128, 128], "float32"), "cE": ([128, 128], "bfloat16"),
     "U2": ([128, 128], "float16"), "I16": ([128, 128], "float16"), "If": ([128, 128], "float32"), "I1k": ([128, 128], "float16"),
-    "EX": ([128, 512], "float16"), "cL": ([128, 144], "bfloat16"), "LI": ([128, 144], "float16"), "j4": ([128, 128], "bfloat16"),
-    "S1": ([128, 56], "float32"), "hk": ([128, 128], "float32"), "sA": ([128, 120], "bfloat16"), "Ms": ([128, 8], "float32"),
+    "EX": ([128, 512], "float16"), "cL": ([128, 144], "bfloat16"), "LI": ([128, 144], "float16"),
+    "S1": ([128, 56], "float32"), "hk": ([128, NP], "float32"), "sA": ([128, 120], "bfloat16"), "Ms": ([128, 8], "float32"),
     "R1c": ([128, 168], "float32"), "scC": ([128, 192], "float32"), "sc4": ([128, 128], "float32"),
     "oKi": ([128, 32], "int32"), "oRi": ([128, 12], "float32"), "oT": ([128, 48], "uint16"),
     "Rs": ([128, 168], "float32"), "cQ": ([128, 192], "float32"), "cD": ([128, 72], "bfloat16"), "bc": ([128, 128], "bfloat16"),
     "cOw": ([128, NK], "float32"), "cO16": ([128, 40], "float16"), "cS": ([128, 8], "float32"),
     "rk": ([128, 32], "int32"), "ci": ([128, 32], "int32"), "ti": ([128, 32], "int32"), "rkB": ([128, 8], "int32"),
-    "oh1": ([128, 192], "float16"), "ohA": ([128, 192], "float16"), "ohB": ([128, 64], "float16"), "ex": ([128, NP], "float16"),
-    "exB": ([128, 128], "float16"), "scn": ([128, 64], "float32"), "zz": ([128, 64], "float32"), "mx": ([128, 56], "float32"),
-    "z1": ([128, 168], "float16"), "z2": ([128, 192], "float16"), "PK": ([128, NP], "int32"), "PKB": ([128, 128], "int32"),
-    "su": ([128, 96], "uint16"), "W1": ([128, WIN], "int32"), "W2": ([128, WIN], "int32"), "sd": ([128, 128], "float32"),
+    "oh1": ([128, 192], "float16"), "ohA": ([128, 192], "float16"), "ohB": ([128, 64], "float16"), "ex": ([128, 512], "float16"),
+    "scn": ([128, 64], "float32"), "zz": ([128, 64], "float32"), "mx": ([128, 56], "float32"),
+    "z1": ([128, 168], "float16"), "z2": ([128, 192], "float16"), "PK": ([128, 512], "float32"),
+    "su": ([128, 96], "uint16"), "W1": ([128, WIN], "float32"), "W2": ([128, WIN], "float32"), "sd": ([128, 128], "float32"),
     "MB1": ([128, 56], "float16"), "MB2": ([128, 56], "float16"), "RP1": ([128, 16], "float32"), "RP2": ([128, 16], "float32"),
     "sB": ([128, 16], "float32"),
-    "Lo": ([128, NK], "float32"), "wO": ([128, NK], "uint16"), "Lv0": ([128, 8], "float32"), "Lv": ([128, 8], "float32"), "wv": ([128, 8], "uint16"),
-    "Lb": ([128, 8], "float32"), "wr": ([128, 8], "uint16"),
+    "Lo": ([128, NK], "float32"), "Lm": ([128, NK], "float32"), "wO": ([128, NK], "uint16"), "Lv0": ([128, 8], "float32"),
+    "Lv": ([128, 8], "float32"), "wV": ([128, 8], "uint16"), "Lb": ([128, 8], "float32"), "Lr": ([128, 8], "float32"), "wR": ([128, 8], "uint16"),
     "sm": ([128, 64], "float32"), "exv": ([128, 128], "float32"), "vW": ([128, 136], "float32"), "gv": ([128, NP], "float32"),
     "sv": ([128, NP], "float32"), "vO": ([128, NK], "float32"), "vt": ([128, NK], "int32"), "tau": ([128, NK], "uint16"),
     "dW": ([128, 136], "float32"),
@@ -44,24 +43,27 @@ _sb = {
 for _t, _n in (("O", 3), ("V", 1), ("R", 1)):
     _sb["pr" + _t] = ([128, 128 * _n], "float32")
     _sb["pa" + _t] = ([128, 128 * _n], "bfloat16")
-    _sb["u" + _t] = ([128, 56 * _n + 8], "float32")
+    _sb["u" + _t] = ([128, 64 * _n], "float32")
     _sb["k" + _t] = ([128, 56 * _n], "float32")
-    _sb["q" + _t] = ([128, QW * _n + 80], "float32")
+    _sb["q" + _t] = ([128, (QW + 80) * _n], "float32")
     _sb["e" + _t] = ([128, 128 * _n], "float32")
 SCRATCH = {_k: ("sbuf", _v[0], _v[1]) for _k, _v in _sb.items()}
 SCRATCH["A1"] = ("dram", [128, 128], "float16")
 SCRATCH["A2"] = ("dram", [128, 32], "float16")
 SCRATCH["A3"] = ("dram", [128, 32], "uint16")
-PSUM = ("oK", "oP", "oL", "vK", "vP", "vL", "rA", "rB")
+PSUM = ("o0", "o1", "o2", "vK", "vP", "vL", "rA", "rB")
 for _k in PSUM:
     SCRATCH[_k] = ("psum", [128, 512], "float32")
 SEMAPHORES = ["sV", "sS", "sT", "sG", "ldA", "ldP", "ldZ", "ldD", "ldN", "lr0", "ln0", "lr1", "ln1", "st", "rq1", "rq2", "rp1", "rp2",
               "hA", "hB", "hC", "tA", "tB", "tC", "loc"]
 
-FLY = (3.0, 3.0, 3.0, 3.0)
-FLY_T = (10.0, 10.0, 9.5)
-WAKE, SLACK, SLACK2 = 0.1, 0.1, 0.1
-P_T, P_TO, P_O1, P_O2, P_A, P_O3, P_R, P_C = -8, 1, 2, 2, 1, 5, 4, 4
+FLY = (2.8, 2.8, 2.8, 2.8)
+FLY_T = (8.0, 8.5, 8.0)
+WAKE, MARGIN, ROUNDS, FAC, CALL = 0.2, 0.03, 8, 1.25, 0.3
+LAT0 = 2.5
+MERGE, PARTS, FIX, ADD = False, ((0, 3),), 64, False
+DELAY = False
+PLANS = {}
 
 
 def wiring(T, topo, core):
@@ -75,13 +77,9 @@ def wiring(T, topo, core):
     return peers, partner, rel[:2]
 
 
-def emask(engs):
-    return sum(1 << e for e in engs)
-
-
 def transfer(topo, src_core, dst_core, es, sem, s_ap, d_ap):
     rid, pid = topo.addr(dst_core, src_core)
-    return RemoteDMATransfer(dst_ids=[DstId(rid=rid, pnc=pid)], dma_engine_mask=emask(es), remote_sem=sem, src=s_ap, dst=d_ap)
+    return RemoteDMATransfer(dst_ids=[DstId(rid=rid, pnc=pid)], dma_engine_mask=sum(1 << e for e in es), remote_sem=sem, src=s_ap, dst=d_ap)
 
 
 def relay_program(g, core, T, topo, owner):
@@ -95,49 +93,65 @@ def relay_program(g, core, T, topo, owner):
     g.wait_ge(T.sem.loc, len(es) * len(pieces))
 
 
-def plan(tasks):
+def place(tasks, pre, key):
     n = len(tasks)
-    fin, free, order, ready = {}, {}, {}, {}
-    pre = [t["deps"] | t["odeps"] | ({t["aft"][0]} if t["aft"] else set()) for t in tasks]
-    pend = [len(x) for x in pre]
     succ = [[] for _ in tasks]
+    pend = [len(x) for x in pre]
     for i, x in enumerate(pre):
         for d in x:
             succ[d].append(i)
-    tail = [0.0] * n
-    for i in range(n - 1, -1, -1):
-        tail[i] = tasks[i]["cost"] + WAKE + max([0.0] + [tail[x] for x in succ[i] if tasks[x]["prio"] <= tasks[i]["prio"]])
-
-    def enter(i):
-        t = tasks[i]
-        e = max([0.0] + [fin[d] + WAKE for d in t["deps"]] + [fin[d] for d in t["odeps"]])
-        if t["aft"]:
-            e = max(e, fin[t["aft"][0]] + t["aft"][1])
-        ready.setdefault(t["q"], {})[i] = e
-    for i in range(n):
-        if pend[i] == 0:
-            enter(i)
-    while len(fin) < n:
-        m, q = min((max(free.get(q, 0.0), min(l.values())), q) for q, l in ready.items() if l)
-        l, fr = ready[q], free.get(q, 0.0)
-        st = {i: max(fr, e) for i, e in l.items()}
-        pick = min(l, key=lambda i: (tasks[i]["prio"], max(st[i] - m - SLACK, 0.0), -tail[i], i))
-        if st[pick] > m + SLACK:
-            fits = [i for i in l if st[i] + tasks[i]["cost"] <= st[pick] + SLACK2]
-            now = [i for i in fits if st[i] <= m + SLACK]
-            if now:
-                pick = min(now, key=lambda i: (tasks[i]["prio"], -tail[i], i))
-            elif fits:
-                pick = min(fits, key=lambda i: (st[i], tasks[i]["prio"], i))
-        fin[pick] = st[pick] + tasks[pick]["cost"]
-        free[q] = fin[pick]
-        fin[pick] += tasks[pick]["lat"]
-        order.setdefault(q, []).append(pick)
-        del l[pick]
-        for x in succ[pick]:
+    fin, busy = [0.0] * n, {}
+    ready = [i for i in range(n) if pend[i] == 0]
+    while ready:
+        i = min(ready, key=lambda j: (key[j], j))
+        ready.remove(i)
+        c = tasks[i]["cost"]
+        s = max([0.0] + [fin[d] + w for d, w in pre[i].items()])
+        l = busy.setdefault(tasks[i]["q"], [])
+        for a, z in l:
+            if s + c + MARGIN <= a:
+                break
+            s = max(s, z)
+        fin[i] = s + c
+        l.append((s, s + c))
+        l.sort()
+        for x in succ[i]:
             pend[x] -= 1
             if pend[x] == 0:
-                enter(x)
+                ready.append(x)
+    return fin
+
+
+def plan(tasks):
+    n = len(tasks)
+    if n in PLANS:
+        return PLANS[n]
+    pre = []
+    for t in tasks:
+        p = {d: 0.0 for d in t["odeps"]}
+        p.update({d: WAKE + tasks[d]["lat"] for d in t["deps"]})
+        if t["aft"]:
+            p[t["aft"][0]] = max(p.get(t["aft"][0], 0.0), t["aft"][1])
+        pre.append(p)
+    post = [{} for _ in tasks]
+    for i, p in enumerate(pre):
+        for d, w in p.items():
+            post[d][i] = w
+    tail = [0.0] * n
+    for i in range(n - 1, -1, -1):
+        tail[i] = tasks[i]["cost"] + max([0.0] + [tail[x] + w for x, w in post[i].items()])
+    key, best = [-x for x in tail], None
+    for _ in range(ROUNDS):
+        fin = place(tasks, pre, key)
+        if best is None or max(fin) < max(best):
+            best = fin
+        back = place(tasks, post, [-x for x in fin])
+        key = [-x for x in back]
+    order = {}
+    for i in sorted(range(n), key=lambda j: (best[j] - tasks[j]["cost"], j)):
+        order.setdefault(tasks[i]["q"], []).append(i)
+    PLANS[n] = order
+    PLANS["t"] = max(best)
     return order
 
 
@@ -154,9 +168,10 @@ def rank_program(g, core, T, topo):
     SH = base - LO
     tasks, wr, rd = [], {}, {}
     V, S, E = g.vector, g.scalar, g.tensor
-    cy = 0.00083
+    cy = 0.00083 * FAC
+    cost = lambda n: cy * (FIX + (n if n != 64 else 30) if ADD else max(64, n))
 
-    def add(q, fn, reads, writes, cost, prio=1, ext=(), aft=None):
+    def add(q, fn, reads, writes, cost, ext=(), aft=None):
         i = len(tasks)
         deps, odeps = set(), set()
         for b in reads:
@@ -168,7 +183,7 @@ def rank_program(g, core, T, topo):
             if b in wr:
                 (odeps if q == "T" and tasks[wr[b]]["q"] == "T" else deps).add(wr[b])
             deps.update(rd.get(b, ()))
-        tasks.append(dict(q=q, fn=fn, deps=deps, odeps=odeps, cost=cost, prio=prio, ext=tuple(ext), aft=aft, dma=None, lat=0.0))
+        tasks.append(dict(q=q, fn=fn, deps=deps, odeps=odeps, cost=cost, ext=tuple(ext), aft=aft, dma=None, lat=0.0))
         for b in reads:
             rd.setdefault(b, []).append(i)
         for b in writes:
@@ -176,401 +191,419 @@ def rank_program(g, core, T, topo):
             rd[b] = []
         return i
 
-    def vop(fn, reads, writes, n, prio=1, ext=(), aft=None, f=1.0):
-        return add("V", lambda: [fn()], reads, writes, (0.02 if f == int(f) else 0.07) + 1.15 * cy * max(64, n * f), prio, ext, aft)
+    def vop(fn, reads, writes, n=64, ext=(), aft=None, f=1.0):
+        return add("V", lambda: [fn()], reads, writes, cost(n * f) if f == int(f) else 0.05 + cy * n * f, ext, aft)
 
-    def ts(out, on, in0, inn, s1, s2, op0, op1=None, n=24, prio=1, ext=(), aft=None, extra=()):
+    def ts(out, on, in0, ins, s1, s2, op0, op1=None, n=64, ext=(), aft=None):
         if op1 is None:
-            return vop(lambda: V.tensor_scalar(out, in0, s1, None, op0), [inn] + list(extra), [on], n, prio, ext, aft)
-        return vop(lambda: V.tensor_scalar(out, in0, s1, s2, op0, op1), [inn] + list(extra), [on], n, prio, ext, aft)
+            return vop(lambda: V.tensor_scalar(out, in0, s1, None, op0), ins.split(), [on], n, ext, aft)
+        return vop(lambda: V.tensor_scalar(out, in0, s1, s2, op0, op1), ins.split(), [on], n, ext, aft)
 
-    def tt(out, on, in0, n0, in1, n1, op, n=24, prio=1, ext=(), aft=None, extra=(), f=1.0):
-        return vop(lambda: V.tensor_tensor(out, in0, in1, op), [n0, n1] + list(extra), [on], n, prio, ext, aft, f)
+    def tt(out, on, in0, in1, ins, op, n=64, ext=(), aft=None, f=1.0):
+        return vop(lambda: V.tensor_tensor(out, in0, in1, op), ins.split(), [on], n, ext, aft, f)
 
-    def cp(out, on, in_, inn, n=24, prio=1, extra=(), f=1.0):
-        return vop(lambda: V.tensor_copy(out, in_), [inn] + list(extra), [on], n, prio, f=f)
+    def cp(out, on, in_, ins, n=64, f=1.0):
+        return vop(lambda: V.tensor_copy(out, in_), ins.split(), [on], n, f=f)
 
-    def fill(ap, on, v, n, prio=1):
-        return vop(lambda: V.memset(ap, v), [], [on], n, prio)
+    def scan(out, on, d0, d1, ins, op0, op1, n=64):
+        return vop(lambda: V.tensor_tensor_scan(out, d0, d1, 0.0, op0, op1), ins.split(), [on], n)
 
-    def act(out, on, in_, inn, n, prio=1, fn=F.Copy, **kw):
-        return add("S", lambda: [S.activation(out, in_, fn, **kw)], inn, [on], 0.03 + 1.15 * cy * max(64, n), prio)
+    def act(out, on, in_, ins, n=64, fn=F.Copy, f=1.0, **kw):
+        return add("S", lambda: [S.activation(out, in_, fn, **kw)], ins.split(), [on], cost(n) if f == 1 else 0.065 + cy * n * f)
 
-    def iota(ap, on, pat, b, ch, n, prio=1, fl=True):
+    def sfill(ap, on, v, n):
+        return act(ap, on, T.bc[:, 0:n], "one", n, scale=0.0, bias=float(v))
+
+    def iota(ap, on, pat, b, ch, n, fl=True):
         if fl:
-            return add("G", lambda: [g.iota(ap, pat, b, ch, allow_small_or_imprecise_dtypes=True)], [], [on], 0.15 + 2.2 * cy * n, prio)
-        return add("G", lambda: [g.iota(ap, pat, b, ch)], [], [on], 0.15 + 2.2 * cy * n, prio)
+            return add("G", lambda: [g.iota(ap, pat, b, ch, allow_small_or_imprecise_dtypes=True)], [], [on], 0.13 + 2 * cy * n)
+        return add("G", lambda: [g.iota(ap, pat, b, ch)], [], [on], 0.13 + 2 * cy * n)
 
-    def gfill(ap, on, v, n, prio=1):
-        return iota(ap, on, [[0, n]], v, 0, n, prio)
-
-    def mm(lst, reads, bank, prio=1, ext=(), aft=None):
-        c = sum((0.01 + 1.15 * cy * max(64, n) * (4 if f4 else 1)) for (_, n, f4) in lst)
-        return add("T", lambda: [E.matmul(*a) for (a, n, f4) in lst], reads, [bank], c, prio, ext, aft)
+    def mm(lst, ins, bank, ext=(), aft=None):
+        c = sum(cy * max(64, n) * (4 if f4 else 1) for (_, n, f4) in lst)
+        return add("T", lambda: [E.matmul(*a) for (a, n, f4) in lst], ins.split(), [bank], c, ext, aft)
 
     loads = {}
 
-    def load(q, sem, fn, cnt, deps, writes, cost, lat, prio=0, ext=(), aft=None):
-        i = add(q, fn, deps, writes, cost, prio, ext, aft)
+    def load(q, sem, pairs, ins, on, lat, ext=(), aft=None):
+        eng = g.sync if q == "Y" else g.scalar
+        i = add(q, lambda: [eng.dma_start(o, x) for o, x in pairs], ins.split(), on.split(), 0.1 * len(pairs), ext, aft)
         tasks[i]["dma"] = sem
         tasks[i]["lat"] = lat
-        loads[sem] = loads.get(sem, 0) + 16 * cnt
+        loads[sem] = loads.get(sem, 0) + 16 * len(pairs)
         return i
-
-    def ld_pts(q, fs):
-        return [q.dma_start(T.X[4 * f + i:128:16, :], T.pts[i:24:3, :]) for f in fs for i in range(3)]
 
     nloc = [0]
 
-    def remote(calls, reads, prio):
+    def remote(calls, ins):
         def fn():
             for c in calls:
                 g.remote_dma_fused([transfer(topo, core, d, es, T.sem[s], a, b) for d, es, s, a, b in c], local_sem=T.sem.loc)
                 nloc[0] += sum(len(x[1]) for x in c)
             return []
-        return add("G", fn, reads, [], 0.5 * len(calls), prio)
+        return add("G", fn, ins.split(), [], CALL * len(calls))
     E8 = topo.engines(core, peers[0])
+    GAT, SCA = 1.6, 3.8
 
-    fill(T.X[:], "X", 1, NP, -10)
-    fill(T.bc[:, 0:128], "one", 1.0, 64, -10)
-    load("Y", "ldN", lambda: [g.sync.dma_start(T.Zn[:], T.nbr[:])], 1, [], ["Zn"], 0.1, 2.0, -11)
-    load("S", "ldZ", lambda: [g.scalar.dma_start(T.Zp[:], T.planes[:])], 1, [], ["Zp"], 0.1, 2.3, -11)
-    load("Y", "ldA", lambda: [g.sync.dma_start(T.L0[:], T.tet0[:])], 1, [], ["L0"], 0.1, 2.5, -10)
-    load("S", "ldD", lambda: [g.scalar.dma_start(T.Zd[:], T.planes[3:16:4, :])], 1, [], ["Zd"], 0.1, 2.7, -10)
-    load("Y", "ldP", lambda: ld_pts(g.sync, range(4)), 12, [], ["X"], 1.2, 2.0)
+    vop(lambda: V.memset(T.bc[:], 1.0), [], ["one"])
+    vop(lambda: V.memset(T.X[:], 1), [], ["X"], NP)
+    a = load("Y", "ldN", [(T.Zn[:], T.nbr[:])], "", "Zn", 2.0)
+    b = load("S", "ldZ", [(T.Zp[:], T.planes[:])], "", "Zp", 2.3)
+    tasks[load("S", "ldD", [(T.Zd[:], T.planes[3:16:4, :])], "", "Zd", 2.7)]["odeps"].add(b)
+    tasks[load("Y", "ldA", [(T.L0[:], T.tet0[:])], "", "L0", 2.9)]["odeps"].add(a)
+    load("Y", "ldP", [(T.X[4 * f + i:128:16, :], T.pts[i:24:3, :]) for f in range(4) for i in range(3)], "", "X", 2.5)
 
-    cp(T.NU[:], "NU", T.Zn[:], "Zn", 32, P_T - 1)
-    sC = remote([[(rel[1], E8, "hC", T.NU[:], T.A3[:])]], ["NU"], P_T - 1)
-    ts(T.H1[:], "H1", T.Zp[:], "Zp", 1.0 / 64, None, A.mult, n=128, prio=P_T)
-    sA = remote([[(rel[0], E8, "hA", T.H1[:], T.A1[:])]], ["H1"], P_T)
-    tasks[sA]["odeps"].add(sC)
     xd, tI, Ld, Hd = T.st[:, 64:96], T.st[:, 96:128], T.Ld[:, 0:32], T.Ld[:, 32:64]
-    ts(xd, "xd", T.Zd[:], "Zd", 1.0 / 64, None, A.mult, n=32, prio=P_T)
-    ts(Hd, "Hd", T.Zd[:], "Zd", 1.0 / 64, None, A.mult, n=32, prio=P_T)
-    tt(Ld, "Ld", xd, "xd", Hd, "Hd", A.subtract, n=32, prio=P_T, f=2)
-    sB = remote([[(rel[1], E8, "hB", Ld, T.A2[:])]], ["Ld"], P_T)
+    cp(T.NU[:], "NU", T.Zn[:], "Zn")
+    sC = remote([[(rel[1], E8, "hC", T.NU[:], T.A3[:])]], "NU")
+    ts(T.H1[:], "H1", T.Zp[:], "Zp", 1.0 / 64, None, A.mult, n=128)
+    sA = remote([[(rel[0], E8, "hA", T.H1[:], T.A1[:])]], "H1")
+    ts(xd, "xd", T.Zd[:], "Zd", 1.0 / 64, None, A.mult)
+    ts(Hd, "Hd", T.Zd[:], "Zd", 1.0 / 64, None, A.mult)
+    tt(Ld, "Ld", xd, Hd, "xd Hd", A.subtract)
+    sB = remote([[(rel[1], E8, "hB", Ld, T.A2[:])]], "Ld")
+    tasks[sA]["odeps"].add(sC)
     tasks[sB]["odeps"].add(sA)
 
-    iota(T.pi[:], "pi", [[0, 4]], 0, 1, 4, -9, False)
-    iota(T.jm[:, 0:128], "jm", [[0, 8], [1, 16]], 0, 0, 128, -8)
-    iota(T.oRi[:], "oRi", [[0, 4], [-8, 3]], 16, 0, 12, -8)
-    iota(T.md16[:], "md16", [[1, 8], [0, 16]], 0, 0, 128, -7)
-    iota(T.mk[:], "mk", [[1, 128]], 0, -1, 128, -7)
-    iota(T.oKi[:], "oKi", [[1, 32]], 0, 0, 32, -6, False)
-    iota(T.cOw[:], "cOw", [[16, 24]], 128, 1, 24, -3)
-    iota(T.cD[:, 0:8], "cD", [[32, 4], [1, 2]], -2, 0, 8, -3)
-    iota(T.cE[:], "cE", [[4, 8], [0, 4], [1, 4]], 0, 0, 128, -2)
-    gfill(T.Rs[:, 0:168], "Rs", 1, 168, -2)
-    gfill(T.Rs[:, 0:168:24], "Rs", 0, 7, -2)
-    iota(tI, "tI", [[1, 32]], 0, 32, 32, -1)
-    iota(T.j4[:], "j4", [[0, 32], [1, 4]], 0, 0, 128, 0)
-    iota(T.W1[:, 0:128], "W1", [[0, 128]], NONE, 0, 128, 0, False)
-    CQ = []
+    iota(T.pi[:], "pi", [[0, 4]], 0, 1, 4, False)
+    iota(T.jm[:], "jm", [[0, 8], [1, 16]], 0, 0, 128)
+    iota(T.oRi[:], "oRi", [[0, 4], [-8, 3]], 16, 0, 12)
+    iota(T.md16[:], "md16", [[1, 8], [0, 16]], 0, 0, 128)
+    iota(T.mk[:], "mk", [[1, 128]], 0, -1, 128)
+    iota(T.oKi[:], "oKi", [[1, 32]], 0, 0, 32, False)
+    iota(T.cOw[:], "cOw", [[16, 24]], 128, 1, 24)
+    iota(T.cD[:, 0:8], "cD", [[32, 4], [1, 2]], -2, 0, 8)
+    iota(T.cD[:, 8:72], "cB", [[-32, 4], [-1, 2], [0, 8]], 0, 0, 64)
+    iota(T.cE[:], "cE", [[4, 8], [0, 4], [1, 4]], 0, 0, 128)
+    iota(tI, "tI", [[1, 32]], 0, 32, 32)
+    iota(T.sA[:, 0:57], "sA", [[1, 57]], -2, 0, 57)
+    iota(T.cL[:, 0:140], "cL", [[1, 140]], -12, 0, 140)
     for k, v in enumerate(owners):
-        act(T.cQ[:, 24 * k:24 * k + 24], "cQ%d" % k, T.bc[:, 0:24], ["one"], 24, -8, scale=0.0, bias=float(v))
-        CQ.append("cQ%d" % k)
+        sfill(T.cQ[:, 24 * k:24 * k + 24], "cQ%d" % k, v, 24)
+    CQ = " ".join("cQ%d" % k for k in range(8))
+    act(T.Rs[:], "Rs", T.cQ[:, 0:168], CQ, 168, scale=0.0, bias=1.0)
+    sfill(T.Rs[:, 0:168:24], "Rs", 0, 7)
     ones = T.bc[0:1, 0:128]
     for k, (w, a, o1, b, o2) in enumerate(((1, 15, A.bitwise_and, None, None), (1, 4, A.arith_shift_right, None, None),
-                                           (1, 2, A.arith_shift_right, None, None), (1, 3, A.bitwise_and, None, None),
-                                           (1, 2, A.arith_shift_right, 3, A.bitwise_and), (1, 5, A.arith_shift_right, None, None),
-                                           (2, 1, A.bitwise_and, None, None))):
-        ts(T.pj[:, k:k + w], "pj%d" % k, T.pi[:, 0:w], "pi", a, b, o1, o2, n=1, prio=-9)
-    vop(lambda: V.tensor_copy(T.pf[:, 0:8], T.pj[:, 0:8]), ["pj%d" % k for k in range(7)], ["pf"], 8, -9)
+                                           (1, 3, A.bitwise_and, None, None), (1, 2, A.arith_shift_right, 3, A.bitwise_and),
+                                           (1, 5, A.arith_shift_right, None, None), (2, 1, A.bitwise_and, None, None))):
+        ts(T.pj[:, k:k + w], "pj%d" % k, T.pi[:, 0:w], "pi", a, b, o1, o2)
+    cp(T.pf[:, 0:7], "pf", T.pj[:, 0:7], " ".join("pj%d" % k for k in range(6)))
     col = lambda k: T.pf[:, k:k + 1]
-    p16, pg, p4, pi_, pf_, p5, par = [col(k) for k in range(7)]
-    cf, s3, hL, ck, cl, c3, c1, lo, hi, pK, pK4, m3, xm, c2 = [col(k) for k in range(8, 22)]
-    for ap, nm, src, sc, bi, pr in ((c3, "c3", pg, 4.0, 3.0, -4), (cf, "cf", p5, 1024.0, 0.0, -2), (s3, "s3", pg, 3.0, 1.0, -2),
-                                    (pK4, "pK4", pf_, float(K4), -3.0 * K4, -1), (lo, "lo", par, float(PWID), 0.0, 2),
-                                    (hi, "hi", par, float(PWID), float(HI), 2), (pK, "pK", p16, float(K16), -15.0 * K16, 5)):
-        act(ap, nm, src, ["pf"], 1, pr, scale=sc, bias=bi)
-    act(hL, "hL", p16, ["pf", "s3"], 1, -2, F.Identity, scale=s3, bias=s3)
+    p16, pg, pi_, pf_, p5, par = [col(k) for k in range(6)]
+    cf, g31, hL, ck, cl, c3, c1, lo, hi, pK, pK4, m3, xm, c2 = [col(k) for k in range(8, 22)]
+    for ap, nm, src, sc, bi in ((c3, "c3", pg, 4.0, 3.0), (cf, "cf", p5, 1024.0, 0.0), (g31, "g31", pg, 3.0, 1.0),
+                                (pK4, "pK4", pf_, float(K4), -3.0 * K4), (lo, "lo", par, float(PWID), 0.0), (hi, "hi", par, float(PWID), float(HI))):
+        act(ap, nm, src, "pf", scale=sc, bias=bi)
+    act(hL, "hL", p16, "pf g31", fn=F.Identity, scale=g31, bias=g31)
     for ap, nm, sc, bi in ((ck, "ck", 4.0, pi_), (cl, "cl", 16.0, pf_), (c1, "c1", float(GW), pi_), (c2, "c2", float(GW), pf_)):
-        act(ap, nm, pg, ["pf"], 1, 2, F.Identity, scale=sc, bias=bi)
+        act(ap, nm, pg, "pf", fn=F.Identity, scale=sc, bias=bi)
     oK, oR, oB8 = T.oT[:, 0:24], T.oT[:, 24:36], T.oT[:, 40:44]
-    ts(oR, "oR", T.oRi[:], "oRi", p16, None, A.add, n=12, prio=-6, extra=["pf"])
-    ts(T.G2[:], "G2", T.md16[:], "md16", pg, 2.0, A.is_equal, A.mult, n=64, prio=-3, extra=["pf"])
-    ts(T.I16[:], "I16", T.mk[:], "mk", 0.0, None, A.is_equal, n=128, prio=-1)
-    ts(T.mk[:], "mk", T.mk[:], "mk", 0.0, -1.0, A.is_lt, A.mult, n=128, prio=0)
-    tt(T.U2[:], "U2", T.mk[:], "mk", T.G2[:], "G2", A.mult, n=128, prio=0, f=2)
-    cp(T.cO16[:, 0:24], "cO16", T.cOw[:], "cOw", 24, -1)
-    cp(oK, "oK", T.oKi[:, 0:24], "oKi", 24, -1)
-    ts(T.m16[:, 0:128], "m16", T.jm[:], "jm", p16, None, A.is_equal, n=64, prio=-1, extra=["pf"])
-    act(T.m16[:, 128:256], "m16b", T.m16[:, 0:128], ["m16"], 128, -1)
-    act(T.m16[:, 256:384], "m16c", T.m16[:, 0:128], ["m16"], 128, -1)
-    M16 = ["m16", "m16b", "m16c"]
-    ts(T.G3[:], "G3", T.cE[:], "cE", c3, None, A.is_equal, n=64, prio=-1, extra=["c3"])
-    ts(T.j4[:], "j4", T.j4[:], "j4", pf_, None, A.is_equal, n=64, prio=0, extra=["pf"])
-    act(T.sc4[:], "sc4", T.j4[:], ["j4"], 128, 0, scale=-float(BIG + K4), bias=float(K4))
-    ts(T.LP[0:20, :], "LP", T.jm[0:20, :], "jm", 1.0, T.pf[0:20, 10:11], A.add, A.is_equal, n=64, prio=P_TO, extra=["hL"])
-
-    def steps_rows(src, srcn, b, c, HL, N, sem, prio, ext=(), aft=None):
-        st = T.st[:, c:c + 32]
-        ts(st, "st%d" % c, src, srcn, cf, float(-b), A.add, A.add, n=32, prio=prio, extra=["cf"], ext=ext, aft=aft)
-        tt(st, "st%d" % c, st, "st%d" % c, tI, "tI", A.subtract, n=32, prio=prio, f=2)
-        cp(T[HL][:, 0:32], HL, st, "st%d" % c, 32, prio)
-        tt(T[HL][:, 32:64], HL + "b", st, "st%d" % c, T[HL][:, 0:32], HL, A.subtract, n=32, prio=prio, f=2)
-        load("Y", sem, lambda: [g.sync.dma_start(T[N][4 * h:4 * h + 4, :], T[HL][:, 32 * h:32 * h + 32]) for h in range(2)], 2,
-             [HL, HL + "b"], [N], 0.2, 2.0, prio)
-
-    def windows(t, R, Rn, N, banks, on, prio):
-        c = PWID * t + LO
-        for h in range(2):
-            mm([((T[banks[2 + h]][:], T.m16[0:8, 0:128], T[N][0:8, 512 * h:512 * h + 512], True, True), 512, 0)], ["m16", N], banks[2 + h], prio)
-            o, nm = T.ND[:, c + 512 * h:c + 512 * h + 512], "ND%d%d" % (t, h)
-            if on[2 + h] == "S":
-                act(o, nm, T[banks[2 + h]][:], [banks[2 + h]], 512, prio)
-            else:
-                cp(o, nm, T[banks[2 + h]][:], banks[2 + h], 512, prio)
-        for h in range(2):
-            mm([((T[banks[h]][:], T.LP[0:20, :], T[R][0:20, 512 * h:512 * h + 512], True, True), 512, 0)], ["LP"] + Rn, banks[h], prio)
-            o, nm = T.PW[:, c + 512 * h:c + 512 * h + 512], "PW%d%d" % (t, h)
-            if on[h] == "S":
-                act(o, nm, T[banks[h]][:], [banks[h]], 512, prio, scale=64.0)
-            else:
-                ts(o, nm, T[banks[h]][:], banks[h], 64.0, None, A.mult, n=512, prio=prio)
-
-    load("Y", "lr0", lambda: [g.sync.dma_start(T.R0[0:16, :], T.H1[:]), g.sync.dma_start(T.R0[16:20, :], Ld)], 2, ["H1", "Ld"], ["R0"],
-         0.2, 2.0, P_TO)
-    steps_rows(T.Zn[:], "Zn", base, 0, "HL0", "N0", "ln0", P_TO)
-    windows(1, "R0", ["R0"], "N0", ("oK", "oP", "vK", "vP"), "SSSS", P_TO)
+    m16 = T.m16[:, 0:128]
+    ts(oR, "oR", T.oRi[:], "oRi pf", p16, None, A.add)
+    ts(T.G2[:], "G2", T.md16[:], "md16 pf", pg, 2.0, A.is_equal, A.mult)
+    ts(T.I16[:], "I16", T.mk[:], "mk", 0.0, None, A.is_equal, n=128)
+    ts(T.mk[:], "mk", T.mk[:], "mk", 0.0, -1.0, A.is_lt, A.mult, n=128)
+    tt(T.U2[:], "U2", T.mk[:], T.G2[:], "mk G2", A.mult, n=128, f=2)
+    cp(T.cO16[:, 0:24], "cO16", T.cOw[:], "cOw")
+    cp(oK, "oK", T.oKi[:, 0:24], "oKi")
+    ts(m16, "m16", T.jm[:], "jm pf", p16, None, A.is_equal)
+    ts(T.G3[:], "G3", T.cE[:], "cE c3", c3, None, A.is_equal)
+    ts(T.pf[:, 24:28], "mf", T.oKi[:, 0:4], "oKi pf", pf_, None, A.is_equal)
+    act(T.pf[:, 28:32], "m4", T.pf[:, 24:28], "mf", scale=-float(BIG + K4))
+    for j in range(4):
+        act(T.sc4[:, j:128:4], "sc4%d" % j, T.bc[:, 0:32], "one m4", scale=col(28 + j), bias=float(K4))
+    ts(T.LP[0:20, :], "LP", T.jm[0:20, :], "jm hL", 1.0, T.pf[0:20, 10:11], A.add, A.is_equal)
+    sfill(T.W1[:, 0:128], "W1", NONE, 128)
+    sfill(T.W2[:, 0:128], "W2", NONE, 128)
+    act(T.R1c[:], "R1c", T.cQ[:, 0:168], CQ, 168, scale=0.0, bias=-float(BIG))
+    sfill(T.R1c[:, 6:168:GW], "R1c", BIG, 24)
+    ts(T.S1[:], "S1", T.sA[:, 1:57], "sA c2", c2, None, A.is_equal)
+    ts(T.sA[:, 0:57], "sA", T.sA[:, 0:57], "sA c1", c1, 1.0 / HOLD, A.is_equal, A.mult)
+    tt(T.sA[:, 64:120], "S2", T.sA[:, 0:56], T.sA[:, 1:57], "sA", A.subtract, n=56, f=2)
+    act(T.If[:], "If", T.I16[:], "I16", 128)
+    ts(T.xB[:], "xB", T.jm[:], "jm pf", p16, None, A.is_lt, n=128)
+    act(T.exv[:], "exv", m16, "m16", 128, scale=HOLD)
+    tt(T.hk[:, 0:128], "hk", T.xB[:], T.exv[:], "xB exv", A.add, n=128, f=2)
+    ts(T.Ms[:], "Ms", T.oKi[:, 0:8], "oKi pf hk", pg, T.hk[:, 0:1], A.is_equal, A.mult)
+    sfill(T.hk[:, 0:128:16], "hk", 0, 8)
+    act(T.hk[:, 128:256], "hkb", T.hk[:, 0:128], "hk", 128)
+    act(T.hk[:, 256:384], "hkb", T.hk[:, 0:128], "hk", 128)
+    for t, b in (("O", 0), ("O", 1), ("O", 2), ("V", 0), ("R", 0)):
+        c = (QW if MERGE else QW + 80) * b
+        sfill(T["q" + t][:, c + 80:c + 80 + QW:GW], "q%s%d" % (t, b), 0, 128)
+        sfill(T["u" + t][:, 64 * b:64 * b + 1], "u0%s%d" % (t, b), BIG, 1)
     PZ = []
     for w in ("PW", "ND"):
         for a, z in ((0, LO), (HI, PWID + LO), (PWID + HI, 2 * PWID)):
-            gfill(T[w][:, a:z], "z%s%d" % (w, a), 0, z - a, 2)
+            sfill(T[w][:, a:z], "z%s%d" % (w, a), 0, z - a)
             PZ.append("z%s%d" % (w, a))
+    ts(m3, "m3", pi_, "pf", 3.0, None, A.is_equal)
+    act(xm, "xm", m3, "m3", scale=-1.0, bias=1.0)
+    for f in range(4):
+        ts(T.EX[:, 128 * f:128 * f + 128], "EX%d" % f, T.cE[:], "cE ck mf", ck, col(24 + f), A.is_equal, A.mult)
+    ts(T.LI[:, 0:140], "LI", T.cL[:, 0:140], "cL cl m3", cl, m3, A.is_equal, A.mult, n=70)
+    ts(T.cO16[:, 32:40], "off", T.bc[:, 0:8], "one lo", lo, float(LO - 1), A.mult, A.add)
+    for k in range(4):
+        a, b = owners[2 * k], owners[2 * k + 1]
+        act(T.cS[:, 2 * k:2 * k + 2], "cS%d" % k, T.pf[:, 5:7], "pf", scale=float(NT * (b - a)), bias=float(NT * a - SH - 1) - DEAD)
+    sfill(T.scn[:, 56:64], "scnz", 0, 8)
+    sfill(T.RP2[:, 0:2], "RP2p", 0, 2)
+    ts(T.cO16[:, 24:32], "cOn", T.cOw[:, 0:8], "cOw", -1.0, 129.0, A.mult, A.add)
+    ts(T.I1k[:], "I1k", T.I16[:], "I16", 1024.0, None, A.mult)
+    ts(T.pj[:, 8:12], "pj8", T.pi[:], "pi", 7, None, A.bitwise_and)
+    cp(oB8, "oB8", T.pj[:, 8:12], "pj8")
+    act(T.Gf[:], "Gf", T.G2[:], "G2", 128, scale=0.5)
+    sfill(T.vW[:, 128:136], "vW0", 0, 8)
+    sfill(T.dW[:, 128:136], "dW0", 8192, 8)
+    act(T.gv[:, 0:128], "gv0", m16, "m16", 128, scale=-float(BIG))
+    act(T.gv[:, 129:256], "gv1", T.m16[:, 0:127], "m16", 128, scale=float(MID))
+    sfill(T.gv[:, 128:129], "gv1", 0, 1)
+    tt(T.scC[:, 0:128], "scC", T.gv[:, 0:128], T.gv[:, 128:256], "gv0 gv1", A.add, n=128, f=2)
+    act(T.scC[:, 128:192], "scCb", T.scC[:, 0:64], "scC")
+    ts(pK, "pK", p16, "pf", 14.5, -float(MID + 16384), A.is_lt, A.mult)
+
+    def steps_rows(src, srcn, b, c, HL, N, sem, ext=(), aft=None):
+        st, sn = T.st[:, c:c + 32], "st%d" % c
+        ts(st, sn, src, srcn + " cf", cf, float(-b), A.add, A.add, ext=ext, aft=aft)
+        tt(st, sn, st, tI, sn + " tI", A.subtract)
+        cp(T[HL][:, 0:32], HL, st, sn)
+        tt(T[HL][:, 32:64], HL + "b", st, T[HL][:, 0:32], sn + " " + HL, A.subtract)
+        load("Y", sem, [(T[N][4 * h:4 * h + 4, :], T[HL][:, 32 * h:32 * h + 32]) for h in range(2)], HL + " " + HL + "b", N, 2.3 if aft else LAT0)
+
+    def windows(t, R, Rn, N, banks, on):
+        c = PWID * t + LO
+        for k, (bk, q) in enumerate(zip(banks, on)):
+            h = k % 2
+            if k < 2:
+                mm([((T[bk][:], T.m16[0:8, 0:128], T[N][0:8, 512 * h:512 * h + 512], True, True), 512, 0)], "m16 " + N, bk)
+            else:
+                mm([((T[bk][:], T.LP[0:20, :], T[R][0:20, 512 * h:512 * h + 512], True, True), 512, 0)], "LP " + Rn, bk)
+            w, sc = ("ND", 1.0) if k < 2 else ("PW", 64.0)
+            o, nm = T[w][:, c + 512 * h:c + 512 * h + 512], "%s%d%d" % (w, t, h)
+            if q == "S":
+                act(o, nm, T[bk][:], bk, 512, scale=sc)
+            else:
+                ts(o, nm, T[bk][:], bk, sc, None, A.mult, n=512)
+
+    load("Y", "lr0", [(T.R0[0:16, :], T.H1[:]), (T.R0[16:20, :], Ld)], "H1 Ld", "R0", LAT0)
+    steps_rows(T.Zn[:], "Zn", base, 0, "HL0", "N0", "ln0")
+    windows(1, "R0", "R0", "N0", ("vK", "vP", "o0", "o1"), "SSSS")
 
     su1, suA, suB, s1c = T.su[:, 0:24], T.su[:, 24:48], T.su[:, 48:56], T.su[:, 64:88]
 
-    def slots(oh, ohn, su, sun, prio):
+    def slots(oh, ohn, su, sun):
         M, n7, n8 = 24, 168, 192
         z1, z2 = T.z1, T.z2
-        mm([((T.rB[:, n7:n8], T.I16[:], T.cO16[:, 0:M], True, True), M, 0)], ["I16", "cO16"], "rB", prio)
-        vop(lambda: V.tensor_tensor(oh[:], T.rk[:, 0:32].indirect(oR), T.cQ[:], A.is_equal), ["rka", "rkb", "oR"] + CQ, [ohn], n8, prio, f=1.6)
+        mm([((T.rB[:, n7:n8], T.I16[:], T.cO16[:, 0:M], True, True), M, 0)], "I16 cO16", "rB")
+        tt(oh[:], ohn, T.rk[:, 0:32].indirect(oR), T.cQ[:], "rka rkb oR " + CQ, A.is_equal, n8, f=GAT)
         mm([((T.rA[:, 0:n7], T.G2[:], oh[:, 0:n7], True, False), n7, 0), ((T.rA[:, 0:n7:M], ones, T.cD[0:1, 0:7], False, True), 7, 0)],
-           ["G2", ohn, "one", "cD"], "rA", prio)
-        mm([((T.rB[:, 0:n7], T.U2[:], oh[:, 0:n7], True, True), n7, 0)], ["U2", ohn], "rB", prio)
+           "G2 one cD " + ohn, "rA")
+        mm([((T.rB[:, 0:n7], T.U2[:], oh[:, 0:n7], True, True), n7, 0)], "U2 " + ohn, "rB")
         sc = T.rA[:, 256:256 + n7]
-        vop(lambda: V.tensor_tensor_scan(sc, T.Rs[:], T.rA[:, 0:n7], 0.0, A.mult, A.add), ["Rs", "rA"], ["sc"], n7, prio)
-        vop(lambda: V.tensor_tensor(z2[:, 0:n8], T.rB[:, 0:n8], oh[:, 0:n8], A.mult), ["rB", ohn], ["z2"], n8, prio)
-        vop(lambda: V.tensor_tensor(z1[:, 0:n7], sc, oh[:, 0:n7], A.mult), ["sc", "rA", ohn], ["z1"], n7, prio)
-        mm([((T.rB[:, 0:M], T.I16[:], z2[:, M * b:M * b + M], b == 0, False), M, 0) for b in range(8)], ["I16", "z2"], "rB", prio)
-        mm([((T.rB[:, 0:M], T.I16[:], z1[:, M * b:M * b + M], False, b == 6), M, 0) for b in range(7)], ["I16", "z1"], "rB", prio)
-        cp(su, sun, T.rB[:, 0:M], "rB", M, prio)
+        scan(sc, "sc", T.Rs[:], T.rA[:, 0:n7], "Rs rA", A.mult, A.add, n7)
+        tt(z2[:], "z2", T.rB[:, 0:n8], oh[:, 0:n8], "rB " + ohn, A.mult, n8)
+        tt(z1[:], "z1", sc, oh[:, 0:n7], "sc rA " + ohn, A.mult, n7)
+        mm([((T.rB[:, 0:M], T.I16[:], z2[:, M * b:M * b + M], b == 0, False), M, 0) for b in range(8)], "I16 z2", "rB")
+        mm([((T.rB[:, 0:M], T.I16[:], z1[:, M * b:M * b + M], False, b == 6), M, 0) for b in range(7)], "I16 z1", "rB")
+        cp(su, sun, T.rB[:, 0:M], "rB")
 
-    def pack(ex, exn, PK, PKn, xap, xn, tib, tin, k, bank, prio):
-        n = 16 * k
-        vop(lambda: V.tensor_tensor(ex, tib.indirect(T.oT[:, 0:k]), T.m16[:, 0:n], A.mult), [tin, "oK"] + M16, [exn], n, prio, f=1.6)
-        mm([((T[bank][:, 0:n], T.G3[:], ex, True, True), n, 0)], ["G3", exn], bank, prio)
-        tt(PK, PKn, T[bank][:, 0:n], bank, xap, xn, A.add, n=n, prio=prio)
+    def pack(b, x, xn, tin, bank, W, wn, su, sun):
+        ex, PK, ps = T.ex[:, 128 * b:128 * b + 128], T.PK[:, 128 * b:128 * b + 128], T[bank][:, 256:384]
+        tt(ex, "ex%d" % b, T.ti[:, 8 * b:8 * b + 8].indirect(T.oT[:, 0:8]), m16, tin + " oK m16", A.mult, 128, f=GAT)
+        mm([((ps, T.G3[:], ex, True, True), 128, 0)], "G3 ex%d" % b, bank)
+        tt(PK, "PK%d" % b, ps, x, bank + " " + xn, A.add, 128)
+        cp(W[:].indirect(su), wn, PK, "PK%d %s" % (b, sun), 128, f=SCA)
 
-    def message(W, wn, MB, mn, prio):
-        vop(lambda: V.tensor_tensor_scan(T.sd[:], T.sc4[:], W[:, 0:128], 0.0, A.add, A.max), ["sc4", wn], ["sd"], 128, prio)
-        ts(MB[:, 0:32], mn, T.sd[:, 3:128:4], "sd", pK4, None, A.add, n=32, prio=prio, extra=["pK4"])
+    def message(W, wn, MB, mn):
+        scan(T.sd[:], "sd", T.sc4[:], W[:, 0:128], "sc40 sc41 sc42 sc43 " + wn, A.add, A.max, 128)
+        ts(MB[:, 0:32], mn, T.sd[:, 3:128:4], "sd pK4", pK4, None, A.add)
 
-    def send(buf, reads, sem, w, src, dst, prio):
+    def send(buf, ins, sem, w, src, dst):
         x = [(d, sem, buf[:, src + w * k:src + w * k + w], buf[:, dst + w * k:dst + w * k + w]) for k, d in enumerate(peers)]
-        return remote([[(x[0][0], E8[:4]) + x[0][1:], (x[1][0], E8[4:]) + x[1][1:]], [(x[2][0], E8) + x[2][1:]]], reads, prio)
+        return remote([[(x[0][0], E8[:4]) + x[0][1:], (x[1][0], E8[4:]) + x[1][1:]], [(x[2][0], E8) + x[2][1:]]], ins)
     ARR = 2 * len(E8)
 
-    def step(t, X, xn, w, wn, c0, bK, bP, bL, Lr, Lwn, clo, chi, prio, last=False):
-        B = 3 if t == "O" else 1
-        Lw = T[Lwn]
-        m, k = 56 * B, 8 * B
-        pr, pa, u, kk, re, e = [T[x + t] for x in ("pr", "pa", "u", "k", "q", "e")]
-        nm = lambda x: x + t
-        part = lambda x, q: x + t + ("" if B == 1 else "_%d" % q)
-        pc = 256 if bK == bP else 0
-        tabs = ("1",) if c0 else ("0", "1")
-        PWn, NDn = [[x + a + h for a in tabs for h in "01"] + PZ for x in ("PW", "ND")]
-        for q, (a, z) in enumerate(((0, 16), (16, 24)) if B == 3 else ((0, k),)):
-            vop(lambda a=a, z=z: V.tensor_tensor(pr[:, 16 * a:16 * z], T.PW[:, c0:].indirect(w[:, a:z]), X[:, 16 * a:16 * z], A.mult),
-                PWn + [wn, xn], [part("pr", q)], 16 * (z - a), prio, f=1.6)
-            add("S", lambda a=a, z=z: [S.activation(pa[:, 16 * a:16 * z], T.ND[:, c0:].indirect(w[:, a:z]), F.Copy)], NDn + [wn], [part("pa", q)],
-                0.07 + 1.8 * cy * 16 * (z - a), prio)
-        for b in range(B):
-            first = mm([((T[bK][:, 56 * b:56 * b + 56], pr[:, 128 * b:128 * b + 128], T.S1[:], True, True), 56, 1)],
-                       [part("pr", b // 2), "S1"], bK, prio)
-        for b in range(B):
-            second = mm([((T[bP][:, pc + 56 * b:pc + 56 * b + 56], pa[:, 128 * b:128 * b + 128], T.sA[:, 64:120], True, True), 56, 0)],
-                        [part("pa", b // 2), "S2"], bP, prio)
-        if B == 1:
+    def step(t, b, X, xn, banks, Lr, Lw, last=False):
+        n = "%s%d" % (t, b)
+        pr, pa, e = [T[x + t][:, 128 * b:128 * b + 128] for x in ("pr", "pa", "e")]
+        u, kk, c, w = T["u" + t], T["k" + t][:, 56 * b:56 * b + 56], (QW + 80) * b, T["w" + t][:, 8 * b:8 * b + 8]
+        bK, bP, bL = banks if len(banks) == 3 else banks * 3
+        pK_, pP, pL = T[bK][:, 0:56], T[bP][:, 64:120], T[bL][:, 128:136] if bL == bK else T[bL][:, 0:8]
+        c0, clo, chi = (0, lo, hi) if t == "V" else (PWID, 0.0, float(HI))
+        PWn, NDn = [" ".join([x + a + h for a in ("01" if t == "V" else "1") for h in "01"] + PZ) for x in ("PW", "ND")]
+        Lin, Lout = [T[x][:, 8 * b:8 * b + 8] if x else None for x in (Lr, Lw)]
+        tt(pr, "pr" + n, T.PW[:, c0:].indirect(w), X, "%s w%s %s" % (PWn, n, xn), A.mult, 128, f=GAT)
+        act(pa, "pa" + n, T.ND[:, c0:].indirect(w), "%s w%s" % (NDn, n), 128, f=GAT)
+        first = mm([((pK_, pr, T.S1[:], True, True), 56, 1)], "S1 pr" + n, bK)
+        second = mm([((pP, pa, T.sA[:, 64:120], True, True), 56, 0)], "S2 pa" + n, bP)
+        if bL != bK:
             tasks[second]["odeps"].add(first)
-        third = mm([((T[bL][:, 0:k], T.If[:], T[Lr][:], True, False), k, 1)], ["If", Lr], bL, prio)
-        tasks[third]["odeps"].add(second)
-        vop(lambda: V.tensor_tensor_scan(u[:, 1:m + 1], T[bK][:, 0:m], T.R1c[:, 0:m], 0.0, A.min, A.max), ["R1c", bK], [nm("u")], m, prio)
-        vop(lambda: V.tensor_tensor(kk[:], T[bK][:, 0:m], u[:, 0:m], A.is_ge), [bK, nm("u"), nm("u0")], [nm("k")], m, prio)
-        vop(lambda: V.tensor_tensor_scan(re[:, 0:16 * m:16], T[bP][:, pc:pc + m], kk[:], 0.0, A.add, A.mult), [nm("k"), bP], [nm("re")], m, prio)
-        for b in range(B):
-            vop(lambda b=b: V.tensor_tensor_scan(e[:, 128 * b:128 * b + 128], T.hk[:], re[:, QW * b + 80:QW * b + 80 + QW:GW], 0.0, A.mult, A.add),
-                ["hk", nm("re"), nm("rz")], [nm("e%d" % b)], 128, prio)
-            mm([((T[bL][:, 8 * b:8 * b + 8], e[:, 128 * b:128 * b + 128], T.Ms[:], False, b == B - 1), 8, 1)], [nm("e%d" % b), "Ms"], bL, prio)
-        if not last:
-            ts(w[:, 0:k], wn, T[bL][:, 0:k], bL, clo, chi, A.max, A.min, n=k, prio=prio, extra=["lo", "hi"])
-            act(Lw[:], Lwn, T[bL][:, 0:k], [bL], k, prio)
+            tasks[mm([((pL, T.If[:], Lin, True, False), 8, 1)], "If %s%d" % (Lr, b), bL)]["odeps"].add(second)
+        scan(u[:, 64 * b + 1:64 * b + 57], "u" + n, pK_, T.R1c[:, 0:56], "R1c " + bK, A.min, A.max)
+        tt(kk, "k" + n, pK_, u[:, 64 * b:64 * b + 56], "%s u%s u0%s" % (bK, n, n), A.is_ge)
+        scan(T["q" + t][:, c:c + QW:16], "q" + n, pP, kk, "%s k%s" % (bP, n), A.add, A.mult)
+        scan(e, "e" + n, T.hk[:, 0:128], T["q" + t][:, c + 80:c + 80 + QW:GW], "hk q" + n, A.mult, A.add, 128)
+        mm([((pL, e, T.Ms[:], bL == bK, True), 8, 1)], "Ms e" + n, bL)
+        if bL == bK:
+            tt(Lout, "%s%d" % (Lw, b), pL, Lin, "%s %s%d" % (bL, Lr, b), A.add)
+            if not last:
+                ts(w, "w" + n, Lout, "%s%d" % (Lw, b), clo, chi, A.max, A.min)
+        elif not last:
+            ts(w, "w" + n, pL, bL + " lo hi", clo, chi, A.max, A.min)
+            act(Lout, "%s%d" % (Lw, b), pL, bL)
 
-    ts(T.rk[:, 16:32], "rka", T.L0[:, 0:16], "L0", 10, None, A.arith_shift_right, prio=-4)
-    ts(T.rk[:, 0:16], "rkb", T.L0[:, 8:24], "L0", 10, None, A.arith_shift_right, prio=-4)
-    slots(T.oh1, "oh1", su1, "su1", 0)
-    ts(T.ti[:, 0:24], "ti", T.L0[:], "L0", 1023, None, A.bitwise_and, prio=0)
-    pack(T.ex[:], "ex", T.PK[:], "PK", T.X[:], "X", T.ti[:, 0:24], "ti", 24, "vL", 0)
-    cp(T.W1[:].indirect(su1), "W1", T.PK[:], "PK", NP, 0, extra=["su1"], f=3.8)
-    message(T.W1, "W1", T.MB1, "msg1", 0)
-    s1 = send(T.MB1, ["msg1"], "rq1", 8, 0, 32, 0)
+    ts(T.rk[:, 16:32], "rka", T.L0[:, 0:16], "L0", 10, None, A.arith_shift_right)
+    ts(T.rk[:, 0:16], "rkb", T.L0[:, 8:24], "L0", 10, None, A.arith_shift_right)
+    slots(T.oh1, "oh1", su1, "su1")
+    if DELAY:
+        tasks[sC]["deps"].add(wr["su1"])
+    ts(T.ti[:, 0:24], "ti", T.L0[:], "L0", 1023, None, A.bitwise_and)
+    for b, bank in enumerate(("vL", "o2", "vL")):
+        pack(b, T.X[:, 128 * b:128 * b + 128], "X", "ti", bank, T.W1, "W1", T.su[:, 8 * b:8 * b + 8], "su1")
+    message(T.W1, "W1", T.MB1, "msg1")
+    s1 = send(T.MB1, "msg1", "rq1", 8, 0, 32)
 
-    iota(T.sA[:, 0:57], "sA", [[1, 57]], -2, 0, 57, 1)
-    act(T.R1c[:], "R1c", T.cQ[:, 0:168], CQ, 168, 1, scale=0.0, bias=-float(BIG))
-    act(T.R1c[:, 6:168:GW], "R1c", T.bc[:, 0:24], ["one"], 24, 1, scale=float(BIG))
-    iota(T.cL[:, 0:140], "cL", [[1, 140]], -12, 0, 140, 2)
-    ts(T.S1[:], "S1", T.sA[:, 1:57], "sA", c2, None, A.is_equal, n=56, prio=2, extra=["c2"])
-    ts(T.sA[:, 0:57], "sA", T.sA[:, 0:57], "sA", c1, 1.0 / HOLD, A.is_equal, A.mult, n=57, prio=2, extra=["c1"])
-    tt(T.sA[:, 64:120], "S2", T.sA[:, 0:56], "sA", T.sA[:, 1:57], "sA", A.subtract, n=56, prio=2, f=2)
-    act(T.If[:], "If", T.I16[:], ["I16"], 128, 2)
-    ts(T.xB[:], "xB", T.jm[:], "jm", p16, None, A.is_lt, n=128, prio=2, extra=["pf"])
-    act(T.exv[:], "exv", T.m16[:, 0:128], ["m16"], 128, 2, scale=HOLD)
-    tt(T.hk[:], "hk", T.xB[:], "xB", T.exv[:], "exv", A.add, n=128, prio=2, f=2)
-    ts(T.Ms[:], "Ms", T.oKi[:, 0:8], "oKi", pg, T.hk[:, 0:1], A.is_equal, A.mult, n=8, prio=2, extra=["pf", "hk"])
-    act(T.hk[:, 0:128:16], "hk", T.bc[:, 0:8], ["one"], 8, 2, scale=0.0)
-    for t, n, pr in (("O", 3, 2), ("V", 1, 2), ("R", 1, 4)):
-        for b in range(n):
-            act(T["q" + t][:, QW * b + 80:QW * b + 80 + QW:GW], "re" + t, T.bc[:], ["one"], 128, pr, scale=0.0)
-        gfill(T["u" + t][:, 0:1], "u0" + t, BIG, 1, pr)
-    ts(m3, "m3", pi_, "pf", 3.0, None, A.is_equal, n=1, prio=2)
-    ts(xm, "xm", pi_, "pf", 3.0, None, A.is_lt, n=1, prio=2)
-    ts(T.pf[:, 24:28], "mf", T.oKi[:, 0:4], "oKi", pf_, None, A.is_equal, n=4, prio=2, extra=["pf"])
-    for f in range(4):
-        ts(T.EX[:, 128 * f:128 * f + 128], "EX%d" % f, T.cE[:], "cE", ck, col(24 + f), A.is_equal, A.mult, n=64, prio=2, extra=["ck", "mf"])
-    ts(T.LI[:, 0:140], "LI", T.cL[:, 0:140], "cL", cl, m3, A.is_equal, A.mult, n=70, prio=2, extra=["cl", "m3"])
-    ts(T.cO16[:, 32:40], "off", T.bc[:, 0:8], "one", lo, float(LO - 1), A.mult, A.add, n=8, prio=2, extra=["lo"])
-    ts(T.Lo[:], "Lo", T.L0[:], "L0", float(-SH) - DEAD, None, A.add, prio=2)
-    tt(T.Lo[:], "Lo", T.Lo[:], "Lo", T.oh1[:, 168:192], "oh1", A.mult, prio=2)
-    ts(T.Lo[:], "Lo", T.Lo[:], "Lo", DEAD, None, A.add, prio=2)
-    ts(T.wO[:], "wO", T.Lo[:], "Lo", 0.0, float(HI), A.max, A.min, prio=2)
-    own = lambda pr, last=False: step("O", T.X, "X", T.wO, "wO", PWID, "oK", "oP", "oL", "Lo", "Lo", 0.0, float(HI), pr, last)
-    own(P_O1)
-
-    def to_list(out, MB, c0, reads, bank, start, prio, ext=(), aft=None):
+    def to_list(out, MB, c0, ins, bank, start, ext=(), aft=None):
         return mm([((out, T.LI[:, 12 - 4 * c:140 - 4 * c], MB[:, c0 + c:c0 + 32:4], start and c == 0, c == 3), 8, 0) for c in range(4)],
-                  ["LI"] + reads, bank, prio, ext, aft)
+                  "LI " + ins, bank, ext, aft)
+
+    sBv, sBg = T.sB[:, 0:8], T.sB[:, 8:16]
+    to_list(T.rA[:, 0:8], T.MB1, 0, "msg1", "rA", True)
+    tt(sBv, "sBv", T.rA[:, 0:8], T.cS[:], "rA cS0 cS1 cS2 cS3", A.add)
+    ts(sBg, "sBg", T.rA[:, 0:8], "rA", 2000.0, None, A.is_lt)
+    tt(sBv, "sBv", sBv, sBg, "sBv sBg", A.mult)
+    act(sBv, "sBv", sBv, "sBv", bias=DEAD)
+    act(T.xB[:], "xB", T.W1[:, 0:128], "W1 xm m3", 128, F.Identity, scale=xm, bias=m3)
+
+    LO3 = "Lo0 Lo1 Lo2"
+    ts(T.Lm[:], "Lm0", T.L0[:], "L0", float(-SH) - DEAD, None, A.add)
+    tt(T.Lm[:], "Lm0", T.Lm[:], T.oh1[:, 168:192], "Lm0 oh1", A.mult)
+    vop(lambda: V.tensor_scalar(T.Lo[:], T.Lm[:], DEAD, None, A.add), ["Lm0"], LO3.split())
+    vop(lambda: V.tensor_scalar(T.wO[:], T.Lo[:], 0.0, float(HI), A.max, A.min), LO3.split(), ["wO0", "wO1", "wO2"])
+
+    def own(s):
+        if MERGE:
+            Lr, Lw = "Lm" if s == 3 else "Lo", "Lm" if s == 2 else "Lo"
+            all3 = lambda x: " ".join(x + str(b) for b in range(3))
+            PWn, NDn = [" ".join([x + "10", x + "11"] + PZ) for x in ("PW", "ND")]
+            for a, z in PARTS:
+                add("V", lambda a=a, z=z: [V.tensor_tensor(T.prO[:, 128 * a:128 * z], T.PW[:, PWID:].indirect(T.wO[:, 8 * a:8 * z]), T.X[:, 128 * a:128 * z], A.mult)],
+                    (PWn + " wO0 X").split(), ["prO%d" % b for b in range(a, z)], 0.05 + cy * GAT * 128 * (z - a))
+                add("S", lambda a=a, z=z: [S.activation(T.paO[:, 128 * a:128 * z], T.ND[:, PWID:].indirect(T.wO[:, 8 * a:8 * z]), F.Copy)],
+                    (NDn + " wO0").split(), ["paO%d" % b for b in range(a, z)], 0.065 + cy * GAT * 128 * (z - a))
+            for b in range(3):
+                mm([((T.o0[:, 56 * b:56 * b + 56], T.prO[:, 128 * b:128 * b + 128], T.S1[:], True, True), 56, 1)], "S1 prO%d" % b, "o0")
+            for b in range(3):
+                mm([((T.o1[:, 56 * b:56 * b + 56], T.paO[:, 128 * b:128 * b + 128], T.sA[:, 64:120], True, True), 56, 0)], "S2 paO%d" % b, "o1")
+            mm([((T.o2[:, 0:24], T.If[:], T[Lr][:], True, False), 24, 1)], "If " + all3(Lr), "o2")
+            scan(T.uO[:, 1:169], "uO0", T.o0[:, 0:168], T.R1c[:], "R1c o0", A.min, A.max, 168)
+            tt(T.kO[:], "kO0", T.o0[:, 0:168], T.uO[:, 0:168], "o0 uO0 u0O0", A.is_ge, 168)
+            scan(T.qO[:, 0:3 * QW:16], "qO0", T.o1[:, 0:168], T.kO[:], "o1 kO0 qO1 qO2", A.add, A.mult, 168)
+            for a, z in PARTS:
+                add("V", lambda a=a, z=z: [V.tensor_tensor_scan(T.eO[:, 128 * a:128 * z], T.hk[:, 0:128 * (z - a)], T.qO[:, 80 + QW * a:80 + QW * z:GW], 0.0, A.mult, A.add)],
+                    ["hk", "hkb", "qO0"], ["eO%d" % b for b in range(a, z)], cy * (FIX + 128 * (z - a)))
+            for b in range(3):
+                mm([((T.o2[:, 8 * b:8 * b + 8], T.eO[:, 128 * b:128 * b + 128], T.Ms[:], False, b == 2), 8, 1)], "Ms eO%d" % b, "o2")
+            if s < 5:
+                ts(T.wO[:], "wO0", T.o2[:, 0:24], "o2", 0.0, float(HI), A.max, A.min, 24)
+            add("S", lambda: [S.activation(T[Lw][:], T.o2[:, 0:24], F.Copy)], ["o2"], all3(Lw).split(), cy * 90)
+            return
+        for b in range(3):
+            step("O", b, T.X[:, 128 * b:128 * b + 128], "X", ("o%d" % b,), "Lm" if s == 3 else "Lo", "Lm" if s == 2 else "Lo", s == 5)
+    for s in range(3):
+        own(s)
+
+    RKC = (SH - 511.1875) / 1024.0
+    ts(T.rk[:, 16:32], "rka", T.Lm[:, 0:16], "Lm0 Lm1", 1.0 / 1024, RKC, A.mult, A.add)
+    ts(T.rk[:, 0:16], "rkb", T.Lm[:, 8:24], "Lm1 Lm2", 1.0 / 1024, RKC, A.mult, A.add)
+    ts(T.ci[:, 0:24], "ci", T.Lm[:], "Lm0 Lm1 Lm2", float(SH), None, A.add)
+    ts(T.ti[:, 0:24], "ti", T.ci[:, 0:24], "ci", 1023, None, A.bitwise_and)
+    slots(T.ohA, "ohA", suA, "suA")
+    for b in range(3):
+        pack(b, T.X[:, 128 * b:128 * b + 128], "X", "ti", "o%d" % b, T.W2, "W2", T.su[:, 24 + 8 * b:32 + 8 * b], "suA")
+    for s in range(3, 6):
+        own(s)
 
     def arrive(MB, mn, sem, sent, fly):
-        mm([((T.vL[:, 0:8], T.I16[:], T.cO16[:, 32:40], True, False), 8, 0)], ["I16", "off"], "vL", 0)
+        mm([((T.vL[:, 0:8], T.I16[:], T.cO16[:, 32:40], True, False), 8, 0)], "I16 off", "vL")
         a = mm([((T.vP[:, f:128:4], T.EX[:, 128 * f:128 * f + 128], MB[:, 24:56], True, True), 32, 0) for f in range(4)],
-               ["EX%d" % f for f in range(4)] + [mn], "vP", 0, [(sem, ARR)], (sent, fly))
-        b = to_list(T.vL[:, 0:8], MB, 24, [mn], "vL", False, 0, [(sem, ARR)], (sent, fly))
-        tasks[b]["odeps"].add(a)
-        ts(T.Xv[:], "Xv", T.vP[:, 0:128], "vP", xm, m3, A.mult, A.add, n=128, prio=0, extra=["xm", "m3"])
-        ts(T.wv[:], "wv", T.vL[:, 0:8], "vL", lo, hi, A.max, A.min, n=8, prio=0, extra=["lo", "hi"])
-        act(T.Lv0[:], "Lv0", T.vL[:, 0:8], ["vL"], 8, 0)
+               "EX0 EX1 EX2 EX3 " + mn, "vP", [(sem, ARR)], (sent, fly))
+        tasks[to_list(T.vL[:, 0:8], MB, 24, mn, "vL", False, [(sem, ARR)], (sent, fly))]["odeps"].add(a)
+        ts(T.Xv[:], "Xv", T.vP[:, 0:128], "vP xm m3", xm, m3, A.mult, A.add, n=128)
+        ts(T.wV[:], "wV0", T.vL[:, 0:8], "vL lo hi", lo, hi, A.max, A.min)
+        act(T.Lv0[:], "Lv00", T.vL[:, 0:8], "vL")
 
     def visitors(RP, outn):
         for s in range(3):
-            step("V", T.Xv, "Xv", T.wv, "wv", 0, "vK", "vP", "vL", "Lv" if s else "Lv0", "Lv", lo, hi, 0, s == 2)
-        tt(RP[:, 8:16], outn, T.vL[:, 0:8], "vL", T.Lv0[:], "Lv0", A.subtract, n=8, prio=0)
+            step("V", 0, T.Xv[:], "Xv", ("vK", "vP", "vL"), "Lv" if s else "Lv0", "Lv", s == 2)
+        tt(RP[:, 8:16], outn, T.vL[:, 0:8], T.Lv0[:], "vL Lv00", A.subtract)
 
     arrive(T.MB1, "msg1", "rq1", s1, FLY[0])
-    steps_rows(T.NP[:], "NP", NT * owners[6], 32, "HL1", "N1", "ln1", 0, [("tC", len(E8))], (sC, FLY_T[0]))
-    load("Y", "lr1", lambda: [g.sync.dma_start(T.R1[0:16, :], T.A1[:])], 1, [], ["R1"], 0.1, 2.0, 0, [("tA", len(E8))], (sA, FLY_T[1]))
-    load("Y", "lr1", lambda: [g.sync.dma_start(T.R1[16:20, :], T.A2[:])], 1, [], ["R1b"], 0.1, 2.0, 0, [("tB", len(E8))], (sB, FLY_T[2]))
-    windows(0, "R1", ["R1", "R1b"], "N1", ("rA", "rB", "vK", "vP"), "VSSV", 0)
+    steps_rows(T.NP[:], "NP", NT * owners[6], 32, "HL1", "N1", "ln1", [("tC", len(E8))], (sC, FLY_T[0]))
+    load("S", "lr1", [(T.R1[16:20, :], T.A2[:])], "", "R1b", 2.0, [("tB", len(E8))], (sB, FLY_T[2]))
+    load("S", "lr1", [(T.R1[0:16, :], T.A1[:])], "", "R1", 2.0, [("tA", len(E8))], (sA, FLY_T[1]))
+    windows(0, "R1", "R1 R1b", "N1", ("vK", "vP", "vL", "vK"), "SVVS")
     visitors(T.RP1, "out1")
-    s2 = send(T.RP1, ["out1"], "rp1", 2, 10, 2, 0)
-
-    for k in range(4):
-        a, b = owners[2 * k], owners[2 * k + 1]
-        act(T.cS[:, 2 * k:2 * k + 2], "cS%d" % k, T.pf[:, 6:8], ["pf"], 2, 4, scale=float(NT * (b - a)), bias=float(NT * a - SH - 1) - DEAD)
-    sBv, sBg = T.sB[:, 0:8], T.sB[:, 8:16]
-    to_list(T.rA[:, 0:8], T.MB1, 0, ["msg1"], "rA", True, 3)
-    tt(sBv, "sBv", T.rA[:, 0:8], "rA", T.cS[:], "cS0", A.add, n=8, prio=3, extra=["cS1", "cS2", "cS3"])
-    ts(sBg, "sBg", T.rA[:, 0:8], "rA", 2000.0, None, A.is_lt, n=8, prio=3)
-    tt(sBv, "sBv", sBv, "sBv", sBg, "sBg", A.mult, n=8, prio=3)
-    ts(sBv, "sBv", sBv, "sBv", DEAD, None, A.add, n=8, prio=3)
-    ts(T.xB[:], "xB", T.W1[:, 0:128], "W1", xm, m3, A.mult, A.add, n=128, prio=3, extra=["xm", "m3"])
-    iota(T.W2[:, 0:128], "W2", [[0, 128]], NONE, 0, 128, 3, False)
-    iota(T.cD[:, 8:72], "cB", [[-32, 4], [-1, 2], [0, 8]], 0, 0, 64, 3)
-    gfill(T.scn[:, 56:64], "scnz", 0, 8, 4)
-    gfill(T.RP2[:, 0:2], "RP2p", 0, 2, 3)
-    ts(T.cO16[:, 24:32], "cOn", T.cOw[:, 0:8], "cOw", -1.0, 129.0, A.mult, A.add, n=8, prio=3)
-    ts(T.I1k[:], "I1k", T.I16[:], "I16", 1024.0, None, A.mult, n=64, prio=3)
-    ts(T.pj[:, 8:12], "pj8", T.pi[:], "pi", 7, None, A.bitwise_and, n=4, prio=3)
-    cp(oB8, "oB8", T.pj[:, 8:12], "pj8", 4, 3)
-    own(P_O2)
-    own(P_O2)
-
-    RKC = (SH - 511.1875) / 1024.0
-    ts(T.rk[:, 16:32], "rka", T.Lo[:, 0:16], "Lo", 1.0 / 1024, RKC, A.mult, A.add, prio=P_A)
-    ts(T.rk[:, 0:16], "rkb", T.Lo[:, 8:24], "Lo", 1.0 / 1024, RKC, A.mult, A.add, prio=P_A)
-    ts(T.ci[:, 0:24], "ci", T.Lo[:], "Lo", float(SH), None, A.add, prio=P_A)
-    ts(T.ti[:, 0:24], "ti", T.ci[:, 0:24], "ci", 1023, None, A.bitwise_and, prio=P_A)
-    slots(T.ohA, "ohA", suA, "suA", P_A)
-    pack(T.ex[:], "ex", T.PK[:], "PK", T.X[:], "X", T.ti[:, 0:24], "ti", 24, "oP", P_A)
-    cp(T.W2[:].indirect(suA), "W2", T.PK[:], "PK", NP, P_A, extra=["suA"], f=3.8)
+    s2 = send(T.RP1, "out1", "rp1", 2, 10, 2)
 
     mm([((T.vP[:, 0:64], ones, T.cD[0:1, 8:72], True, False), 64, 0), ((T.vP[:, 56:64], T.I16[:], T.cO16[:, 24:32], False, False), 8, 0)],
-       ["one", "cB", "I16", "cOn"], "vP", 1)
-    vop(lambda: V.tensor_tensor(T.Lb[:], sBv, T.RP1[:, 2:10], A.add), ["sBv", "out1"], ["Lb"], 8, 0, [("rp1", ARR)], (s2, FLY[1]))
-    ts(T.rkB[:], "rkB", T.Lb[:], "Lb", 1.0 / 1024, RKC, A.mult, A.add, n=8, prio=0)
-    ts(T.ci[:, 24:32], "ciB", T.Lb[:], "Lb", float(SH), None, A.add, n=8, prio=0)
-    ts(T.ti[:, 24:32], "tiB", T.ci[:, 24:32], "ciB", 1023, None, A.bitwise_and, n=8, prio=0)
-    vop(lambda: V.tensor_tensor(T.ohB[:], T.rkB[:].indirect(oB8), T.cQ[:, 0:192:3], A.is_equal), ["rkB", "oB8"] + CQ, ["ohB"], 64, 0, f=1.6)
-    mm([((T.vK[:, 0:56], T.G2[:], T.ohB[:, 0:56], True, True), 56, 0)], ["G2", "ohB"], "vK", 0)
+       "one cB I16 cOn", "vP")
+    tt(T.Lb[:], "Lb0", sBv, T.RP1[:, 2:10], "sBv out1", A.add, ext=[("rp1", ARR)], aft=(s2, FLY[1]))
+    ts(T.rkB[:], "rkB", T.Lb[:], "Lb0", 1.0 / 1024, RKC, A.mult, A.add)
+    ts(T.ci[:, 24:32], "ciB", T.Lb[:], "Lb0", float(SH), None, A.add)
+    ts(T.ti[:, 24:32], "tiB", T.ci[:, 24:32], "ciB", 1023, None, A.bitwise_and)
+    tt(T.ohB[:], "ohB", T.rkB[:].indirect(oB8), T.cQ[:, 0:192:3], "rkB oB8 " + CQ, A.is_equal, 64, f=GAT)
+    mm([((T.vK[:, 0:56], T.G2[:], T.ohB[:, 0:56], True, True), 56, 0)], "G2 ohB", "vK")
     mm([((T.vP[:, 0:64], T.I1k[:], T.ohB[:], False, False), 64, 0), ((T.vP[:, 0:56], T.U2[:], T.ohB[:, 0:56], False, True), 56, 0)],
-       ["I1k", "U2", "ohB"], "vP", 0)
-    vop(lambda: V.tensor_tensor_scan(T.scn[:, 0:56], T.Rs[:, 0:168:3], T.vK[:, 0:56], 0.0, A.mult, A.add), ["Rs", "vK"], ["scn"], 56, 0)
-    vop(lambda: V.tensor_tensor(T.zz[:], T.scn[:], T.vP[:, 0:64], A.add), ["scn", "scnz", "vP"], ["zz"], 64, 0)
-    tt(T.mx[:, 0:32], "mx0", T.zz[:, 0:32], "zz", T.zz[:, 32:64], "zz", A.max, n=32, prio=0)
-    tt(T.mx[:, 32:48], "mx1", T.mx[:, 0:16], "mx0", T.mx[:, 16:32], "mx0", A.max, n=16, prio=0)
-    tt(T.mx[:, 48:56], "mx2", T.mx[:, 32:40], "mx1", T.mx[:, 40:48], "mx1", A.max, n=8, prio=0)
-    ts(suB, "suB", T.mx[:, 48:56], "mx2", -1.0, 1056.0, A.mult, A.add, n=8, prio=0)
-    pack(T.exB[:], "exB", T.PKB[:], "PKB", T.xB[:], "xB", T.ti[:, 24:32], "tiB", 8, "vL", 0)
-    cp(T.W2[:].indirect(suB), "W2", T.PKB[:], "PKB", 128, 0, extra=["suB"], f=3.8)
-    message(T.W2, "W2", T.MB2, "msg2", 0)
-    s3 = send(T.MB2, ["msg2", "RP2p"], "rq2", 8, 0, 32, 0)
+       "I1k U2 ohB", "vP")
+    scan(T.scn[:, 0:56], "scn", T.Rs[:, 0:168:3], T.vK[:, 0:56], "Rs vK", A.mult, A.add)
+    tt(T.zz[:], "zz", T.scn[:], T.vP[:, 0:64], "scn scnz vP", A.add)
+    tt(T.mx[:, 0:32], "mx0", T.zz[:, 0:32], T.zz[:, 32:64], "zz", A.max)
+    tt(T.mx[:, 32:48], "mx1", T.mx[:, 0:16], T.mx[:, 16:32], "mx0", A.max)
+    tt(T.mx[:, 48:56], "mx2", T.mx[:, 32:40], T.mx[:, 40:48], "mx1", A.max)
+    ts(suB, "suB", T.mx[:, 48:56], "mx2", -1.0, 1056.0, A.mult, A.add)
+    pack(3, T.xB[:], "xB", "tiB", "vL", T.W2, "W2", suB, "suB")
+    message(T.W2, "W2", T.MB2, "msg2")
+    s3 = send(T.MB2, "msg2 RP2p", "rq2", 8, 0, 32)
 
-    ts(T.wr[:], "wr", T.Lb[:], "Lb", 0.0, float(HI), A.max, A.min, n=8, prio=P_C)
-    act(T.Gf[:], "Gf", T.G2[:], ["G2"], 128, P_C, scale=0.5)
-    gfill(T.vW[:, 128:136], "vW0", 0, 8, 4)
-    gfill(T.dW[:, 128:136], "dW0", 8192, 8, 4)
-    act(T.scC[:], "scC", T.m16[:, 0:192], M16, 192, 5, scale=-float(BIG + K16), bias=float(K16))
-    ts(T.Rd[:, 0:128], "Rd", T.jm[:], "jm", 1.0, None, A.min, n=128, prio=5)
-    act(T.Rd[:, 128:256], "Rdb", T.Rd[:, 0:128], ["Rd"], 128, 5)
-    act(T.Rd[:, 256:384], "Rdc", T.Rd[:, 0:128], ["Rd"], 128, 5)
+    ts(T.wR[:], "wR0", T.Lb[:], "Lb0", 0.0, float(HI), A.max, A.min)
     for s in range(3):
-        step("R", T.xB, "xB", T.wr, "wr", PWID, "rA", "rA", "rB", "Lb", "Lb", 0.0, float(HI), P_R, s == 2)
-        own(P_O3, s == 2)
+        step("R", 0, T.xB[:], "xB", ("rA",), "Lr" if s else "Lb", "Lr", s == 2)
     arrive(T.MB2, "msg2", "rq2", s3, FLY[2])
     visitors(T.RP2, "out2")
-    s4 = send(T.RP2, ["out2"], "rp2", 2, 10, 2, 0)
+    s4 = send(T.RP2, "out2", "rp2", 2, 10, 2)
 
-    smA, smB, vB = T.sm[:, 0:24], T.sm[:, 24:32], T.sm[:, 32:40]
-    ts(s1c, "s1c", su1, "su1", 128.0, None, A.min, prio=P_C)
-    ts(smA, "smA", suA, "suA", 128.0, None, A.min, prio=P_C)
-    ts(smB, "smB", suB, "suB", 128.0, None, A.min, n=8, prio=P_C)
-    ts(vB, "vB", T.rB[:, 0:8], "rB", 8192.0, 256.0, A.add, A.mult, n=8, prio=P_C)
-    tt(vB, "vB", vB, "vB", smB, "smB", A.add, n=8, prio=P_C)
-    vop(lambda: V.tensor_tensor(T.exv[:], vB.indirect(T.oT[:, 0:8]), T.m16[:, 0:128], A.mult), ["vB", "oK"] + M16, ["exv"], 128, P_C, f=1.6)
-    mm([((T.rA[:, 0:128], T.Gf[:], T.exv[:], True, True), 128, 1)], ["Gf", "exv"], "rA", P_C)
-    act(T.vW[:, 0:128], "vW", T.rA[:, 0:128], ["rA"], 128, P_C)
-    vop(lambda: V.tensor_tensor(T.gv[:], T.vW[:].indirect(s1c), T.m16[:], A.mult), ["vW", "vW0", "s1c"] + M16, ["gv", "gvb"], NP, P_C, f=1.6)
-    vop(lambda: V.tensor_tensor_scan(T.sv[:], T.Rd[:], T.gv[:], 0.0, A.mult, A.add), ["Rd", "Rdb", "Rdc", "gv", "gvb"], ["sv", "svb"], NP, P_C)
-    ts(T.vO[:], "vO", T.oL[:, 0:24], "oL", 8192.0, 256.0, A.add, A.mult, prio=P_C)
-    tt(T.vO[:], "vO", T.vO[:], "vO", smA, "smA", A.add, prio=P_C)
-    tt(T.vO[:], "vO", T.vO[:], "vO", T.oh1[:, 168:192], "oh1", A.mult, prio=P_C)
-    tt(T.vt[:], "vt", T.vO[:], "vO", T.sv[:, 15:NP:16], "sv", A.add, prio=P_C, extra=["svb"])
-    ts(T.ci[:, 0:24], "ci", T.vt[:], "vt", 255, None, A.bitwise_and, prio=P_C)
-    cp(T.tau[:], "tau", T.ci[:, 0:24], "ci", 24, P_C)
-    ts(T.vt[:], "vt", T.vt[:], "vt", 8, None, A.arith_shift_right, prio=P_C)
-    ts(T.sm[:, 40:64], "Yb", T.vt[:], "vt", float(SH - 16384), pK, A.add, A.add, prio=P_C, extra=["pK"])
+    smA, smB, vB, Yb = T.sm[:, 0:24], T.sm[:, 24:32], T.sm[:, 32:40], T.sm[:, 40:64]
+    ts(s1c, "s1c", su1, "su1", 128.0, None, A.min)
+    ts(smA, "smA", suA, "suA", 128.0, None, A.min)
+    ts(smB, "smB", suB, "suB", 128.0, None, A.min)
+    act(vB, "vB", T.Lr[:], "Lr0", scale=256.0, bias=256.0 * SH)
+    tt(vB, "vB", vB, smB, "vB smB", A.add)
+    tt(T.exv[:], "exv", vB.indirect(T.oT[:, 0:8]), m16, "vB oK m16", A.mult, 128, f=GAT)
+    mm([((T.rB[:, 0:128], T.Gf[:], T.exv[:], True, True), 128, 1)], "Gf exv", "rB")
+    act(T.vW[:, 0:128], "vW", T.rB[:, 0:128], "rB", 128)
+    for b in range(3):
+        act(T.gv[:, 128 * b:128 * b + 128], "gv%d" % b, T.vW[:].indirect(T.su[:, 64 + 8 * b:72 + 8 * b]), "vW vW0 s1c", 128, f=GAT)
+        scan(T.sv[:, 128 * b:128 * b + 128], "sv%d" % b, T.scC[:, 0:128], T.gv[:, 128 * b:128 * b + 128], "scC gv%d" % b, A.add, A.max, 128)
+    act(T.vO[:], "vO", T.Lo[:], LO3, scale=256.0, bias=256.0 * SH)
+    tt(T.vO[:], "vO", T.vO[:], smA, "vO smA", A.add)
+    tt(T.vO[:], "vO", T.vO[:], T.oh1[:, 168:192], "vO oh1", A.mult)
+    tt(T.vt[:], "vt", T.vO[:], T.sv[:, 15:NP:16], "vO sv0 sv1 sv2", A.add)
+    ts(T.ci[:, 0:24], "ci", T.vt[:], "vt", 255, None, A.bitwise_and)
+    cp(T.tau[:], "tau", T.ci[:, 0:24], "ci")
+    ts(T.vt[:], "vt", T.vt[:], "vt", 8, None, A.arith_shift_right)
+    ts(Yb, "Yb", T.vt[:], "vt pK", -8192.0, pK, A.add, A.add)
 
-    vop(lambda: V.tensor_tensor(T.exv[:], T.RP2[:, 0:10].indirect(T.oT[:, 2:10]), T.m16[:, 0:128], A.mult), ["oK", "out2", "RP2p"] + M16,
-        ["exv"], 128, 0, [("rp2", ARR)], (s4, FLY[3]), f=1.6)
-    mm([((T.rA[:, 0:128], T.Gf[:], T.exv[:], True, True), 128, 1)], ["Gf", "exv"], "rA", 0)
-    ts(T.dW[:, 0:128], "dW", T.rA[:, 0:128], "rA", 8192.0, None, A.add, n=128, prio=0)
-    add("S", lambda: [S.activation(T.gv[:, 192:NP], T.dW[:].indirect(T.tau[:, 12:24]), F.Copy)], ["dW", "dW0", "tau"], ["gvb"], 0.4, 0)
-    vop(lambda: V.tensor_copy(T.gv[:, 0:192], T.dW[:].indirect(T.tau[:, 0:12])), ["dW", "dW0", "tau"], ["gv"], 192, 0, f=1.6)
-    for h, n in ((0, ""), (192, "b")):
-        vop(lambda h=h: V.tensor_tensor_scan(T.sv[:, h:h + 192], T.scC[:], T.gv[:, h:h + 192], 0.0, A.add, A.max), ["scC", "gv" + n], ["sv" + n], 192, 0)
-    tt(T.vO[:], "vO", T.sv[:, 15:NP:16], "sv", T.sm[:, 40:64], "Yb", A.add, prio=0, extra=["svb"])
-    load("Y", "st", lambda: [g.sync.dma_start(T.y[:], T.vO[:])], 1, ["vO"], [], 0.1, 0.0)
+    tt(T.exv[:], "exv", T.RP2[:, 0:10].indirect(T.oT[:, 2:10]), m16, "oK out2 RP2p m16", A.mult, 128, [("rp2", ARR)], (s4, FLY[3]), GAT)
+    mm([((T.rB[:, 0:128], T.Gf[:], T.exv[:], True, True), 128, 1)], "Gf exv", "rB")
+    ts(T.dW[:, 0:128], "dW", T.rB[:, 0:128], "rB", 8192.0, None, A.add, n=128)
+    add("S", lambda: [S.activation(T.gv[:, 192:NP], T.dW[:].indirect(T.tau[:, 12:24]), F.Copy)], ["dW", "dW0", "tau", "gv1"], ["gv2"], 0.36)
+    add("V", lambda: [V.tensor_copy(T.gv[:, 0:192], T.dW[:].indirect(T.tau[:, 0:12]))], ["dW", "dW0", "tau", "vt"], ["gv0", "gvx"], 0.35)
+    add("V", lambda: [V.tensor_tensor_scan(T.sv[:, 0:192], T.scC[:], T.gv[:, 0:192], 0.0, A.add, A.max)], ["scC", "scCb", "gv0"], ["sv0", "sv1"], cy * 192)
+    add("V", lambda: [V.tensor_tensor_scan(T.sv[:, 192:NP], T.scC[:], T.gv[:, 192:NP], 0.0, A.add, A.max)], ["scC", "scCb", "gv2"], ["sv2"], cy * 192)
+    tt(T.vO[:], "vO", T.sv[:, 15:NP:16], Yb, "sv0 sv2 Yb", A.add)
+    load("Y", "st", [(T.y[:], T.vO[:])], "vO", "", 0.0)
 
     order = plan(tasks)
     queue = {"V": V, "S": S, "T": E, "G": g, "Y": g.sync}

@@ -18,25 +18,24 @@ _sb = {
     "HL0": ([128, 64], "bfloat16"), "HL1": ([128, 64], "bfloat16"), "R0": ([128, NT], "float16"), "R1": ([128, NT], "float16"),
     "N0": ([128, NT], "bfloat16"), "N1": ([128, NT], "bfloat16"), "LP": ([128, 128], "float16"),
     "pi": ([128, 4], "int32"), "pj": ([128, 12], "int32"), "pf": ([128, 32], "float32"), "jm": ([128, 128], "bfloat16"),
-    "mk": ([128, 128], "float32"), "md16": ([128, 128], "bfloat16"), "m16": ([128, 192], "bfloat16"),
+    "mk": ([128, 128], "bfloat16"), "md16": ([128, 128], "bfloat16"), "m16": ([128, 128], "bfloat16"),
     "G2": ([128, 128], "float16"), "G3": ([128, 128], "float16"), "Gf": ([128, 128], "float32"), "cE": ([128, 128], "bfloat16"),
-    "U2": ([128, 128], "float16"), "I16": ([128, 128], "float16"), "If": ([128, 128], "float32"), "I1k": ([128, 128], "float16"),
+    "Ib": ([128, 128], "bfloat16"), "X16": ([128, NP], "float16"), "inj": ([128, NP], "float32"), "U2": ([128, 256], "float16"), "I16": ([128, 128], "float16"), "If": ([128, 128], "float32"), "I1k": ([128, 128], "float16"),
     "EX": ([128, 512], "float16"), "cL": ([128, 144], "bfloat16"), "LI": ([128, 144], "float16"),
-    "S1": ([128, 56], "float32"), "hk": ([128, NP], "float32"), "sA": ([128, 120], "bfloat16"), "Ms": ([128, 8], "float32"),
+    "S1": ([128, 56], "float32"), "hk": ([128, 128], "float32"), "sA": ([128, 120], "bfloat16"), "Ms": ([128, 8], "float32"),
     "R1c": ([128, 168], "float32"), "scC": ([128, 192], "float32"), "sc4": ([128, 128], "float32"),
     "oKi": ([128, 32], "int32"), "oRi": ([128, 12], "float32"), "oT": ([128, 48], "uint16"),
     "Rs": ([128, 168], "float32"), "cQ": ([128, 192], "float32"), "cD": ([128, 72], "bfloat16"), "bc": ([128, 128], "bfloat16"),
     "cOw": ([128, NK], "float32"), "cO16": ([128, 40], "float16"), "cS": ([128, 8], "float32"),
     "rk": ([128, 32], "int32"), "ci": ([128, 32], "int32"), "ti": ([128, 32], "int32"), "rkB": ([128, 8], "int32"),
     "oh1": ([128, 192], "float16"), "ohA": ([128, 192], "float16"), "ohB": ([128, 64], "float16"), "ex": ([128, 512], "float16"),
-    "scn": ([128, 64], "float32"), "zz": ([128, 64], "float32"), "mx": ([128, 56], "float32"),
+    "zz": ([128, 192], "float32"), "LW": ([128, 128], "float16"),
     "z1": ([128, 168], "float16"), "z2": ([128, 192], "float16"), "PK": ([128, 512], "float32"),
     "su": ([128, 96], "uint16"), "W1": ([128, WIN], "float32"), "W2": ([128, WIN], "float32"), "sd": ([128, 128], "float32"),
-    "MB1": ([128, 56], "float16"), "MB2": ([128, 56], "float16"), "RP1": ([128, 16], "float32"), "RP2": ([128, 16], "float32"),
-    "sB": ([128, 16], "float32"),
+    "MB1": ([128, 56], "float16"), "MB2": ([128, 56], "float16"), "RP1": ([128, 16], "int32"), "RP2": ([128, 16], "float32"),
     "Lo": ([128, NK], "float32"), "Lm": ([128, NK], "float32"), "wO": ([128, NK], "uint16"), "Lv0": ([128, 8], "float32"),
     "Lv": ([128, 8], "float32"), "wV": ([128, 8], "uint16"), "Lb": ([128, 8], "float32"), "Lr": ([128, 8], "float32"), "wR": ([128, 8], "uint16"),
-    "sm": ([128, 64], "float32"), "exv": ([128, 128], "float32"), "vW": ([128, 136], "float32"), "gv": ([128, NP], "float32"),
+    "sm": ([128, 80], "float32"), "exv": ([128, 128], "float32"), "vW": ([128, 136], "float32"), "gv": ([128, NP], "float32"),
     "sv": ([128, NP], "float32"), "vO": ([128, NK], "float32"), "vt": ([128, NK], "int32"), "tau": ([128, NK], "uint16"),
     "dW": ([128, 136], "float32"),
 }
@@ -57,12 +56,15 @@ for _k in PSUM:
 SEMAPHORES = ["sV", "sS", "sT", "sG", "ldA", "ldP", "ldZ", "ldD", "ldN", "lr0", "ln0", "lr1", "ln1", "st", "rq1", "rq2", "rp1", "rp2",
               "hA", "hB", "hC", "tA", "tB", "tC", "loc"]
 
-FLY = (2.8, 2.8, 2.8, 2.8)
-FLY_T = (8.0, 8.5, 8.0)
-WAKE, MARGIN, ROUNDS, FAC, CALL = 0.2, 0.03, 8, 1.25, 0.3
-LAT0 = 2.5
+FLY = (2.2, 2.2, 2.2, 2.2)
+FLY_T = (7.0, 7.5, 7.0)
+WAKE, MARGIN, ROUNDS, FAC, CALL = 0.2, 0.03, 200, 1.25, 0.3
+LAT0 = 1.7
 MERGE, PARTS, FIX, ADD = False, ((0, 3),), 64, False
 DELAY = False
+SHAKE = 1.0
+LDL, GF = (1.7, 1.6, 2.0, 2.2, 1.7), ("u0", "zP", "zN", "RP", "vW", "dW", "Rs", "cB", "W2", "qR", "qV")
+IL, SG, RSG, WON, WON0, WB, RQ, LAT1 = False, (3, 4, 5), True, "SVVS", "SSSS", ("vK", "vP", "rA", "rB"), "Y", 1.8
 PLANS = {}
 
 
@@ -101,24 +103,27 @@ def place(tasks, pre, key):
         for d in x:
             succ[d].append(i)
     fin, busy = [0.0] * n, {}
-    ready = [i for i in range(n) if pend[i] == 0]
+    ready = [(key[i], i) for i in range(n) if pend[i] == 0]
     while ready:
-        i = min(ready, key=lambda j: (key[j], j))
+        i = min(ready)
         ready.remove(i)
+        i = i[1]
         c = tasks[i]["cost"]
         s = max([0.0] + [fin[d] + w for d, w in pre[i].items()])
         l = busy.setdefault(tasks[i]["q"], [])
-        for a, z in l:
-            if s + c + MARGIN <= a:
-                break
-            s = max(s, z)
+        lo, hi = 0, len(l)
+        while lo < hi:
+            mid = (lo + hi) // 2
+            lo, hi = (mid + 1, hi) if l[mid][1] <= s else (lo, mid)
+        while lo < len(l) and s + c + MARGIN > l[lo][0]:
+            s = l[lo][1]
+            lo += 1
         fin[i] = s + c
-        l.append((s, s + c))
-        l.sort()
+        l.insert(lo, (s, s + c))
         for x in succ[i]:
             pend[x] -= 1
             if pend[x] == 0:
-                ready.append(x)
+                ready.append((key[x], x))
     return fin
 
 
@@ -140,18 +145,24 @@ def plan(tasks):
     tail = [0.0] * n
     for i in range(n - 1, -1, -1):
         tail[i] = tasks[i]["cost"] + max([0.0] + [tail[x] + w for x, w in post[i].items()])
-    key, best = [-x for x in tail], None
-    for _ in range(ROUNDS):
+    key, best, bkey, seed = [-x for x in tail], None, None, 1
+    for r in range(ROUNDS):
         fin = place(tasks, pre, key)
         if best is None or max(fin) < max(best):
-            best = fin
+            best, bkey = fin, key
         back = place(tasks, post, [-x for x in fin])
         key = [-x for x in back]
+        if r % 3 == 2:
+            key = []
+            for x in bkey:
+                seed = seed * 16807 % 2147483647
+                key.append(x + SHAKE * seed / 2147483647)
     order = {}
     for i in sorted(range(n), key=lambda j: (best[j] - tasks[j]["cost"], j)):
         order.setdefault(tasks[i]["q"], []).append(i)
     PLANS[n] = order
     PLANS["t"] = max(best)
+    PLANS["dbg"] = (tasks, pre, post, tail, best)
     return order
 
 
@@ -183,7 +194,7 @@ def rank_program(g, core, T, topo):
             if b in wr:
                 (odeps if q == "T" and tasks[wr[b]]["q"] == "T" else deps).add(wr[b])
             deps.update(rd.get(b, ()))
-        tasks.append(dict(q=q, fn=fn, deps=deps, odeps=odeps, cost=cost, ext=tuple(ext), aft=aft, dma=None, lat=0.0))
+        tasks.append(dict(nm=(list(writes) + ["-"])[0], q=q, fn=fn, deps=deps, odeps=odeps, cost=cost, ext=tuple(ext), aft=aft, dma=None, lat=0.0))
         for b in reads:
             rd.setdefault(b, []).append(i)
         for b in writes:
@@ -212,6 +223,8 @@ def rank_program(g, core, T, topo):
         return add("S", lambda: [S.activation(out, in_, fn, **kw)], ins.split(), [on], cost(n) if f == 1 else 0.065 + cy * n * f)
 
     def sfill(ap, on, v, n):
+        if on[:2] in GF:
+            return iota(ap, on, [[0, n]], v, 0, n)
         return act(ap, on, T.bc[:, 0:n], "one", n, scale=0.0, bias=float(v))
 
     def iota(ap, on, pat, b, ch, n, fl=True):
@@ -247,11 +260,11 @@ def rank_program(g, core, T, topo):
 
     vop(lambda: V.memset(T.bc[:], 1.0), [], ["one"])
     vop(lambda: V.memset(T.X[:], 1), [], ["X"], NP)
-    a = load("Y", "ldN", [(T.Zn[:], T.nbr[:])], "", "Zn", 2.0)
-    b = load("S", "ldZ", [(T.Zp[:], T.planes[:])], "", "Zp", 2.3)
-    tasks[load("S", "ldD", [(T.Zd[:], T.planes[3:16:4, :])], "", "Zd", 2.7)]["odeps"].add(b)
-    tasks[load("Y", "ldA", [(T.L0[:], T.tet0[:])], "", "L0", 2.9)]["odeps"].add(a)
-    load("Y", "ldP", [(T.X[4 * f + i:128:16, :], T.pts[i:24:3, :]) for f in range(4) for i in range(3)], "", "X", 2.5)
+    a = load("Y", "ldN", [(T.Zn[:], T.nbr[:])], "", "Zn", LDL[0])
+    b = load("S", "ldZ", [(T.Zp[:], T.planes[:])], "", "Zp", LDL[1])
+    tasks[load("S", "ldD", [(T.Zd[:], T.planes[3:16:4, :])], "", "Zd", LDL[2])]["odeps"].add(b)
+    tasks[load("Y", "ldA", [(T.L0[:], T.tet0[:])], "", "L0", LDL[3])]["odeps"].add(a)
+    load("Y", "ldP", [(T.X[4 * f + i:128:16, :], T.pts[i:24:3, :]) for f in range(4) for i in range(3)], "", "X", LDL[4])
 
     xd, tI, Ld, Hd = T.st[:, 64:96], T.st[:, 96:128], T.Ld[:, 0:32], T.Ld[:, 32:64]
     cp(T.NU[:], "NU", T.Zn[:], "Zn")
@@ -273,7 +286,7 @@ def rank_program(g, core, T, topo):
     iota(T.oKi[:], "oKi", [[1, 32]], 0, 0, 32, False)
     iota(T.cOw[:], "cOw", [[16, 24]], 128, 1, 24)
     iota(T.cD[:, 0:8], "cD", [[32, 4], [1, 2]], -2, 0, 8)
-    iota(T.cD[:, 8:72], "cB", [[-32, 4], [-1, 2], [0, 8]], 0, 0, 64)
+    iota(T.cD[:, 8:72], "cB", [[0, 8], [-32, 4], [-1, 2]], 0, 0, 64)
     iota(T.cE[:], "cE", [[4, 8], [0, 4], [1, 4]], 0, 0, 128)
     iota(tI, "tI", [[1, 32]], 0, 32, 32)
     iota(T.sA[:, 0:57], "sA", [[1, 57]], -2, 0, 57)
@@ -286,13 +299,16 @@ def rank_program(g, core, T, topo):
     ones = T.bc[0:1, 0:128]
     for k, (w, a, o1, b, o2) in enumerate(((1, 15, A.bitwise_and, None, None), (1, 4, A.arith_shift_right, None, None),
                                            (1, 3, A.bitwise_and, None, None), (1, 2, A.arith_shift_right, 3, A.bitwise_and),
-                                           (1, 5, A.arith_shift_right, None, None), (2, 1, A.bitwise_and, None, None))):
+                                           (1, 3, A.arith_shift_right, 1, A.bitwise_and), (1, 5, A.arith_shift_right, None, None),
+                                           (2, 1, A.bitwise_and, None, None))):
         ts(T.pj[:, k:k + w], "pj%d" % k, T.pi[:, 0:w], "pi", a, b, o1, o2)
-    cp(T.pf[:, 0:7], "pf", T.pj[:, 0:7], " ".join("pj%d" % k for k in range(6)))
+    cp(T.pf[:, 0:8], "pf", T.pj[:, 0:8], " ".join("pj%d" % k for k in range(7)))
     col = lambda k: T.pf[:, k:k + 1]
-    p16, pg, pi_, pf_, p5, par = [col(k) for k in range(6)]
-    cf, g31, hL, ck, cl, c3, c1, lo, hi, pK, pK4, m3, xm, c2 = [col(k) for k in range(8, 22)]
-    for ap, nm, src, sc, bi in ((c3, "c3", pg, 4.0, 3.0), (cf, "cf", p5, 1024.0, 0.0), (g31, "g31", pg, 3.0, 1.0),
+    p16, pg, pi_, pf_, p8, p5, par = [col(k) for k in range(7)]
+    act(col(23), "cf", p5, "pf", scale=-1024.0, bias=float(base))
+    act(tI, "tI", tI, "tI cf", fn=F.Identity, bias=col(23))
+    cv, g31, hL, ck, cl, c3, c1, lo, hi, pK, pK4, m3, xm, c2, he = [col(k) for k in range(8, 23)]
+    for ap, nm, src, sc, bi in ((c3, "c3", pg, 4.0, 3.0), (g31, "g31", pg, 3.0, 1.0),
                                 (pK4, "pK4", pf_, float(K4), -3.0 * K4), (lo, "lo", par, float(PWID), 0.0), (hi, "hi", par, float(PWID), float(HI))):
         act(ap, nm, src, "pf", scale=sc, bias=bi)
     act(hL, "hL", p16, "pf g31", fn=F.Identity, scale=g31, bias=g31)
@@ -302,9 +318,9 @@ def rank_program(g, core, T, topo):
     m16 = T.m16[:, 0:128]
     ts(oR, "oR", T.oRi[:], "oRi pf", p16, None, A.add)
     ts(T.G2[:], "G2", T.md16[:], "md16 pf", pg, 2.0, A.is_equal, A.mult)
-    ts(T.I16[:], "I16", T.mk[:], "mk", 0.0, None, A.is_equal, n=128)
-    ts(T.mk[:], "mk", T.mk[:], "mk", 0.0, -1.0, A.is_lt, A.mult, n=128)
-    tt(T.U2[:], "U2", T.mk[:], T.G2[:], "mk G2", A.mult, n=128, f=2)
+    ts(T.I16[:], "I16", T.mk[:], "mk", 0.0, None, A.is_equal)
+    ts(T.U2[:, 0:128], "U2", T.mk[:], "mk", 0.0, -2.0, A.is_lt, A.mult)
+    ts(T.U2[:, 128:256], "U2b", T.md16[:], "md16 pf", pg, 2.0, A.is_lt, A.mult)
     cp(T.cO16[:, 0:24], "cO16", T.cOw[:], "cOw")
     cp(oK, "oK", T.oKi[:, 0:24], "oKi")
     ts(m16, "m16", T.jm[:], "jm pf", p16, None, A.is_equal)
@@ -322,13 +338,17 @@ def rank_program(g, core, T, topo):
     ts(T.sA[:, 0:57], "sA", T.sA[:, 0:57], "sA c1", c1, 1.0 / HOLD, A.is_equal, A.mult)
     tt(T.sA[:, 64:120], "S2", T.sA[:, 0:56], T.sA[:, 1:57], "sA", A.subtract, n=56, f=2)
     act(T.If[:], "If", T.I16[:], "I16", 128)
-    ts(T.xB[:], "xB", T.jm[:], "jm pf", p16, None, A.is_lt, n=128)
-    act(T.exv[:], "exv", m16, "m16", 128, scale=HOLD)
-    tt(T.hk[:, 0:128], "hk", T.xB[:], T.exv[:], "xB exv", A.add, n=128, f=2)
+    act(T.Ib[:], "Ib", T.I16[:], "I16", 128)
+    ts(T.paO[:, 0:128], "paO0", T.jm[:], "jm pf", p16, None, A.is_lt)
+    act(T.paO[:, 128:256], "paO1", m16, "m16", 128, scale=HOLD)
+    mm([((T.o2[:, 0:128], T.Ib[:], T.paO[:, 128 * h:128 * h + 128], h == 0, h == 1), 128, 0) for h in range(2)], "Ib paO0 paO1", "o2")
+    act(T.hk[:], "hk", T.o2[:, 0:128], "o2", 128)
+    act(he, "he", T.hk[:, 0:1], "hk", scale=1.0 / HOLD)
     ts(T.Ms[:], "Ms", T.oKi[:, 0:8], "oKi pf hk", pg, T.hk[:, 0:1], A.is_equal, A.mult)
     sfill(T.hk[:, 0:128:16], "hk", 0, 8)
-    act(T.hk[:, 128:256], "hkb", T.hk[:, 0:128], "hk", 128)
-    act(T.hk[:, 256:384], "hkb", T.hk[:, 0:128], "hk", 128)
+    for b in range(3):
+        sfill(T.inj[:, 128 * b:128 * b + 128], "inj", 0, 128)
+    cp(T.X16[:], "X16", T.X[:], "X", NP)
     for t, b in (("O", 0), ("O", 1), ("O", 2), ("V", 0), ("R", 0)):
         c = (QW if MERGE else QW + 80) * b
         sfill(T["q" + t][:, c + 80:c + 80 + QW:GW], "q%s%d" % (t, b), 0, 128)
@@ -344,39 +364,50 @@ def rank_program(g, core, T, topo):
         ts(T.EX[:, 128 * f:128 * f + 128], "EX%d" % f, T.cE[:], "cE ck mf", ck, col(24 + f), A.is_equal, A.mult)
     ts(T.LI[:, 0:140], "LI", T.cL[:, 0:140], "cL cl m3", cl, m3, A.is_equal, A.mult, n=70)
     ts(T.cO16[:, 32:40], "off", T.bc[:, 0:8], "one lo", lo, float(LO - 1), A.mult, A.add)
-    for k in range(4):
-        a, b = owners[2 * k], owners[2 * k + 1]
-        act(T.cS[:, 2 * k:2 * k + 2], "cS%d" % k, T.pf[:, 5:7], "pf", scale=float(NT * (b - a)), bias=float(NT * a - SH - 1) - DEAD)
-    sfill(T.scn[:, 56:64], "scnz", 0, 8)
+    dt = NT * (owners[7] - owners[6])
+    act(cv, "cv", par, "pf", scale=float(PWID - dt), bias=float(LO - NT * owners[6]))
+    for k, a in enumerate([rank] + owners[1:6:2]):
+        act(T.cS[:, 2 * k:2 * k + 2], "cS%d" % k, T.pf[:, 6:8], "pf", scale=float(dt), bias=float(NONE - 1 + NT * (owners[6] - a)))
     sfill(T.RP2[:, 0:2], "RP2p", 0, 2)
-    ts(T.cO16[:, 24:32], "cOn", T.cOw[:, 0:8], "cOw", -1.0, 129.0, A.mult, A.add)
+    sfill(T.cD[:, 15:72:8], "cB", -384, 8)
+    act(T.zz[:, 0:8], "cQc", T.cQ[:, 0:192:24], CQ)
+    for n in (8, 16, 32):
+        act(T.zz[:, n:2 * n], "cQc", T.zz[:, 0:n], "cQc")
+    sfill(T.zz[:, 64:128], "RsM", 0, 64)
+    sfill(T.zz[:, 64:128:8], "RsM", -BIG, 8)
     ts(T.I1k[:], "I1k", T.I16[:], "I16", 1024.0, None, A.mult)
-    ts(T.pj[:, 8:12], "pj8", T.pi[:], "pi", 7, None, A.bitwise_and)
-    cp(oB8, "oB8", T.pj[:, 8:12], "pj8")
+    mm([((T.rA[:, 128:256], T.I16[:], x, k == 0, k == 3), 128, 0) for k, x in enumerate((T.G2[:], T.U2[:, 0:128], T.U2[:, 128:256], T.I1k[:]))],
+       "I16 G2 U2 U2b I1k", "rA")
+    act(T.LW[:], "LW", T.rA[:, 128:256], "rA", 128)
+    ts(oB8, "oB8", T.oKi[:, 0:4], "oKi pf", 2.0, p8, A.mult, A.add)
     act(T.Gf[:], "Gf", T.G2[:], "G2", 128, scale=0.5)
     sfill(T.vW[:, 128:136], "vW0", 0, 8)
     sfill(T.dW[:, 128:136], "dW0", 8192, 8)
-    act(T.gv[:, 0:128], "gv0", m16, "m16", 128, scale=-float(BIG))
-    act(T.gv[:, 129:256], "gv1", T.m16[:, 0:127], "m16", 128, scale=float(MID))
-    sfill(T.gv[:, 128:129], "gv1", 0, 1)
-    tt(T.scC[:, 0:128], "scC", T.gv[:, 0:128], T.gv[:, 128:256], "gv0 gv1", A.add, n=128, f=2)
+    act(T.paR[:], "paR0", m16, "m16", 128, scale=-float(BIG))
+    act(T.paV[:], "paV0", m16, "m16", 128, scale=float(MID))
+    mm([((T.rA[:, 0:128], T.Ib[:], T.paR[:], True, False), 128, 0), ((T.rA[:, 1:128], T.Ib[:], T.paV[:, 0:127], False, True), 128, 0)],
+       "Ib paR0 paV0", "rA")
+    act(T.scC[:, 0:128], "scC", T.rA[:, 0:128], "rA", 128)
     act(T.scC[:, 128:192], "scCb", T.scC[:, 0:64], "scC")
     ts(pK, "pK", p16, "pf", 14.5, -float(MID + 16384), A.is_lt, A.mult)
 
-    def steps_rows(src, srcn, b, c, HL, N, sem, ext=(), aft=None):
-        st, sn = T.st[:, c:c + 32], "st%d" % c
-        ts(st, sn, src, srcn + " cf", cf, float(-b), A.add, A.add, ext=ext, aft=aft)
-        tt(st, sn, st, tI, sn + " tI", A.subtract)
-        cp(T[HL][:, 0:32], HL, st, sn)
+    def steps_rows(src, srcn, k, ext=(), aft=None):
+        st, sn, HL, N = T.st[:, 32 * k:32 * k + 32], "st%d" % k, "HL%d" % k, "N%d" % k
+        if k:
+            ts(xd, "xd", src, srcn, float(base - NT * owners[6]), None, A.add, ext=ext, aft=aft)
+            src, srcn = xd, "xd"
+        tt(T[HL][:, 0:32], HL, src, tI, srcn + " tI", A.subtract)
+        tt(st, sn, src, tI, srcn + " tI", A.subtract)
         tt(T[HL][:, 32:64], HL + "b", st, T[HL][:, 0:32], sn + " " + HL, A.subtract)
-        load("Y", sem, [(T[N][4 * h:4 * h + 4, :], T[HL][:, 32 * h:32 * h + 32]) for h in range(2)], HL + " " + HL + "b", N, 2.3 if aft else LAT0)
+        for h in range(2):
+            load("Y", "ln%d" % k, [(T[N][4 * h:4 * h + 4, :], T[HL][:, 32 * h:32 * h + 32])], HL + "b" * h, N + "b" * h, LAT1 if k else LAT0)
 
     def windows(t, R, Rn, N, banks, on):
         c = PWID * t + LO
         for k, (bk, q) in enumerate(zip(banks, on)):
             h = k % 2
             if k < 2:
-                mm([((T[bk][:], T.m16[0:8, 0:128], T[N][0:8, 512 * h:512 * h + 512], True, True), 512, 0)], "m16 " + N, bk)
+                mm([((T[bk][:], T.m16[0:8, 0:128], T[N][0:8, 512 * h:512 * h + 512], True, True), 512, 0)], "m16 %s %sb" % (N, N), bk)
             else:
                 mm([((T[bk][:], T.LP[0:20, :], T[R][0:20, 512 * h:512 * h + 512], True, True), 512, 0)], "LP " + Rn, bk)
             w, sc = ("ND", 1.0) if k < 2 else ("PW", 64.0)
@@ -387,8 +418,8 @@ def rank_program(g, core, T, topo):
                 ts(o, nm, T[bk][:], bk, sc, None, A.mult, n=512)
 
     load("Y", "lr0", [(T.R0[0:16, :], T.H1[:]), (T.R0[16:20, :], Ld)], "H1 Ld", "R0", LAT0)
-    steps_rows(T.Zn[:], "Zn", base, 0, "HL0", "N0", "ln0")
-    windows(1, "R0", "R0", "N0", ("vK", "vP", "o0", "o1"), "SSSS")
+    steps_rows(T.Zn[:], "Zn", 0)
+    windows(1, "R0", "R0", "N0", ("vK", "vP", "o0", "o1"), WON0)
 
     su1, suA, suB, s1c = T.su[:, 0:24], T.su[:, 24:48], T.su[:, 48:56], T.su[:, 64:88]
 
@@ -399,7 +430,7 @@ def rank_program(g, core, T, topo):
         tt(oh[:], ohn, T.rk[:, 0:32].indirect(oR), T.cQ[:], "rka rkb oR " + CQ, A.is_equal, n8, f=GAT)
         mm([((T.rA[:, 0:n7], T.G2[:], oh[:, 0:n7], True, False), n7, 0), ((T.rA[:, 0:n7:M], ones, T.cD[0:1, 0:7], False, True), 7, 0)],
            "G2 one cD " + ohn, "rA")
-        mm([((T.rB[:, 0:n7], T.U2[:], oh[:, 0:n7], True, True), n7, 0)], "U2 " + ohn, "rB")
+        mm([((T.rB[:, 0:n7], T.U2[:, 128 * h:128 * h + 128], oh[:, 0:n7], h == 0, h == 1), n7, 0) for h in range(2)], "U2 U2b " + ohn, "rB")
         sc = T.rA[:, 256:256 + n7]
         scan(sc, "sc", T.Rs[:], T.rA[:, 0:n7], "Rs rA", A.mult, A.add, n7)
         tt(z2[:], "z2", T.rB[:, 0:n8], oh[:, 0:n8], "rB " + ohn, A.mult, n8)
@@ -410,9 +441,15 @@ def rank_program(g, core, T, topo):
 
     def pack(b, x, xn, tin, bank, W, wn, su, sun):
         ex, PK, ps = T.ex[:, 128 * b:128 * b + 128], T.PK[:, 128 * b:128 * b + 128], T[bank][:, 256:384]
-        tt(ex, "ex%d" % b, T.ti[:, 8 * b:8 * b + 8].indirect(T.oT[:, 0:8]), m16, tin + " oK m16", A.mult, 128, f=GAT)
-        mm([((ps, T.G3[:], ex, True, True), 128, 0)], "G3 ex%d" % b, bank)
-        tt(PK, "PK%d" % b, ps, x, bank + " " + xn, A.add, 128)
+        if x is None:
+            scan(ex, "ex%d" % b, T.hk[:, 0:128], T.inj[:, 128 * b:128 * b + 128], "hk inj", A.mult, A.add, 128)
+            mm([((ps, T.I16[:], T.X16[:, 128 * b:128 * b + 128], True, False), 128, 0)], "I16 X16", bank)
+            mm([((ps, T.G3[:], ex, False, True), 128, 0)], "G3 ex%d" % b, bank)
+            act(PK, "PK%d" % b, ps, bank, 128)
+        else:
+            tt(ex, "ex%d" % b, T.ti[:, 8 * b:8 * b + 8].indirect(T.oT[:, 0:8]), m16, tin + " oK m16", A.mult, 128, f=GAT)
+            mm([((ps, T.G3[:], ex, True, True), 128, 0)], "G3 ex%d" % b, bank)
+            tt(PK, "PK%d" % b, ps, x, bank + " " + xn, A.add, 128)
         cp(W[:].indirect(su), wn, PK, "PK%d %s" % (b, sun), 128, f=SCA)
 
     def message(W, wn, MB, mn):
@@ -433,24 +470,33 @@ def rank_program(g, core, T, topo):
         c0, clo, chi = (0, lo, hi) if t == "V" else (PWID, 0.0, float(HI))
         PWn, NDn = [" ".join([x + a + h for a in ("01" if t == "V" else "1") for h in "01"] + PZ) for x in ("PW", "ND")]
         Lin, Lout = [T[x][:, 8 * b:8 * b + 8] if x else None for x in (Lr, Lw)]
-        tt(pr, "pr" + n, T.PW[:, c0:].indirect(w), X, "%s w%s %s" % (PWn, n, xn), A.mult, 128, f=GAT)
+        if X is not None:
+            tt(pr, "pr" + n, T.PW[:, c0:].indirect(w), X, "%s w%s %s" % (PWn, n, xn), A.mult, 128, f=GAT)
+        else:
+            act(e, "e" + n, T.PW[:, c0:].indirect(w), "%s w%s" % (PWn, n), 128, f=GAT)
+            tt(pr, "pr" + n, e, T[bK][:, 384:512], "e%s %s" % (n, bK), A.mult, 128)
         act(pa, "pa" + n, T.ND[:, c0:].indirect(w), "%s w%s" % (NDn, n), 128, f=GAT)
         first = mm([((pK_, pr, T.S1[:], True, True), 56, 1)], "S1 pr" + n, bK)
         second = mm([((pP, pa, T.sA[:, 64:120], True, True), 56, 0)], "S2 pa" + n, bP)
+        il = lambda: mm([((pL, T.If[:], Lin, True, False), 8, 1)], "If %s%d" % (Lr, b), bL)
         if bL != bK:
             tasks[second]["odeps"].add(first)
-            tasks[mm([((pL, T.If[:], Lin, True, False), 8, 1)], "If %s%d" % (Lr, b), bL)]["odeps"].add(second)
+            tasks[il()]["odeps"].add(second)
         scan(u[:, 64 * b + 1:64 * b + 57], "u" + n, pK_, T.R1c[:, 0:56], "R1c " + bK, A.min, A.max)
         tt(kk, "k" + n, pK_, u[:, 64 * b:64 * b + 56], "%s u%s u0%s" % (bK, n, n), A.is_ge)
         scan(T["q" + t][:, c:c + QW:16], "q" + n, pP, kk, "%s k%s" % (bP, n), A.add, A.mult)
+        if bL == bK and IL:
+            il()
         scan(e, "e" + n, T.hk[:, 0:128], T["q" + t][:, c + 80:c + 80 + QW:GW], "hk q" + n, A.mult, A.add, 128)
-        mm([((pL, e, T.Ms[:], bL == bK, True), 8, 1)], "Ms e" + n, bL)
-        if bL == bK:
+        mm([((pL, e, T.Ms[:], bL == bK and not IL, True), 8, 1)], "Ms e" + n, bL)
+        if bL == bK and not IL:
             tt(Lout, "%s%d" % (Lw, b), pL, Lin, "%s %s%d" % (bL, Lr, b), A.add)
             if not last:
                 ts(w, "w" + n, Lout, "%s%d" % (Lw, b), clo, chi, A.max, A.min)
-        elif not last:
+            return
+        if not last:
             ts(w, "w" + n, pL, bL + " lo hi", clo, chi, A.max, A.min)
+        if not last or t != "V":
             act(Lout, "%s%d" % (Lw, b), pL, bL)
 
     ts(T.rk[:, 16:32], "rka", T.L0[:, 0:16], "L0", 10, None, A.arith_shift_right)
@@ -459,22 +505,30 @@ def rank_program(g, core, T, topo):
     if DELAY:
         tasks[sC]["deps"].add(wr["su1"])
     ts(T.ti[:, 0:24], "ti", T.L0[:], "L0", 1023, None, A.bitwise_and)
+    ts(T.inj[:, 0:NP:16], "inj", T.ti[:, 0:24], "ti he", he, None, A.mult)
     for b, bank in enumerate(("vL", "o2", "vL")):
-        pack(b, T.X[:, 128 * b:128 * b + 128], "X", "ti", bank, T.W1, "W1", T.su[:, 8 * b:8 * b + 8], "su1")
+        pack(b, None, "X", "ti", bank, T.W1, "W1", T.su[:, 8 * b:8 * b + 8], "su1")
     message(T.W1, "W1", T.MB1, "msg1")
     s1 = send(T.MB1, "msg1", "rq1", 8, 0, 32)
 
-    def to_list(out, MB, c0, ins, bank, start, ext=(), aft=None):
-        return mm([((out, T.LI[:, 12 - 4 * c:140 - 4 * c], MB[:, c0 + c:c0 + 32:4], start and c == 0, c == 3), 8, 0) for c in range(4)],
-                  "LI " + ins, bank, ext, aft)
-
-    sBv, sBg = T.sB[:, 0:8], T.sB[:, 8:16]
-    to_list(T.rA[:, 0:8], T.MB1, 0, "msg1", "rA", True)
-    tt(sBv, "sBv", T.rA[:, 0:8], T.cS[:], "rA cS0 cS1 cS2 cS3", A.add)
-    ts(sBg, "sBg", T.rA[:, 0:8], "rA", 2000.0, None, A.is_lt)
-    tt(sBv, "sBv", sBv, sBg, "sBv sBg", A.mult)
-    act(sBv, "sBv", sBv, "sBv", bias=DEAD)
     act(T.xB[:], "xB", T.W1[:, 0:128], "W1 xm m3", 128, F.Identity, scale=xm, bias=m3)
+
+    def arrive(MB, mn, sem, sent, fly):
+        mm([((T.vL[:, 0:8], T.I16[:], T.cO16[:, 32:40], True, False), 8, 0)], "I16 off", "vL")
+        a = mm([((T.vP[:, f:128:4], T.EX[:, 128 * f:128 * f + 128], MB[:, 24:56], True, True), 32, 0) for f in range(4)],
+               "EX0 EX1 EX2 EX3 " + mn, "vP", [(sem, ARR)], (sent, fly))
+        b = mm([((T.vL[:, 0:8], T.LI[:, 12 - 4 * c:140 - 4 * c], MB[:, 24 + c:56:4], False, c == 3), 8, 0) for c in range(4)],
+               "LI " + mn, "vL", [(sem, ARR)], (sent, fly))
+        tasks[b]["odeps"].add(a)
+        act(T.Xv[:], "Xv", T.vP[:, 0:128], "vP xm m3", 128, F.Identity, scale=xm, bias=m3)
+        ts(T.wV[:], "wV0", T.vL[:, 0:8], "vL lo hi", lo, hi, A.max, A.min)
+        act(T.Lv0[:], "Lv00", T.vL[:, 0:8], "vL")
+
+    arrive(T.MB1, "msg1", "rq1", s1, FLY[0])
+    steps_rows(T.NP[:], "NP", 1, [("tC", len(E8))], (sC, FLY_T[0]))
+    load(RQ, "lr1", [(T.R1[16:20, :], T.A2[:])], "", "R1b", LAT1, [("tB", len(E8))], (sB, FLY_T[2]))
+    load(RQ, "lr1", [(T.R1[0:16, :], T.A1[:])], "", "R1", LAT1, [("tA", len(E8))], (sA, FLY_T[1]))
+    windows(0, "R1", "R1 R1b", "N1", WB, WON)
 
     LO3 = "Lo0 Lo1 Lo2"
     ts(T.Lm[:], "Lm0", T.L0[:], "L0", float(-SH) - DEAD, None, A.add)
@@ -510,7 +564,9 @@ def rank_program(g, core, T, topo):
             add("S", lambda: [S.activation(T[Lw][:], T.o2[:, 0:24], F.Copy)], ["o2"], all3(Lw).split(), cy * 90)
             return
         for b in range(3):
-            step("O", b, T.X[:, 128 * b:128 * b + 128], "X", ("o%d" % b,), "Lm" if s == 3 else "Lo", "Lm" if s == 2 else "Lo", s == 5)
+            step("O", b, None if s in SG else T.X16[:, 128 * b:128 * b + 128], "X16", ("o%d" % b,), "Lm" if s == 3 else "Lo", "Lm" if s == 2 else "Lo", s == 5)
+    for b in range(3):
+        mm([((T["o%d" % b][:, 384:512], T.I16[:], T.X16[:, 128 * b:128 * b + 128], True, True), 128, 0)], "I16 X16", "o%d" % b)
     for s in range(3):
         own(s)
 
@@ -520,58 +576,43 @@ def rank_program(g, core, T, topo):
     ts(T.ci[:, 0:24], "ci", T.Lm[:], "Lm0 Lm1 Lm2", float(SH), None, A.add)
     ts(T.ti[:, 0:24], "ti", T.ci[:, 0:24], "ci", 1023, None, A.bitwise_and)
     slots(T.ohA, "ohA", suA, "suA")
+    ts(T.inj[:, 0:NP:16], "inj", T.ti[:, 0:24], "ti he", he, None, A.mult)
     for b in range(3):
-        pack(b, T.X[:, 128 * b:128 * b + 128], "X", "ti", "o%d" % b, T.W2, "W2", T.su[:, 24 + 8 * b:32 + 8 * b], "suA")
+        pack(b, None, "X", "ti", "o%d" % b, T.W2, "W2", T.su[:, 24 + 8 * b:32 + 8 * b], "suA")
     for s in range(3, 6):
         own(s)
 
-    def arrive(MB, mn, sem, sent, fly):
-        mm([((T.vL[:, 0:8], T.I16[:], T.cO16[:, 32:40], True, False), 8, 0)], "I16 off", "vL")
-        a = mm([((T.vP[:, f:128:4], T.EX[:, 128 * f:128 * f + 128], MB[:, 24:56], True, True), 32, 0) for f in range(4)],
-               "EX0 EX1 EX2 EX3 " + mn, "vP", [(sem, ARR)], (sent, fly))
-        tasks[to_list(T.vL[:, 0:8], MB, 24, mn, "vL", False, [(sem, ARR)], (sent, fly))]["odeps"].add(a)
-        ts(T.Xv[:], "Xv", T.vP[:, 0:128], "vP xm m3", xm, m3, A.mult, A.add, n=128)
-        ts(T.wV[:], "wV0", T.vL[:, 0:8], "vL lo hi", lo, hi, A.max, A.min)
-        act(T.Lv0[:], "Lv00", T.vL[:, 0:8], "vL")
-
-    def visitors(RP, outn):
+    def visitors(RP, outn, sub, subn):
         for s in range(3):
             step("V", 0, T.Xv[:], "Xv", ("vK", "vP", "vL"), "Lv" if s else "Lv0", "Lv", s == 2)
-        tt(RP[:, 8:16], outn, T.vL[:, 0:8], T.Lv0[:], "vL Lv00", A.subtract)
+        tt(RP[:, 8:16], outn, T.vL[:, 0:8], sub, "vL " + subn, A.subtract)
 
-    arrive(T.MB1, "msg1", "rq1", s1, FLY[0])
-    steps_rows(T.NP[:], "NP", NT * owners[6], 32, "HL1", "N1", "ln1", [("tC", len(E8))], (sC, FLY_T[0]))
-    load("S", "lr1", [(T.R1[16:20, :], T.A2[:])], "", "R1b", 2.0, [("tB", len(E8))], (sB, FLY_T[2]))
-    load("S", "lr1", [(T.R1[0:16, :], T.A1[:])], "", "R1", 2.0, [("tA", len(E8))], (sA, FLY_T[1]))
-    windows(0, "R1", "R1 R1b", "N1", ("vK", "vP", "vL", "vK"), "SVVS")
-    visitors(T.RP1, "out1")
+    Cn = T.sm[:, 64:72]
+    ts(Cn, "Cn", T.Lv0[:], "Lv00", 3000.0, None, A.is_gt)
+    tt(Cn, "Cn", Cn, T.cS[:], "Cn cS0 cS1 cS2 cS3", A.mult)
+    act(Cn, "Cn", Cn, "Cn cv", fn=F.Identity, bias=cv)
+    visitors(T.RP1, "out1", Cn, "Cn")
     s2 = send(T.RP1, "out1", "rp1", 2, 10, 2)
 
-    mm([((T.vP[:, 0:64], ones, T.cD[0:1, 8:72], True, False), 64, 0), ((T.vP[:, 56:64], T.I16[:], T.cO16[:, 24:32], False, False), 8, 0)],
-       "one cB I16 cOn", "vP")
-    tt(T.Lb[:], "Lb0", sBv, T.RP1[:, 2:10], "sBv out1", A.add, ext=[("rp1", ARR)], aft=(s2, FLY[1]))
-    ts(T.rkB[:], "rkB", T.Lb[:], "Lb0", 1.0 / 1024, RKC, A.mult, A.add)
-    ts(T.ci[:, 24:32], "ciB", T.Lb[:], "Lb0", float(SH), None, A.add)
-    ts(T.ti[:, 24:32], "tiB", T.ci[:, 24:32], "ciB", 1023, None, A.bitwise_and)
-    tt(T.ohB[:], "ohB", T.rkB[:].indirect(oB8), T.cQ[:, 0:192:3], "rkB oB8 " + CQ, A.is_equal, 64, f=GAT)
-    mm([((T.vK[:, 0:56], T.G2[:], T.ohB[:, 0:56], True, True), 56, 0)], "G2 ohB", "vK")
-    mm([((T.vP[:, 0:64], T.I1k[:], T.ohB[:], False, False), 64, 0), ((T.vP[:, 0:56], T.U2[:], T.ohB[:, 0:56], False, True), 56, 0)],
-       "I1k U2 ohB", "vP")
-    scan(T.scn[:, 0:56], "scn", T.Rs[:, 0:168:3], T.vK[:, 0:56], "Rs vK", A.mult, A.add)
-    tt(T.zz[:], "zz", T.scn[:], T.vP[:, 0:64], "scn scnz vP", A.add)
-    tt(T.mx[:, 0:32], "mx0", T.zz[:, 0:32], T.zz[:, 32:64], "zz", A.max)
-    tt(T.mx[:, 32:48], "mx1", T.mx[:, 0:16], T.mx[:, 16:32], "mx0", A.max)
-    tt(T.mx[:, 48:56], "mx2", T.mx[:, 32:40], T.mx[:, 40:48], "mx1", A.max)
-    ts(suB, "suB", T.mx[:, 48:56], "mx2", -1.0, 1056.0, A.mult, A.add)
+    mm([((T.vP[:, 0:64], ones, T.cD[0:1, 8:72], True, False), 64, 0)], "one cB", "vP")
+    back = dict(ext=[("rp1", ARR)], aft=(s2, FLY[1]))
+    ts(T.rkB[:], "rkB", T.RP1[:, 2:10], "out1", 10, None, A.arith_shift_right, **back)
+    ts(T.ti[:, 24:32], "tiB", T.RP1[:, 2:10], "out1", 1023, None, A.bitwise_and, **back)
+    ts(T.Lb[:], "Lb0", T.RP1[:, 2:10], "out1", float(-SH), None, A.add, **back)
+    tt(T.ohB[:], "ohB", T.rkB[:].indirect(oB8), T.zz[:, 0:64], "rkB oB8 cQc", A.is_equal, 64, f=GAT)
+    mm([((T.vP[:, 8 * d:64], T.G2[:] if d else T.LW[:], T.ohB[:, 0:64 - 8 * d], False, d == 7), 64, 0) for d in range(8)], "G2 LW ohB", "vP")
+    scan(T.zz[:, 128:192], "zz", T.zz[:, 64:128], T.vP[:, 0:64], "RsM vP", A.add, A.max)
+    ts(suB, "suB", T.zz[:, 135:192:8], "zz", -1.0, 1056.0, A.mult, A.add)
     pack(3, T.xB[:], "xB", "tiB", "vL", T.W2, "W2", suB, "suB")
     message(T.W2, "W2", T.MB2, "msg2")
     s3 = send(T.MB2, "msg2 RP2p", "rq2", 8, 0, 32)
 
     ts(T.wR[:], "wR0", T.Lb[:], "Lb0", 0.0, float(HI), A.max, A.min)
+    act(T.rA[:, 384:512], "rA", T.xB[:], "xB", 128)
     for s in range(3):
-        step("R", 0, T.xB[:], "xB", ("rA",), "Lr" if s else "Lb", "Lr", s == 2)
+        step("R", 0, None if RSG else T.xB[:], "xB", ("rA",), "Lr" if s else "Lb", "Lr", s == 2)
     arrive(T.MB2, "msg2", "rq2", s3, FLY[2])
-    visitors(T.RP2, "out2")
+    visitors(T.RP2, "out2", T.Lv0[:], "Lv00")
     s4 = send(T.RP2, "out2", "rp2", 2, 10, 2)
 
     smA, smB, vB, Yb = T.sm[:, 0:24], T.sm[:, 24:32], T.sm[:, 32:40], T.sm[:, 40:64]

@@ -3,68 +3,47 @@ from concourse.mybir import AluOpType as A, ActivationFunctionType as F
 
 NT, NP, NK = 1024, 384, 24
 LO, HI, PWID = 8, 1032, 1040
-DEAD = 7.375
-WIN = 640
+DEAD = PWID + HI - 0.5
 BIG, MID, K4 = 8388608, 4194304, 8192
 NONE = 4096
-HOLD = 2.0 ** 60
+HOLD = 2.0 ** 50
 GW, QW = 7, 896
 
+_f, _h, _b, _i, _u = "float32", "float16", "bfloat16", "int32", "uint16"
 _sb = {
-    "X": ([128, NP], "int32"), "L0": ([128, NK], "int32"), "PW": ([128, 2 * PWID], "float32"), "ND": ([128, 2 * PWID], "bfloat16"),
-    "Xv": ([128, 128], "float32"), "xB": ([128, 128], "float32"),
-    "Zp": ([128, 128], "int32"), "Zd": ([128, 32], "int32"), "Zn": ([128, 32], "int32"), "H1": ([128, 128], "float16"),
-    "Ld": ([128, 64], "float16"), "NU": ([128, 32], "uint16"), "NP": ([128, 32], "uint16"), "st": ([128, 128], "float32"),
-    "HL0": ([128, 64], "bfloat16"), "HL1": ([128, 64], "bfloat16"), "R0": ([128, NT], "float16"), "R1": ([128, NT], "float16"),
-    "N0": ([128, NT], "bfloat16"), "N1": ([128, NT], "bfloat16"), "LP": ([128, 128], "float16"),
-    "pi": ([128, 4], "int32"), "pj": ([128, 12], "int32"), "pf": ([128, 32], "float32"), "jm": ([128, 128], "bfloat16"),
-    "mk": ([128, 128], "bfloat16"), "md16": ([128, 128], "bfloat16"), "m16": ([128, 128], "bfloat16"),
-    "G2": ([128, 128], "float16"), "G3": ([128, 128], "float16"), "Gf": ([128, 128], "float32"), "cE": ([128, 128], "bfloat16"),
-    "Ib": ([128, 128], "bfloat16"), "X16": ([128, NP], "float16"), "inj": ([128, NP], "float32"), "U2": ([128, 256], "float16"), "I16": ([128, 128], "float16"), "If": ([128, 128], "float32"), "I1k": ([128, 128], "float16"),
-    "EX": ([128, 512], "float16"), "cL": ([128, 144], "bfloat16"), "LI": ([128, 144], "float16"),
-    "S1": ([128, 56], "float32"), "hk": ([128, 128], "float32"), "sA": ([128, 120], "bfloat16"), "Ms": ([128, 8], "float32"),
-    "R1c": ([128, 168], "float32"), "scC": ([128, 192], "float32"), "sc4": ([128, 128], "float32"),
-    "oKi": ([128, 32], "int32"), "oRi": ([128, 12], "float32"), "oT": ([128, 48], "uint16"),
-    "Rs": ([128, 168], "float32"), "cQ": ([128, 192], "float32"), "cD": ([128, 72], "bfloat16"), "bc": ([128, 128], "bfloat16"),
-    "cOw": ([128, NK], "float32"), "cO16": ([128, 40], "float16"), "cS": ([128, 8], "float32"),
-    "rk": ([128, 32], "int32"), "ci": ([128, 32], "int32"), "ti": ([128, 32], "int32"), "rkB": ([128, 8], "int32"),
-    "oh1": ([128, 192], "float16"), "ohA": ([128, 192], "float16"), "ohB": ([128, 64], "float16"), "ex": ([128, 512], "float16"),
-    "zz": ([128, 192], "float32"), "LW": ([128, 128], "float16"),
-    "z1": ([128, 168], "float16"), "z2": ([128, 192], "float16"), "PK": ([128, 512], "float32"),
-    "su": ([128, 96], "uint16"), "W1": ([128, WIN], "float32"), "W2": ([128, WIN], "float32"), "sd": ([128, 128], "float32"),
-    "MB1": ([128, 56], "float16"), "MB2": ([128, 56], "float16"), "RP1": ([128, 16], "int32"), "RP2": ([128, 16], "float32"),
-    "Lo": ([128, NK], "float32"), "Lm": ([128, NK], "float32"), "wO": ([128, NK], "uint16"), "Lv0": ([128, 8], "float32"),
-    "Lv": ([128, 8], "float32"), "wV": ([128, 8], "uint16"), "Lb": ([128, 8], "float32"), "Lr": ([128, 8], "float32"), "wR": ([128, 8], "uint16"),
-    "sm": ([128, 80], "float32"), "exv": ([128, 128], "float32"), "vW": ([128, 136], "float32"), "gv": ([128, NP], "float32"),
-    "sv": ([128, NP], "float32"), "vO": ([128, NK], "float32"), "vt": ([128, NK], "int32"), "tau": ([128, NK], "uint16"),
-    "dW": ([128, 136], "float32"),
+    "X": (NP, _i), "X16": (NP, _h), "XT": (NP, _h), "Yt": (128, _i), "Xp": (NP, _h), "L0": (NK, _i),
+    "PW": (2 * PWID, _f), "ND": (2 * PWID, _b), "Xv": (128, _f), "Xw": (128, _f), "xB": (128, _f), "Zr": (128, _h), "Ur": (128, _f),
+    "Zp": (128, _i), "Zd": (32, _i), "Zn": (32, _i), "H1": (128, _h), "Ld": (64, _h), "NU": (32, _u), "NP": (32, _u), "st": (160, _f),
+    "HL0": (64, _b), "HL1": (64, _b), "CC": (128, _b), "R0": (NT, _h), "R1": (NT, _h), "N0": (NT, _b), "N1": (NT, _b), "LP": (128, _h),
+    "pi": (4, _i), "pj": (12, _i), "pf": (48, _f), "jm": (128, _b), "mk": (128, _b), "md16": (128, _b), "m16": (128, _b), "bc": (128, _b),
+    "G2": (128, _h), "G3": (128, _h), "Gf": (128, _f), "Ib": (128, _b), "U2": (256, _h), "I16": (128, _h), "I2": (256, _h), "I1k": (128, _h),
+    "LW": (128, _h), "EX": (512, _h), "cL": (144, _b), "LI": (144, _h), "S1": (56, _f), "sA": (192, _b), "Ms": (56, _f), "hk": (256, _f),
+    "R1c": (56, _f), "scC": (192, _f), "sc4": (128, _f), "tb": (256, _b), "oKi": (32, _i), "oRi": (12, _f), "oT": (64, _u),
+    "Rs": (168, _f), "cQ": (192, _f), "cD": (72, _b), "cOw": (NK, _f), "cO16": (40, _h), "cS": (8, _f),
+    "rk": (32, _i), "ci": (32, _i), "ti": (32, _i), "rkB": (8, _i), "oh1": (192, _h), "ohA": (192, _h), "ohB": (64, _h), "inj": (NP, _f),
+    "ex": (512, _h), "zz": (192, _f), "mA": (160, _f), "z1": (168, _h), "z2": (192, _h), "PK": (512, _f), "su": (96, _u),
+    "W1": (640, _f), "W2": (640, _f), "W3": (416, _f), "sd": (128, _f), "MB1": (56, _h), "MB2": (56, _h), "RP1": (16, _i), "RP2": (16, _f),
+    "Lm": (NK, _f), "wO": (NK, _u), "Lv0": (8, _f), "wV": (8, _u), "sm": (80, _f), "exv": (128, _f), "vW": (136, _f), "gv": (NP, _f),
+    "sv": (NP, _f), "vO": (NK, _f), "tau": (NK, _u), "dW": (136, _f),
 }
-for _t, _n in (("O", 3), ("V", 1), ("R", 1)):
-    _sb["pr" + _t] = ([128, 128 * _n], "float32")
-    _sb["pa" + _t] = ([128, 128 * _n], "bfloat16")
-    _sb["u" + _t] = ([128, 64 * _n], "float32")
-    _sb["k" + _t] = ([128, 56 * _n], "float32")
-    _sb["q" + _t] = ([128, (QW + 80) * _n], "float32")
-    _sb["e" + _t] = ([128, 128 * _n], "float32")
-SCRATCH = {_k: ("sbuf", _v[0], _v[1]) for _k, _v in _sb.items()}
-SCRATCH["A1"] = ("dram", [128, 128], "float16")
-SCRATCH["A2"] = ("dram", [128, 32], "float16")
-SCRATCH["A3"] = ("dram", [128, 32], "uint16")
+for _t, _n in (("O", 3), ("V", 1)):
+    _sb.update({"pr" + _t: (128 * _n, _f), "pa" + _t: (128 * _n, _b), "u" + _t: (64 * _n, _f), "k" + _t: (56 * _n, _f),
+                "q" + _t: ((QW + 80) * _n, _f), "e" + _t: (128 * _n, _f)})
+SCRATCH = {_k: ("sbuf", [128, _v[0]], _v[1]) for _k, _v in _sb.items()}
+SCRATCH.update({"A1": ("dram", [128, 128], _h), "A2": ("dram", [128, 32], _h), "A3": ("dram", [128, 32], _u)})
 PSUM = ("o0", "o1", "o2", "vK", "vP", "vL", "rA", "rB")
 for _k in PSUM:
-    SCRATCH[_k] = ("psum", [128, 512], "float32")
-SEMAPHORES = ["sV", "sS", "sT", "sG", "ldA", "ldP", "ldZ", "ldD", "ldN", "lr0", "ln0", "lr1", "ln1", "st", "rq1", "rq2", "rp1", "rp2",
+    SCRATCH[_k] = ("psum", [128, 512], _f)
+SEMAPHORES = ["sV", "sS", "sT", "sG", "ldA", "ldP", "ldZ", "ldD", "ldN", "ldT", "lr0", "ln0", "lr1", "ln1", "st", "rq1", "rq2", "rp1", "rp2",
               "hA", "hB", "hC", "tA", "tB", "tC", "loc"]
 
-FLY = (2.2, 2.2, 2.2, 2.2)
-FLY_T = (7.0, 7.5, 7.0)
-WAKE, MARGIN, ROUNDS, FAC, CALL = 0.2, 0.03, 200, 1.25, 0.3
-LAT0 = 1.7
-MERGE, PARTS, FIX, ADD = False, ((0, 3),), 64, False
-DELAY = False
-SHAKE = 1.0
-LDL, GF = (1.7, 1.6, 2.0, 2.2, 1.7), ("u0", "zP", "zN", "RP", "vW", "dW", "Rs", "cB", "W2", "qR", "qV")
-IL, SG, RSG, WON, WON0, WB, RQ, LAT1 = False, (3, 4, 5), True, "SVVS", "SSSS", ("vK", "vP", "rA", "rB"), "Y", 1.8
+FLY, FLY_T = 2.0, (7.0, 7.5, 7.0)
+WAKE, FAC, CALL, LAT, GAT, SCA = 0.2, 1.3, 0.2, 1.5, 1.8, 4.6
+CASES = ((0.9, 0.16, 0.7, 0.85), (1.0, 0.2, 1.25, 1.0), (1.15, 0.17, 0.9, 1.2))
+ROUNDS, SHAKE, PULL, SPAN = 3600, 0.1, 3.0, 1.5
+GF = ("u0", "zP", "RP", "vW", "dW", "Rs", "cB", "W2", "qV")
+WON, WON0, WB = "SSSS", "SSSS", ("vK", "vP", "rA", "rB")
+CUT = ((0, 12), (12, 24))
 PLANS = {}
 
 
@@ -115,7 +94,7 @@ def place(tasks, pre, key):
         while lo < hi:
             mid = (lo + hi) // 2
             lo, hi = (mid + 1, hi) if l[mid][1] <= s else (lo, mid)
-        while lo < len(l) and s + c + MARGIN > l[lo][0]:
+        while lo < len(l) and s + c > l[lo][0]:
             s = l[lo][1]
             lo += 1
         fin[i] = s + c
@@ -145,20 +124,47 @@ def plan(tasks):
     tail = [0.0] * n
     for i in range(n - 1, -1, -1):
         tail[i] = tasks[i]["cost"] + max([0.0] + [tail[x] + w for x, w in post[i].items()])
-    key, best, bkey, seed = [-x for x in tail], None, None, 1
+    cases = []
+    for calls, wake, way, ind in CASES:
+        e = [[(d, 0.0) for d in t["odeps"]] + [(d, wake + way * tasks[d]["lat"]) for d in t["deps"]] +
+             ([(t["aft"][0], way * t["aft"][1])] if t["aft"] else []) for t in tasks]
+        cases.append(([t["cost"] * (way * way if t["dma"] else calls * ind if t["ind"] else calls) for t in tasks], e))
+
+    def length(start):
+        total, seq = 0.0, sorted(range(n), key=lambda j: (start[j], j))
+        for calls, e in cases:
+            end, free = [0.0] * n, {}
+            for i in seq:
+                q = tasks[i]["q"]
+                end[i] = free[q] = max([free.get(q, 0.0)] + [end[d] + w for d, w in e[i]]) + calls[i]
+            total += max(end)
+        return total
+    key, best, bkey, seed, low = [-x for x in tail], None, None, 1, 0.0
     for r in range(ROUNDS):
         fin = place(tasks, pre, key)
-        if best is None or max(fin) < max(best):
-            best, bkey = fin, key
-        back = place(tasks, post, [-x for x in fin])
-        key = [-x for x in back]
+        if best is None or max(fin) < max(best) + 1.0:
+            start = [x - t["cost"] for x, t in zip(fin, tasks)]
+            x = max(fin) + length(start)
+            if best is None or x < low:
+                best, bkey, low = fin, start, x
+        key = [-x for x in place(tasks, post, [-x for x in fin])]
         if r % 3 == 2:
             key = []
             for x in bkey:
                 seed = seed * 16807 % 2147483647
                 key.append(x + SHAKE * seed / 2147483647)
+            i = seed % n
+            seed = seed * 16807 % 2147483647
+            pull, todo, seen = PULL * seed / 2147483647, [i], {i}
+            while todo:
+                j = todo.pop()
+                key[j] -= pull
+                for x in post[j]:
+                    if x not in seen and bkey[x] < bkey[i] + SPAN:
+                        seen.add(x)
+                        todo.append(x)
     order = {}
-    for i in sorted(range(n), key=lambda j: (best[j] - tasks[j]["cost"], j)):
+    for i in sorted(range(n), key=lambda j: (bkey[j], j)):
         order.setdefault(tasks[i]["q"], []).append(i)
     PLANS[n] = order
     PLANS["t"] = max(best)
@@ -177,13 +183,13 @@ def rank_program(g, core, T, topo):
     owners = [T.cores.index(c) for s in peers + [core] for c in (partner[s], s)]
     base = NT * rank
     SH = base - LO
+    SA = SH - PWID
     tasks, wr, rd = [], {}, {}
     V, S, E = g.vector, g.scalar, g.tensor
     cy = 0.00083 * FAC
-    cost = lambda n: cy * (FIX + (n if n != 64 else 30) if ADD else max(64, n))
 
-    def add(q, fn, reads, writes, cost, ext=(), aft=None):
-        i = len(tasks)
+    def add(q, fn, reads, writes, cost, ext=(), aft=None, ind=False):
+        i, reads, writes = len(tasks), reads.split(), writes.split()
         deps, odeps = set(), set()
         for b in reads:
             if b in wr:
@@ -194,7 +200,7 @@ def rank_program(g, core, T, topo):
             if b in wr:
                 (odeps if q == "T" and tasks[wr[b]]["q"] == "T" else deps).add(wr[b])
             deps.update(rd.get(b, ()))
-        tasks.append(dict(nm=(list(writes) + ["-"])[0], q=q, fn=fn, deps=deps, odeps=odeps, cost=cost, ext=tuple(ext), aft=aft, dma=None, lat=0.0))
+        tasks.append(dict(nm=(writes + ["-"])[0], q=q, fn=fn, deps=deps, odeps=odeps, cost=cost, ext=tuple(ext), aft=aft, dma=None, lat=0.0, ind=ind))
         for b in reads:
             rd.setdefault(b, []).append(i)
         for b in writes:
@@ -202,51 +208,51 @@ def rank_program(g, core, T, topo):
             rd[b] = []
         return i
 
-    def vop(fn, reads, writes, n=64, ext=(), aft=None, f=1.0):
-        return add("V", lambda: [fn()], reads, writes, cost(n * f) if f == int(f) else 0.05 + cy * n * f, ext, aft)
+    def vop(fn, ins, on, n=64, ext=(), aft=None, f=1):
+        return add("V", lambda: [fn()], ins, on, 0.05 + cy * n * f if f != 1 else cy * max(64, n), ext, aft, f != 1)
 
     def ts(out, on, in0, ins, s1, s2, op0, op1=None, n=64, ext=(), aft=None):
         if op1 is None:
-            return vop(lambda: V.tensor_scalar(out, in0, s1, None, op0), ins.split(), [on], n, ext, aft)
-        return vop(lambda: V.tensor_scalar(out, in0, s1, s2, op0, op1), ins.split(), [on], n, ext, aft)
+            return vop(lambda: V.tensor_scalar(out, in0, s1, None, op0), ins, on, n, ext, aft)
+        return vop(lambda: V.tensor_scalar(out, in0, s1, s2, op0, op1), ins, on, n, ext, aft)
 
-    def tt(out, on, in0, in1, ins, op, n=64, ext=(), aft=None, f=1.0):
-        return vop(lambda: V.tensor_tensor(out, in0, in1, op), ins.split(), [on], n, ext, aft, f)
+    def tt(out, on, in0, in1, ins, op, n=64, ext=(), aft=None, f=1):
+        return vop(lambda: V.tensor_tensor(out, in0, in1, op), ins, on, n, ext, aft, f)
 
-    def cp(out, on, in_, ins, n=64, f=1.0):
-        return vop(lambda: V.tensor_copy(out, in_), ins.split(), [on], n, f=f)
+    def cp(out, on, in_, ins, n=64, f=1):
+        return vop(lambda: V.tensor_copy(out, in_), ins, on, n, f=f)
 
     def scan(out, on, d0, d1, ins, op0, op1, n=64):
-        return vop(lambda: V.tensor_tensor_scan(out, d0, d1, 0.0, op0, op1), ins.split(), [on], n)
+        return vop(lambda: V.tensor_tensor_scan(out, d0, d1, 0.0, op0, op1), ins, on, n)
 
-    def act(out, on, in_, ins, n=64, fn=F.Copy, f=1.0, **kw):
-        return add("S", lambda: [S.activation(out, in_, fn, **kw)], ins.split(), [on], cost(n) if f == 1 else 0.065 + cy * n * f)
+    def act(out, on, in_, ins, n=64, fn=F.Copy, f=1, **kw):
+        return add("S", lambda: [S.activation(out, in_, fn, **kw)], ins, on, 0.065 + cy * n * f if f != 1 else cy * max(64, n), ind=f != 1)
 
-    def sfill(ap, on, v, n):
+    def iota(ap, on, pat, b, ch, n, fl=True):
+        if fl:
+            return add("G", lambda: [g.iota(ap, pat, b, ch, allow_small_or_imprecise_dtypes=True)], "", on, 0.13 + 2 * cy * n)
+        return add("G", lambda: [g.iota(ap, pat, b, ch)], "", on, 0.13 + 2 * cy * n)
+
+    def fill(ap, on, v, n):
         if on[:2] in GF:
             return iota(ap, on, [[0, n]], v, 0, n)
         return act(ap, on, T.bc[:, 0:n], "one", n, scale=0.0, bias=float(v))
 
-    def iota(ap, on, pat, b, ch, n, fl=True):
-        if fl:
-            return add("G", lambda: [g.iota(ap, pat, b, ch, allow_small_or_imprecise_dtypes=True)], [], [on], 0.13 + 2 * cy * n)
-        return add("G", lambda: [g.iota(ap, pat, b, ch)], [], [on], 0.13 + 2 * cy * n)
+    def select(ap, on, pat, b):
+        return add("G", lambda: [g.affine_select(ap, T.ohA[:, 0:128], pat, A.is_equal, 0.0, b, 1)], "ohA", on, 0.17 + 256 * cy)
 
     def mm(lst, ins, bank, ext=(), aft=None):
         c = sum(cy * max(64, n) * (4 if f4 else 1) for (_, n, f4) in lst)
-        return add("T", lambda: [E.matmul(*a) for (a, n, f4) in lst], ins.split(), [bank], c, ext, aft)
+        return add("T", lambda: [E.matmul(*a) for (a, n, f4) in lst], ins, bank, c, ext, aft)
 
-    loads = {}
+    loads, nloc = {}, [0]
 
-    def load(q, sem, pairs, ins, on, lat, ext=(), aft=None):
+    def load(q, sem, pairs, ins, on, lat=LAT, ext=(), aft=None):
         eng = g.sync if q == "Y" else g.scalar
-        i = add(q, lambda: [eng.dma_start(o, x) for o, x in pairs], ins.split(), on.split(), 0.1 * len(pairs), ext, aft)
-        tasks[i]["dma"] = sem
-        tasks[i]["lat"] = lat
+        i = add(q, lambda: [eng.dma_start(o, x) for o, x in pairs], ins, on, 0.1 * len(pairs), ext, aft)
+        tasks[i]["dma"], tasks[i]["lat"] = sem, lat
         loads[sem] = loads.get(sem, 0) + 16 * len(pairs)
         return i
-
-    nloc = [0]
 
     def remote(calls, ins):
         def fn():
@@ -254,24 +260,24 @@ def rank_program(g, core, T, topo):
                 g.remote_dma_fused([transfer(topo, core, d, es, T.sem[s], a, b) for d, es, s, a, b in c], local_sem=T.sem.loc)
                 nloc[0] += sum(len(x[1]) for x in c)
             return []
-        return add("G", fn, ins.split(), [], CALL * len(calls))
+        return add("G", fn, ins, "", CALL * len(calls))
     E8 = topo.engines(core, peers[0])
-    GAT, SCA = 1.6, 3.8
+    blk = lambda t, b, w=128: t[:, w * b:w * b + w]
 
-    vop(lambda: V.memset(T.bc[:], 1.0), [], ["one"])
-    vop(lambda: V.memset(T.X[:], 1), [], ["X"], NP)
-    a = load("Y", "ldN", [(T.Zn[:], T.nbr[:])], "", "Zn", LDL[0])
-    b = load("S", "ldZ", [(T.Zp[:], T.planes[:])], "", "Zp", LDL[1])
-    tasks[load("S", "ldD", [(T.Zd[:], T.planes[3:16:4, :])], "", "Zd", LDL[2])]["odeps"].add(b)
-    tasks[load("Y", "ldA", [(T.L0[:], T.tet0[:])], "", "L0", LDL[3])]["odeps"].add(a)
-    load("Y", "ldP", [(T.X[4 * f + i:128:16, :], T.pts[i:24:3, :]) for f in range(4) for i in range(3)], "", "X", LDL[4])
+    vop(lambda: V.memset(T.bc[:], 1.0), "", "one")
+    vop(lambda: V.memset(T.X[:], 1), "", "X", NP)
+    a = load("Y", "ldN", [(T.Zn[:], T.nbr[:])], "", "Zn")
+    b = load("S", "ldZ", [(T.Zp[:], T.planes[:])], "", "Zp")
+    tasks[load("S", "ldD", [(T.Zd[:], T.planes[3:16:4, :])], "", "Zd", LAT + 0.2)]["odeps"].add(b)
+    tasks[load("Y", "ldA", [(T.L0[:], T.tet0[:])], "", "L0", LAT + 0.3)]["odeps"].add(a)
+    load("Y", "ldP", [(T.X[4 * f + i:128:16, :], T.pts[i:24:3, :]) for f in range(4) for i in range(3)], "", "X")
 
-    xd, tI, Ld, Hd = T.st[:, 64:96], T.st[:, 96:128], T.Ld[:, 0:32], T.Ld[:, 32:64]
+    xd, tI, xp, Ld, Hd = T.st[:, 64:96], T.st[:, 96:128], T.st[:, 128:160], T.Ld[:, 0:32], T.Ld[:, 32:64]
     cp(T.NU[:], "NU", T.Zn[:], "Zn")
     sC = remote([[(rel[1], E8, "hC", T.NU[:], T.A3[:])]], "NU")
     ts(T.H1[:], "H1", T.Zp[:], "Zp", 1.0 / 64, None, A.mult, n=128)
     sA = remote([[(rel[0], E8, "hA", T.H1[:], T.A1[:])]], "H1")
-    ts(xd, "xd", T.Zd[:], "Zd", 1.0 / 64, None, A.mult)
+    act(xd, "xd", T.Zd[:], "Zd", scale=1.0 / 64)
     ts(Hd, "Hd", T.Zd[:], "Zd", 1.0 / 64, None, A.mult)
     tt(Ld, "Ld", xd, Hd, "xd Hd", A.subtract)
     sB = remote([[(rel[1], E8, "hB", Ld, T.A2[:])]], "Ld")
@@ -287,137 +293,152 @@ def rank_program(g, core, T, topo):
     iota(T.cOw[:], "cOw", [[16, 24]], 128, 1, 24)
     iota(T.cD[:, 0:8], "cD", [[32, 4], [1, 2]], -2, 0, 8)
     iota(T.cD[:, 8:72], "cB", [[0, 8], [-32, 4], [-1, 2]], 0, 0, 64)
-    iota(T.cE[:], "cE", [[4, 8], [0, 4], [1, 4]], 0, 0, 128)
     iota(tI, "tI", [[1, 32]], 0, 32, 32)
     iota(T.sA[:, 0:57], "sA", [[1, 57]], -2, 0, 57)
     iota(T.cL[:, 0:140], "cL", [[1, 140]], -12, 0, 140)
+    iota(T.CC[:, 0:64], "CH", [[1024, 2], [0, 32]], 0, 32, 64)
+    iota(T.CC[:, 64:128], "CL", [[PWID - 1024, 2], [1, 32]], LO, 0, 64)
     for k, v in enumerate(owners):
-        sfill(T.cQ[:, 24 * k:24 * k + 24], "cQ%d" % k, v, 24)
+        fill(blk(T.cQ, k, 24), "cQ%d" % k, v, 24)
     CQ = " ".join("cQ%d" % k for k in range(8))
     act(T.Rs[:], "Rs", T.cQ[:, 0:168], CQ, 168, scale=0.0, bias=1.0)
-    sfill(T.Rs[:, 0:168:24], "Rs", 0, 7)
+    fill(T.Rs[:, 0:168:24], "Rs", 0, 7)
     ones = T.bc[0:1, 0:128]
-    for k, (w, a, o1, b, o2) in enumerate(((1, 15, A.bitwise_and, None, None), (1, 4, A.arith_shift_right, None, None),
-                                           (1, 3, A.bitwise_and, None, None), (1, 2, A.arith_shift_right, 3, A.bitwise_and),
-                                           (1, 3, A.arith_shift_right, 1, A.bitwise_and), (1, 5, A.arith_shift_right, None, None),
-                                           (2, 1, A.bitwise_and, None, None))):
-        ts(T.pj[:, k:k + w], "pj%d" % k, T.pi[:, 0:w], "pi", a, b, o1, o2)
+    sh, an = A.arith_shift_right, A.bitwise_and
+    for k, x in enumerate(((15, None, an), (4, None, sh), (3, None, an), (2, 3, sh, an), (3, 1, sh, an), (5, None, sh))):
+        ts(T.pj[:, k:k + 1], "pj%d" % k, T.pi[:, 0:1], "pi", *x)
+    ts(T.pj[:, 6:8], "pj6", T.pi[:, 0:2], "pi", 1, None, an)
     cp(T.pf[:, 0:8], "pf", T.pj[:, 0:8], " ".join("pj%d" % k for k in range(7)))
     col = lambda k: T.pf[:, k:k + 1]
     p16, pg, pi_, pf_, p8, p5, par = [col(k) for k in range(7)]
-    act(col(23), "cf", p5, "pf", scale=-1024.0, bias=float(base))
-    act(tI, "tI", tI, "tI cf", fn=F.Identity, bias=col(23))
-    cv, g31, hL, ck, cl, c3, c1, lo, hi, pK, pK4, m3, xm, c2, he = [col(k) for k in range(8, 23)]
-    for ap, nm, src, sc, bi in ((c3, "c3", pg, 4.0, 3.0), (g31, "g31", pg, 3.0, 1.0),
-                                (pK4, "pK4", pf_, float(K4), -3.0 * K4), (lo, "lo", par, float(PWID), 0.0), (hi, "hi", par, float(PWID), float(HI))):
+    cv, g31, hL, cf, cl, c1, c2, lo, hi, pK, pK4, pL, m3, xm, m34, he, he2, f15, g15, p15, m89, k8, cA, cB = [col(k) for k in range(8, 32)]
+    act(cf, "cf", p5, "pf", scale=-1024.0, bias=float(base))
+    act(tI, "tI", tI, "tI cf", fn=F.Identity, bias=cf)
+    for ap, nm, src, sc, bi in ((g31, "g31", pg, 3.0, 1.0), (pK4, "pK4", pf_, float(K4), -3.0 * K4), (lo, "lo", par, float(PWID), 0.0),
+                                (hi, "hi", par, float(PWID), float(HI))):
         act(ap, nm, src, "pf", scale=sc, bias=bi)
     act(hL, "hL", p16, "pf g31", fn=F.Identity, scale=g31, bias=g31)
-    for ap, nm, sc, bi in ((ck, "ck", 4.0, pi_), (cl, "cl", 16.0, pf_), (c1, "c1", float(GW), pi_), (c2, "c2", float(GW), pf_)):
+    for ap, nm, sc, bi in ((cl, "cl", 16.0, pf_), (c1, "c1", float(GW), pi_), (c2, "c2", float(GW), pf_)):
         act(ap, nm, pg, "pf", fn=F.Identity, scale=sc, bias=bi)
+    act(c1, "c1", p8, "pf c1", fn=F.Identity, scale=200.0, bias=c1)
     oK, oR, oB8 = T.oT[:, 0:24], T.oT[:, 24:36], T.oT[:, 40:44]
-    m16 = T.m16[:, 0:128]
+    m16 = T.m16[:]
     ts(oR, "oR", T.oRi[:], "oRi pf", p16, None, A.add)
     ts(T.G2[:], "G2", T.md16[:], "md16 pf", pg, 2.0, A.is_equal, A.mult)
     ts(T.I16[:], "I16", T.mk[:], "mk", 0.0, None, A.is_equal)
     ts(T.U2[:, 0:128], "U2", T.mk[:], "mk", 0.0, -2.0, A.is_lt, A.mult)
     ts(T.U2[:, 128:256], "U2b", T.md16[:], "md16 pf", pg, 2.0, A.is_lt, A.mult)
-    cp(T.cO16[:, 0:24], "cO16", T.cOw[:], "cOw")
+    act(T.cO16[:, 0:24], "cO16", T.cOw[:], "cOw")
     cp(oK, "oK", T.oKi[:, 0:24], "oKi")
     ts(m16, "m16", T.jm[:], "jm pf", p16, None, A.is_equal)
-    ts(T.G3[:], "G3", T.cE[:], "cE c3", c3, None, A.is_equal)
-    ts(T.pf[:, 24:28], "mf", T.oKi[:, 0:4], "oKi pf", pf_, None, A.is_equal)
-    act(T.pf[:, 28:32], "m4", T.pf[:, 24:28], "mf", scale=-float(BIG + K4))
+    fill(T.G3[:], "G3", 0, 128)
+    act(T.G3[:, 3:128:4], "G3", T.G2[:, 3:128:4], "G2", scale=0.5)
+    ts(T.pf[:, 32:36], "m4", T.oKi[:, 0:4], "oKi pf", pf_, -float(BIG + K4), A.is_equal, A.mult)
     for j in range(4):
-        act(T.sc4[:, j:128:4], "sc4%d" % j, T.bc[:, 0:32], "one m4", scale=col(28 + j), bias=float(K4))
+        act(T.sc4[:, j:128:4], "sc4%d" % j, T.bc[:, 0:32], "one m4", scale=col(32 + j), bias=float(K4))
+    SC4 = "sc40 sc41 sc42 sc43 "
     ts(T.LP[0:20, :], "LP", T.jm[0:20, :], "jm hL", 1.0, T.pf[0:20, 10:11], A.add, A.is_equal)
-    sfill(T.W1[:, 0:128], "W1", NONE, 128)
-    sfill(T.W2[:, 0:128], "W2", NONE, 128)
-    act(T.R1c[:], "R1c", T.cQ[:, 0:168], CQ, 168, scale=0.0, bias=-float(BIG))
-    sfill(T.R1c[:, 6:168:GW], "R1c", BIG, 24)
-    ts(T.S1[:], "S1", T.sA[:, 1:57], "sA c2", c2, None, A.is_equal)
-    ts(T.sA[:, 0:57], "sA", T.sA[:, 0:57], "sA c1", c1, 1.0 / HOLD, A.is_equal, A.mult)
-    tt(T.sA[:, 64:120], "S2", T.sA[:, 0:56], T.sA[:, 1:57], "sA", A.subtract, n=56, f=2)
-    act(T.If[:], "If", T.I16[:], "I16", 128)
-    act(T.Ib[:], "Ib", T.I16[:], "I16", 128)
-    ts(T.paO[:, 0:128], "paO0", T.jm[:], "jm pf", p16, None, A.is_lt)
-    act(T.paO[:, 128:256], "paO1", m16, "m16", 128, scale=HOLD)
-    mm([((T.o2[:, 0:128], T.Ib[:], T.paO[:, 128 * h:128 * h + 128], h == 0, h == 1), 128, 0) for h in range(2)], "Ib paO0 paO1", "o2")
-    act(T.hk[:], "hk", T.o2[:, 0:128], "o2", 128)
-    act(he, "he", T.hk[:, 0:1], "hk", scale=1.0 / HOLD)
-    ts(T.Ms[:], "Ms", T.oKi[:, 0:8], "oKi pf hk", pg, T.hk[:, 0:1], A.is_equal, A.mult)
-    sfill(T.hk[:, 0:128:16], "hk", 0, 8)
-    for b in range(3):
-        sfill(T.inj[:, 128 * b:128 * b + 128], "inj", 0, 128)
-    cp(T.X16[:], "X16", T.X[:], "X", NP)
-    for t, b in (("O", 0), ("O", 1), ("O", 2), ("V", 0), ("R", 0)):
-        c = (QW if MERGE else QW + 80) * b
-        sfill(T["q" + t][:, c + 80:c + 80 + QW:GW], "q%s%d" % (t, b), 0, 128)
-        sfill(T["u" + t][:, 64 * b:64 * b + 1], "u0%s%d" % (t, b), BIG, 1)
-    PZ = []
-    for w in ("PW", "ND"):
-        for a, z in ((0, LO), (HI, PWID + LO), (PWID + HI, 2 * PWID)):
-            sfill(T[w][:, a:z], "z%s%d" % (w, a), 0, z - a)
-            PZ.append("z%s%d" % (w, a))
+    fill(T.W1[:, 0:128], "W1", NONE, 128)
+    fill(T.W2[:, 0:128], "W2", NONE, 128)
     ts(m3, "m3", pi_, "pf", 3.0, None, A.is_equal)
     act(xm, "xm", m3, "m3", scale=-1.0, bias=1.0)
+    act(T.X16[:], "X16", T.X[:], "X", NP)
+    for b in range(3):
+        fill(blk(T.inj, b), "inj", 0, 128)
+    S2, S2a = T.sA[:, 64:120], T.sA[:, 128:184]
+    fill(T.R1c[:], "R1c", -BIG, 56)
+    fill(T.R1c[:, 6:56:GW], "R1c", BIG, 8)
+    ts(T.S1[:], "S1", T.sA[:, 1:57], "sA c2", c2, None, A.is_equal)
+    ts(T.sA[:, 0:57], "sA", T.sA[:, 0:57], "sA c1", c1, None, A.is_equal)
+    tt(S2, "S2", T.sA[:, 0:56], T.sA[:, 1:57], "sA", A.subtract, n=112)
+    tt(m89, "m89", T.m16[:, 8:9], T.m16[:, 9:10], "m16", A.add)
+    ts(T.sm[:, 72:80], "E8", T.oKi[:, 0:8], "oKi pf m89", pg, m89, A.is_equal, A.mult)
+    act(S2a, "S2a", S2, "S2")
+    tt(T.sA[:, 133:184:GW], "S2a", T.sA[:, 69:120:GW], T.sm[:, 72:80], "S2 E8", A.add)
+    act(T.Ib[:], "Ib", T.I16[:], "I16", 128)
+    ts(T.tb[:, 0:128], "tb0", T.jm[:], "jm pf", p16, None, A.is_lt)
+    act(T.tb[:, 128:256], "tb1", m16, "m16", 128, scale=HOLD)
+    mm([((T.o2[:, 0:128], T.Ib[:], blk(T.tb, h), h == 0, h == 1), 128, 0) for h in range(2)], "Ib tb0 tb1", "o2")
+    act(T.hk[:, 0:128], "hk", T.o2[:, 0:128], "o2", 128)
+    act(T.hk[:, 128:256], "hk2", T.o2[:, 0:128], "o2", 128)
+    act(he, "he", T.hk[:, 0:1], "hk", scale=1.0 / HOLD)
+    fill(T.hk[:, 0:128:16], "hk", 0, 8)
+    ts(f15, "f15", p16, "pf", 14.5, 1.0 / HOLD, A.is_lt, A.max)
+    ts(g15, "g15", p16, "pf", 14.5, HOLD, A.is_gt, A.mult)
+    ts(g15, "g15", g15, "g15", 1.0, None, A.max)
+    act(he2, "he2", he, "he f15", scale=f15)
+    act(T.hk[:, 128:256:16], "hk2", T.bc[:, 0:8], "one he2", scale=he2)
+    fill(T.Ms[:], "Ms", 0, 56)
+    ts(T.Ms[:, 5:56:GW], "Ms", T.oKi[:, 0:8], "oKi pf g15", pg, g15, A.is_equal, A.mult)
+    for t, b in (("O", 0), ("O", 1), ("O", 2), ("V", 0)):
+        c = (QW + 80) * b
+        fill(T["q" + t][:, c + 80:c + 80 + QW:GW], "q%s%d" % (t, b), 0, 128)
+        fill(T["u" + t][:, 64 * b:64 * b + 1], "u0%s%d" % (t, b), BIG, 1)
+    act(k8, "k8", T.m16[:, 8:9], "m16", scale=1024.0)
+    act(cA, "cA", T.m16[:, 9:10], "m16 k8", fn=F.Identity, scale=HI - 1024.0, bias=k8)
+    act(k8, "k8", k8, "k8", scale=2.0)
+    act(cB, "cBd", T.m16[:, 9:10], "m16 k8", fn=F.Identity, scale=DEAD - 2048.0, bias=k8)
+    for a, z in ((0, LO), (HI, PWID + LO), (PWID + HI, 2 * PWID)):
+        fill(T.PW[:, a:z], "zP%d" % a, 0, z - a)
+    fill(T.ND[:, 0:LO], "zN0", 0, LO)
+    for k, (a, c, cn) in enumerate(((HI, cA, "cA"), (PWID, cB, "cBd"), (PWID + HI, cB, "cBd"))):
+        act(T.ND[:, a:a + LO], "zN%d" % (k + 1), T.bc[:, 0:LO], "one " + cn, scale=c)
+    PZ = {"PW": " zP0 zP%d zP%d" % (HI, PWID + HI), "ND": " zN0 zN1 zN2 zN3"}
+    fill(T.ohA[:, 0:128], "ohA", 1, 128)
     for f in range(4):
-        ts(T.EX[:, 128 * f:128 * f + 128], "EX%d" % f, T.cE[:], "cE ck mf", ck, col(24 + f), A.is_equal, A.mult)
+        select(blk(T.EX, f), "EX%d" % f, [[-16, 8], [0, 4], [-1, 4]], -4 * f)
     ts(T.LI[:, 0:140], "LI", T.cL[:, 0:140], "cL cl m3", cl, m3, A.is_equal, A.mult, n=70)
-    ts(T.cO16[:, 32:40], "off", T.bc[:, 0:8], "one lo", lo, float(LO - 1), A.mult, A.add)
+    act(T.cO16[:, 32:40], "off", T.bc[:, 0:8], "one lo", scale=lo, bias=float(LO - 1))
     dt = NT * (owners[7] - owners[6])
     act(cv, "cv", par, "pf", scale=float(PWID - dt), bias=float(LO - NT * owners[6]))
     for k, a in enumerate([rank] + owners[1:6:2]):
-        act(T.cS[:, 2 * k:2 * k + 2], "cS%d" % k, T.pf[:, 6:8], "pf", scale=float(dt), bias=float(NONE - 1 + NT * (owners[6] - a)))
-    sfill(T.RP2[:, 0:2], "RP2p", 0, 2)
-    sfill(T.cD[:, 15:72:8], "cB", -384, 8)
+        act(T.cS[:, 2 * k:2 * k + 2], "cS%d" % k, T.pf[:, 6:8], "pf", scale=float(dt - 1), bias=float(HI - LO + NT * (owners[6] - a)))
+    iota(T.RP1[:, 0:2], "RP1p", [[0, 2]], 0, 0, 2, False)
+    fill(T.RP2[:, 0:2], "RP2p", 0, 2)
+    fill(T.cD[:, 15:72:8], "cB", -384, 8)
     act(T.zz[:, 0:8], "cQc", T.cQ[:, 0:192:24], CQ)
     for n in (8, 16, 32):
         act(T.zz[:, n:2 * n], "cQc", T.zz[:, 0:n], "cQc")
-    sfill(T.zz[:, 64:128], "RsM", 0, 64)
-    sfill(T.zz[:, 64:128:8], "RsM", -BIG, 8)
-    ts(T.I1k[:], "I1k", T.I16[:], "I16", 1024.0, None, A.mult)
-    mm([((T.rA[:, 128:256], T.I16[:], x, k == 0, k == 3), 128, 0) for k, x in enumerate((T.G2[:], T.U2[:, 0:128], T.U2[:, 128:256], T.I1k[:]))],
-       "I16 G2 U2 U2b I1k", "rA")
-    act(T.LW[:], "LW", T.rA[:, 128:256], "rA", 128)
+    fill(T.zz[:, 64:128], "RsM", 0, 64)
+    fill(T.zz[:, 64:128:8], "RsM", -BIG, 8)
     ts(oB8, "oB8", T.oKi[:, 0:4], "oKi pf", 2.0, p8, A.mult, A.add)
+    iota(T.ci[:, 0:8], "ci", [[16, 8]], 0, 1, 8, False)
+    iota(T.ci[:, 8:16], "cib", [[-16, 8]], 128, 1, 8, False)
+    ts(T.ci[:, 0:16], "ci", T.ci[:, 0:16], "ci cib", 127, None, an)
+    cp(T.oT[:, 48:64], "rot", T.ci[:, 0:16], "ci")
+    act(T.I2[:, 0:128], "I2", T.I16[:], "I16", 128)
+    act(T.I2[:, 128:256], "I2b", T.I16[:], "I16", 128)
     act(T.Gf[:], "Gf", T.G2[:], "G2", 128, scale=0.5)
-    sfill(T.vW[:, 128:136], "vW0", 0, 8)
-    sfill(T.dW[:, 128:136], "dW0", 8192, 8)
-    act(T.paR[:], "paR0", m16, "m16", 128, scale=-float(BIG))
-    act(T.paV[:], "paV0", m16, "m16", 128, scale=float(MID))
-    mm([((T.rA[:, 0:128], T.Ib[:], T.paR[:], True, False), 128, 0), ((T.rA[:, 1:128], T.Ib[:], T.paV[:, 0:127], False, True), 128, 0)],
-       "Ib paR0 paV0", "rA")
-    act(T.scC[:, 0:128], "scC", T.rA[:, 0:128], "rA", 128)
-    act(T.scC[:, 128:192], "scCb", T.scC[:, 0:64], "scC")
-    ts(pK, "pK", p16, "pf", 14.5, -float(MID + 16384), A.is_lt, A.mult)
+    fill(T.vW[:, 128:136], "vW0", 0, 8)
+    fill(T.dW[:, 128:136], "dW0", 8192, 8)
+    ts(p15, "p15", p16, "pf", 14.5, None, A.is_lt)
+    act(pK, "pK", p15, "p15", scale=-float(MID), bias=float(SA - 8192))
+    act(pL, "pL", p15, "p15", scale=-float(MID), bias=float(-SH))
 
     def steps_rows(src, srcn, k, ext=(), aft=None):
-        st, sn, HL, N = T.st[:, 32 * k:32 * k + 32], "st%d" % k, "HL%d" % k, "N%d" % k
+        st, sn, HL, N, t = blk(T.st, k, 32), "st%d" % k, "HL%d" % k, "N%d" % k, 1 - k
+        load("Y", "ln%d" % k, [(T[N][8 + h:9 + h, :], T.CC[0:32, 64 * h + 32 * t:64 * h + 32 * t + 32]) for h in range(2)], "CH CL", N + "c")
         if k:
-            ts(xd, "xd", src, srcn, float(base - NT * owners[6]), None, A.add, ext=ext, aft=aft)
-            src, srcn = xd, "xd"
+            ts(xp, "xp", src, srcn, float(base - NT * owners[6]), None, A.add, ext=ext, aft=aft)
+            src, srcn = xp, "xp"
         tt(T[HL][:, 0:32], HL, src, tI, srcn + " tI", A.subtract)
         tt(st, sn, src, tI, srcn + " tI", A.subtract)
         tt(T[HL][:, 32:64], HL + "b", st, T[HL][:, 0:32], sn + " " + HL, A.subtract)
         for h in range(2):
-            load("Y", "ln%d" % k, [(T[N][4 * h:4 * h + 4, :], T[HL][:, 32 * h:32 * h + 32])], HL + "b" * h, N + "b" * h, LAT1 if k else LAT0)
+            load("Y", "ln%d" % k, [(T[N][4 * h:4 * h + 4, :], blk(T[HL], h, 32))], HL + "b" * h, N + "b" * h)
 
     def windows(t, R, Rn, N, banks, on):
-        c = PWID * t + LO
         for k, (bk, q) in enumerate(zip(banks, on)):
-            h = k % 2
-            if k < 2:
-                mm([((T[bk][:], T.m16[0:8, 0:128], T[N][0:8, 512 * h:512 * h + 512], True, True), 512, 0)], "m16 %s %sb" % (N, N), bk)
-            else:
-                mm([((T[bk][:], T.LP[0:20, :], T[R][0:20, 512 * h:512 * h + 512], True, True), 512, 0)], "LP " + Rn, bk)
-            w, sc = ("ND", 1.0) if k < 2 else ("PW", 64.0)
-            o, nm = T[w][:, c + 512 * h:c + 512 * h + 512], "%s%d%d" % (w, t, h)
+            h, c = k % 2, PWID * t + LO + 512 * (k % 2)
+            w, sc, lhs, rhs, ins = (("ND", 1.0, T.m16[0:10, :], T[N], "m16 %s %sb %sc" % (N, N, N)), ("PW", 64.0, T.LP[0:20, :], T[R], "LP " + Rn))[k // 2]
+            for a in (0, 256):
+                mm([((T[bk][:, a:a + 256], lhs, rhs[0:10 * (1 + k // 2), 512 * h + a:512 * h + a + 256], True, True), 256, 0)], ins, bk)
             if q == "S":
-                act(o, nm, T[bk][:], bk, 512, scale=sc)
+                act(T[w][:, c:c + 512], "%s%d%d" % (w, t, h), T[bk][:], bk, 512, scale=sc)
             else:
-                ts(o, nm, T[bk][:], bk, sc, None, A.mult, n=512)
+                ts(T[w][:, c:c + 512], "%s%d%d" % (w, t, h), T[bk][:], bk, sc, None, A.mult, n=512)
 
-    load("Y", "lr0", [(T.R0[0:16, :], T.H1[:]), (T.R0[16:20, :], Ld)], "H1 Ld", "R0", LAT0)
+    load("Y", "lr0", [(T.R0[0:16, :], T.H1[:]), (T.R0[16:20, :], Ld)], "H1 Ld", "R0")
     steps_rows(T.Zn[:], "Zn", 0)
     windows(1, "R0", "R0", "N0", ("vK", "vP", "o0", "o1"), WON0)
 
@@ -425,225 +446,203 @@ def rank_program(g, core, T, topo):
 
     def slots(oh, ohn, su, sun):
         M, n7, n8 = 24, 168, 192
-        z1, z2 = T.z1, T.z2
         mm([((T.rB[:, n7:n8], T.I16[:], T.cO16[:, 0:M], True, True), M, 0)], "I16 cO16", "rB")
         tt(oh[:], ohn, T.rk[:, 0:32].indirect(oR), T.cQ[:], "rka rkb oR " + CQ, A.is_equal, n8, f=GAT)
         mm([((T.rA[:, 0:n7], T.G2[:], oh[:, 0:n7], True, False), n7, 0), ((T.rA[:, 0:n7:M], ones, T.cD[0:1, 0:7], False, True), 7, 0)],
            "G2 one cD " + ohn, "rA")
-        mm([((T.rB[:, 0:n7], T.U2[:, 128 * h:128 * h + 128], oh[:, 0:n7], h == 0, h == 1), n7, 0) for h in range(2)], "U2 U2b " + ohn, "rB")
+        mm([((T.rB[:, 0:n7], blk(T.U2, h), oh[:, 0:n7], h == 0, h == 1), n7, 0) for h in range(2)], "U2 U2b " + ohn, "rB")
         sc = T.rA[:, 256:256 + n7]
         scan(sc, "sc", T.Rs[:], T.rA[:, 0:n7], "Rs rA", A.mult, A.add, n7)
-        tt(z2[:], "z2", T.rB[:, 0:n8], oh[:, 0:n8], "rB " + ohn, A.mult, n8)
-        tt(z1[:], "z1", sc, oh[:, 0:n7], "sc rA " + ohn, A.mult, n7)
-        mm([((T.rB[:, 0:M], T.I16[:], z2[:, M * b:M * b + M], b == 0, False), M, 0) for b in range(8)], "I16 z2", "rB")
-        mm([((T.rB[:, 0:M], T.I16[:], z1[:, M * b:M * b + M], False, b == 6), M, 0) for b in range(7)], "I16 z1", "rB")
+        tt(T.z2[:], "z2", T.rB[:, 0:n8], oh[:, 0:n8], "rB " + ohn, A.mult, n8)
+        tt(T.z1[:], "z1", sc, oh[:, 0:n7], "sc rA " + ohn, A.mult, n7)
+        mm([((T.rB[:, 0:M], T.I16[:], blk(T.z2, b, M), b == 0, False), M, 0) for b in range(8)], "I16 z2", "rB")
+        mm([((T.rB[:, 0:M], T.I16[:], blk(T.z1, b, M), False, b == 6), M, 0) for b in range(7)], "I16 z1", "rB")
         cp(su, sun, T.rB[:, 0:M], "rB")
 
-    def pack(b, x, xn, tin, bank, W, wn, su, sun):
-        ex, PK, ps = T.ex[:, 128 * b:128 * b + 128], T.PK[:, 128 * b:128 * b + 128], T[bank][:, 256:384]
-        if x is None:
-            scan(ex, "ex%d" % b, T.hk[:, 0:128], T.inj[:, 128 * b:128 * b + 128], "hk inj", A.mult, A.add, 128)
-            mm([((ps, T.I16[:], T.X16[:, 128 * b:128 * b + 128], True, False), 128, 0)], "I16 X16", bank)
-            mm([((ps, T.G3[:], ex, False, True), 128, 0)], "G3 ex%d" % b, bank)
-            act(PK, "PK%d" % b, ps, bank, 128)
-        else:
-            tt(ex, "ex%d" % b, T.ti[:, 8 * b:8 * b + 8].indirect(T.oT[:, 0:8]), m16, tin + " oK m16", A.mult, 128, f=GAT)
-            mm([((ps, T.G3[:], ex, True, True), 128, 0)], "G3 ex%d" % b, bank)
-            tt(PK, "PK%d" % b, ps, x, bank + " " + xn, A.add, 128)
-        cp(W[:].indirect(su), wn, PK, "PK%d %s" % (b, sun), 128, f=SCA)
-
-    def message(W, wn, MB, mn):
-        scan(T.sd[:], "sd", T.sc4[:], W[:, 0:128], "sc40 sc41 sc42 sc43 " + wn, A.add, A.max, 128)
-        ts(MB[:, 0:32], mn, T.sd[:, 3:128:4], "sd pK4", pK4, None, A.add)
+    def pack(banks):
+        ts(T.inj[:, 0:NP:16], "inj", T.ti[:, 0:24], "ti he", he, None, A.mult)
+        for b, bank in enumerate(banks):
+            ps = T[bank][:, 256:384]
+            scan(blk(T.ex, b), "ex%d" % b, T.hk[:, 0:128], blk(T.inj, b), "hk inj", A.mult, A.add, 128)
+            mm([((ps, T.I16[:], blk(T.X16, b), True, False), 128, 0)], "I16 X16", bank)
+            mm([((ps, T.G3[:], blk(T.ex, b), False, True), 128, 0)], "G3 ex%d" % b, bank)
+            act(blk(T.PK, b), "PK%d" % b, ps, bank, 128)
 
     def send(buf, ins, sem, w, src, dst):
         x = [(d, sem, buf[:, src + w * k:src + w * k + w], buf[:, dst + w * k:dst + w * k + w]) for k, d in enumerate(peers)]
         return remote([[(x[0][0], E8[:4]) + x[0][1:], (x[1][0], E8[4:]) + x[1][1:]], [(x[2][0], E8) + x[2][1:]]], ins)
     ARR = 2 * len(E8)
 
-    def step(t, b, X, xn, banks, Lr, Lw, last=False):
-        n = "%s%d" % (t, b)
-        pr, pa, e = [T[x + t][:, 128 * b:128 * b + 128] for x in ("pr", "pa", "e")]
-        u, kk, c, w = T["u" + t], T["k" + t][:, 56 * b:56 * b + 56], (QW + 80) * b, T["w" + t][:, 8 * b:8 * b + 8]
-        bK, bP, bL = banks if len(banks) == 3 else banks * 3
-        pK_, pP, pL = T[bK][:, 0:56], T[bP][:, 64:120], T[bL][:, 128:136] if bL == bK else T[bL][:, 0:8]
-        c0, clo, chi = (0, lo, hi) if t == "V" else (PWID, 0.0, float(HI))
-        PWn, NDn = [" ".join([x + a + h for a in ("01" if t == "V" else "1") for h in "01"] + PZ) for x in ("PW", "ND")]
-        Lin, Lout = [T[x][:, 8 * b:8 * b + 8] if x else None for x in (Lr, Lw)]
-        if X is not None:
-            tt(pr, "pr" + n, T.PW[:, c0:].indirect(w), X, "%s w%s %s" % (PWn, n, xn), A.mult, 128, f=GAT)
-        else:
-            act(e, "e" + n, T.PW[:, c0:].indirect(w), "%s w%s" % (PWn, n), 128, f=GAT)
-            tt(pr, "pr" + n, e, T[bK][:, 384:512], "e%s %s" % (n, bK), A.mult, 128)
+    def turn(t, b, out, rhs, bank, stop):
+        n, c, e = "%s%d" % (t, b), (QW + 80) * b, blk(T["e" + t], b)
+        scan(e, "e" + n, T["q" + t][:, c + 80:c + 80 + QW:GW], T.hk[:, 128:256], "hk2 q" + n, A.add, A.mult, 128)
+        mm([((out, e, rhs, True, stop), 8, 1)], "Ms e" + n, bank)
+
+    def step(t, b, s, X, xn, bK, bP):
+        n, c = "%s%d" % (t, b), (QW + 80) * b
+        pr, pa, kk, w, u = blk(T["pr" + t], b), blk(T["pa" + t], b), blk(T["k" + t], b, 56), blk(T["w" + t], b, 8), T["u" + t]
+        pK_, pP, c0 = T[bK][:, 0:56], T[bP][:, 64:120], 0 if t == "V" else PWID
+        PWn, NDn = [" ".join(x + a + h for a in ("01" if t == "V" else "1") for h in "01") + PZ[x] for x in ("PW", "ND")]
+        tt(pr, "pr" + n, T.PW[:, c0:].indirect(w), X, "%s w%s %s" % (PWn, n, xn), A.mult, 128, f=GAT)
         act(pa, "pa" + n, T.ND[:, c0:].indirect(w), "%s w%s" % (NDn, n), 128, f=GAT)
-        first = mm([((pK_, pr, T.S1[:], True, True), 56, 1)], "S1 pr" + n, bK)
-        second = mm([((pP, pa, T.sA[:, 64:120], True, True), 56, 0)], "S2 pa" + n, bP)
-        il = lambda: mm([((pL, T.If[:], Lin, True, False), 8, 1)], "If %s%d" % (Lr, b), bL)
-        if bL != bK:
-            tasks[second]["odeps"].add(first)
-            tasks[il()]["odeps"].add(second)
-        scan(u[:, 64 * b + 1:64 * b + 57], "u" + n, pK_, T.R1c[:, 0:56], "R1c " + bK, A.min, A.max)
+        if s:
+            turn(t, b, pP, T.Ms[:], bP, False)
+        mm([((pP, pa, S2 if s else S2a, not s, True), 56, 0)], "S2 S2a pa" + n, bP)
+        mm([((pK_, pr, T.S1[:], True, True), 56, 1)], "S1 pr" + n, bK)
+        scan(u[:, 64 * b + 1:64 * b + 57], "u" + n, pK_, T.R1c[:], "R1c " + bK, A.min, A.max)
         tt(kk, "k" + n, pK_, u[:, 64 * b:64 * b + 56], "%s u%s u0%s" % (bK, n, n), A.is_ge)
         scan(T["q" + t][:, c:c + QW:16], "q" + n, pP, kk, "%s k%s" % (bP, n), A.add, A.mult)
-        if bL == bK and IL:
-            il()
-        scan(e, "e" + n, T.hk[:, 0:128], T["q" + t][:, c + 80:c + 80 + QW:GW], "hk q" + n, A.mult, A.add, 128)
-        mm([((pL, e, T.Ms[:], bL == bK and not IL, True), 8, 1)], "Ms e" + n, bL)
-        if bL == bK and not IL:
-            tt(Lout, "%s%d" % (Lw, b), pL, Lin, "%s %s%d" % (bL, Lr, b), A.add)
-            if not last:
-                ts(w, "w" + n, Lout, "%s%d" % (Lw, b), clo, chi, A.max, A.min)
-            return
-        if not last:
-            ts(w, "w" + n, pL, bL + " lo hi", clo, chi, A.max, A.min)
-        if not last or t != "V":
-            act(Lout, "%s%d" % (Lw, b), pL, bL)
+        places = T["q" + t][:, c + 80:c + QW:16 * GW]
+        if s < 2 and t == "V":
+            ts(w, "w" + n, places, "lo hi q" + n, lo, hi, A.max, A.min)
+        elif s < 2:
+            ts(w, "w" + n, places, "q" + n, -float(PWID), float(HI), A.add, A.min)
 
-    ts(T.rk[:, 16:32], "rka", T.L0[:, 0:16], "L0", 10, None, A.arith_shift_right)
-    ts(T.rk[:, 0:16], "rkb", T.L0[:, 8:24], "L0", 10, None, A.arith_shift_right)
-    slots(T.oh1, "oh1", su1, "su1")
-    if DELAY:
-        tasks[sC]["deps"].add(wr["su1"])
-    ts(T.ti[:, 0:24], "ti", T.L0[:], "L0", 1023, None, A.bitwise_and)
-    ts(T.inj[:, 0:NP:16], "inj", T.ti[:, 0:24], "ti he", he, None, A.mult)
-    for b, bank in enumerate(("vL", "o2", "vL")):
-        pack(b, None, "X", "ti", bank, T.W1, "W1", T.su[:, 8 * b:8 * b + 8], "su1")
-    message(T.W1, "W1", T.MB1, "msg1")
-    s1 = send(T.MB1, "msg1", "rq1", 8, 0, 32)
-
-    act(T.xB[:], "xB", T.W1[:, 0:128], "W1 xm m3", 128, F.Identity, scale=xm, bias=m3)
-
-    def arrive(MB, mn, sem, sent, fly):
-        mm([((T.vL[:, 0:8], T.I16[:], T.cO16[:, 32:40], True, False), 8, 0)], "I16 off", "vL")
-        a = mm([((T.vP[:, f:128:4], T.EX[:, 128 * f:128 * f + 128], MB[:, 24:56], True, True), 32, 0) for f in range(4)],
-               "EX0 EX1 EX2 EX3 " + mn, "vP", [(sem, ARR)], (sent, fly))
-        b = mm([((T.vL[:, 0:8], T.LI[:, 12 - 4 * c:140 - 4 * c], MB[:, 24 + c:56:4], False, c == 3), 8, 0) for c in range(4)],
-               "LI " + mn, "vL", [(sem, ARR)], (sent, fly))
-        tasks[b]["odeps"].add(a)
-        act(T.Xv[:], "Xv", T.vP[:, 0:128], "vP xm m3", 128, F.Identity, scale=xm, bias=m3)
-        ts(T.wV[:], "wV0", T.vL[:, 0:8], "vL lo hi", lo, hi, A.max, A.min)
-        act(T.Lv0[:], "Lv00", T.vL[:, 0:8], "vL")
-
-    arrive(T.MB1, "msg1", "rq1", s1, FLY[0])
-    steps_rows(T.NP[:], "NP", 1, [("tC", len(E8))], (sC, FLY_T[0]))
-    load(RQ, "lr1", [(T.R1[16:20, :], T.A2[:])], "", "R1b", LAT1, [("tB", len(E8))], (sB, FLY_T[2]))
-    load(RQ, "lr1", [(T.R1[0:16, :], T.A1[:])], "", "R1", LAT1, [("tA", len(E8))], (sA, FLY_T[1]))
-    windows(0, "R1", "R1 R1b", "N1", WB, WON)
-
-    LO3 = "Lo0 Lo1 Lo2"
-    ts(T.Lm[:], "Lm0", T.L0[:], "L0", float(-SH) - DEAD, None, A.add)
-    tt(T.Lm[:], "Lm0", T.Lm[:], T.oh1[:, 168:192], "Lm0 oh1", A.mult)
-    vop(lambda: V.tensor_scalar(T.Lo[:], T.Lm[:], DEAD, None, A.add), ["Lm0"], LO3.split())
-    vop(lambda: V.tensor_scalar(T.wO[:], T.Lo[:], 0.0, float(HI), A.max, A.min), LO3.split(), ["wO0", "wO1", "wO2"])
-
-    def own(s):
-        if MERGE:
-            Lr, Lw = "Lm" if s == 3 else "Lo", "Lm" if s == 2 else "Lo"
-            all3 = lambda x: " ".join(x + str(b) for b in range(3))
-            PWn, NDn = [" ".join([x + "10", x + "11"] + PZ) for x in ("PW", "ND")]
-            for a, z in PARTS:
-                add("V", lambda a=a, z=z: [V.tensor_tensor(T.prO[:, 128 * a:128 * z], T.PW[:, PWID:].indirect(T.wO[:, 8 * a:8 * z]), T.X[:, 128 * a:128 * z], A.mult)],
-                    (PWn + " wO0 X").split(), ["prO%d" % b for b in range(a, z)], 0.05 + cy * GAT * 128 * (z - a))
-                add("S", lambda a=a, z=z: [S.activation(T.paO[:, 128 * a:128 * z], T.ND[:, PWID:].indirect(T.wO[:, 8 * a:8 * z]), F.Copy)],
-                    (NDn + " wO0").split(), ["paO%d" % b for b in range(a, z)], 0.065 + cy * GAT * 128 * (z - a))
-            for b in range(3):
-                mm([((T.o0[:, 56 * b:56 * b + 56], T.prO[:, 128 * b:128 * b + 128], T.S1[:], True, True), 56, 1)], "S1 prO%d" % b, "o0")
-            for b in range(3):
-                mm([((T.o1[:, 56 * b:56 * b + 56], T.paO[:, 128 * b:128 * b + 128], T.sA[:, 64:120], True, True), 56, 0)], "S2 paO%d" % b, "o1")
-            mm([((T.o2[:, 0:24], T.If[:], T[Lr][:], True, False), 24, 1)], "If " + all3(Lr), "o2")
-            scan(T.uO[:, 1:169], "uO0", T.o0[:, 0:168], T.R1c[:], "R1c o0", A.min, A.max, 168)
-            tt(T.kO[:], "kO0", T.o0[:, 0:168], T.uO[:, 0:168], "o0 uO0 u0O0", A.is_ge, 168)
-            scan(T.qO[:, 0:3 * QW:16], "qO0", T.o1[:, 0:168], T.kO[:], "o1 kO0 qO1 qO2", A.add, A.mult, 168)
-            for a, z in PARTS:
-                add("V", lambda a=a, z=z: [V.tensor_tensor_scan(T.eO[:, 128 * a:128 * z], T.hk[:, 0:128 * (z - a)], T.qO[:, 80 + QW * a:80 + QW * z:GW], 0.0, A.mult, A.add)],
-                    ["hk", "hkb", "qO0"], ["eO%d" % b for b in range(a, z)], cy * (FIX + 128 * (z - a)))
-            for b in range(3):
-                mm([((T.o2[:, 8 * b:8 * b + 8], T.eO[:, 128 * b:128 * b + 128], T.Ms[:], False, b == 2), 8, 1)], "Ms eO%d" % b, "o2")
-            if s < 5:
-                ts(T.wO[:], "wO0", T.o2[:, 0:24], "o2", 0.0, float(HI), A.max, A.min, 24)
-            add("S", lambda: [S.activation(T[Lw][:], T.o2[:, 0:24], F.Copy)], ["o2"], all3(Lw).split(), cy * 90)
-            return
-        for b in range(3):
-            step("O", b, None if s in SG else T.X16[:, 128 * b:128 * b + 128], "X16", ("o%d" % b,), "Lm" if s == 3 else "Lo", "Lm" if s == 2 else "Lo", s == 5)
-    for b in range(3):
-        mm([((T["o%d" % b][:, 384:512], T.I16[:], T.X16[:, 128 * b:128 * b + 128], True, True), 128, 0)], "I16 X16", "o%d" % b)
-    for s in range(3):
-        own(s)
-
-    RKC = (SH - 511.1875) / 1024.0
-    ts(T.rk[:, 16:32], "rka", T.Lm[:, 0:16], "Lm0 Lm1", 1.0 / 1024, RKC, A.mult, A.add)
-    ts(T.rk[:, 0:16], "rkb", T.Lm[:, 8:24], "Lm1 Lm2", 1.0 / 1024, RKC, A.mult, A.add)
-    ts(T.ci[:, 0:24], "ci", T.Lm[:], "Lm0 Lm1 Lm2", float(SH), None, A.add)
-    ts(T.ti[:, 0:24], "ti", T.ci[:, 0:24], "ci", 1023, None, A.bitwise_and)
-    slots(T.ohA, "ohA", suA, "suA")
-    ts(T.inj[:, 0:NP:16], "inj", T.ti[:, 0:24], "ti he", he, None, A.mult)
-    for b in range(3):
-        pack(b, None, "X", "ti", "o%d" % b, T.W2, "W2", T.su[:, 24 + 8 * b:32 + 8 * b], "suA")
-    for s in range(3, 6):
-        own(s)
-
-    def visitors(RP, outn, sub, subn):
+    def own(out, c, on, bias):
         for s in range(3):
-            step("V", 0, T.Xv[:], "Xv", ("vK", "vP", "vL"), "Lv" if s else "Lv0", "Lv", s == 2)
-        tt(RP[:, 8:16], outn, T.vL[:, 0:8], sub, "vL " + subn, A.subtract)
+            for b in range(3):
+                step("O", b, s, blk(T.XT if s == 1 else T.X16, b), "XT" if s == 1 else "X16", "o%d" % b, "o%d" % b)
+        for b in range(3):
+            bk = "o%d" % b
+            turn("O", b, T[bk][:, 128:136], T.Ms[:, 5:56:GW], bk, True)
+            act(blk(out, b + c, 8), on + str(b), T[bk][:, 128:136], bk + " pK", fn=F.Identity, bias=bias)
+
+    def arrive(MB, mn, sem, sent):
+        mm([((T.vL[:, 0:8], T.I16[:], T.cO16[:, 32:40], True, False), 8, 0)], "I16 off", "vL")
+        a = mm([((T.vP[:, 128 + f:256:4], blk(T.EX, f), MB[:, 24:56], True, True), 32, 0) for f in range(4)],
+               "EX0 EX1 EX2 EX3 " + mn, "vP", [(sem, ARR)], (sent, FLY))
+        b = mm([((T.vL[:, 0:8], T.LI[:, 12 - 4 * c:140 - 4 * c], MB[:, 24 + c:56:4], False, c == 3), 8, 0) for c in range(4)],
+               "LI " + mn, "vL", [(sem, ARR)], (sent, FLY))
+        tasks[b]["odeps"].add(a)
+        act(T.Xv[:], "Xv", T.vP[:, 128:256], "vP xm m3", 128, F.Identity, scale=xm, bias=m3)
+        ts(T.wV[:], "wV0", T.vL[:, 0:8], "vL lo hi", lo, hi, A.max, A.min)
+
+    def visitors():
+        act(T.Zr[:], "Zr", T.Xv[:].indirect(T.oT[:, 48:56]), "Xv rot", 128, f=GAT)
+        for h in range(0, 8, 2):
+            mm([((T.vL[:, 128 + 16 * d:144 + 16 * d], T.I2[:, 128 - 16 * d:256 - 16 * d], blk(T.Zr, d, 16), True, True), 16, 0) for d in (h, h + 1)],
+               "I2 I2b Zr", "vL")
+        act(T.Ur[:], "Ur", T.vL[:, 128:256], "vL", 128)
+        act(T.Xw[:], "Xw", T.Ur[:].indirect(T.oT[:, 56:64]), "Ur rot", 128, f=GAT)
+        for s in range(3):
+            step("V", 0, s, (T.Xw if s == 1 else T.Xv)[:], "Xw" if s == 1 else "Xv", "vK", "vP")
+        turn("V", 0, T.vL[:, 0:8], T.Ms[:, 5:56:GW], "vL", True)
+
+    ts(T.rk[:, 16:32], "rka", T.L0[:, 0:16], "L0", 10, None, sh)
+    ts(T.rk[:, 0:16], "rkb", T.L0[:, 8:24], "L0", 10, None, sh)
+    slots(T.oh1, "oh1", su1, "su1")
+    ts(T.ti[:, 0:24], "ti", T.L0[:], "L0", 1023, None, an)
+    pack(("vL", "o2", "vL"))
+    for b in range(3):
+        cp(T.W1[:].indirect(blk(T.su, b, 8)), "W1", blk(T.PK, b), "PK%d su1" % b, 128, f=SCA)
+    scan(T.sd[:], "sd", T.sc4[:], T.W1[:, 0:128], SC4 + "W1", A.add, A.max, 128)
+    ts(T.MB1[:, 0:32], "msg1", T.sd[:, 3:128:4], "sd pK4", pK4, None, A.add)
+    s1 = send(T.MB1, "msg1 RP1p", "rq1", 8, 0, 32)
+    act(m34, "m34", m3, "m3 pK4", fn=F.Identity, bias=pK4)
+    act(T.xB[:], "xB", T.W1[:, 0:128], "W1 xm m34", 128, F.Identity, scale=xm, bias=m34)
+    act(T.W3[:, 0:128], "W3", T.bc[:], "one pK4", 128, F.Identity, scale=float(NONE), bias=pK4)
+
+    load("Y", "ldT", [(T.Yt[0:72, 16 * a:16 * a + 16], T.pts[3 * a:3 * a + 3, :]) for a in range(8)], "HL0b", "Yt")
+    act(T.Zr[0:72, :], "Zr", T.Yt[0:72, :], "Yt", 128)
+    for b in range(3):
+        select(blk(T.Xp, b), "Xp%d" % b, [[-1, 8], [0, 4], [-24, 4]], -8 * b)
+        mm([((blk(T.rA, b), T.Xp[0:72, 128 * b:128 * b + 128], T.Zr[0:72, :], True, True), 128, 0)], "Zr Xp%d" % b, "rA")
+    act(T.XT[:], "XT", T.rA[:, 0:NP], "rA m3", NP, F.Identity, bias=m3)
+
+    arrive(T.MB1, "msg1", "rq1", s1)
+    act(T.Lv0[:], "Lv0", T.vL[:, 0:8], "vL")
+    steps_rows(T.NP[:], "NP", 1, [("tC", len(E8))], (sC, FLY_T[0]))
+    load("Y", "lr1", [(T.R1[16:20, :], T.A2[:])], "", "R1b", LAT, [("tB", len(E8))], (sB, FLY_T[2]))
+    load("Y", "lr1", [(T.R1[0:16, :], T.A1[:])], "", "R1", LAT, [("tA", len(E8))], (sA, FLY_T[1]))
+    windows(0, "R1", "R1 R1b", "N1", WB, WON)
+    act(T.I1k[:], "I1k", T.I16[:], "I16", 128, scale=1024.0)
+    mm([((T.rA[:, 128:256], T.I16[:], x, k == 0, k == 3), 128, 0) for k, x in enumerate((T.G2[:], blk(T.U2, 0), blk(T.U2, 1), T.I1k[:]))],
+       "I16 G2 U2 U2b I1k", "rA")
+    act(T.LW[:], "LW", T.rA[:, 128:256], "rA", 128)
+    act(T.tb[:, 0:128], "tb0", m16, "m16", 128, scale=-float(BIG))
+    act(T.tb[:, 128:256], "tb1", m16, "m16", 128, scale=float(MID))
+    mm([((T.rA[:, 0:128], T.Ib[:], T.tb[:, 0:128], True, False), 128, 0), ((T.rA[:, 1:128], T.Ib[:], T.tb[:, 128:255], False, True), 128, 0)],
+       "Ib tb0 tb1", "rA")
+    act(T.scC[:, 0:128], "scC", T.rA[:, 0:128], "rA", 128)
+    act(T.scC[:, 128:192], "scCb", T.scC[:, 0:64], "scC")
+
+    ts(T.wO[:], "wO0 wO1 wO2", T.L0[:], "L0", float(-SH), float(HI), A.add, A.min)
+    own(T.Lm, 0, "Lm", float(SA))
+    ts(T.rk[:, 16:32], "rka", T.Lm[:, 0:16], "Lm0 Lm1", -511.75, 1.0 / 1024, A.add, A.mult)
+    ts(T.rk[:, 0:16], "rkb", T.Lm[:, 8:24], "Lm1 Lm2", -511.75, 1.0 / 1024, A.add, A.mult)
+    cp(T.ci[:, 0:24], "ci", T.Lm[:], "Lm0 Lm1 Lm2")
+    ts(T.ti[:, 0:24], "ti", T.ci[:, 0:24], "ci", 1023, None, an)
+    slots(T.ohA, "ohA", suA, "suA")
+    pack(("o0", "o1", "o2"))
+    for a, z in CUT:
+        cp(T.W2[:].indirect(T.su[:, 24 + a:24 + z]), "W2", T.PK[:, 16 * a:16 * z], "PK0 PK1 PK2 suA", 16 * (z - a), f=SCA)
+    scan(T.mA[:, 0:128], "sdA", T.sc4[:], T.W2[:, 0:128], SC4 + "W2", A.add, A.max, 128)
+    act(T.mA[:, 128:160], "mA", T.mA[:, 3:128:4], "sdA pK4", fn=F.Identity, bias=pK4)
 
     Cn = T.sm[:, 64:72]
-    ts(Cn, "Cn", T.Lv0[:], "Lv00", 3000.0, None, A.is_gt)
+    ts(Cn, "Cn", T.Lv0[:], "Lv0", 3000.0, None, A.is_gt)
     tt(Cn, "Cn", Cn, T.cS[:], "Cn cS0 cS1 cS2 cS3", A.mult)
     act(Cn, "Cn", Cn, "Cn cv", fn=F.Identity, bias=cv)
-    visitors(T.RP1, "out1", Cn, "Cn")
+    visitors()
+    tt(T.RP1[:, 8:16], "out1", T.vL[:, 0:8], Cn, "vL Cn", A.subtract)
     s2 = send(T.RP1, "out1", "rp1", 2, 10, 2)
 
     mm([((T.vP[:, 0:64], ones, T.cD[0:1, 8:72], True, False), 64, 0)], "one cB", "vP")
-    back = dict(ext=[("rp1", ARR)], aft=(s2, FLY[1]))
-    ts(T.rkB[:], "rkB", T.RP1[:, 2:10], "out1", 10, None, A.arith_shift_right, **back)
-    ts(T.ti[:, 24:32], "tiB", T.RP1[:, 2:10], "out1", 1023, None, A.bitwise_and, **back)
-    ts(T.Lb[:], "Lb0", T.RP1[:, 2:10], "out1", float(-SH), None, A.add, **back)
+    back = dict(ext=[("rp1", ARR)], aft=(s2, FLY))
+    ts(T.rkB[:], "rkB", T.RP1[:, 2:10], "out1", 10, None, sh, **back)
+    ts(T.ti[:, 24:32], "tiB", T.RP1[:, 2:10], "out1", 1023, None, an, **back)
     tt(T.ohB[:], "ohB", T.rkB[:].indirect(oB8), T.zz[:, 0:64], "rkB oB8 cQc", A.is_equal, 64, f=GAT)
     mm([((T.vP[:, 8 * d:64], T.G2[:] if d else T.LW[:], T.ohB[:, 0:64 - 8 * d], False, d == 7), 64, 0) for d in range(8)], "G2 LW ohB", "vP")
     scan(T.zz[:, 128:192], "zz", T.zz[:, 64:128], T.vP[:, 0:64], "RsM vP", A.add, A.max)
     ts(suB, "suB", T.zz[:, 135:192:8], "zz", -1.0, 1056.0, A.mult, A.add)
-    pack(3, T.xB[:], "xB", "tiB", "vL", T.W2, "W2", suB, "suB")
-    message(T.W2, "W2", T.MB2, "msg2")
+    tt(blk(T.ex, 3), "ex3", T.ti[:, 24:32].indirect(T.oT[:, 0:8]), m16, "tiB oK m16", A.mult, 128, f=GAT)
+    mm([((T.vL[:, 256:384], T.G3[:], blk(T.ex, 3), True, True), 128, 0)], "G3 ex3", "vL")
+    tt(blk(T.PK, 3), "PK3", T.vL[:, 256:384], T.xB[:], "vL xB", A.add, 128)
+    cp(T.W3[:].indirect(suB), "W3", blk(T.PK, 3), "PK3 suB", 128, f=SCA)
+    scan(T.sd[:], "sd", T.sc4[:], T.W3[:, 0:128], SC4 + "W3", A.add, A.max, 128)
+    tt(T.MB2[:, 0:32], "msg2", T.sd[:, 3:128:4], T.mA[:, 128:160], "sd mA", A.min)
     s3 = send(T.MB2, "msg2 RP2p", "rq2", 8, 0, 32)
 
-    ts(T.wR[:], "wR0", T.Lb[:], "Lb0", 0.0, float(HI), A.max, A.min)
-    act(T.rA[:, 384:512], "rA", T.xB[:], "xB", 128)
-    for s in range(3):
-        step("R", 0, None if RSG else T.xB[:], "xB", ("rA",), "Lr" if s else "Lb", "Lr", s == 2)
-    arrive(T.MB2, "msg2", "rq2", s3, FLY[2])
-    visitors(T.RP2, "out2", T.Lv0[:], "Lv00")
+    arrive(T.MB2, "msg2", "rq2", s3)
+    visitors()
+    ts(T.RP2[:, 8:16], "out2", T.vL[:, 0:8], "vL cv", cv, None, A.subtract)
     s4 = send(T.RP2, "out2", "rp2", 2, 10, 2)
 
-    smA, smB, vB, Yb = T.sm[:, 0:24], T.sm[:, 24:32], T.sm[:, 32:40], T.sm[:, 40:64]
+    smA, vB, Yb = T.sm[:, 0:24], T.sm[:, 32:40], T.sm[:, 40:64]
     ts(s1c, "s1c", su1, "su1", 128.0, None, A.min)
     ts(smA, "smA", suA, "suA", 128.0, None, A.min)
-    ts(smB, "smB", suB, "suB", 128.0, None, A.min)
-    act(vB, "vB", T.Lr[:], "Lr0", scale=256.0, bias=256.0 * SH)
-    tt(vB, "vB", vB, smB, "vB smB", A.add)
-    tt(T.exv[:], "exv", vB.indirect(T.oT[:, 0:8]), m16, "vB oK m16", A.mult, 128, f=GAT)
+
+    def to_points():
+        for b in range(3):
+            act(blk(T.gv, b), "gv%d" % b, T.vW[:].indirect(T.su[:, 64 + 8 * b:72 + 8 * b]), "vW vW0 s1c", 128, f=GAT)
+            scan(blk(T.sv, b), "sv%d" % b, T.scC[:, 0:128], blk(T.gv, b), "scC gv%d" % b, A.add, A.max, 128)
+    tt(T.exv[:], "exv", T.RP1[:, 0:10].indirect(T.oT[:, 2:10]), m16, "oK out1 RP1p m16", A.mult, 128, f=GAT, **back)
     mm([((T.rB[:, 0:128], T.Gf[:], T.exv[:], True, True), 128, 1)], "Gf exv", "rB")
     act(T.vW[:, 0:128], "vW", T.rB[:, 0:128], "rB", 128)
+    to_points()
+    tt(T.vO[:], "vO", T.Lm[:], T.oh1[:, 168:192], "Lm0 Lm1 Lm2 oh1", A.mult)
+    act(T.vO[:], "vO", T.vO[:], "vO pL", fn=F.Identity, bias=pL)
     for b in range(3):
-        act(T.gv[:, 128 * b:128 * b + 128], "gv%d" % b, T.vW[:].indirect(T.su[:, 64 + 8 * b:72 + 8 * b]), "vW vW0 s1c", 128, f=GAT)
-        scan(T.sv[:, 128 * b:128 * b + 128], "sv%d" % b, T.scC[:, 0:128], T.gv[:, 128 * b:128 * b + 128], "scC gv%d" % b, A.add, A.max, 128)
-    act(T.vO[:], "vO", T.Lo[:], LO3, scale=256.0, bias=256.0 * SH)
-    tt(T.vO[:], "vO", T.vO[:], smA, "vO smA", A.add)
-    tt(T.vO[:], "vO", T.vO[:], T.oh1[:, 168:192], "vO oh1", A.mult)
-    tt(T.vt[:], "vt", T.vO[:], T.sv[:, 15:NP:16], "vO sv0 sv1 sv2", A.add)
-    ts(T.ci[:, 0:24], "ci", T.vt[:], "vt", 255, None, A.bitwise_and)
-    cp(T.tau[:], "tau", T.ci[:, 0:24], "ci")
-    ts(T.vt[:], "vt", T.vt[:], "vt", 8, None, A.arith_shift_right)
-    ts(Yb, "Yb", T.vt[:], "vt pK", -8192.0, pK, A.add, A.add)
+        tt(blk(T.Lm, b, 8), "Lm%d" % b, blk(T.vO, b, 8), T.sv[:, 128 * b + 15:128 * b + 128:16], "vO sv%d" % b, A.add)
+        ts(blk(T.wO, b, 8), "wO%d" % b, blk(T.Lm, b, 8), "Lm%d" % b, float(HI), None, A.min)
+    ts(vB, "vB", T.zz[:, 135:192:8], "zz", -928.0, 0.0, A.add, A.max)
+    tt(blk(T.ex, 0), "ex0", vB.indirect(T.oT[:, 0:8]), m16, "vB oK m16", A.mult, 128, f=GAT)
+    mm([((T.rB[:, 0:128], T.G2[:], blk(T.ex, 0), True, True), 128, 0)], "G2 ex0", "rB")
+    act(T.vW[:, 0:128], "vW", T.rB[:, 0:128], "rB", 128, scale=-0.5, bias=128.0)
+    to_points()
+    tt(smA, "smA", smA, T.oh1[:, 168:192], "smA oh1", A.mult)
+    tt(smA, "smA", smA, T.sv[:, 15:NP:16], "smA sv0 sv1 sv2", A.add)
+    ts(T.tau[:], "tau", smA, "smA pL", pL, float(SH), A.add, A.add)
+    own(T.sm, 5, "Yb", pK)
 
-    tt(T.exv[:], "exv", T.RP2[:, 0:10].indirect(T.oT[:, 2:10]), m16, "oK out2 RP2p m16", A.mult, 128, [("rp2", ARR)], (s4, FLY[3]), GAT)
+    tt(T.exv[:], "exv", T.RP2[:, 0:10].indirect(T.oT[:, 2:10]), m16, "oK out2 RP2p m16", A.mult, 128, [("rp2", ARR)], (s4, FLY), GAT)
     mm([((T.rB[:, 0:128], T.Gf[:], T.exv[:], True, True), 128, 1)], "Gf exv", "rB")
-    ts(T.dW[:, 0:128], "dW", T.rB[:, 0:128], "rB", 8192.0, None, A.add, n=128)
-    add("S", lambda: [S.activation(T.gv[:, 192:NP], T.dW[:].indirect(T.tau[:, 12:24]), F.Copy)], ["dW", "dW0", "tau", "gv1"], ["gv2"], 0.36)
-    add("V", lambda: [V.tensor_copy(T.gv[:, 0:192], T.dW[:].indirect(T.tau[:, 0:12]))], ["dW", "dW0", "tau", "vt"], ["gv0", "gvx"], 0.35)
-    add("V", lambda: [V.tensor_tensor_scan(T.sv[:, 0:192], T.scC[:], T.gv[:, 0:192], 0.0, A.add, A.max)], ["scC", "scCb", "gv0"], ["sv0", "sv1"], cy * 192)
-    add("V", lambda: [V.tensor_tensor_scan(T.sv[:, 192:NP], T.scC[:], T.gv[:, 192:NP], 0.0, A.add, A.max)], ["scC", "scCb", "gv2"], ["sv2"], cy * 192)
-    tt(T.vO[:], "vO", T.sv[:, 15:NP:16], Yb, "sv0 sv2 Yb", A.add)
+    ts(T.dW[:, 0:128], "dW", T.rB[:, 0:128], "rB", 8192.0 - DEAD - SA, None, A.add, n=128)
+    act(T.gv[:, 192:NP], "gv2", T.dW[:].indirect(T.tau[:, 12:24]), "dW dW0 tau", 192, f=GAT)
+    cp(T.gv[:, 0:192], "gv0", T.dW[:].indirect(T.tau[:, 0:12]), "dW dW0 tau", 192, f=GAT)
+    scan(T.sv[:, 0:192], "sv0 sv1", T.scC[:], T.gv[:, 0:192], "scC scCb gv0", A.add, A.max, 192)
+    scan(T.sv[:, 192:NP], "sv2", T.scC[:], T.gv[:, 192:NP], "scC scCb gv2", A.add, A.max, 192)
+    tt(T.vO[:], "vO", T.sv[:, 15:NP:16], Yb, "sv0 sv2 Yb0 Yb1 Yb2", A.add)
     load("Y", "st", [(T.y[:], T.vO[:])], "vO", "", 0.0)
 
     order = plan(tasks)

@@ -1,49 +1,57 @@
+import math
 from concourse.bass import DstId, RemoteDMATransfer
 from concourse.mybir import AluOpType as A, ActivationFunctionType as F
 
 NT, NP, NK = 1024, 384, 24
 LO, HI, PWID = 8, 1032, 1040
 DEAD = PWID + HI - 0.5
-BIG, MID, K4 = 8388608, 4194304, 8192
+BIG, MID, K4 = 8388608, 6291456, 8192
 NONE = 4096
 HOLD = 2.0 ** 50
-GW, QW = 7, 896
+BW = 26
+OFS, RND = 2048, 12582912.0
+GW, SW = 11, 88
+Q0, QB = 160, 1568
+KV, TOP = 16384.0, 2.0 ** 40
 
 _f, _h, _b, _i, _u = "float32", "float16", "bfloat16", "int32", "uint16"
 _sb = {
     "X": (NP, _i), "X16": (NP, _h), "XT": (NP, _h), "Yt": (128, _i), "Xp": (NP, _h), "L0": (NK, _i),
-    "PW": (2 * PWID, _f), "ND": (2 * PWID, _b), "Xv": (128, _f), "Xw": (128, _f), "xB": (128, _f), "Zr": (128, _h), "Ur": (128, _f),
+    "PW": (2 * PWID, _i), "ND": (2 * PWID, _b), "Xv": (128, _f), "Xw": (128, _f), "xB": (128, _h), "Zr": (128, _h), "Ur": (128, _f),
     "Zp": (128, _i), "Zd": (32, _i), "Zn": (32, _i), "H1": (128, _h), "Ld": (64, _h), "NU": (32, _u), "NP": (32, _u), "st": (160, _f),
-    "HL0": (64, _b), "HL1": (64, _b), "CC": (128, _b), "R0": (NT, _h), "R1": (NT, _h), "N0": (NT, _b), "N1": (NT, _b), "LP": (128, _h),
-    "pi": (4, _i), "pj": (12, _i), "pf": (48, _f), "jm": (128, _b), "mk": (128, _b), "md16": (128, _b), "m16": (128, _b), "bc": (128, _b),
+    "HL0": (64, _b), "HL1": (64, _b), "CC": (128, _b), "R1": (NT, _h), "N0": (NT, _b), "N1": (NT, _b), "LP": (128, _h),
+    "pi": (4, _i), "pj": (12, _i), "pf": (48, _f), "jm": (128, _b), "mk": (128, _b), "md16": (128, _b), "m16": (128, _b), "bc": (192, _b), "xq": (256, _b),
     "G2": (128, _h), "G3": (128, _h), "Gf": (128, _f), "Ib": (128, _b), "U2": (256, _h), "I16": (128, _h), "I2": (256, _h), "I1k": (128, _h),
-    "LW": (128, _h), "EX": (512, _h), "cL": (144, _b), "LI": (144, _h), "S1": (56, _f), "sA": (192, _b), "Ms": (56, _f), "hk": (256, _f),
-    "R1c": (56, _f), "scC": (192, _f), "sc4": (128, _f), "tb": (256, _b), "oKi": (32, _i), "oRi": (12, _f), "oT": (64, _u),
-    "Rs": (168, _f), "cQ": (192, _f), "cD": (72, _b), "cOw": (NK, _f), "cO16": (40, _h), "cS": (8, _f),
-    "rk": (32, _i), "ci": (32, _i), "ti": (32, _i), "rkB": (8, _i), "oh1": (192, _h), "ohA": (192, _h), "ohB": (64, _h), "inj": (NP, _f),
-    "ex": (512, _h), "zz": (192, _f), "mA": (160, _f), "z1": (168, _h), "z2": (192, _h), "PK": (512, _f), "su": (96, _u),
-    "W1": (640, _f), "W2": (640, _f), "W3": (416, _f), "sd": (128, _f), "MB1": (56, _h), "MB2": (56, _h), "RP1": (16, _i), "RP2": (16, _f),
+    "Ip": (128, _f), "EX": (512, _h), "cL": (144, _b), "LI": (144, _h), "S1": (44, _f), "sA": (336, _b), "Ms": (56, _f), "hk": (256, _f),
+    "R1c": (SW, _f), "pt": (2 * SW, _b), "scC": (192, _f), "sc4": (128, _f), "tb": (256, _b), "oKi": (32, _i), "oRi": (32, _f), "oT": (72, _u),
+    "Rs": (8 * BW, _f), "cQ": (8 * BW, _f), "cD": (72, _b), "cOw": (BW, _f), "cO16": (40, _h), "cS": (8, _f),
+    "rk": (32, _i), "ci": (32, _i), "ti": (32, _i), "rkB": (8, _i), "oh1": (8 * BW, _h), "ohA": (8 * BW, _h), "ohB": (64, _h), "inj": (NP, _f),
+    "ex": (512, _h), "zz": (192, _f), "z2": (8 * BW, _h), "PK": (512, _f), "su": (96, _u), "cj": (48, _i),
+    "W1": (640, _f), "W2": (640, _f), "sd": (128, _f), "MB1": (56, _h), "MB2": (56, _h), "RP1": (16, _i), "RP2": (32, _u), "RF": (32, _f),
     "Lm": (NK, _f), "wO": (NK, _u), "Lv0": (8, _f), "wV": (8, _u), "sm": (80, _f), "exv": (128, _f), "vW": (136, _f), "gv": (NP, _f),
     "sv": (NP, _f), "vO": (NK, _f), "tau": (NK, _u), "dW": (136, _f),
 }
 for _t, _n in (("O", 3), ("V", 1)):
-    _sb.update({"pr" + _t: (128 * _n, _f), "pa" + _t: (128 * _n, _b), "u" + _t: (64 * _n, _f), "k" + _t: (56 * _n, _f),
-                "q" + _t: ((QW + 80) * _n, _f), "e" + _t: (128 * _n, _f)})
+    _sb.update({"pr" + _t: (128 * _n, _f), "pa" + _t: (128 * _n, _b), "u" + _t: (SW * _n, _f),
+                "q" + _t: (QB * _n, _f), "e" + _t: (128 * _n, _f)})
 SCRATCH = {_k: ("sbuf", [128, _v[0]], _v[1]) for _k, _v in _sb.items()}
 SCRATCH.update({"A1": ("dram", [128, 128], _h), "A2": ("dram", [128, 32], _h), "A3": ("dram", [128, 32], _u)})
 PSUM = ("o0", "o1", "o2", "vK", "vP", "vL", "rA", "rB")
 for _k in PSUM:
     SCRATCH[_k] = ("psum", [128, 512], _f)
-SEMAPHORES = ["sV", "sS", "sT", "sG", "ldA", "ldP", "ldZ", "ldD", "ldN", "ldT", "lr0", "ln0", "lr1", "ln1", "st", "rq1", "rq2", "rp1", "rp2",
-              "hA", "hB", "hC", "tA", "tB", "tC", "loc"]
+SEMAPHORES = ["sV", "sS", "sT", "sG", "ldA", "ldP", "ldZ", "ldD", "ldN", "ldT", "lpw", "lnd", "ln0", "lr1", "ln1", "st", "rq1", "rq2", "rp1", "rp2",
+              "hA", "hB", "hC", "tA", "tB", "tC", "loc", "lt"]
 
 FLY, FLY_T = 2.0, (7.0, 7.5, 7.0)
 WAKE, FAC, CALL, LAT, GAT, SCA = 0.2, 1.3, 0.2, 1.5, 1.8, 4.6
-CASES = ((0.9, 0.16, 0.7, 0.85), (1.0, 0.2, 1.25, 1.0), (1.15, 0.17, 0.9, 1.2))
-ROUNDS, SHAKE, PULL, SPAN = 3600, 0.1, 3.0, 1.5
-GF = ("u0", "zP", "RP", "vW", "dW", "Rs", "cB", "W2", "qV")
-WON, WON0, WB = "SSSS", "SSSS", ("vK", "vP", "rA", "rB")
-CUT = ((0, 12), (12, 24))
+CASES = ((1.0, 0.2, 1.0, 1.0, 0.7), (0.8, 0.2, 0.7, 0.9, 1.2), (1.0, 0.2, 1.25, 1.0, 0.0), (1.15, 0.15, 0.9, 1.2, 1.5))
+WEIGHT = (1.0, 1.2, 1.0, 1.0)
+ROUNDS, MOVES, HEAT, FAR, SEED = 12, 42000, 0.3, 30, 1
+STAY, VPEN, FREE, PWA = 0.1, 0.3, 6, 0
+SOON, MARKS = 0.1, (("ND11", 0), ("suA", 0), ("msg1", 0), ("out1", 0), ("Yb2", 0))
+WON, WON0, WB = "SSSS", "SS", ("vK", "vP", "rA", "rB")
+CUT = ((0, 8), (8, 16), (16, 24))
+SC1, SC2, TAB, NDMA = "SSS", "SSS", 1.3, False
 PLANS = {}
 
 
@@ -74,36 +82,40 @@ def relay_program(g, core, T, topo, owner):
     g.wait_ge(T.sem.loc, len(es) * len(pieces))
 
 
-def place(tasks, pre, key):
-    n = len(tasks)
-    succ = [[] for _ in tasks]
+def place(ways, pre, succ, key, pick, free):
+    n = len(ways)
     pend = [len(x) for x in pre]
-    for i, x in enumerate(pre):
-        for d in x:
-            succ[d].append(i)
-    fin, busy = [0.0] * n, {}
+    fin, busy, pick = [0.0] * n, {q: [] for q in "VSTGY"}, list(pick)
     ready = [(key[i], i) for i in range(n) if pend[i] == 0]
     while ready:
         i = min(ready)
         ready.remove(i)
         i = i[1]
-        c = tasks[i]["cost"]
-        s = max([0.0] + [fin[d] + w for d, w in pre[i].items()])
-        l = busy.setdefault(tasks[i]["q"], [])
-        lo, hi = 0, len(l)
-        while lo < hi:
-            mid = (lo + hi) // 2
-            lo, hi = (mid + 1, hi) if l[mid][1] <= s else (lo, mid)
-        while lo < len(l) and s + c > l[lo][0]:
-            s = l[lo][1]
-            lo += 1
+        s0, best = 0.0, None
+        for d, w in pre[i]:
+            if fin[d] + w > s0:
+                s0 = fin[d] + w
+        for k in (range(len(ways[i])) if free else (pick[i],)):
+            q, c = ways[i][k]
+            s, l = s0, busy[q]
+            lo, hi = 0, len(l)
+            while lo < hi:
+                mid = (lo + hi) // 2
+                lo, hi = (mid + 1, hi) if l[mid][1] <= s else (lo, mid)
+            while lo < len(l) and s + c > l[lo][0]:
+                s = l[lo][1]
+                lo += 1
+            x = s + c + (STAY if k != pick[i] else 0.0) + (VPEN if q == "V" else 0.0)
+            if best is None or x < best[0]:
+                best = (x, k, s, c, l, lo)
+        x, pick[i], s, c, l, lo = best
         fin[i] = s + c
         l.insert(lo, (s, s + c))
-        for x in succ[i]:
+        for x, w in succ[i]:
             pend[x] -= 1
             if pend[x] == 0:
                 ready.append((key[x], x))
-    return fin
+    return fin, pick
 
 
 def plan(tasks):
@@ -128,28 +140,39 @@ def plan(tasks):
     for calls, wake, way, ind in CASES:
         e = [[(d, 0.0) for d in t["odeps"]] + [(d, wake + way * tasks[d]["lat"]) for d in t["deps"]] +
              ([(t["aft"][0], way * t["aft"][1])] if t["aft"] else []) for t in tasks]
-        cases.append(([t["cost"] * (way * way if t["dma"] else calls * ind if t["ind"] else calls) for t in tasks], e))
+        cases.append(([way * way if t["dma"] else calls * ind if t["ind"] else calls for t in tasks], e))
+    ways = [[(t["q"], t["cost"])] + [(q, c) for q, fn, c in t["alt"]] for t in tasks]
+    lpre, lpost = [list(x.items()) for x in pre], [list(x.items()) for x in post]
+    flex = [i for i in range(n) if len(ways[i]) > 1]
 
-    def length(start):
+    def length(start, pick):
         total, seq = 0.0, sorted(range(n), key=lambda j: (start[j], j))
         for calls, e in cases:
-            end, free = [0.0] * n, {}
+            end, free = [0.0] * n, {q: 0.0 for q in "VSTGY"}
             for i in seq:
-                q = tasks[i]["q"]
-                end[i] = free[q] = max([free.get(q, 0.0)] + [end[d] + w for d, w in e[i]]) + calls[i]
+                q, c = ways[i][pick[i]]
+                s = free[q]
+                for d, w in e[i]:
+                    if end[d] + w > s:
+                        s = end[d] + w
+                end[i] = free[q] = s + c * calls[i]
             total += max(end)
         return total
-    key, best, bkey, seed, low = [-x for x in tail], None, None, 1, 0.0
+    key, best, bkey, seed, low, pick, bpick = [-x for x in tail], None, None, 1, 0.0, [0] * n, None
     for r in range(ROUNDS):
-        fin = place(tasks, pre, key)
+        fin, pick = place(ways, lpre, lpost, key, pick, r % FREE == 0)
         if best is None or max(fin) < max(best) + 1.0:
-            start = [x - t["cost"] for x, t in zip(fin, tasks)]
-            x = max(fin) + length(start)
+            start = [fin[i] - ways[i][pick[i]][1] for i in range(n)]
+            x = max(fin) + length(start, pick)
             if best is None or x < low:
-                best, bkey, low = fin, start, x
-        key = [-x for x in place(tasks, post, [-x for x in fin])]
+                best, bkey, low, bpick = fin, start, x, pick
+        key = [-x for x in place(ways, lpost, lpre, [-x for x in fin], pick, False)[0]]
         if r % 3 == 2:
-            key = []
+            key, pick = [], list(bpick)
+            for x in range(FLIPS):
+                seed = seed * 16807 % 2147483647
+                i = flex[seed % len(flex)]
+                pick[i] = (pick[i] + 1 + seed // 1024 % (len(ways[i]) - 1)) % len(ways[i])
             for x in bkey:
                 seed = seed * 16807 % 2147483647
                 key.append(x + SHAKE * seed / 2147483647)
@@ -165,10 +188,117 @@ def plan(tasks):
                         todo.append(x)
     order = {}
     for i in sorted(range(n), key=lambda j: (bkey[j], j)):
-        order.setdefault(tasks[i]["q"], []).append(i)
+        order.setdefault(ways[i][bpick[i]][0], []).append(i)
     PLANS[n] = order
     PLANS["t"] = max(best)
-    PLANS["dbg"] = (tasks, pre, post, tail, best)
+    PLANS["low"] = low
+    PLANS["x"] = (ways, lpre, lpost, cases, bkey, bpick)
+    PLANS["dbg"] = ([dict(t, q=ways[i][bpick[i]][0], cost=ways[i][bpick[i]][1]) for i, t in enumerate(tasks)], pre, post, tail, best)
+    return order
+
+
+def plan(tasks):
+    n = len(tasks)
+    if n in PLANS:
+        return PLANS[n]
+    ways = [[(t["q"], t["cost"])] + [(q, c) for q, fn, c in t["alt"]] for t in tasks]
+    cases = []
+    for calls, wake, way, ind, hold in CASES:
+        e = []
+        for t in tasks:
+            p = {d: 0.0 for d in t["odeps"]}
+            p.update({d: wake + way * tasks[d]["lat"] for d in t["deps"]})
+            if t["aft"]:
+                d, w = t["aft"]
+                p[d] = max(p.get(d, 0.0), way * w - (hold if tasks[d]["tab"] else 0.0))
+            e.append(list(p.items()))
+        cases.append(([1.0 + hold / t["cost"] if t["tab"] == 1 else way * way if t["dma"] else calls * ind if t["ind"] else calls for t in tasks], e))
+    pre, post = cases[0][1], [[] for _ in tasks]
+    for i, p in enumerate(pre):
+        for d, w in p:
+            post[d].append((i, w))
+    tail = [0.0] * n
+    for i in range(n - 1, -1, -1):
+        tail[i] = tasks[i]["cost"] + max([0.0] + [tail[x] + w for x, w in post[i]])
+    key, pick, dep = [-x for x in tail], [0] * n, [set(d for d, w in p) for p in pre]
+    for r in range(ROUNDS):
+        fin, pick = place(ways, pre, post, key, pick, r % FREE == 0)
+        key = [-x for x in place(ways, post, pre, [-x for x in fin], pick, False)[0]]
+    fin, pick = place(ways, pre, post, key, pick, False)
+
+    def run(seq, pick):
+        out = []
+        for calls, e in cases:
+            end, by, free, last = [0.0] * n, [-1] * n, {q: 0.0 for q in "VSTGY"}, {q: -1 for q in "VSTGY"}
+            for i in seq:
+                q, c = ways[i][pick[i]]
+                s, b = free[q], last[q]
+                for d, w in e[i]:
+                    if end[d] + w > s:
+                        s, b = end[d] + w, d
+                end[i] = free[q] = s + c * calls[i]
+                last[q], by[i] = i, b
+            out.append((end, by))
+        return sum((max(x[0]) + SOON * sum(x[0][k] for k in marks)) * w for x, w in zip(out, WEIGHT)), out
+    seed, marks = [SEED], [[k for k in range(n) if tasks[k]["nm"] == nm][m] for nm, m in MARKS]
+
+    def rnd(m):
+        seed[0] = seed[0] * 16807 % 2147483647
+        return seed[0] * m // 2147483647
+    seq = sorted(range(n), key=lambda j: (fin[j] - ways[j][pick[j]][1], j))
+    cur, out = run(seq, pick)
+    best = (cur, seq, pick, out)
+    for r in range(MOVES):
+        end, by = out[rnd(len(out))]
+        i, pairs = marks[rnd(len(marks))] if rnd(2) else end.index(max(end)), []
+        while by[i] >= 0:
+            if by[i] not in dep[i]:
+                pairs.append((by[i], i))
+            i = by[i]
+        if not pairs:
+            continue
+        j, i = pairs[rnd(len(pairs))]
+        s2, p2, kind, far = seq, pick, rnd(10), rnd(2) * rnd(FAR)
+        a, b = seq.index(j), seq.index(i)
+        if kind < 3:
+            x = (j, i)[rnd(2)]
+            if len(ways[x]) < 2:
+                continue
+            p2 = list(pick)
+            p2[x] = (pick[x] + 1 + rnd(len(ways[x]) - 1)) % len(ways[x])
+        elif kind < 7:
+            b = min(n - 1, b + far)
+            moved, go, keep = {j}, [j], []
+            for x in seq[a + 1:b + 1]:
+                if dep[x] & moved:
+                    moved.add(x)
+                    go.append(x)
+                else:
+                    keep.append(x)
+            s2 = seq[:a] + keep + go + seq[b + 1:]
+        else:
+            a = max(0, a - far)
+            need, go, keep = set(dep[i]), [i], []
+            for x in reversed(seq[a:b]):
+                if x in need:
+                    need |= dep[x]
+                    go.append(x)
+                else:
+                    keep.append(x)
+            s2 = seq[:a] + go[::-1] + keep[::-1] + seq[b + 1:]
+        x, o2 = run(s2, p2)
+        if x <= cur - (HEAT * (1 - r / MOVES) + 0.005) * math.log((rnd(1000) + 1) / 1000):
+            start = [o2[0][0][k] - ways[k][p2[k]][1] * cases[0][0][k] for k in range(n)]
+            seq, pick, cur, out = sorted(s2, key=lambda k: round(start[k], 6)), p2, x, o2
+            if cur < best[0]:
+                best = (cur, seq, pick, out)
+    cur, seq, pick, out = best
+    order = {}
+    for i in seq:
+        order.setdefault(ways[i][pick[i]][0], []).append(i)
+    PLANS[n] = order
+    PLANS["t"], PLANS["low"] = max(out[0][0]), [round(max(x[0]), 2) for x in out]
+    PLANS["dbg"] = ([dict(t, q=ways[i][pick[i]][0], cost=ways[i][pick[i]][1]) for i, t in enumerate(tasks)], [dict(p) for p in pre], post, tail, out[0][0])
     return order
 
 
@@ -188,19 +318,20 @@ def rank_program(g, core, T, topo):
     V, S, E = g.vector, g.scalar, g.tensor
     cy = 0.00083 * FAC
 
-    def add(q, fn, reads, writes, cost, ext=(), aft=None, ind=False):
+    def add(q, fn, reads, writes, cost, ext=(), aft=None, ind=False, alt=()):
         i, reads, writes = len(tasks), reads.split(), writes.split()
         deps, odeps = set(), set()
         for b in reads:
             if b in wr:
                 deps.add(wr[b])
             if b in PSUM:
-                deps.update(x for x in rd.get(b, ()) if tasks[x]["q"] != q)
+                deps.update(x for x in rd.get(b, ()) if tasks[x]["q"] != q or alt or tasks[x]["alt"])
         for b in writes:
             if b in wr:
                 (odeps if q == "T" and tasks[wr[b]]["q"] == "T" else deps).add(wr[b])
             deps.update(rd.get(b, ()))
-        tasks.append(dict(nm=(writes + ["-"])[0], q=q, fn=fn, deps=deps, odeps=odeps, cost=cost, ext=tuple(ext), aft=aft, dma=None, lat=0.0, ind=ind))
+        tasks.append(dict(nm=(writes + ["-"])[0], q=q, fn=fn, deps=deps, odeps=odeps, cost=cost, ext=tuple(ext), aft=aft, dma=None, lat=0.0, ind=ind,
+                          alt=tuple(alt), tab=0))
         for b in reads:
             rd.setdefault(b, []).append(i)
         for b in writes:
@@ -225,8 +356,12 @@ def rank_program(g, core, T, topo):
     def scan(out, on, d0, d1, ins, op0, op1, n=64):
         return vop(lambda: V.tensor_tensor_scan(out, d0, d1, 0.0, op0, op1), ins, on, n)
 
-    def act(out, on, in_, ins, n=64, fn=F.Copy, f=1, **kw):
-        return add("S", lambda: [S.activation(out, in_, fn, **kw)], ins, on, 0.065 + cy * n * f if f != 1 else cy * max(64, n), ind=f != 1)
+    def act(out, on, in_, ins, n=64, fn=F.Copy, f=1, half=False, alt=None, **kw):
+        if alt is None and (fn is F.Copy or fn is F.Identity):
+            alt = [("V", lambda: [V.tensor_scalar(out, in_, kw.get("scale", 1.0), kw.get("bias", 0.0), A.mult, A.add)],
+                    0.05 + cy * n * f if f != 1 else cy * max(64, n // 2 if half else n))]
+        return add("S", lambda: [S.activation(out, in_, fn, **kw)], ins, on, 0.065 + cy * n * f if f != 1 else cy * max(64, n), ind=f != 1,
+                   alt=alt or ())
 
     def iota(ap, on, pat, b, ch, n, fl=True):
         if fl:
@@ -234,9 +369,10 @@ def rank_program(g, core, T, topo):
         return add("G", lambda: [g.iota(ap, pat, b, ch)], "", on, 0.13 + 2 * cy * n)
 
     def fill(ap, on, v, n):
-        if on[:2] in GF:
-            return iota(ap, on, [[0, n]], v, 0, n)
-        return act(ap, on, T.bc[:, 0:n], "one", n, scale=0.0, bias=float(v))
+        alt = [("V", lambda: [V.memset(ap, float(v))], cy * max(64, n))]
+        if abs(v) < 2 ** 24:
+            alt.append(("G", lambda: [g.iota(ap, [[0, n]], v, 0, allow_small_or_imprecise_dtypes=True)], 0.13 + 2 * cy * n))
+        return act(ap, on, T.bc[:, 0:n], "one", n, alt=alt, scale=0.0, bias=float(v))
 
     def select(ap, on, pat, b):
         return add("G", lambda: [g.affine_select(ap, T.ohA[:, 0:128], pat, A.is_equal, 0.0, b, 1)], "ohA", on, 0.17 + 256 * cy)
@@ -245,7 +381,7 @@ def rank_program(g, core, T, topo):
         c = sum(cy * max(64, n) * (4 if f4 else 1) for (_, n, f4) in lst)
         return add("T", lambda: [E.matmul(*a) for (a, n, f4) in lst], ins, bank, c, ext, aft)
 
-    loads, nloc = {}, [0]
+    loads, nloc = {}, {}
 
     def load(q, sem, pairs, ins, on, lat=LAT, ext=(), aft=None):
         eng = g.sync if q == "Y" else g.scalar
@@ -254,17 +390,17 @@ def rank_program(g, core, T, topo):
         loads[sem] = loads.get(sem, 0) + 16 * len(pairs)
         return i
 
-    def remote(calls, ins):
+    def remote(calls, ins, left="loc"):
         def fn():
             for c in calls:
-                g.remote_dma_fused([transfer(topo, core, d, es, T.sem[s], a, b) for d, es, s, a, b in c], local_sem=T.sem.loc)
-                nloc[0] += sum(len(x[1]) for x in c)
+                g.remote_dma_fused([transfer(topo, core, d, es, T.sem[s], a, b) for d, es, s, a, b in c], local_sem=T.sem[left])
+                nloc[left] = nloc.get(left, 0) + sum(len(x[1]) for x in c)
             return []
         return add("G", fn, ins, "", CALL * len(calls))
     E8 = topo.engines(core, peers[0])
     blk = lambda t, b, w=128: t[:, w * b:w * b + w]
 
-    vop(lambda: V.memset(T.bc[:], 1.0), "", "one")
+    vop(lambda: V.memset(T.bc[:], 1.0), "", "one", 96)
     vop(lambda: V.memset(T.X[:], 1), "", "X", NP)
     a = load("Y", "ldN", [(T.Zn[:], T.nbr[:])], "", "Zn")
     b = load("S", "ldZ", [(T.Zp[:], T.planes[:])], "", "Zp")
@@ -274,35 +410,38 @@ def rank_program(g, core, T, topo):
 
     xd, tI, xp, Ld, Hd = T.st[:, 64:96], T.st[:, 96:128], T.st[:, 128:160], T.Ld[:, 0:32], T.Ld[:, 32:64]
     cp(T.NU[:], "NU", T.Zn[:], "Zn")
-    sC = remote([[(rel[1], E8, "hC", T.NU[:], T.A3[:])]], "NU")
+    sC = remote([[(rel[1], E8, "hC", T.NU[:], T.A3[:])]], "NU", "lt")
     ts(T.H1[:], "H1", T.Zp[:], "Zp", 1.0 / 64, None, A.mult, n=128)
-    sA = remote([[(rel[0], E8, "hA", T.H1[:], T.A1[:])]], "H1")
+    sA = remote([[(rel[0], E8, "hA", T.H1[:], T.A1[:])]], "H1", "lt")
     act(xd, "xd", T.Zd[:], "Zd", scale=1.0 / 64)
     ts(Hd, "Hd", T.Zd[:], "Zd", 1.0 / 64, None, A.mult)
     tt(Ld, "Ld", xd, Hd, "xd Hd", A.subtract)
-    sB = remote([[(rel[1], E8, "hB", Ld, T.A2[:])]], "Ld")
+    sB = remote([[(rel[1], E8, "hB", Ld, T.A2[:])]], "Ld", "lt")
+    tasks[sC]["tab"], tasks[sA]["tab"], tasks[sB]["tab"] = 1, 2, 2
     tasks[sA]["odeps"].add(sC)
     tasks[sB]["odeps"].add(sA)
 
     iota(T.pi[:], "pi", [[0, 4]], 0, 1, 4, False)
     iota(T.jm[:], "jm", [[0, 8], [1, 16]], 0, 0, 128)
-    iota(T.oRi[:], "oRi", [[0, 4], [-8, 3]], 16, 0, 12)
+    iota(T.oRi[:, 0:13], "oRi", [[16, 13]], 0, 0, 13)
+    iota(T.rk[:, 24:26], "rkp", [[0, 2]], -1, 0, 2, False)
     iota(T.md16[:], "md16", [[1, 8], [0, 16]], 0, 0, 128)
     iota(T.mk[:], "mk", [[1, 128]], 0, -1, 128)
     iota(T.oKi[:], "oKi", [[1, 32]], 0, 0, 32, False)
-    iota(T.cOw[:], "cOw", [[16, 24]], 128, 1, 24)
+    iota(T.cOw[:], "cOw", [[16, BW]], 128, 1, BW)
     iota(T.cD[:, 0:8], "cD", [[32, 4], [1, 2]], -2, 0, 8)
     iota(T.cD[:, 8:72], "cB", [[0, 8], [-32, 4], [-1, 2]], 0, 0, 64)
     iota(tI, "tI", [[1, 32]], 0, 32, 32)
-    iota(T.sA[:, 0:57], "sA", [[1, 57]], -2, 0, 57)
+    iota(T.sA[:, 0:46], "sA", [[1, 46]], 0, 0, 46)
     iota(T.cL[:, 0:140], "cL", [[1, 140]], -12, 0, 140)
     iota(T.CC[:, 0:64], "CH", [[1024, 2], [0, 32]], 0, 32, 64)
     iota(T.CC[:, 64:128], "CL", [[PWID - 1024, 2], [1, 32]], LO, 0, 64)
     for k, v in enumerate(owners):
-        fill(blk(T.cQ, k, 24), "cQ%d" % k, v, 24)
+        fill(blk(T.cQ, k, BW), "cQ%d" % k, v, BW)
     CQ = " ".join("cQ%d" % k for k in range(8))
-    act(T.Rs[:], "Rs", T.cQ[:, 0:168], CQ, 168, scale=0.0, bias=1.0)
-    fill(T.Rs[:, 0:168:24], "Rs", 0, 7)
+    fill(T.Rs[:, 0:7 * BW], "Rs", 1, 7 * BW)
+    fill(T.Rs[:, 0:7 * BW:BW], "Rs", 0, 7)
+    fill(T.Rs[:, 7 * BW:8 * BW], "Rh", 0, BW)
     ones = T.bc[0:1, 0:128]
     sh, an = A.arith_shift_right, A.bitwise_and
     for k, x in enumerate(((15, None, an), (4, None, sh), (3, None, an), (2, 3, sh, an), (3, 1, sh, an), (5, None, sh))):
@@ -314,47 +453,73 @@ def rank_program(g, core, T, topo):
     cv, g31, hL, cf, cl, c1, c2, lo, hi, pK, pK4, pL, m3, xm, m34, he, he2, f15, g15, p15, m89, k8, cA, cB = [col(k) for k in range(8, 32)]
     act(cf, "cf", p5, "pf", scale=-1024.0, bias=float(base))
     act(tI, "tI", tI, "tI cf", fn=F.Identity, bias=cf)
-    for ap, nm, src, sc, bi in ((g31, "g31", pg, 3.0, 1.0), (pK4, "pK4", pf_, float(K4), -3.0 * K4), (lo, "lo", par, float(PWID), 0.0),
+    for ap, nm, src, sc, bi in ((g31, "g31", pg, 3.0, 1.0), (pK4, "pK4", pf_, float(K4), RND - 3.0 * K4), (lo, "lo", par, float(PWID), 0.0),
                                 (hi, "hi", par, float(PWID), float(HI))):
         act(ap, nm, src, "pf", scale=sc, bias=bi)
     act(hL, "hL", p16, "pf g31", fn=F.Identity, scale=g31, bias=g31)
-    for ap, nm, sc, bi in ((cl, "cl", 16.0, pf_), (c1, "c1", float(GW), pi_), (c2, "c2", float(GW), pf_)):
-        act(ap, nm, pg, "pf", fn=F.Identity, scale=sc, bias=bi)
+    act(cl, "cl", pg, "pf", fn=F.Identity, scale=16.0, bias=pf_)
+    nl, sg, w89, wg, sgx, hl, hu, bl, bu, p58, pM = [col(k) for k in range(36, 47)]
+    act(nl, "nl", p5, "pf", scale=-1.0, bias=4.0)
+    act(nl, "nl", pg, "pf nl", fn=F.Identity, scale=6.0, bias=nl)
+    act(sg, "sg", p5, "pf", scale=-4.0, bias=-1.0)
+    act(sg, "sg", pg, "pf sg", fn=F.Identity, scale=2.0, bias=sg)
+    act(c2, "c2", pf_, "pf nl", fn=F.Identity, scale=-1.0, bias=nl)
+    act(c1, "c1", pi_, "pf nl", fn=F.Identity, scale=-1.0, bias=nl)
     act(c1, "c1", p8, "pf c1", fn=F.Identity, scale=200.0, bias=c1)
-    oK, oR, oB8 = T.oT[:, 0:24], T.oT[:, 24:36], T.oT[:, 40:44]
+    oK, oR, oB8, oF = T.oT[:, 0:24], T.oT[:, 24:37], T.oT[:, 40:44], T.oT[:, 64:72]
     m16 = T.m16[:]
-    ts(oR, "oR", T.oRi[:], "oRi pf", p16, None, A.add)
+    jj, jq = T.oRi[:, 0:13], T.oRi[:, 16:29]
+    act(jj, "oRi", jj, "oRi pf", fn=F.Identity, bias=p16)
+    ts(T.ti[:, 0:13], "ti", jj, "oRi", (1 - BW) / 2, 1.0 / BW, A.add, A.mult)
+    act(jq, "jq", T.ti[:, 0:13], "ti", scale=-float(BW))
+    tt(jq, "jq", jq, jj, "jq oRi", A.add)
+    cp(oR, "oR", jq, "jq")
     ts(T.G2[:], "G2", T.md16[:], "md16 pf", pg, 2.0, A.is_equal, A.mult)
     ts(T.I16[:], "I16", T.mk[:], "mk", 0.0, None, A.is_equal)
-    ts(T.U2[:, 0:128], "U2", T.mk[:], "mk", 0.0, -2.0, A.is_lt, A.mult)
-    ts(T.U2[:, 128:256], "U2b", T.md16[:], "md16 pf", pg, 2.0, A.is_lt, A.mult)
-    act(T.cO16[:, 0:24], "cO16", T.cOw[:], "cOw")
+    L2, U2 = T.U2[:, 0:128], T.U2[:, 128:256]
+    for ap, nm, h, b, x in ((L2, "L2", hl, bl, (-0.5, 7.5, 0.5, -7.5)), (U2, "U2", hu, bu, (0.5, -0.5, 0.5, 0.5))):
+        act(h, nm + "h", p16, "pf", scale=x[0], bias=x[1])
+        act(b, nm + "b", p16, "pf", scale=x[2], bias=x[3])
+        act(ap, nm, T.mk[:], "mk %sb" % nm, 128, F.Abs, bias=b)
+        ts(ap, nm, ap, "%s %sh" % (nm, nm), h, 2.0, A.is_le, A.mult)
+    act(T.cO16[:, 0:BW], "cO16", T.cOw[:], "cOw")
     cp(oK, "oK", T.oKi[:, 0:24], "oKi")
     ts(m16, "m16", T.jm[:], "jm pf", p16, None, A.is_equal)
-    fill(T.G3[:], "G3", 0, 128)
+    act(T.G3[:], "G3", T.bc[:, 0:128], "one", 128, half=True, scale=0.0)
     act(T.G3[:, 3:128:4], "G3", T.G2[:, 3:128:4], "G2", scale=0.5)
     ts(T.pf[:, 32:36], "m4", T.oKi[:, 0:4], "oKi pf", pf_, -float(BIG + K4), A.is_equal, A.mult)
     for j in range(4):
         act(T.sc4[:, j:128:4], "sc4%d" % j, T.bc[:, 0:32], "one m4", scale=col(32 + j), bias=float(K4))
     SC4 = "sc40 sc41 sc42 sc43 "
     ts(T.LP[0:20, :], "LP", T.jm[0:20, :], "jm hL", 1.0, T.pf[0:20, 10:11], A.add, A.is_equal)
-    fill(T.W1[:, 0:128], "W1", NONE, 128)
-    fill(T.W2[:, 0:128], "W2", NONE, 128)
+    for W, wn, first in ((T.W1, "W1", "S" in SC1), (T.W2, "W2", "S" not in SC1)):
+        if first:
+            tasks[act(W[:, 0:128], wn + " tab", T.bc[:, 0:128], "one", 128, F.Silu, scale=float(NONE + OFS))]["cost"] += TAB
+        else:
+            fill(W[:, 0:128], wn, NONE + OFS, 128)
     ts(m3, "m3", pi_, "pf", 3.0, None, A.is_equal)
     act(xm, "xm", m3, "m3", scale=-1.0, bias=1.0)
     act(T.X16[:], "X16", T.X[:], "X", NP)
     for b in range(3):
         fill(blk(T.inj, b), "inj", 0, 128)
-    S2, S2a = T.sA[:, 64:120], T.sA[:, 128:184]
-    fill(T.R1c[:], "R1c", -BIG, 56)
-    fill(T.R1c[:, 6:56:GW], "R1c", BIG, 8)
-    ts(T.S1[:], "S1", T.sA[:, 1:57], "sA c2", c2, None, A.is_equal)
-    ts(T.sA[:, 0:57], "sA", T.sA[:, 0:57], "sA c1", c1, None, A.is_equal)
-    tt(S2, "S2", T.sA[:, 0:56], T.sA[:, 1:57], "sA", A.subtract, n=112)
+    S2, S2a = T.sA[:, 144:188], T.sA[:, 192:236]
+    fill(T.R1c[:], "R1c", 0, SW)
+    fill(T.R1c[:, 9:SW:22], "R1c", TOP, 4)
+    fill(T.R1c[:, 21:SW:22], "R1c", TOP, 4)
+    ts(T.sA[:, 48:93], "E1", T.sA[:, 1:46], "sA c2", c2, KV, A.is_equal, A.mult)
+    tt(T.S1[:], "S1", T.sA[:, 49:93], T.sA[:, 48:92], "E1", A.subtract, n=88)
+    act(sgx, "sgx", xm, "xm sg", scale=sg)
+    ts(T.sA[:, 96:140], "E2", T.sA[:, 1:45], "sA c1 sg", c1, sg, A.is_equal, A.mult)
+    ts(T.sA[:, 288:332], "E4", T.sA[:, 2:46], "sA c1 sgx", c1, sgx, A.is_equal, A.mult)
+    tt(S2, "S2", T.sA[:, 96:140], T.sA[:, 288:332], "E2 E4", A.subtract, n=88)
     tt(m89, "m89", T.m16[:, 8:9], T.m16[:, 9:10], "m16", A.add)
-    ts(T.sm[:, 72:80], "E8", T.oKi[:, 0:8], "oKi pf m89", pg, m89, A.is_equal, A.mult)
-    act(S2a, "S2a", S2, "S2")
-    tt(T.sA[:, 133:184:GW], "S2a", T.sA[:, 69:120:GW], T.sm[:, 72:80], "S2 E8", A.add)
+    act(w89, "w89", m89, "m89 sg", scale=sg)
+    ts(T.sA[:, 240:284], "E3", T.sA[:, 0:44], "sA nl w89", nl, w89, A.is_equal, A.mult)
+    tt(S2a, "S2a", S2, T.sA[:, 240:284], "S2 E3", A.add, n=88)
+    fill(T.pt[:, 0:SW], "pt", 0, SW)
+    fill(T.pt[:, 0:SW:22], "pt", -2 * TOP, 4)
+    fill(T.pt[:, 12:SW:22], "pt", -2 * TOP, 4)
+    act(T.pt[:, SW:2 * SW], "pt", T.pt[:, 0:SW], "pt", SW, scale=-1.0)
     act(T.Ib[:], "Ib", T.I16[:], "I16", 128)
     ts(T.tb[:, 0:128], "tb0", T.jm[:], "jm pf", p16, None, A.is_lt)
     act(T.tb[:, 128:256], "tb1", m16, "m16", 128, scale=HOLD)
@@ -368,35 +533,33 @@ def rank_program(g, core, T, topo):
     ts(g15, "g15", g15, "g15", 1.0, None, A.max)
     act(he2, "he2", he, "he f15", scale=f15)
     act(T.hk[:, 128:256:16], "hk2", T.bc[:, 0:8], "one he2", scale=he2)
-    fill(T.Ms[:], "Ms", 0, 56)
-    ts(T.Ms[:, 5:56:GW], "Ms", T.oKi[:, 0:8], "oKi pf g15", pg, g15, A.is_equal, A.mult)
+    act(wg, "wg", g15, "g15 sg", scale=sg)
+    ts(T.Ms[:, 0:44], "Ms", T.sA[:, 0:44], "sA nl wg", nl, wg, A.is_equal, A.mult)
+    ts(T.Ms[:, 48:56], "Mf", T.oKi[:, 0:8], "oKi pf g15", pg, g15, A.is_equal, A.mult)
     for t, b in (("O", 0), ("O", 1), ("O", 2), ("V", 0)):
-        c = (QW + 80) * b
-        fill(T["q" + t][:, c + 80:c + 80 + QW:GW], "q%s%d" % (t, b), 0, 128)
-        fill(T["u" + t][:, 64 * b:64 * b + 1], "u0%s%d" % (t, b), BIG, 1)
+        c = QB * b + Q0
+        fill(T["q" + t][:, c:c + 128 * GW:GW], "q%s%d" % (t, b), 0, 128)
     act(k8, "k8", T.m16[:, 8:9], "m16", scale=1024.0)
     act(cA, "cA", T.m16[:, 9:10], "m16 k8", fn=F.Identity, scale=HI - 1024.0, bias=k8)
     act(k8, "k8", k8, "k8", scale=2.0)
     act(cB, "cBd", T.m16[:, 9:10], "m16 k8", fn=F.Identity, scale=DEAD - 2048.0, bias=k8)
     for a, z in ((0, LO), (HI, PWID + LO), (PWID + HI, 2 * PWID)):
-        fill(T.PW[:, a:z], "zP%d" % a, 0, z - a)
+        iota(T.PW[:, a:z], "zP%d" % a, [[0, z - a]], 0, 0, z - a, False)
     fill(T.ND[:, 0:LO], "zN0", 0, LO)
     for k, (a, c, cn) in enumerate(((HI, cA, "cA"), (PWID, cB, "cBd"), (PWID + HI, cB, "cBd"))):
         act(T.ND[:, a:a + LO], "zN%d" % (k + 1), T.bc[:, 0:LO], "one " + cn, scale=c)
     PZ = {"PW": " zP0 zP%d zP%d" % (HI, PWID + HI), "ND": " zN0 zN1 zN2 zN3"}
-    fill(T.ohA[:, 0:128], "ohA", 1, 128)
+    iota(T.xq[:, 0:128], "xe", [[16, 8], [0, 4], [1, 4]], 0, -1, 128)
     for f in range(4):
-        select(blk(T.EX, f), "EX%d" % f, [[-16, 8], [0, 4], [-1, 4]], -4 * f)
+        ts(blk(T.EX, f), "EX%d" % f, T.xq[:, 0:128], "xe", -4.0 * f, None, A.is_equal)
     ts(T.LI[:, 0:140], "LI", T.cL[:, 0:140], "cL cl m3", cl, m3, A.is_equal, A.mult, n=70)
     act(T.cO16[:, 32:40], "off", T.bc[:, 0:8], "one lo", scale=lo, bias=float(LO - 1))
     dt = NT * (owners[7] - owners[6])
     act(cv, "cv", par, "pf", scale=float(PWID - dt), bias=float(LO - NT * owners[6]))
     for k, a in enumerate([rank] + owners[1:6:2]):
         act(T.cS[:, 2 * k:2 * k + 2], "cS%d" % k, T.pf[:, 6:8], "pf", scale=float(dt - 1), bias=float(HI - LO + NT * (owners[6] - a)))
-    iota(T.RP1[:, 0:2], "RP1p", [[0, 2]], 0, 0, 2, False)
-    fill(T.RP2[:, 0:2], "RP2p", 0, 2)
     fill(T.cD[:, 15:72:8], "cB", -384, 8)
-    act(T.zz[:, 0:8], "cQc", T.cQ[:, 0:192:24], CQ)
+    act(T.zz[:, 0:8], "cQc", T.cQ[:, 0:8 * BW:BW], CQ)
     for n in (8, 16, 32):
         act(T.zz[:, n:2 * n], "cQc", T.zz[:, 0:n], "cQc")
     fill(T.zz[:, 64:128], "RsM", 0, 64)
@@ -409,11 +572,16 @@ def rank_program(g, core, T, topo):
     act(T.I2[:, 0:128], "I2", T.I16[:], "I16", 128)
     act(T.I2[:, 128:256], "I2b", T.I16[:], "I16", 128)
     act(T.Gf[:], "Gf", T.G2[:], "G2", 128, scale=0.5)
-    fill(T.vW[:, 128:136], "vW0", 0, 8)
+    act(T.Ip[:], "Ip", T.I2[:, 32:160], "I2 I2b", 128)
+    act(p58, "p58", p5, "pf", scale=8.0)
+    ts(oF, "oF", T.oKi[:, 0:8], "oKi p58", p58, None, A.add)
+    fill(T.vW[:, 128:136], "vW0", 416, 8)
     fill(T.dW[:, 128:136], "dW0", 8192, 8)
     ts(p15, "p15", p16, "pf", 14.5, None, A.is_lt)
     act(pK, "pK", p15, "p15", scale=-float(MID), bias=float(SA - 8192))
-    act(pL, "pL", p15, "p15", scale=-float(MID), bias=float(-SH))
+    act(pL, "pL", p15, "p15", scale=-float(MID))
+    act(pM, "pM", p15, "p15", scale=-float(MID), bias=-208.0 - 512.0 * SH)
+    act(T.I1k[:], "I1k", T.I16[:], "I16", 128, scale=1024.0)
 
     def steps_rows(src, srcn, k, ext=(), aft=None):
         st, sn, HL, N, t = blk(T.st, k, 32), "st%d" % k, "HL%d" % k, "N%d" % k, 1 - k
@@ -430,7 +598,7 @@ def rank_program(g, core, T, topo):
     def windows(t, R, Rn, N, banks, on):
         for k, (bk, q) in enumerate(zip(banks, on)):
             h, c = k % 2, PWID * t + LO + 512 * (k % 2)
-            w, sc, lhs, rhs, ins = (("ND", 1.0, T.m16[0:10, :], T[N], "m16 %s %sb %sc" % (N, N, N)), ("PW", 64.0, T.LP[0:20, :], T[R], "LP " + Rn))[k // 2]
+            w, sc, lhs, rhs, ins = (("ND", 1.0, T.m16[0:10, :], T[N], "m16 %s %sb %sc" % (N, N, N)), ("PW", 64.0, T.LP[0:20, :], T.R1, "LP " + Rn))[k // 2]
             for a in (0, 256):
                 mm([((T[bk][:, a:a + 256], lhs, rhs[0:10 * (1 + k // 2), 512 * h + a:512 * h + a + 256], True, True), 256, 0)], ins, bk)
             if q == "S":
@@ -438,26 +606,40 @@ def rank_program(g, core, T, topo):
             else:
                 ts(T[w][:, c:c + 512], "%s%d%d" % (w, t, h), T[bk][:], bk, sc, None, A.mult, n=512)
 
-    load("Y", "lr0", [(T.R0[0:16, :], T.H1[:]), (T.R0[16:20, :], Ld)], "H1 Ld", "R0")
+    c = PWID + LO
+    a = load("Y", "lpw", [(T.PW[16 * a:16 * a + 16, c:c + NT], T.planes[:]) for a in range(8)], "", "PW10 PW11", LAT + 1.0,
+             *(([("lt", 3 * len(E8))], (sB, 1.5)) if PWA else ()))
+    tasks[a]["odeps"].add(wr["X"])
     steps_rows(T.Zn[:], "Zn", 0)
-    windows(1, "R0", "R0", "N0", ("vK", "vP", "o0", "o1"), WON0)
+    if NDMA:
+        load("Y", "ln0", [(T.N0[10:16, :], T.CC[0:96, 0:64])], "CH", "N0d")
+        load("Y", "lnd", [(T.ND[16 * a:16 * a + 16, c:c + NT], T.N0[0:16, :]) for a in range(8)], "N0 N0b N0c N0d", "ND10 ND11", LAT + 0.5)
+    else:
+        windows(1, "", "", "N0", ("vK", "vP"), WON0)
 
     su1, suA, suB, s1c = T.su[:, 0:24], T.su[:, 24:48], T.su[:, 48:56], T.su[:, 64:88]
 
     def slots(oh, ohn, su, sun):
-        M, n7, n8 = 24, 168, 192
-        mm([((T.rB[:, n7:n8], T.I16[:], T.cO16[:, 0:M], True, True), M, 0)], "I16 cO16", "rB")
-        tt(oh[:], ohn, T.rk[:, 0:32].indirect(oR), T.cQ[:], "rka rkb oR " + CQ, A.is_equal, n8, f=GAT)
-        mm([((T.rA[:, 0:n7], T.G2[:], oh[:, 0:n7], True, False), n7, 0), ((T.rA[:, 0:n7:M], ones, T.cD[0:1, 0:7], False, True), 7, 0)],
-           "G2 one cD " + ohn, "rA")
-        mm([((T.rB[:, 0:n7], blk(T.U2, h), oh[:, 0:n7], h == 0, h == 1), n7, 0) for h in range(2)], "U2 U2b " + ohn, "rB")
-        sc = T.rA[:, 256:256 + n7]
-        scan(sc, "sc", T.Rs[:], T.rA[:, 0:n7], "Rs rA", A.mult, A.add, n7)
-        tt(T.z2[:], "z2", T.rB[:, 0:n8], oh[:, 0:n8], "rB " + ohn, A.mult, n8)
-        tt(T.z1[:], "z1", sc, oh[:, 0:n7], "sc rA " + ohn, A.mult, n7)
-        mm([((T.rB[:, 0:M], T.I16[:], blk(T.z2, b, M), b == 0, False), M, 0) for b in range(8)], "I16 z2", "rB")
-        mm([((T.rB[:, 0:M], T.I16[:], blk(T.z1, b, M), False, b == 6), M, 0) for b in range(7)], "I16 z1", "rB")
+        M, n7, n8 = 24, 7 * BW, 8 * BW
+        mm([((T.rA[:, n7:n8], T.I16[:], T.cO16[:, 0:BW], True, True), M, 0)], "I16 cO16", "rA")
+        tt(oh[:], ohn, T.rk[:, 0:BW].indirect(oR), T.cQ[:], "rk rkp oR " + CQ, A.is_equal, n8, f=GAT)
+        mm([((T.rA[:, 0:n7], L2, oh[:, 0:n7], True, False), n7, 0), ((T.rA[:, 1:n7], U2, oh[:, 0:n7 - 1], False, False), n7, 0),
+            ((T.rA[:, 0:n7:BW], ones, T.cD[0:1, 0:7], False, True), 7, 0)], "L2 U2 one cD " + ohn, "rA")
+        sc = T.rA[:, 256:256 + n8]
+        scan(sc, "sc", T.Rs[:], T.rA[:, 0:n8], "Rs Rh rA", A.mult, A.add, n8)
+        tt(T.z2[:], "z2", sc, oh[:], "sc rA " + ohn, A.mult, n8)
+        mm([((T.rB[:, 0:M], T.I16[:], T.z2[:, BW * b:BW * b + M], b == 0, b == 7), M, 0) for b in range(8)], "I16 z2", "rB")
         cp(su, sun, T.rB[:, 0:M], "rB")
+
+    def scatter(q, W, wn, l, src, ins, n):
+        if q == "S":
+            return act(W[:].indirect(l), wn, src, ins + " tab", n, F.Silu, SCA,
+                       alt=[("V", lambda: [V.tensor_copy(W[:].indirect(l), src)], 0.05 + cy * n * SCA)])
+        return cp(W[:].indirect(l), wn, src, ins, n, f=SCA)
+
+    def message(W, wn, MB, mn):
+        scan(T.sd[:], "sd", T.sc4[:], W[:, 0:128], SC4 + wn, A.add, A.max, 128)
+        ts(MB[:, 0:32], mn, T.sd[:, 3:128:4], "sd pK4", pK4, -RND - OFS, A.add, A.add)
 
     def pack(banks):
         ts(T.inj[:, 0:NP:16], "inj", T.ti[:, 0:24], "ti he", he, None, A.mult)
@@ -466,33 +648,35 @@ def rank_program(g, core, T, topo):
             scan(blk(T.ex, b), "ex%d" % b, T.hk[:, 0:128], blk(T.inj, b), "hk inj", A.mult, A.add, 128)
             mm([((ps, T.I16[:], blk(T.X16, b), True, False), 128, 0)], "I16 X16", bank)
             mm([((ps, T.G3[:], blk(T.ex, b), False, True), 128, 0)], "G3 ex%d" % b, bank)
-            act(blk(T.PK, b), "PK%d" % b, ps, bank, 128)
+            act(blk(T.PK, b), "PK%d" % b, ps, bank, 128, bias=float(OFS))
 
-    def send(buf, ins, sem, w, src, dst):
-        x = [(d, sem, buf[:, src + w * k:src + w * k + w], buf[:, dst + w * k:dst + w * k + w]) for k, d in enumerate(peers)]
+    def send(buf, ins, sem, w, src, v, dst):
+        x = [(d, sem, buf[:, src + v * k:src + v * k + w], buf[:, dst + w * k:dst + w * k + w]) for k, d in enumerate(peers)]
         return remote([[(x[0][0], E8[:4]) + x[0][1:], (x[1][0], E8[4:]) + x[1][1:]], [(x[2][0], E8) + x[2][1:]]], ins)
     ARR = 2 * len(E8)
 
     def turn(t, b, out, rhs, bank, stop):
-        n, c, e = "%s%d" % (t, b), (QW + 80) * b, blk(T["e" + t], b)
-        scan(e, "e" + n, T["q" + t][:, c + 80:c + 80 + QW:GW], T.hk[:, 128:256], "hk2 q" + n, A.add, A.mult, 128)
-        mm([((out, e, rhs, True, stop), 8, 1)], "Ms e" + n, bank)
+        n, c, e = "%s%d" % (t, b), QB * b + Q0, blk(T["e" + t], b)
+        scan(e, "e" + n, T["q" + t][:, c:c + 128 * GW:GW], T.hk[:, 128:256], "hk2 q" + n, A.add, A.mult, 128)
+        mm([((out, e, rhs, True, stop), 8, 1)], "Ms Mf e" + n, bank)
+
+    def lay(bank, c, a, z):
+        mm([((T[bank][:, c:c + z - a], ones, T.pt[0:1, a:z], True, True), z - a, 0)], "one pt", bank)
 
     def step(t, b, s, X, xn, bK, bP):
-        n, c = "%s%d" % (t, b), (QW + 80) * b
-        pr, pa, kk, w, u = blk(T["pr" + t], b), blk(T["pa" + t], b), blk(T["k" + t], b, 56), blk(T["w" + t], b, 8), T["u" + t]
-        pK_, pP, c0 = T[bK][:, 0:56], T[bP][:, 64:120], 0 if t == "V" else PWID
+        n, c, cP = "%s%d" % (t, b), QB * b, 256 if t == "V" else SW
+        pr, pa, w, u = blk(T["pr" + t], b), blk(T["pa" + t], b), blk(T["w" + t], b, 8), blk(T["u" + t], b, SW)
+        pK_, pP, c0 = T[bK][:, 1:SW:2], T[bP][:, cP + 1:cP + SW:2], 0 if t == "V" else PWID
         PWn, NDn = [" ".join(x + a + h for a in ("01" if t == "V" else "1") for h in "01") + PZ[x] for x in ("PW", "ND")]
         tt(pr, "pr" + n, T.PW[:, c0:].indirect(w), X, "%s w%s %s" % (PWn, n, xn), A.mult, 128, f=GAT)
         act(pa, "pa" + n, T.ND[:, c0:].indirect(w), "%s w%s" % (NDn, n), 128, f=GAT)
         if s:
-            turn(t, b, pP, T.Ms[:], bP, False)
-        mm([((pP, pa, S2 if s else S2a, not s, True), 56, 0)], "S2 S2a pa" + n, bP)
-        mm([((pK_, pr, T.S1[:], True, True), 56, 1)], "S1 pr" + n, bK)
-        scan(u[:, 64 * b + 1:64 * b + 57], "u" + n, pK_, T.R1c[:], "R1c " + bK, A.min, A.max)
-        tt(kk, "k" + n, pK_, u[:, 64 * b:64 * b + 56], "%s u%s u0%s" % (bK, n, n), A.is_ge)
-        scan(T["q" + t][:, c:c + QW:16], "q" + n, pP, kk, "%s k%s" % (bP, n), A.add, A.mult)
-        places = T["q" + t][:, c + 80:c + QW:16 * GW]
+            turn(t, b, pP, T.Ms[:, 0:44], bP, False)
+        mm([((pP, pa, S2 if s else S2a, not s, True), 44, 0)], "S2 S2a pa" + n, bP)
+        mm([((pK_, pr, T.S1[:], True, True), 44, 1)], "S1 pr" + n, bK)
+        scan(u, "u" + n, T[bK][:, 0:SW], T.R1c[:], "R1c " + bK, A.add, A.max, SW)
+        scan(T["q" + t][:, c:c + 16 * SW:16], "q" + n, T[bP][:, cP:cP + SW], u, "%s u%s" % (bP, n), A.subtract, A.min, SW)
+        places = T["q" + t][:, c + Q0:c + 16 * SW:16 * GW]
         if s < 2 and t == "V":
             ts(w, "w" + n, places, "lo hi q" + n, lo, hi, A.max, A.min)
         elif s < 2:
@@ -504,8 +688,8 @@ def rank_program(g, core, T, topo):
                 step("O", b, s, blk(T.XT if s == 1 else T.X16, b), "XT" if s == 1 else "X16", "o%d" % b, "o%d" % b)
         for b in range(3):
             bk = "o%d" % b
-            turn("O", b, T[bk][:, 128:136], T.Ms[:, 5:56:GW], bk, True)
-            act(blk(out, b + c, 8), on + str(b), T[bk][:, 128:136], bk + " pK", fn=F.Identity, bias=bias)
+            turn("O", b, T[bk][:, 192:200], T.Ms[:, 48:56], bk, True)
+            act(blk(out, b + c, 8), on + str(b), T[bk][:, 192:200], bk + " pK", fn=F.Identity, bias=bias)
 
     def arrive(MB, mn, sem, sent):
         mm([((T.vL[:, 0:8], T.I16[:], T.cO16[:, 32:40], True, False), 8, 0)], "I16 off", "vL")
@@ -517,7 +701,7 @@ def rank_program(g, core, T, topo):
         act(T.Xv[:], "Xv", T.vP[:, 128:256], "vP xm m3", 128, F.Identity, scale=xm, bias=m3)
         ts(T.wV[:], "wV0", T.vL[:, 0:8], "vL lo hi", lo, hi, A.max, A.min)
 
-    def visitors():
+    def visitors(back):
         act(T.Zr[:], "Zr", T.Xv[:].indirect(T.oT[:, 48:56]), "Xv rot", 128, f=GAT)
         for h in range(0, 8, 2):
             mm([((T.vL[:, 128 + 16 * d:144 + 16 * d], T.I2[:, 128 - 16 * d:256 - 16 * d], blk(T.Zr, d, 16), True, True), 16, 0) for d in (h, h + 1)],
@@ -526,26 +710,25 @@ def rank_program(g, core, T, topo):
         act(T.Xw[:], "Xw", T.Ur[:].indirect(T.oT[:, 56:64]), "Ur rot", 128, f=GAT)
         for s in range(3):
             step("V", 0, s, (T.Xw if s == 1 else T.Xv)[:], "Xw" if s == 1 else "Xv", "vK", "vP")
-        turn("V", 0, T.vL[:, 0:8], T.Ms[:, 5:56:GW], "vL", True)
+        if back:
+            turn("V", 0, T.vL[:, 0:8], T.Ms[:, 48:56], "vL", True)
 
-    ts(T.rk[:, 16:32], "rka", T.L0[:, 0:16], "L0", 10, None, sh)
-    ts(T.rk[:, 0:16], "rkb", T.L0[:, 8:24], "L0", 10, None, sh)
+    ts(T.rk[:, 0:24], "rk", T.L0[:], "L0", 10, None, sh)
     slots(T.oh1, "oh1", su1, "su1")
     ts(T.ti[:, 0:24], "ti", T.L0[:], "L0", 1023, None, an)
     pack(("vL", "o2", "vL"))
     for b in range(3):
-        cp(T.W1[:].indirect(blk(T.su, b, 8)), "W1", blk(T.PK, b), "PK%d su1" % b, 128, f=SCA)
-    scan(T.sd[:], "sd", T.sc4[:], T.W1[:, 0:128], SC4 + "W1", A.add, A.max, 128)
-    ts(T.MB1[:, 0:32], "msg1", T.sd[:, 3:128:4], "sd pK4", pK4, None, A.add)
-    s1 = send(T.MB1, "msg1 RP1p", "rq1", 8, 0, 32)
-    act(m34, "m34", m3, "m3 pK4", fn=F.Identity, bias=pK4)
+        scatter(SC1[b], T.W1, "W1", blk(T.su, b, 8), blk(T.PK, b), "PK%d su1" % b, 128)
+    message(T.W1, "W1", T.MB1, "msg1")
+    s1 = send(T.MB1, "msg1", "rq1", 8, 0, 8, 32)
+    act(m34, "m34", xm, "m3 xm", fn=F.Identity, scale=-float(OFS), bias=m3)
     act(T.xB[:], "xB", T.W1[:, 0:128], "W1 xm m34", 128, F.Identity, scale=xm, bias=m34)
-    act(T.W3[:, 0:128], "W3", T.bc[:], "one pK4", 128, F.Identity, scale=float(NONE), bias=pK4)
 
     load("Y", "ldT", [(T.Yt[0:72, 16 * a:16 * a + 16], T.pts[3 * a:3 * a + 3, :]) for a in range(8)], "HL0b", "Yt")
     act(T.Zr[0:72, :], "Zr", T.Yt[0:72, :], "Yt", 128)
+    iota(T.xq[:, 128:256], "xx", [[1, 8], [0, 4], [24, 4]], 0, -1, 128)
     for b in range(3):
-        select(blk(T.Xp, b), "Xp%d" % b, [[-1, 8], [0, 4], [-24, 4]], -8 * b)
+        ts(blk(T.Xp, b), "Xp%d" % b, T.xq[:, 128:256], "xx", -8.0 * b, None, A.is_equal)
         mm([((blk(T.rA, b), T.Xp[0:72, 128 * b:128 * b + 128], T.Zr[0:72, :], True, True), 128, 0)], "Zr Xp%d" % b, "rA")
     act(T.XT[:], "XT", T.rA[:, 0:NP], "rA m3", NP, F.Identity, bias=m3)
 
@@ -555,12 +738,12 @@ def rank_program(g, core, T, topo):
     load("Y", "lr1", [(T.R1[16:20, :], T.A2[:])], "", "R1b", LAT, [("tB", len(E8))], (sB, FLY_T[2]))
     load("Y", "lr1", [(T.R1[0:16, :], T.A1[:])], "", "R1", LAT, [("tA", len(E8))], (sA, FLY_T[1]))
     windows(0, "R1", "R1 R1b", "N1", WB, WON)
-    act(T.I1k[:], "I1k", T.I16[:], "I16", 128, scale=1024.0)
-    mm([((T.rA[:, 128:256], T.I16[:], x, k == 0, k == 3), 128, 0) for k, x in enumerate((T.G2[:], blk(T.U2, 0), blk(T.U2, 1), T.I1k[:]))],
-       "I16 G2 U2 U2b I1k", "rA")
-    act(T.LW[:], "LW", T.rA[:, 128:256], "rA", 128)
-    act(T.tb[:, 0:128], "tb0", m16, "m16", 128, scale=-float(BIG))
-    act(T.tb[:, 128:256], "tb1", m16, "m16", 128, scale=float(MID))
+    lay("vK", 0, 0, SW)
+    lay("vP", 256, SW, 2 * SW)
+    for b in range(3):
+        lay("o%d" % b, 0, 0, 2 * SW)
+    act(T.tb[:, 0:128], "tb0", m16, "m16", 128, half=True, scale=-2.0 * BIG)
+    act(T.tb[:, 128:256], "tb1", m16, "m16", 128, half=True, scale=float(MID))
     mm([((T.rA[:, 0:128], T.Ib[:], T.tb[:, 0:128], True, False), 128, 0), ((T.rA[:, 1:128], T.Ib[:], T.tb[:, 128:255], False, True), 128, 0)],
        "Ib tb0 tb1", "rA")
     act(T.scC[:, 0:128], "scC", T.rA[:, 0:128], "rA", 128)
@@ -568,78 +751,74 @@ def rank_program(g, core, T, topo):
 
     ts(T.wO[:], "wO0 wO1 wO2", T.L0[:], "L0", float(-SH), float(HI), A.add, A.min)
     own(T.Lm, 0, "Lm", float(SA))
-    ts(T.rk[:, 16:32], "rka", T.Lm[:, 0:16], "Lm0 Lm1", -511.75, 1.0 / 1024, A.add, A.mult)
-    ts(T.rk[:, 0:16], "rkb", T.Lm[:, 8:24], "Lm1 Lm2", -511.75, 1.0 / 1024, A.add, A.mult)
+    ts(T.rk[:, 0:24], "rk", T.Lm[:], "Lm0 Lm1 Lm2", -511.75, 1.0 / 1024, A.add, A.mult)
     cp(T.ci[:, 0:24], "ci", T.Lm[:], "Lm0 Lm1 Lm2")
     ts(T.ti[:, 0:24], "ti", T.ci[:, 0:24], "ci", 1023, None, an)
     slots(T.ohA, "ohA", suA, "suA")
     pack(("o0", "o1", "o2"))
-    for a, z in CUT:
-        cp(T.W2[:].indirect(T.su[:, 24 + a:24 + z]), "W2", T.PK[:, 16 * a:16 * z], "PK0 PK1 PK2 suA", 16 * (z - a), f=SCA)
-    scan(T.mA[:, 0:128], "sdA", T.sc4[:], T.W2[:, 0:128], SC4 + "W2", A.add, A.max, 128)
-    act(T.mA[:, 128:160], "mA", T.mA[:, 3:128:4], "sdA pK4", fn=F.Identity, bias=pK4)
+    for q, (a, z) in zip(SC2, CUT):
+        scatter(q, T.W2, "W2", T.su[:, 24 + a:24 + z], T.PK[:, 16 * a:16 * z], " ".join("PK%d" % b for b in range(a // 8, (z + 7) // 8)) + " suA",
+                16 * (z - a))
 
     Cn = T.sm[:, 64:72]
     ts(Cn, "Cn", T.Lv0[:], "Lv0", 3000.0, None, A.is_gt)
     tt(Cn, "Cn", Cn, T.cS[:], "Cn cS0 cS1 cS2 cS3", A.mult)
     act(Cn, "Cn", Cn, "Cn cv", fn=F.Identity, bias=cv)
-    visitors()
+    visitors(True)
     tt(T.RP1[:, 8:16], "out1", T.vL[:, 0:8], Cn, "vL Cn", A.subtract)
-    s2 = send(T.RP1, "out1", "rp1", 2, 10, 2)
+    s2 = send(T.RP1, "out1", "rp1", 2, 10, 2, 2)
 
     mm([((T.vP[:, 0:64], ones, T.cD[0:1, 8:72], True, False), 64, 0)], "one cB", "vP")
     back = dict(ext=[("rp1", ARR)], aft=(s2, FLY))
     ts(T.rkB[:], "rkB", T.RP1[:, 2:10], "out1", 10, None, sh, **back)
     ts(T.ti[:, 24:32], "tiB", T.RP1[:, 2:10], "out1", 1023, None, an, **back)
     tt(T.ohB[:], "ohB", T.rkB[:].indirect(oB8), T.zz[:, 0:64], "rkB oB8 cQc", A.is_equal, 64, f=GAT)
-    mm([((T.vP[:, 8 * d:64], T.G2[:] if d else T.LW[:], T.ohB[:, 0:64 - 8 * d], False, d == 7), 64, 0) for d in range(8)], "G2 LW ohB", "vP")
+    mm([((T.vP[:, 8 * d:64], x, T.ohB[:, 0:64 - 8 * d], False, d == 7), 64, 0) for d, x in [(0, T.I1k[:]), (0, L2)] + [(d, T.G2[:]) for d in range(1, 8)]],
+       "G2 L2 I1k ohB", "vP")
     scan(T.zz[:, 128:192], "zz", T.zz[:, 64:128], T.vP[:, 0:64], "RsM vP", A.add, A.max)
     ts(suB, "suB", T.zz[:, 135:192:8], "zz", -1.0, 1056.0, A.mult, A.add)
     tt(blk(T.ex, 3), "ex3", T.ti[:, 24:32].indirect(T.oT[:, 0:8]), m16, "tiB oK m16", A.mult, 128, f=GAT)
-    mm([((T.vL[:, 256:384], T.G3[:], blk(T.ex, 3), True, True), 128, 0)], "G3 ex3", "vL")
-    tt(blk(T.PK, 3), "PK3", T.vL[:, 256:384], T.xB[:], "vL xB", A.add, 128)
-    cp(T.W3[:].indirect(suB), "W3", blk(T.PK, 3), "PK3 suB", 128, f=SCA)
-    scan(T.sd[:], "sd", T.sc4[:], T.W3[:, 0:128], SC4 + "W3", A.add, A.max, 128)
-    tt(T.MB2[:, 0:32], "msg2", T.sd[:, 3:128:4], T.mA[:, 128:160], "sd mA", A.min)
-    s3 = send(T.MB2, "msg2 RP2p", "rq2", 8, 0, 32)
+    mm([((T.vL[:, 256:384], T.I16[:], T.xB[:], True, False), 128, 0)], "I16 xB", "vL")
+    mm([((T.vL[:, 256:384], T.G3[:], blk(T.ex, 3), False, True), 128, 0)], "G3 ex3", "vL")
+    act(blk(T.PK, 3), "PK3", T.vL[:, 256:384], "vL", 128, bias=float(OFS))
+    scatter("S", T.W2, "W2", suB, blk(T.PK, 3), "PK3 suB", 128)
+    message(T.W2, "W2", T.MB2, "msg2")
+    s3 = send(T.MB2, "msg2", "rq2", 8, 0, 8, 32)
 
     arrive(T.MB2, "msg2", "rq2", s3)
-    visitors()
-    ts(T.RP2[:, 8:16], "out2", T.vL[:, 0:8], "vL cv", cv, None, A.subtract)
-    s4 = send(T.RP2, "out2", "rp2", 2, 10, 2)
+    visitors(False)
+    ts(T.RP2[:, 0:8], "out2", T.qV[:, Q0:16 * SW:16 * GW], "qV0 cv", cv, None, A.subtract)
+    s4 = send(T.RP2, "out2", "rp2", 8, 0, 0, 8)
 
     smA, vB, Yb = T.sm[:, 0:24], T.sm[:, 32:40], T.sm[:, 40:64]
     ts(s1c, "s1c", su1, "su1", 128.0, None, A.min)
-    ts(smA, "smA", suA, "suA", 128.0, None, A.min)
-
-    def to_points():
-        for b in range(3):
-            act(blk(T.gv, b), "gv%d" % b, T.vW[:].indirect(T.su[:, 64 + 8 * b:72 + 8 * b]), "vW vW0 s1c", 128, f=GAT)
-            scan(blk(T.sv, b), "sv%d" % b, T.scC[:, 0:128], blk(T.gv, b), "scC gv%d" % b, A.add, A.max, 128)
-    tt(T.exv[:], "exv", T.RP1[:, 0:10].indirect(T.oT[:, 2:10]), m16, "oK out1 RP1p m16", A.mult, 128, f=GAT, **back)
+    cp(smA, "smA", suA, "suA")
+    home, cj, cd = T.oh1[:, 7 * BW:7 * BW + 24], T.cj[:, 0:24], T.cj[:, 24:48]
+    act(vB, "vB", T.RP1[:, 2:10], "rkB", scale=512.0, bias=-640.0)
+    tt(vB, "vB", vB, T.zz[:, 135:192:8], "vB zz", A.add)
+    tt(T.exv[:], "exv", vB.indirect(T.oT[:, 0:8]), m16, "oK vB m16", A.mult, 128, f=GAT)
     mm([((T.rB[:, 0:128], T.Gf[:], T.exv[:], True, True), 128, 1)], "Gf exv", "rB")
     act(T.vW[:, 0:128], "vW", T.rB[:, 0:128], "rB", 128)
-    to_points()
-    tt(T.vO[:], "vO", T.Lm[:], T.oh1[:, 168:192], "Lm0 Lm1 Lm2 oh1", A.mult)
-    act(T.vO[:], "vO", T.vO[:], "vO pL", fn=F.Identity, bias=pL)
     for b in range(3):
-        tt(blk(T.Lm, b, 8), "Lm%d" % b, blk(T.vO, b, 8), T.sv[:, 128 * b + 15:128 * b + 128:16], "vO sv%d" % b, A.add)
-        ts(blk(T.wO, b, 8), "wO%d" % b, blk(T.Lm, b, 8), "Lm%d" % b, float(HI), None, A.min)
-    ts(vB, "vB", T.zz[:, 135:192:8], "zz", -928.0, 0.0, A.add, A.max)
-    tt(blk(T.ex, 0), "ex0", vB.indirect(T.oT[:, 0:8]), m16, "vB oK m16", A.mult, 128, f=GAT)
-    mm([((T.rB[:, 0:128], T.G2[:], blk(T.ex, 0), True, True), 128, 0)], "G2 ex0", "rB")
-    act(T.vW[:, 0:128], "vW", T.rB[:, 0:128], "rB", 128, scale=-0.5, bias=128.0)
-    to_points()
-    tt(smA, "smA", smA, T.oh1[:, 168:192], "smA oh1", A.mult)
-    tt(smA, "smA", smA, T.sv[:, 15:NP:16], "smA sv0 sv1 sv2", A.add)
-    ts(T.tau[:], "tau", smA, "smA pL", pL, float(SH), A.add, A.add)
+        act(blk(T.gv, b), "gv%d" % b, T.vW[:].indirect(T.su[:, 64 + 8 * b:72 + 8 * b]), "vW vW0 s1c", 128, f=GAT)
+        scan(blk(T.sv, b), "sv%d" % b, T.scC[:, 0:128], blk(T.gv, b), "scC gv%d" % b, A.add, A.max, 128)
+    tt(T.vO[:], "vO", T.Lm[:], home, "Lm0 Lm1 Lm2 oh1", A.mult)
+    act(T.vO[:], "vO", T.vO[:], "vO pM", fn=F.Identity, scale=512.0, bias=pM)
+    tt(T.vO[:], "vO", T.vO[:], T.sv[:, 15:NP:16], "vO sv0 sv1 sv2", A.add)
+    ts(T.wO[:], "wO0 wO1 wO2", T.vO[:], "vO", 1.0 / 512, float(HI), A.mult, A.min)
+    ts(cj, "cj", T.sv[:, 15:NP:16], "sv0 sv1 sv2 pL", pL, None, A.add)
+    ts(cd, "cd", cj, "cj", 511, None, an)
+    tt(smA, "smA", smA, home, "smA oh1", A.mult)
+    tt(smA, "smA", smA, cd, "smA cd", A.subtract)
+    ts(T.tau[:], "tau", smA, "smA", 416.0, 128.0, A.add, A.min)
     own(T.sm, 5, "Yb", pK)
 
-    tt(T.exv[:], "exv", T.RP2[:, 0:10].indirect(T.oT[:, 2:10]), m16, "oK out2 RP2p m16", A.mult, 128, [("rp2", ARR)], (s4, FLY), GAT)
-    mm([((T.rB[:, 0:128], T.Gf[:], T.exv[:], True, True), 128, 1)], "Gf exv", "rB")
-    ts(T.dW[:, 0:128], "dW", T.rB[:, 0:128], "rB", 8192.0 - DEAD - SA, None, A.add, n=128)
+    ts(T.RF[:], "RF", T.RP2[:], "out2", 8192.0 - DEAD - SA, None, A.add, ext=[("rp2", ARR)], aft=(s4, FLY))
+    act(T.exv[:], "exv", T.RF[:].indirect(oF), "RF oF", 128, f=GAT)
+    mm([((T.rB[:, 0:128], T.exv[:], T.Ip[:], True, True), 128, 1)], "Ip exv", "rB")
+    act(T.dW[:, 0:128], "dW", T.rB[:, 0:128], "rB", n=128)
     act(T.gv[:, 192:NP], "gv2", T.dW[:].indirect(T.tau[:, 12:24]), "dW dW0 tau", 192, f=GAT)
-    cp(T.gv[:, 0:192], "gv0", T.dW[:].indirect(T.tau[:, 0:12]), "dW dW0 tau", 192, f=GAT)
+    act(T.gv[:, 0:192], "gv0", T.dW[:].indirect(T.tau[:, 0:12]), "dW dW0 tau", 192, f=GAT)
     scan(T.sv[:, 0:192], "sv0 sv1", T.scC[:], T.gv[:, 0:192], "scC scCb gv0", A.add, A.max, 192)
     scan(T.sv[:, 192:NP], "sv2", T.scC[:], T.gv[:, 192:NP], "scC scCb gv2", A.add, A.max, 192)
     tt(T.vO[:], "vO", T.sv[:, 15:NP:16], Yb, "sv0 sv2 Yb0 Yb1 Yb2", A.add)
@@ -678,7 +857,7 @@ def rank_program(g, core, T, topo):
                     if kq.get(s, 0) < v:
                         queue[q].wait_ge(T.sem[s], v)
                         kq[s] = v
-                ins = t["fn"]()
+                ins = ([t["fn"]] if q == t["q"] else [fn for x, fn, c in t["alt"] if x == q])[0]()
                 if t["dma"]:
                     for x in ins:
                         x.then_inc(T.sem[t["dma"]], 16)
@@ -706,4 +885,5 @@ def rank_program(g, core, T, topo):
         g.wait_ge(T.sem[s], ARR)
     for s in ("tA", "tB", "tC"):
         g.wait_ge(T.sem[s], len(E8))
-    g.wait_ge(T.sem.loc, nloc[0])
+    for s, v in nloc.items():
+        g.wait_ge(T.sem[s], v)

@@ -8,7 +8,7 @@ DEAD = PWID + HI - 0.5
 BIG, MID, K4 = 8388608, 6291456, 8192
 NONE = 4096
 HOLD = 2.0 ** 50
-BW = 26
+BW = NK
 OFS, RND = 2048, 12582912.0
 GW, SW = 11, 88
 Q0, QB = 160, 1568
@@ -20,8 +20,8 @@ _sb = {
     "PW": (2 * PWID, _i), "ND": (2 * PWID, _b), "Xv": (128, _f), "Xw": (128, _f), "xB": (128, _h), "Zr": (128, _h), "Ur": (128, _f),
     "Zp": (128, _i), "Zd": (32, _i), "Zn": (32, _i), "H1": (128, _h), "Ld": (64, _h), "NU": (32, _u), "NP": (32, _u), "st": (160, _f),
     "HL0": (64, _b), "HL1": (64, _b), "CC": (128, _b), "R1": (NT, _h), "N0": (NT, _b), "N1": (NT, _b), "LP": (128, _h),
-    "pi": (4, _i), "pj": (12, _i), "pf": (48, _f), "jm": (128, _b), "mk": (128, _b), "md16": (128, _b), "m16": (128, _b), "bc": (192, _b), "xq": (256, _b),
-    "G2": (128, _h), "G3": (128, _h), "Gf": (128, _f), "Ib": (128, _b), "U2": (256, _h), "I16": (128, _h), "I2": (256, _h), "I1k": (128, _h),
+    "pi": (4, _i), "pj": (12, _i), "pf": (56, _f), "jm": (128, _b), "mk": (128, _b), "md16": (128, _b), "m16": (128, _b), "bc": (192, _b), "xq": (256, _b), "zb": (64, _b),
+    "G2": (128, _h), "G3": (128, _h), "Gf": (128, _f), "Ib": (128, _b), "U2": (384, _h), "I16": (128, _h), "I2": (256, _h), "I1k": (128, _h),
     "Ip": (128, _f), "EX": (512, _h), "cL": (144, _b), "LI": (144, _h), "S1": (44, _f), "sA": (336, _b), "Ms": (56, _f), "hk": (256, _f),
     "R1c": (SW, _f), "pt": (2 * SW, _b), "scC": (192, _f), "sc4": (128, _f), "tb": (256, _b), "oKi": (32, _i), "oRi": (32, _f), "oT": (72, _u),
     "Rs": (8 * BW, _f), "cQ": (8 * BW, _f), "cD": (72, _b), "cOw": (BW, _f), "cO16": (40, _h), "cS": (8, _f),
@@ -29,7 +29,7 @@ _sb = {
     "ex": (512, _h), "zz": (192, _f), "z2": (8 * BW, _h), "PK": (512, _f), "su": (96, _u), "cj": (48, _i),
     "W1": (640, _f), "W2": (640, _f), "sd": (128, _f), "MB1": (56, _h), "MB2": (56, _h), "RP1": (16, _i), "RP2": (32, _u), "RF": (32, _f),
     "Lm": (NK, _f), "wO": (NK, _u), "Lv0": (8, _f), "wV": (8, _u), "sm": (80, _f), "exv": (128, _f), "vW": (136, _f), "gv": (NP, _f),
-    "sv": (NP, _f), "vO": (NK, _f), "tau": (NK, _u), "dW": (136, _f),
+    "sv": (NP, _f), "vO": (NK, _f), "tau": (NK, _u), "dW": (136, _f), "ra": (6 * SW, _f), "Dd": (48, _f),
 }
 for _t, _n in (("O", 3), ("V", 1)):
     _sb.update({"pr" + _t: (128 * _n, _f), "pa" + _t: (128 * _n, _b), "u" + _t: (SW * _n, _f),
@@ -39,19 +39,19 @@ SCRATCH.update({"A1": ("dram", [128, 128], _h), "A2": ("dram", [128, 32], _h), "
 PSUM = ("o0", "o1", "o2", "vK", "vP", "vL", "rA", "rB")
 for _k in PSUM:
     SCRATCH[_k] = ("psum", [128, 512], _f)
-SEMAPHORES = ["sV", "sS", "sT", "sG", "ldA", "ldP", "ldZ", "ldD", "ldN", "ldT", "lpw", "lnd", "ln0", "lr1", "ln1", "st", "rq1", "rq2", "rp1", "rp2",
+SEMAPHORES = ["sV", "sS", "sT", "sG", "ldA", "ldP", "ldZ", "ldD", "ldN", "ldT", "lpw", "ld0", "ld1", "ln0", "lr1", "ln1", "st", "rq1", "rq2", "rp1", "rp2",
               "hA", "hB", "hC", "tA", "tB", "tC", "loc", "lt"]
 
 FLY, FLY_T = 2.0, (7.0, 7.5, 7.0)
 WAKE, FAC, CALL, LAT, GAT, SCA = 0.2, 1.3, 0.2, 1.5, 1.8, 4.6
 CASES = ((1.0, 0.2, 1.0, 1.0, 0.7), (0.8, 0.2, 0.7, 0.9, 1.2), (1.0, 0.2, 1.25, 1.0, 0.0), (1.15, 0.15, 0.9, 1.2, 1.5))
 WEIGHT = (1.0, 1.2, 1.0, 1.0)
-ROUNDS, MOVES, HEAT, FAR, SEED = 12, 42000, 0.3, 30, 1
+ROUNDS, MOVES, HEAT, FAR, SEED = 12, 60000, 0.3, 30, 1
 STAY, VPEN, FREE, PWA = 0.1, 0.3, 6, 0
-SOON, MARKS = 0.1, (("ND11", 0), ("suA", 0), ("msg1", 0), ("out1", 0), ("Yb2", 0))
-WON, WON0, WB = "SSSS", "SS", ("vK", "vP", "rA", "rB")
-CUT = ((0, 8), (8, 16), (16, 24))
-SC1, SC2, TAB, NDMA = "SSS", "SSS", 1.3, False
+SOON, MARKS = 0.1, (("paO0", 0), ("suA", 0), ("msg1", 0), ("out1", 0), ("Yb2", 0))
+WON, WON0, WB = "SSSS", "SS", ("vK", "vK", "rA", "rB")
+CUT, CUT1 = ((0, 8), (8, 16), (16, 24)), ((0, 24),)
+SC1, SC2, TAB, NDMA = "SSS", "SSS", 1.3, (1, 0)
 PLANS = {}
 
 
@@ -226,17 +226,21 @@ def plan(tasks):
         key = [-x for x in place(ways, post, pre, [-x for x in fin], pick, False)[0]]
     fin, pick = place(ways, pre, post, key, pick, False)
 
-    def run(seq, pick):
-        out = []
-        for calls, e in cases:
-            end, by, free, last = [0.0] * n, [-1] * n, {q: 0.0 for q in "VSTGY"}, {q: -1 for q in "VSTGY"}
-            for i in seq:
-                q, c = ways[i][pick[i]]
-                s, b = free[q], last[q]
+    def run(seq, pick, old=None, a=0):
+        out, first = [], {q: n for q in "VSTGY"}
+        for i in seq[:a]:
+            first[ways[i][pick[i]][0]] = i
+        todo = [(i,) + ways[i][pick[i]] for i in seq[a:]]
+        for k, (calls, e) in enumerate(cases):
+            end, by = (list(old[k][0]), list(old[k][1])) if a else ([0.0] * (n + 1), [n] * n)
+            last = dict(first)
+            for i, q, c in todo:
+                b = last[q]
+                s = end[b]
                 for d, w in e[i]:
                     if end[d] + w > s:
                         s, b = end[d] + w, d
-                end[i] = free[q] = s + c * calls[i]
+                end[i] = s + c * calls[i]
                 last[q], by[i] = i, b
             out.append((end, by))
         return sum((max(x[0]) + SOON * sum(x[0][k] for k in marks)) * w for x, w in zip(out, WEIGHT)), out
@@ -251,7 +255,7 @@ def plan(tasks):
     for r in range(MOVES):
         end, by = out[rnd(len(out))]
         i, pairs = marks[rnd(len(marks))] if rnd(2) else end.index(max(end)), []
-        while by[i] >= 0:
+        while by[i] < n:
             if by[i] not in dep[i]:
                 pairs.append((by[i], i))
             i = by[i]
@@ -286,7 +290,7 @@ def plan(tasks):
                 else:
                     keep.append(x)
             s2 = seq[:a] + go[::-1] + keep[::-1] + seq[b + 1:]
-        x, o2 = run(s2, p2)
+        x, o2 = run(s2, p2, out, a)
         if x <= cur - (HEAT * (1 - r / MOVES) + 0.005) * math.log((rnd(1000) + 1) / 1000):
             start = [o2[0][0][k] - ways[k][p2[k]][1] * cases[0][0][k] for k in range(n)]
             seq, pick, cur, out = sorted(s2, key=lambda k: round(start[k], 6)), p2, x, o2
@@ -297,6 +301,7 @@ def plan(tasks):
     for i in seq:
         order.setdefault(ways[i][pick[i]][0], []).append(i)
     PLANS[n] = order
+    PLANS["x"] = (ways, cases, seq, pick, out, dep)
     PLANS["t"], PLANS["low"] = max(out[0][0]), [round(max(x[0]), 2) for x in out]
     PLANS["dbg"] = ([dict(t, q=ways[i][pick[i]][0], cost=ways[i][pick[i]][1]) for i, t in enumerate(tasks)], [dict(p) for p in pre], post, tail, out[0][0])
     return order
@@ -423,15 +428,13 @@ def rank_program(g, core, T, topo):
 
     iota(T.pi[:], "pi", [[0, 4]], 0, 1, 4, False)
     iota(T.jm[:], "jm", [[0, 8], [1, 16]], 0, 0, 128)
-    iota(T.oRi[:, 0:13], "oRi", [[16, 13]], 0, 0, 13)
-    iota(T.rk[:, 24:26], "rkp", [[0, 2]], -1, 0, 2, False)
+    iota(T.oRi[:, 0:12], "oRi", [[0, 4], [-8, 3]], 16, 0, 12)
     iota(T.md16[:], "md16", [[1, 8], [0, 16]], 0, 0, 128)
     iota(T.mk[:], "mk", [[1, 128]], 0, -1, 128)
     iota(T.oKi[:], "oKi", [[1, 32]], 0, 0, 32, False)
     iota(T.cOw[:], "cOw", [[16, BW]], 128, 1, BW)
     iota(T.cD[:, 0:8], "cD", [[32, 4], [1, 2]], -2, 0, 8)
     iota(T.cD[:, 8:72], "cB", [[0, 8], [-32, 4], [-1, 2]], 0, 0, 64)
-    iota(tI, "tI", [[1, 32]], 0, 32, 32)
     iota(T.sA[:, 0:46], "sA", [[1, 46]], 0, 0, 46)
     iota(T.cL[:, 0:140], "cL", [[1, 140]], -12, 0, 140)
     iota(T.CC[:, 0:64], "CH", [[1024, 2], [0, 32]], 0, 32, 64)
@@ -451,8 +454,6 @@ def rank_program(g, core, T, topo):
     col = lambda k: T.pf[:, k:k + 1]
     p16, pg, pi_, pf_, p8, p5, par = [col(k) for k in range(7)]
     cv, g31, hL, cf, cl, c1, c2, lo, hi, pK, pK4, pL, m3, xm, m34, he, he2, f15, g15, p15, m89, k8, cA, cB = [col(k) for k in range(8, 32)]
-    act(cf, "cf", p5, "pf", scale=-1024.0, bias=float(base))
-    act(tI, "tI", tI, "tI cf", fn=F.Identity, bias=cf)
     for ap, nm, src, sc, bi in ((g31, "g31", pg, 3.0, 1.0), (pK4, "pK4", pf_, float(K4), RND - 3.0 * K4), (lo, "lo", par, float(PWID), 0.0),
                                 (hi, "hi", par, float(PWID), float(HI))):
         act(ap, nm, src, "pf", scale=sc, bias=bi)
@@ -464,16 +465,12 @@ def rank_program(g, core, T, topo):
     act(sg, "sg", p5, "pf", scale=-4.0, bias=-1.0)
     act(sg, "sg", pg, "pf sg", fn=F.Identity, scale=2.0, bias=sg)
     act(c2, "c2", pf_, "pf nl", fn=F.Identity, scale=-1.0, bias=nl)
-    act(c1, "c1", pi_, "pf nl", fn=F.Identity, scale=-1.0, bias=nl)
-    act(c1, "c1", p8, "pf c1", fn=F.Identity, scale=200.0, bias=c1)
-    oK, oR, oB8, oF = T.oT[:, 0:24], T.oT[:, 24:37], T.oT[:, 40:44], T.oT[:, 64:72]
+    act(c1, "c1", p8, "pf", fn=F.Identity, scale=-4.0, bias=pi_)
+    ts(c1, "c1", c1, "c1", -1.0, -1.0, A.max, A.mult)
+    act(c1, "c1", c1, "c1 nl", fn=F.Identity, bias=nl)
+    oK, oR, oB8, oF = T.oT[:, 0:24], T.oT[:, 24:36], T.oT[:, 40:44], T.oT[:, 64:72]
     m16 = T.m16[:]
-    jj, jq = T.oRi[:, 0:13], T.oRi[:, 16:29]
-    act(jj, "oRi", jj, "oRi pf", fn=F.Identity, bias=p16)
-    ts(T.ti[:, 0:13], "ti", jj, "oRi", (1 - BW) / 2, 1.0 / BW, A.add, A.mult)
-    act(jq, "jq", T.ti[:, 0:13], "ti", scale=-float(BW))
-    tt(jq, "jq", jq, jj, "jq oRi", A.add)
-    cp(oR, "oR", jq, "jq")
+    ts(oR, "oR", T.oRi[:, 0:12], "oRi pf", p16, None, A.add)
     ts(T.G2[:], "G2", T.md16[:], "md16 pf", pg, 2.0, A.is_equal, A.mult)
     ts(T.I16[:], "I16", T.mk[:], "mk", 0.0, None, A.is_equal)
     L2, U2 = T.U2[:, 0:128], T.U2[:, 128:256]
@@ -482,6 +479,7 @@ def rank_program(g, core, T, topo):
         act(b, nm + "b", p16, "pf", scale=x[2], bias=x[3])
         act(ap, nm, T.mk[:], "mk %sb" % nm, 128, F.Abs, bias=b)
         ts(ap, nm, ap, "%s %sh" % (nm, nm), h, 2.0, A.is_le, A.mult)
+    act(T.U2[:, 256:384], "U2n", U2, "U2", 128, half=True, scale=-1.0)
     act(T.cO16[:, 0:BW], "cO16", T.cOw[:], "cOw")
     cp(oK, "oK", T.oKi[:, 0:24], "oKi")
     ts(m16, "m16", T.jm[:], "jm pf", p16, None, A.is_equal)
@@ -511,11 +509,9 @@ def rank_program(g, core, T, topo):
     act(sgx, "sgx", xm, "xm sg", scale=sg)
     ts(T.sA[:, 96:140], "E2", T.sA[:, 1:45], "sA c1 sg", c1, sg, A.is_equal, A.mult)
     ts(T.sA[:, 288:332], "E4", T.sA[:, 2:46], "sA c1 sgx", c1, sgx, A.is_equal, A.mult)
-    tt(S2, "S2", T.sA[:, 96:140], T.sA[:, 288:332], "E2 E4", A.subtract, n=88)
-    tt(m89, "m89", T.m16[:, 8:9], T.m16[:, 9:10], "m16", A.add)
-    act(w89, "w89", m89, "m89 sg", scale=sg)
-    ts(T.sA[:, 240:284], "E3", T.sA[:, 0:44], "sA nl w89", nl, w89, A.is_equal, A.mult)
-    tt(S2a, "S2a", S2, T.sA[:, 240:284], "S2 E3", A.add, n=88)
+    tt(S2a, "S2a", T.sA[:, 96:140], T.sA[:, 288:332], "E2 E4", A.subtract, n=88)
+    act(w89, "w89", p8, "pf", scale=-1.0, bias=1.0)
+    act(S2, "S2", S2a, "S2a w89", scale=w89)
     fill(T.pt[:, 0:SW], "pt", 0, SW)
     fill(T.pt[:, 0:SW:22], "pt", -2 * TOP, 4)
     fill(T.pt[:, 12:SW:22], "pt", -2 * TOP, 4)
@@ -534,26 +530,31 @@ def rank_program(g, core, T, topo):
     act(he2, "he2", he, "he f15", scale=f15)
     act(T.hk[:, 128:256:16], "hk2", T.bc[:, 0:8], "one he2", scale=he2)
     act(wg, "wg", g15, "g15 sg", scale=sg)
-    ts(T.Ms[:, 0:44], "Ms", T.sA[:, 0:44], "sA nl wg", nl, wg, A.is_equal, A.mult)
+    ts(T.sA[:, 240:285], "E3", T.sA[:, 0:45], "sA nl wg", nl, wg, A.is_equal, A.mult)
+    tt(T.Ms[:, 0:44], "Ms", T.sA[:, 240:284], T.sA[:, 241:285], "E3", A.subtract, n=88)
     ts(T.Ms[:, 48:56], "Mf", T.oKi[:, 0:8], "oKi pf g15", pg, g15, A.is_equal, A.mult)
     for t, b in (("O", 0), ("O", 1), ("O", 2), ("V", 0)):
         c = QB * b + Q0
         fill(T["q" + t][:, c:c + 128 * GW:GW], "q%s%d" % (t, b), 0, 128)
-    act(k8, "k8", T.m16[:, 8:9], "m16", scale=1024.0)
-    act(cA, "cA", T.m16[:, 9:10], "m16 k8", fn=F.Identity, scale=HI - 1024.0, bias=k8)
-    act(k8, "k8", k8, "k8", scale=2.0)
+    m9 = col(47)
+    act(m9, "m9", T.m16[:, 9:10], "m16")
+    act(cA, "cA", T.m16[:, 8:9], "m16", scale=float(HI))
+    act(k8, "k8", T.m16[:, 8:9], "m16", scale=2048.0)
     act(cB, "cBd", T.m16[:, 9:10], "m16 k8", fn=F.Identity, scale=DEAD - 2048.0, bias=k8)
     for a, z in ((0, LO), (HI, PWID + LO), (PWID + HI, 2 * PWID)):
         iota(T.PW[:, a:z], "zP%d" % a, [[0, z - a]], 0, 0, z - a, False)
     fill(T.ND[:, 0:LO], "zN0", 0, LO)
-    for k, (a, c, cn) in enumerate(((HI, cA, "cA"), (PWID, cB, "cBd"), (PWID + HI, cB, "cBd"))):
-        act(T.ND[:, a:a + LO], "zN%d" % (k + 1), T.bc[:, 0:LO], "one " + cn, scale=c)
+    for k, a, c, cn in ((1, HI, cA, "cA"), (3, PWID + HI, cB, "cBd")):
+        act(T.ND[:, a:a + LO], "zN%d" % k, T.bc[:, 0:LO], "one " + cn, scale=c)
+    act(cf, "cf", T.m16[:, 8:9], "m16", scale=float(PWID))
+    act(T.ND[:, PWID:PWID + LO], "zN2", T.oKi[:, 0:LO], "oKi m9 cf", fn=F.Identity, scale=m9, bias=cf)
     PZ = {"PW": " zP0 zP%d zP%d" % (HI, PWID + HI), "ND": " zN0 zN1 zN2 zN3"}
     iota(T.xq[:, 0:128], "xe", [[16, 8], [0, 4], [1, 4]], 0, -1, 128)
     for f in range(4):
         ts(blk(T.EX, f), "EX%d" % f, T.xq[:, 0:128], "xe", -4.0 * f, None, A.is_equal)
     ts(T.LI[:, 0:140], "LI", T.cL[:, 0:140], "cL cl m3", cl, m3, A.is_equal, A.mult, n=70)
-    act(T.cO16[:, 32:40], "off", T.bc[:, 0:8], "one lo", scale=lo, bias=float(LO - 1))
+    off = col(48)
+    act(off, "off", par, "pf", scale=float(PWID), bias=float(LO - 1))
     dt = NT * (owners[7] - owners[6])
     act(cv, "cv", par, "pf", scale=float(PWID - dt), bias=float(LO - NT * owners[6]))
     for k, a in enumerate([rank] + owners[1:6:2]):
@@ -580,23 +581,28 @@ def rank_program(g, core, T, topo):
     ts(p15, "p15", p16, "pf", 14.5, None, A.is_lt)
     act(pK, "pK", p15, "p15", scale=-float(MID), bias=float(SA - 8192))
     act(pL, "pL", p15, "p15", scale=-float(MID))
-    act(pM, "pM", p15, "p15", scale=-float(MID), bias=-208.0 - 512.0 * SH)
+    act(pM, "pM", p15, "p15", scale=-float(MID), bias=512.0 * LO - 208.0)
     act(T.I1k[:], "I1k", T.I16[:], "I16", 128, scale=1024.0)
 
     def steps_rows(src, srcn, k, ext=(), aft=None):
         st, sn, HL, N, t = blk(T.st, k, 32), "st%d" % k, "HL%d" % k, "N%d" % k, 1 - k
         load("Y", "ln%d" % k, [(T[N][8 + h:9 + h, :], T.CC[0:32, 64 * h + 32 * t:64 * h + 32 * t + 32]) for h in range(2)], "CH CL", N + "c")
-        if k:
-            ts(xp, "xp", src, srcn, float(base - NT * owners[6]), None, A.add, ext=ext, aft=aft)
-            src, srcn = xp, "xp"
-        tt(T[HL][:, 0:32], HL, src, tI, srcn + " tI", A.subtract)
-        tt(st, sn, src, tI, srcn + " tI", A.subtract)
+        to = float(LO - NT * owners[6] if k else -SA)
+        ts(T[HL][:, 0:32], HL, src, srcn, to, None, A.add, ext=ext, aft=aft)
+        ts(st, sn, src, srcn, to, None, A.add, ext=ext, aft=aft)
         tt(T[HL][:, 32:64], HL + "b", st, T[HL][:, 0:32], sn + " " + HL, A.subtract)
         for h in range(2):
             load("Y", "ln%d" % k, [(T[N][4 * h:4 * h + 4, :], blk(T[HL], h, 32))], HL + "b" * h, N + "b" * h)
 
     def windows(t, R, Rn, N, banks, on):
+        if NDMA[t]:
+            c = PWID * t + LO
+            load("Y", "ln%d" % (1 - t), [(T[N][10:16, :], T.zb[0:96, :])], "zb", N + "d")
+            load("Y", "ld%d" % t, [(T.ND[16 * a:16 * a + 16, c:c + NT], T[N][0:16, :]) for a in range(8)], "%s %sb %sc %sd" % (N, N, N, N),
+                 "ND%d0 ND%d1" % (t, t), LAT + 0.6)
         for k, (bk, q) in enumerate(zip(banks, on)):
+            if NDMA[t] and k < 2:
+                continue
             h, c = k % 2, PWID * t + LO + 512 * (k % 2)
             w, sc, lhs, rhs, ins = (("ND", 1.0, T.m16[0:10, :], T[N], "m16 %s %sb %sc" % (N, N, N)), ("PW", 64.0, T.LP[0:20, :], T.R1, "LP " + Rn))[k // 2]
             for a in (0, 256):
@@ -610,21 +616,20 @@ def rank_program(g, core, T, topo):
     a = load("Y", "lpw", [(T.PW[16 * a:16 * a + 16, c:c + NT], T.planes[:]) for a in range(8)], "", "PW10 PW11", LAT + 1.0,
              *(([("lt", 3 * len(E8))], (sB, 1.5)) if PWA else ()))
     tasks[a]["odeps"].add(wr["X"])
+    if sum(NDMA):
+        fill(T.zb[:], "zb", 0, 64)
     steps_rows(T.Zn[:], "Zn", 0)
-    if NDMA:
-        load("Y", "ln0", [(T.N0[10:16, :], T.CC[0:96, 0:64])], "CH", "N0d")
-        load("Y", "lnd", [(T.ND[16 * a:16 * a + 16, c:c + NT], T.N0[0:16, :]) for a in range(8)], "N0 N0b N0c N0d", "ND10 ND11", LAT + 0.5)
-    else:
-        windows(1, "", "", "N0", ("vK", "vP"), WON0)
+    windows(1, "", "", "N0", ("vK", "vP"), WON0)
 
     su1, suA, suB, s1c = T.su[:, 0:24], T.su[:, 24:48], T.su[:, 48:56], T.su[:, 64:88]
 
     def slots(oh, ohn, su, sun):
         M, n7, n8 = 24, 7 * BW, 8 * BW
         mm([((T.rA[:, n7:n8], T.I16[:], T.cO16[:, 0:BW], True, True), M, 0)], "I16 cO16", "rA")
-        tt(oh[:], ohn, T.rk[:, 0:BW].indirect(oR), T.cQ[:], "rk rkp oR " + CQ, A.is_equal, n8, f=GAT)
+        tt(oh[:], ohn, T.rk[:, 0:32].indirect(oR), T.cQ[:], "rka rkb oR " + CQ, A.is_equal, n8, f=GAT)
         mm([((T.rA[:, 0:n7], L2, oh[:, 0:n7], True, False), n7, 0), ((T.rA[:, 1:n7], U2, oh[:, 0:n7 - 1], False, False), n7, 0),
-            ((T.rA[:, 0:n7:BW], ones, T.cD[0:1, 0:7], False, True), 7, 0)], "L2 U2 one cD " + ohn, "rA")
+            ((T.rA[:, M:n7:M], T.U2[:, 256:384], oh[:, M - 1:n7 - 1:M], False, False), 6, 0),
+            ((T.rA[:, 0:n7:M], ones, T.cD[0:1, 0:7], False, True), 7, 0)], "L2 U2 U2n one cD " + ohn, "rA")
         sc = T.rA[:, 256:256 + n8]
         scan(sc, "sc", T.Rs[:], T.rA[:, 0:n8], "Rs Rh rA", A.mult, A.add, n8)
         tt(T.z2[:], "z2", sc, oh[:], "sc rA " + ohn, A.mult, n8)
@@ -670,36 +675,45 @@ def rank_program(g, core, T, topo):
         PWn, NDn = [" ".join(x + a + h for a in ("01" if t == "V" else "1") for h in "01") + PZ[x] for x in ("PW", "ND")]
         tt(pr, "pr" + n, T.PW[:, c0:].indirect(w), X, "%s w%s %s" % (PWn, n, xn), A.mult, 128, f=GAT)
         act(pa, "pa" + n, T.ND[:, c0:].indirect(w), "%s w%s" % (NDn, n), 128, f=GAT)
-        if s:
+        carry = s and t == "V"
+        if carry:
             turn(t, b, pP, T.Ms[:, 0:44], bP, False)
-        mm([((pP, pa, S2 if s else S2a, not s, True), 44, 0)], "S2 S2a pa" + n, bP)
+        mm([((pP, pa, S2 if carry else S2a, not carry, True), 44, 0)], ("S2" if carry else "S2a") + " pa" + n, bP)
         mm([((pK_, pr, T.S1[:], True, True), 44, 1)], "S1 pr" + n, bK)
         scan(u, "u" + n, T[bK][:, 0:SW], T.R1c[:], "R1c " + bK, A.add, A.max, SW)
+        if s < 2 and t == "O":
+            r = blk(T.ra, 3 * s + b, SW)
+            scan(r, "r%d%d" % (s, b), T[bP][:, cP:cP + SW], u, "%s u%s" % (bP, n), A.subtract, A.min, SW)
+            ts(w, "w" + n, T.ra[:, SW * (3 * s + b) + GW - 1:SW * (3 * s + b + 1):GW], "r%d%d" % (s, b), -float(PWID), float(HI), A.add, A.min)
+            return
         scan(T["q" + t][:, c:c + 16 * SW:16], "q" + n, T[bP][:, cP:cP + SW], u, "%s u%s" % (bP, n), A.subtract, A.min, SW)
-        places = T["q" + t][:, c + Q0:c + 16 * SW:16 * GW]
-        if s < 2 and t == "V":
-            ts(w, "w" + n, places, "lo hi q" + n, lo, hi, A.max, A.min)
-        elif s < 2:
-            ts(w, "w" + n, places, "q" + n, -float(PWID), float(HI), A.add, A.min)
+        if s < 2:
+            ts(w, "w" + n, T.qV[:, Q0:16 * SW:16 * GW], "lo hi q" + n, lo, hi, A.max, A.min)
 
     def own(out, c, on, bias):
         for s in range(3):
             for b in range(3):
                 step("O", b, s, blk(T.XT if s == 1 else T.X16, b), "XT" if s == 1 else "X16", "o%d" % b, "o%d" % b)
+            if s < 2:
+                pl, D, rn = T.ra[:, 3 * SW * s + GW - 1:3 * SW * (s + 1):GW], blk(T.Dd, s, 24), " r%d0 r%d1 r%d2" % (s, s, s)
+                ts(D, "D%d" % s, pl, rn, float(PWID), DEAD, A.max, A.min)
+                tt(D, "D%d" % s, pl, D, "D%d" % s + rn, A.subtract)
+        if bias is not None:
+            act(blk(T.Dd, 1, 24), "D1", blk(T.Dd, 1, 24), "D1 pK", fn=F.Identity, bias=bias)
         for b in range(3):
-            bk = "o%d" % b
+            bk, pl = "o%d" % b, T.qO[:, QB * b + Q0:QB * b + 16 * SW:16 * GW]
+            tt(pl, "qO%d" % b, pl, blk(T.Dd, b, 8), "D0 qO%d" % b, A.add)
             turn("O", b, T[bk][:, 192:200], T.Ms[:, 48:56], bk, True)
-            act(blk(out, b + c, 8), on + str(b), T[bk][:, 192:200], bk + " pK", fn=F.Identity, bias=bias)
+            tt(blk(out, b + c, 8), on + str(b), T[bk][:, 192:200], blk(T.Dd, 3 + b, 8), bk + " D1", A.add)
 
     def arrive(MB, mn, sem, sent):
-        mm([((T.vL[:, 0:8], T.I16[:], T.cO16[:, 32:40], True, False), 8, 0)], "I16 off", "vL")
         a = mm([((T.vP[:, 128 + f:256:4], blk(T.EX, f), MB[:, 24:56], True, True), 32, 0) for f in range(4)],
                "EX0 EX1 EX2 EX3 " + mn, "vP", [(sem, ARR)], (sent, FLY))
-        b = mm([((T.vL[:, 0:8], T.LI[:, 12 - 4 * c:140 - 4 * c], MB[:, 24 + c:56:4], False, c == 3), 8, 0) for c in range(4)],
+        b = mm([((T.vL[:, 0:8], T.LI[:, 12 - 4 * c:140 - 4 * c], MB[:, 24 + c:56:4], c == 0, c == 3), 8, 0) for c in range(4)],
                "LI " + mn, "vL", [(sem, ARR)], (sent, FLY))
         tasks[b]["odeps"].add(a)
         act(T.Xv[:], "Xv", T.vP[:, 128:256], "vP xm m3", 128, F.Identity, scale=xm, bias=m3)
-        ts(T.wV[:], "wV0", T.vL[:, 0:8], "vL lo hi", lo, hi, A.max, A.min)
+        ts(T.wV[:], "wV0", T.vL[:, 0:8], "vL off hi", off, hi, A.add, A.min)
 
     def visitors(back):
         act(T.Zr[:], "Zr", T.Xv[:].indirect(T.oT[:, 48:56]), "Xv rot", 128, f=GAT)
@@ -713,12 +727,13 @@ def rank_program(g, core, T, topo):
         if back:
             turn("V", 0, T.vL[:, 0:8], T.Ms[:, 48:56], "vL", True)
 
-    ts(T.rk[:, 0:24], "rk", T.L0[:], "L0", 10, None, sh)
+    ts(T.rk[:, 16:32], "rka", T.L0[:, 0:16], "L0", 10, None, sh)
+    ts(T.rk[:, 0:16], "rkb", T.L0[:, 8:24], "L0", 10, None, sh)
     slots(T.oh1, "oh1", su1, "su1")
     ts(T.ti[:, 0:24], "ti", T.L0[:], "L0", 1023, None, an)
     pack(("vL", "o2", "vL"))
-    for b in range(3):
-        scatter(SC1[b], T.W1, "W1", blk(T.su, b, 8), blk(T.PK, b), "PK%d su1" % b, 128)
+    for q, (a, z) in zip(SC1, CUT1):
+        scatter(q, T.W1, "W1", T.su[:, a:z], T.PK[:, 16 * a:16 * z], " ".join("PK%d" % b for b in range(a // 8, (z + 7) // 8)) + " su1", 16 * (z - a))
     message(T.W1, "W1", T.MB1, "msg1")
     s1 = send(T.MB1, "msg1", "rq1", 8, 0, 8, 32)
     act(m34, "m34", xm, "m3 xm", fn=F.Identity, scale=-float(OFS), bias=m3)
@@ -749,10 +764,14 @@ def rank_program(g, core, T, topo):
     act(T.scC[:, 0:128], "scC", T.rA[:, 0:128], "rA", 128)
     act(T.scC[:, 128:192], "scCb", T.scC[:, 0:64], "scC")
 
-    ts(T.wO[:], "wO0 wO1 wO2", T.L0[:], "L0", float(-SH), float(HI), A.add, A.min)
-    own(T.Lm, 0, "Lm", float(SA))
-    ts(T.rk[:, 0:24], "rk", T.Lm[:], "Lm0 Lm1 Lm2", -511.75, 1.0 / 1024, A.add, A.mult)
-    cp(T.ci[:, 0:24], "ci", T.Lm[:], "Lm0 Lm1 Lm2")
+    cj, cd, cr = T.cj[:, 0:24], T.cj[:, 24:48], T.ci[:, 24:32]
+    ts(cj, "cj", T.L0[:], "L0", 8192.0 - base, None, A.add)
+    ts(cj, "cj", cj, "cj", 8191, None, an)
+    ts(T.wO[:], "wO0 wO1 wO2", cj, "cj", float(LO), float(HI), A.add, A.min)
+    own(T.Lm, 0, "Lm", None)
+    ts(T.rk[:, 16:32], "rka", T.Lm[:, 0:16], "Lm0 Lm1", SA - 511.75, 1.0 / 1024, A.add, A.mult)
+    ts(T.rk[:, 0:16], "rkb", T.Lm[:, 8:24], "Lm1 Lm2", SA - 511.75, 1.0 / 1024, A.add, A.mult)
+    ts(T.ci[:, 0:24], "ci", T.Lm[:], "Lm0 Lm1 Lm2", 8192.0 - PWID - LO, None, A.add)
     ts(T.ti[:, 0:24], "ti", T.ci[:, 0:24], "ci", 1023, None, an)
     slots(T.ohA, "ohA", suA, "suA")
     pack(("o0", "o1", "o2"))
@@ -793,8 +812,10 @@ def rank_program(g, core, T, topo):
     smA, vB, Yb = T.sm[:, 0:24], T.sm[:, 32:40], T.sm[:, 40:64]
     ts(s1c, "s1c", su1, "su1", 128.0, None, A.min)
     cp(smA, "smA", suA, "suA")
-    home, cj, cd = T.oh1[:, 7 * BW:7 * BW + 24], T.cj[:, 0:24], T.cj[:, 24:48]
-    act(vB, "vB", T.RP1[:, 2:10], "rkB", scale=512.0, bias=-640.0)
+    home = T.oh1[:, 7 * BW:7 * BW + 24]
+    ts(cr, "cr", T.RP1[:, 2:10], "rkB", 8192.0 - base, None, A.add)
+    ts(cr, "cr", cr, "cr", 8191, None, an)
+    act(vB, "vB", cr, "cr", scale=512.0, bias=-640.0)
     tt(vB, "vB", vB, T.zz[:, 135:192:8], "vB zz", A.add)
     tt(T.exv[:], "exv", vB.indirect(T.oT[:, 0:8]), m16, "oK vB m16", A.mult, 128, f=GAT)
     mm([((T.rB[:, 0:128], T.Gf[:], T.exv[:], True, True), 128, 1)], "Gf exv", "rB")
@@ -802,7 +823,8 @@ def rank_program(g, core, T, topo):
     for b in range(3):
         act(blk(T.gv, b), "gv%d" % b, T.vW[:].indirect(T.su[:, 64 + 8 * b:72 + 8 * b]), "vW vW0 s1c", 128, f=GAT)
         scan(blk(T.sv, b), "sv%d" % b, T.scC[:, 0:128], blk(T.gv, b), "scC gv%d" % b, A.add, A.max, 128)
-    tt(T.vO[:], "vO", T.Lm[:], home, "Lm0 Lm1 Lm2 oh1", A.mult)
+    ts(cd, "cd", T.ci[:, 0:24], "ci", 8191, None, an)
+    tt(T.vO[:], "vO", cd, home, "cd oh1", A.mult)
     act(T.vO[:], "vO", T.vO[:], "vO pM", fn=F.Identity, scale=512.0, bias=pM)
     tt(T.vO[:], "vO", T.vO[:], T.sv[:, 15:NP:16], "vO sv0 sv1 sv2", A.add)
     ts(T.wO[:], "wO0 wO1 wO2", T.vO[:], "vO", 1.0 / 512, float(HI), A.mult, A.min)

import math
from concourse.bass import DstId, RemoteDMATransfer
from concourse.mybir import AluOpType as A, ActivationFunctionType as F

NT, NP, NK = 1024, 384, 24
LO, HI, PWID = 8, 1032, 1040
DEAD = PWID + HI - 0.5
BIG, MID, K4 = 8388608, 6291456, 8192
NONE = 4096
HOLD = 2.0 ** 50
BW = NK
OFS, RND = 2048, 12582912.0
GW, SW = 11, 88
Q0, QB = 160, 1568
KV, TOP = 16384.0, 2.0 ** 40

_f, _h, _b, _i, _u = "float32", "float16", "bfloat16", "int32", "uint16"
_sb = {
    "X": (NP, _i), "X16": (NP, _h), "XT": (NP, _h), "Yt": (128, _i), "Xp": (NP, _h), "L0": (NK, _i),
    "PW": (2 * PWID, _i), "ND": (2 * PWID, _b), "Xv": (128, _f), "Xw": (128, _f), "xB": (128, _h), "Zr": (128, _h), "Ur": (128, _f),
    "Zp": (128, _i), "Zd": (32, _i), "Zn": (32, _i), "H1": (128, _h), "Ld": (64, _h), "NU": (32, _u), "NP": (32, _u), "st": (160, _f),
    "HL0": (64, _b), "HL1": (64, _b), "CC": (128, _b), "R1": (NT, _h), "N0": (NT, _b), "N1": (NT, _b), "LP": (128, _h),
    "pi": (4, _i), "pj": (12, _i), "pf": (56, _f), "jm": (128, _b), "mk": (128, _b), "md16": (128, _b), "m16": (128, _b), "bc": (192, _b), "xq": (256, _b), "zb": (64, _b),
    "G2": (128, _h), "G3": (128, _h), "Gf": (128, _f), "Ib": (128, _b), "U2": (384, _h), "I16": (128, _h), "I2": (256, _h), "I1k": (128, _h),
    "Ip": (128, _f), "EX": (512, _h), "cL": (144, _b), "LI": (144, _h), "S1": (44, _f), "sA": (336, _b), "Ms": (56, _f), "hk": (256, _f),
    "R1c": (SW, _f), "pt": (2 * SW, _b), "scC": (192, _f), "sc4": (128, _f), "tb": (256, _b), "oKi": (32, _i), "oRi": (32, _f), "oT": (72, _u),
    "Rs": (8 * BW, _f), "cQ": (8 * BW, _f), "cD": (72, _b), "cOw": (BW, _f), "cO16": (40, _h), "cS": (8, _f),
    "rk": (32, _i), "ci": (32, _i), "ti": (32, _i), "rkB": (8, _i), "oh1": (8 * BW, _h), "ohA": (8 * BW, _h), "ohB": (64, _h), "inj": (NP, _f),
    "ex": (512, _h), "zz": (192, _f), "z2": (8 * BW, _h), "PK": (512, _f), "su": (96, _u), "cj": (48, _i),
    "W1": (640, _f), "W2": (640, _f), "sd": (128, _f), "MB1": (56, _h), "MB2": (56, _h), "RP1": (16, _i), "RP2": (32, _u), "RF": (32, _f),
    "Lm": (NK, _f), "wO": (NK, _u), "Lv0": (8, _f), "wV": (8, _u), "sm": (80, _f), "exv": (128, _f), "vW": (136, _f), "gv": (NP, _f),
    "sv": (NP, _f), "vO": (NK, _f), "tau": (NK, _u), "dW": (136, _f), "ra": (6 * SW, _f), "Dd": (48, _f),
}
for _t, _n in (("O", 3), ("V", 1)):
    _sb.update({"pr" + _t: (128 * _n, _f), "pa" + _t: (128 * _n, _b), "u" + _t: (SW * _n, _f),
                "q" + _t: (QB * _n, _f), "e" + _t: (128 * _n, _f)})
SCRATCH = {_k: ("sbuf", [128, _v[0]], _v[1]) for _k, _v in _sb.items()}
SCRATCH.update({"A1": ("dram", [128, 128], _h), "A2": ("dram", [128, 32], _h), "A3": ("dram", [128, 32], _u)})
PSUM = ("o0", "o1", "o2", "vK", "vP", "vL", "rA", "rB")
for _k in PSUM:
    SCRATCH[_k] = ("psum", [128, 512], _f)
SEMAPHORES = ["sV", "sS", "sT", "sG", "ldA", "ldP", "ldZ", "ldD", "ldN", "ldT", "lpw", "ld0", "ld1", "ln0", "lr1", "ln1", "st", "rq1", "rq2", "rp1", "rp2",
              "hA", "hB", "hC", "tA", "tB", "tC", "loc", "lt"]

FLY, FLY_T = 2.0, (7.0, 7.5, 7.0)
WAKE, FAC, CALL, LAT, GAT, SCA = 0.2, 1.3, 0.2, 1.5, 1.8, 4.6
CASES = ((1.0, 0.2, 1.0, 1.0, 0.7), (0.8, 0.2, 0.7, 0.9, 1.2), (1.0, 0.2, 1.25, 1.0, 0.0), (1.15, 0.15, 0.9, 1.2, 1.5))
WEIGHT = (1.0, 1.2, 1.0, 1.0)
ROUNDS, MOVES, HEAT, FAR, SEED = 12, 60000, 0.3, 30, 1
STAY, VPEN, FREE, PWA = 0.1, 0.3, 6, 0
SOON, MARKS = 0.1, (("paO0", 0), ("suA", 0), ("msg1", 0), ("out1", 0), ("Yb2", 0))
WON, WON0, WB = "SSSS", "SS", ("vK", "vK", "rA", "rB")
CUT, CUT1 = ((0, 8), (8, 16), (16, 24)), ((0, 24),)
SC1, SC2, TAB, NDMA = "SSS", "SSS", 1.3, (1, 0)
PLANS = {}


def wiring(T, topo, core):
    mine = [c for c in T.cores if c == core or topo.may_write(core, c)]
    other = [c for c in T.cores if c not in mine]
    i = mine.index(core)
    peers = [mine[i ^ k] for k in range(1, len(mine))]
    partner = dict(zip(mine, other))
    rel = [c for c in topo.cores_of(core) if c not in T.cores and topo.may_write(c, partner[core])]
    rel.sort(key=lambda c: (topo.die(c) != topo.die(core), c))
    return peers, partner, rel[:2]


def transfer(topo, src_core, dst_core, es, sem, s_ap, d_ap):
    rid, pid = topo.addr(dst_core, src_core)
    return RemoteDMATransfer(dst_ids=[DstId(rid=rid, pnc=pid)], dma_engine_mask=sum(1 << e for e in es), remote_sem=sem, src=s_ap, dst=d_ap)


def relay_program(g, core, T, topo, owner):
    peers, partner, rel = wiring(T, topo, owner)
    d = partner[owner]
    es = topo.engines(core, d)
    pieces = ((("A", T.A1, T.A1),), (("C", T.A3, T.NP), ("B", T.A2, T.A2)))[rel.index(core)]
    for s, src, dst in pieces:
        g.wait_ge(T.sem["h" + s], len(es))
        g.remote_dma_fused([transfer(topo, core, d, es, T.sem["t" + s], src[:], dst[:])], local_sem=T.sem.loc)
    g.wait_ge(T.sem.loc, len(es) * len(pieces))


def place(ways, pre, succ, key, pick, free):
    n = len(ways)
    pend = [len(x) for x in pre]
    fin, busy, pick = [0.0] * n, {q: [] for q in "VSTGY"}, list(pick)
    ready = [(key[i], i) for i in range(n) if pend[i] == 0]
    while ready:
        i = min(ready)
        ready.remove(i)
        i = i[1]
        s0, best = 0.0, None
        for d, w in pre[i]:
            if fin[d] + w > s0:
                s0 = fin[d] + w
        for k in (range(len(ways[i])) if free else (pick[i],)):
            q, c = ways[i][k]
            s, l = s0, busy[q]
            lo, hi = 0, len(l)
            while lo < hi:
                mid = (lo + hi) // 2
                lo, hi = (mid + 1, hi) if l[mid][1] <= s else (lo, mid)
            while lo < len(l) and s + c > l[lo][0]:
                s = l[lo][1]
                lo += 1
            x = s + c + (STAY if k != pick[i] else 0.0) + (VPEN if q == "V" else 0.0)
            if best is None or x < best[0]:
                best = (x, k, s, c, l, lo)
        x, pick[i], s, c, l, lo = best
        fin[i] = s + c
        l.insert(lo, (s, s + c))
        for x, w in succ[i]:
            pend[x] -= 1
            if pend[x] == 0:
                ready.append((key[x], x))
    return fin, pick


def plan(tasks):
    n = len(tasks)
    if n in PLANS:
        return PLANS[n]
    pre = []
    for t in tasks:
        p = {d: 0.0 for d in t["odeps"]}
        p.update({d: WAKE + tasks[d]["lat"] for d in t["deps"]})
        if t["aft"]:
            p[t["aft"][0]] = max(p.get(t["aft"][0], 0.0), t["aft"][1])
        pre.append(p)
    post = [{} for _ in tasks]
    for i, p in enumerate(pre):
        for d, w in p.items():
            post[d][i] = w
    tail = [0.0] * n
    for i in range(n - 1, -1, -1):
        tail[i] = tasks[i]["cost"] + max([0.0] + [tail[x] + w for x, w in post[i].items()])
    cases = []
    for calls, wake, way, ind in CASES:
        e = [[(d, 0.0) for d in t["odeps"]] + [(d, wake + way * tasks[d]["lat"]) for d in t["deps"]] +
             ([(t["aft"][0], way * t["aft"][1])] if t["aft"] else []) for t in tasks]
        cases.append(([way * way if t["dma"] else calls * ind if t["ind"] else calls for t in tasks], e))
    ways = [[(t["q"], t["cost"])] + [(q, c) for q, fn, c in t["alt"]] for t in tasks]
    lpre, lpost = [list(x.items()) for x in pre], [list(x.items()) for x in post]
    flex = [i for i in range(n) if len(ways[i]) > 1]

    def length(start, pick):
        total, seq = 0.0, sorted(range(n), key=lambda j: (start[j], j))
        for calls, e in cases:
            end, free = [0.0] * n, {q: 0.0 for q in "VSTGY"}
            for i in seq:
                q, c = ways[i][pick[i]]
                s = free[q]
                for d, w in e[i]:
                    if end[d] + w > s:
                        s = end[d] + w
                end[i] = free[q] = s + c * calls[i]
            total += max(end)
        return total
    key, best, bkey, seed, low, pick, bpick = [-x for x in tail], None, None, 1, 0.0, [0] * n, None
    for r in range(ROUNDS):
        fin, pick = place(ways, lpre, lpost, key, pick, r % FREE == 0)
        if best is None or max(fin) < max(best) + 1.0:
            start = [fin[i] - ways[i][pick[i]][1] for i in range(n)]
            x = max(fin) + length(start, pick)
            if best is None or x < low:
                best, bkey, low, bpick = fin, start, x, pick
        key = [-x for x in place(ways, lpost, lpre, [-x for x in fin], pick, False)[0]]
        if r % 3 == 2:
            key, pick = [], list(bpick)
            for x in range(FLIPS):
                seed = seed * 16807 % 2147483647
                i = flex[seed % len(flex)]
                pick[i] = (pick[i] + 1 + seed // 1024 % (len(ways[i]) - 1)) % len(ways[i])
            for x in bkey:
                seed = seed * 16807 % 2147483647
                key.append(x + SHAKE * seed / 2147483647)
            i = seed % n
            seed = seed * 16807 % 2147483647
            pull, todo, seen = PULL * seed / 2147483647, [i], {i}
            while todo:
                j = todo.pop()
                key[j] -= pull
                for x in post[j]:
                    if x not in seen and bkey[x] < bkey[i] + SPAN:
                        seen.add(x)
                        todo.append(x)
    order = {}
    for i in sorted(range(n), key=lambda j: (bkey[j], j)):
        order.setdefault(ways[i][bpick[i]][0], []).append(i)
    PLANS[n] = order
    PLANS["t"] = max(best)
    PLANS["low"] = low
    PLANS["x"] = (ways, lpre, lpost, cases, bkey, bpick)
    PLANS["dbg"] = ([dict(t, q=ways[i][bpick[i]][0], cost=ways[i][bpick[i]][1]) for i, t in enumerate(tasks)], pre, post, tail, best)
    return order


def plan(tasks):
    n = len(tasks)
    if n in PLANS:
        return PLANS[n]
    ways = [[(t["q"], t["cost"])] + [(q, c) for q, fn, c in t["alt"]] for t in tasks]
    cases = []
    for calls, wake, way, ind, hold in CASES:
        e = []
        for t in tasks:
            p = {d: 0.0 for d in t["odeps"]}
            p.update({d: wake + way * tasks[d]["lat"] for d in t["deps"]})
            if t["aft"]:
                d, w = t["aft"]
                p[d] = max(p.get(d, 0.0), way * w - (hold if tasks[d]["tab"] else 0.0))
            e.append(list(p.items()))
        cases.append(([1.0 + hold / t["cost"] if t["tab"] == 1 else way * way if t["dma"] else calls * ind if t["ind"] else calls for t in tasks], e))
    pre, post = cases[0][1], [[] for _ in tasks]
    for i, p in enumerate(pre):
        for d, w in p:
            post[d].append((i, w))
    tail = [0.0] * n
    for i in range(n - 1, -1, -1):
        tail[i] = tasks[i]["cost"] + max([0.0] + [tail[x] + w for x, w in post[i]])
    key, pick, dep = [-x for x in tail], [0] * n, [set(d for d, w in p) for p in pre]
    for r in range(ROUNDS):
        fin, pick = place(ways, pre, post, key, pick, r % FREE == 0)
        key = [-x for x in place(ways, post, pre, [-x for x in fin], pick, False)[0]]
    fin, pick = place(ways, pre, post, key, pick, False)

    def run(seq, pick, old=None, a=0):
        out, first = [], {q: n for q in "VSTGY"}
        for i in seq[:a]:
            first[ways[i][pick[i]][0]] = i
        todo = [(i,) + ways[i][pick[i]] for i in seq[a:]]
        for k, (calls, e) in enumerate(cases):
            end, by = (list(old[k][0]), list(old[k][1])) if a else ([0.0] * (n + 1), [n] * n)
            last = dict(first)
            for i, q, c in todo:
                b = last[q]
                s = end[b]
                for d, w in e[i]:
                    if end[d] + w > s:
                        s, b = end[d] + w, d
                end[i] = s + c * calls[i]
                last[q], by[i] = i, b
            out.append((end, by))
        return sum((max(x[0]) + SOON * sum(x[0][k] for k in marks)) * w for x, w in zip(out, WEIGHT)), out
    seed, marks = [SEED], [[k for k in range(n) if tasks[k]["nm"] == nm][m] for nm, m in MARKS]

    def rnd(m):
        seed[0] = seed[0] * 16807 % 2147483647
        return seed[0] * m // 2147483647
    seq = sorted(range(n), key=lambda j: (fin[j] - ways[j][pick[j]][1], j))
    cur, out = run(seq, pick)
    best = (cur, seq, pick, out)
    for r in range(MOVES):
        end, by = out[rnd(len(out))]
        i, pairs = marks[rnd(len(marks))] if rnd(2) else end.index(max(end)), []
        while by[i] < n:
            if by[i] not in dep[i]:
                pairs.append((by[i], i))
            i = by[i]
        if not pairs:
            continue
        j, i = pairs[rnd(len(pairs))]
        s2, p2, kind, far = seq, pick, rnd(10), rnd(2) * rnd(FAR)
        a, b = seq.index(j), seq.index(i)
        if kind < 3:
            x = (j, i)[rnd(2)]
            if len(ways[x]) < 2:
                continue
            p2 = list(pick)
            p2[x] = (pick[x] + 1 + rnd(len(ways[x]) - 1)) % len(ways[x])
        elif kind < 7:
            b = min(n - 1, b + far)
            moved, go, keep = {j}, [j], []
            for x in seq[a + 1:b + 1]:
                if dep[x] & moved:
                    moved.add(x)
                    go.append(x)
                else:
                    keep.append(x)
            s2 = seq[:a] + keep + go + seq[b + 1:]
        else:
            a = max(0, a - far)
            need, go, keep = set(dep[i]), [i], []
            for x in reversed(seq[a:b]):
                if x in need:
                    need |= dep[x]
                    go.append(x)
                else:
                    keep.append(x)
            s2 = seq[:a] + go[::-1] + keep[::-1] + seq[b + 1:]
        x, o2 = run(s2, p2, out, a)
        if x <= cur - (HEAT * (1 - r / MOVES) + 0.005) * math.log((rnd(1000) + 1) / 1000):
            start = [o2[0][0][k] - ways[k][p2[k]][1] * cases[0][0][k] for k in range(n)]
            seq, pick, cur, out = sorted(s2, key=lambda k: round(start[k], 6)), p2, x, o2
            if cur < best[0]:
                best = (cur, seq, pick, out)
    cur, seq, pick, out = best
    order = {}
    for i in seq:
        order.setdefault(ways[i][pick[i]][0], []).append(i)
    PLANS[n] = order
    PLANS["x"] = (ways, cases, seq, pick, out, dep)
    PLANS["t"], PLANS["low"] = max(out[0][0]), [round(max(x[0]), 2) for x in out]
    PLANS["dbg"] = ([dict(t, q=ways[i][pick[i]][0], cost=ways[i][pick[i]][1]) for i, t in enumerate(tasks)], [dict(p) for p in pre], post, tail, out[0][0])
    return order


def rank_program(g, core, T, topo):
    rank = T.rank_of(core)
    if rank is None:
        for c in T.cores:
            if c in topo.cores_of(core) and core in wiring(T, topo, c)[2]:
                relay_program(g, core, T, topo, c)
        return
    peers, partner, rel = wiring(T, topo, core)
    owners = [T.cores.index(c) for s in peers + [core] for c in (partner[s], s)]
    base = NT * rank
    SH = base - LO
    SA = SH - PWID
    tasks, wr, rd = [], {}, {}
    V, S, E = g.vector, g.scalar, g.tensor
    cy = 0.00083 * FAC

    def add(q, fn, reads, writes, cost, ext=(), aft=None, ind=False, alt=()):
        i, reads, writes = len(tasks), reads.split(), writes.split()
        deps, odeps = set(), set()
        for b in reads:
            if b in wr:
                deps.add(wr[b])
            if b in PSUM:
                deps.update(x for x in rd.get(b, ()) if tasks[x]["q"] != q or alt or tasks[x]["alt"])
        for b in writes:
            if b in wr:
                (odeps if q == "T" and tasks[wr[b]]["q"] == "T" else deps).add(wr[b])
            deps.update(rd.get(b, ()))
        tasks.append(dict(nm=(writes + ["-"])[0], q=q, fn=fn, deps=deps, odeps=odeps, cost=cost, ext=tuple(ext), aft=aft, dma=None, lat=0.0, ind=ind,
                          alt=tuple(alt), tab=0))
        for b in reads:
            rd.setdefault(b, []).append(i)
        for b in writes:
            wr[b] = i
            rd[b] = []
        return i

    def vop(fn, ins, on, n=64, ext=(), aft=None, f=1):
        return add("V", lambda: [fn()], ins, on, 0.05 + cy * n * f if f != 1 else cy * max(64, n), ext, aft, f != 1)

    def ts(out, on, in0, ins, s1, s2, op0, op1=None, n=64, ext=(), aft=None):
        if op1 is None:
            return vop(lambda: V.tensor_scalar(out, in0, s1, None, op0), ins, on, n, ext, aft)
        return vop(lambda: V.tensor_scalar(out, in0, s1, s2, op0, op1), ins, on, n, ext, aft)

    def tt(out, on, in0, in1, ins, op, n=64, ext=(), aft=None, f=1):
        return vop(lambda: V.tensor_tensor(out, in0, in1, op), ins, on, n, ext, aft, f)

    def cp(out, on, in_, ins, n=64, f=1):
        return vop(lambda: V.tensor_copy(out, in_), ins, on, n, f=f)

    def scan(out, on, d0, d1, ins, op0, op1, n=64):
        return vop(lambda: V.tensor_tensor_scan(out, d0, d1, 0.0, op0, op1), ins, on, n)

    def act(out, on, in_, ins, n=64, fn=F.Copy, f=1, half=False, alt=None, **kw):
        if alt is None and (fn is F.Copy or fn is F.Identity):
            alt = [("V", lambda: [V.tensor_scalar(out, in_, kw.get("scale", 1.0), kw.get("bias", 0.0), A.mult, A.add)],
                    0.05 + cy * n * f if f != 1 else cy * max(64, n // 2 if half else n))]
        return add("S", lambda: [S.activation(out, in_, fn, **kw)], ins, on, 0.065 + cy * n * f if f != 1 else cy * max(64, n), ind=f != 1,
                   alt=alt or ())

    def iota(ap, on, pat, b, ch, n, fl=True):
        if fl:
            return add("G", lambda: [g.iota(ap, pat, b, ch, allow_small_or_imprecise_dtypes=True)], "", on, 0.13 + 2 * cy * n)
        return add("G", lambda: [g.iota(ap, pat, b, ch)], "", on, 0.13 + 2 * cy * n)

    def fill(ap, on, v, n):
        alt = [("V", lambda: [V.memset(ap, float(v))], cy * max(64, n))]
        if abs(v) < 2 ** 24:
            alt.append(("G", lambda: [g.iota(ap, [[0, n]], v, 0, allow_small_or_imprecise_dtypes=True)], 0.13 + 2 * cy * n))
        return act(ap, on, T.bc[:, 0:n], "one", n, alt=alt, scale=0.0, bias=float(v))

    def select(ap, on, pat, b):
        return add("G", lambda: [g.affine_select(ap, T.ohA[:, 0:128], pat, A.is_equal, 0.0, b, 1)], "ohA", on, 0.17 + 256 * cy)

    def mm(lst, ins, bank, ext=(), aft=None):
        c = sum(cy * max(64, n) * (4 if f4 else 1) for (_, n, f4) in lst)
        return add("T", lambda: [E.matmul(*a) for (a, n, f4) in lst], ins, bank, c, ext, aft)

    loads, nloc = {}, {}

    def load(q, sem, pairs, ins, on, lat=LAT, ext=(), aft=None):
        eng = g.sync if q == "Y" else g.scalar
        i = add(q, lambda: [eng.dma_start(o, x) for o, x in pairs], ins, on, 0.1 * len(pairs), ext, aft)
        tasks[i]["dma"], tasks[i]["lat"] = sem, lat
        loads[sem] = loads.get(sem, 0) + 16 * len(pairs)
        return i

    def remote(calls, ins, left="loc"):
        def fn():
            for c in calls:
                g.remote_dma_fused([transfer(topo, core, d, es, T.sem[s], a, b) for d, es, s, a, b in c], local_sem=T.sem[left])
                nloc[left] = nloc.get(left, 0) + sum(len(x[1]) for x in c)
            return []
        return add("G", fn, ins, "", CALL * len(calls))
    E8 = topo.engines(core, peers[0])
    blk = lambda t, b, w=128: t[:, w * b:w * b + w]

    vop(lambda: V.memset(T.bc[:], 1.0), "", "one", 96)
    vop(lambda: V.memset(T.X[:], 1), "", "X", NP)
    a = load("Y", "ldN", [(T.Zn[:], T.nbr[:])], "", "Zn")
    b = load("S", "ldZ", [(T.Zp[:], T.planes[:])], "", "Zp")
    tasks[load("S", "ldD", [(T.Zd[:], T.planes[3:16:4, :])], "", "Zd", LAT + 0.2)]["odeps"].add(b)
    tasks[load("Y", "ldA", [(T.L0[:], T.tet0[:])], "", "L0", LAT + 0.3)]["odeps"].add(a)
    load("Y", "ldP", [(T.X[4 * f + i:128:16, :], T.pts[i:24:3, :]) for f in range(4) for i in range(3)], "", "X")

    xd, tI, xp, Ld, Hd = T.st[:, 64:96], T.st[:, 96:128], T.st[:, 128:160], T.Ld[:, 0:32], T.Ld[:, 32:64]
    cp(T.NU[:], "NU", T.Zn[:], "Zn")
    sC = remote([[(rel[1], E8, "hC", T.NU[:], T.A3[:])]], "NU", "lt")
    ts(T.H1[:], "H1", T.Zp[:], "Zp", 1.0 / 64, None, A.mult, n=128)
    sA = remote([[(rel[0], E8, "hA", T.H1[:], T.A1[:])]], "H1", "lt")
    act(xd, "xd", T.Zd[:], "Zd", scale=1.0 / 64)
    ts(Hd, "Hd", T.Zd[:], "Zd", 1.0 / 64, None, A.mult)
    tt(Ld, "Ld", xd, Hd, "xd Hd", A.subtract)
    sB = remote([[(rel[1], E8, "hB", Ld, T.A2[:])]], "Ld", "lt")
    tasks[sC]["tab"], tasks[sA]["tab"], tasks[sB]["tab"] = 1, 2, 2
    tasks[sA]["odeps"].add(sC)
    tasks[sB]["odeps"].add(sA)

    iota(T.pi[:], "pi", [[0, 4]], 0, 1, 4, False)
    iota(T.jm[:], "jm", [[0, 8], [1, 16]], 0, 0, 128)
    iota(T.oRi[:, 0:12], "oRi", [[0, 4], [-8, 3]], 16, 0, 12)
    iota(T.md16[:], "md16", [[1, 8], [0, 16]], 0, 0, 128)
    iota(T.mk[:], "mk", [[1, 128]], 0, -1, 128)
    iota(T.oKi[:], "oKi", [[1, 32]], 0, 0, 32, False)
    iota(T.cOw[:], "cOw", [[16, BW]], 128, 1, BW)
    iota(T.cD[:, 0:8], "cD", [[32, 4], [1, 2]], -2, 0, 8)
    iota(T.cD[:, 8:72], "cB", [[0, 8], [-32, 4], [-1, 2]], 0, 0, 64)
    iota(T.sA[:, 0:46], "sA", [[1, 46]], 0, 0, 46)
    iota(T.cL[:, 0:140], "cL", [[1, 140]], -12, 0, 140)
    iota(T.CC[:, 0:64], "CH", [[1024, 2], [0, 32]], 0, 32, 64)
    iota(T.CC[:, 64:128], "CL", [[PWID - 1024, 2], [1, 32]], LO, 0, 64)
    for k, v in enumerate(owners):
        fill(blk(T.cQ, k, BW), "cQ%d" % k, v, BW)
    CQ = " ".join("cQ%d" % k for k in range(8))
    fill(T.Rs[:, 0:7 * BW], "Rs", 1, 7 * BW)
    fill(T.Rs[:, 0:7 * BW:BW], "Rs", 0, 7)
    fill(T.Rs[:, 7 * BW:8 * BW], "Rh", 0, BW)
    ones = T.bc[0:1, 0:128]
    sh, an = A.arith_shift_right, A.bitwise_and
    for k, x in enumerate(((15, None, an), (4, None, sh), (3, None, an), (2, 3, sh, an), (3, 1, sh, an), (5, None, sh))):
        ts(T.pj[:, k:k + 1], "pj%d" % k, T.pi[:, 0:1], "pi", *x)
    ts(T.pj[:, 6:8], "pj6", T.pi[:, 0:2], "pi", 1, None, an)
    cp(T.pf[:, 0:8], "pf", T.pj[:, 0:8], " ".join("pj%d" % k for k in range(7)))
    col = lambda k: T.pf[:, k:k + 1]
    p16, pg, pi_, pf_, p8, p5, par = [col(k) for k in range(7)]
    cv, g31, hL, cf, cl, c1, c2, lo, hi, pK, pK4, pL, m3, xm, m34, he, he2, f15, g15, p15, m89, k8, cA, cB = [col(k) for k in range(8, 32)]
    for ap, nm, src, sc, bi in ((g31, "g31", pg, 3.0, 1.0), (pK4, "pK4", pf_, float(K4), RND - 3.0 * K4), (lo, "lo", par, float(PWID), 0.0),
                                (hi, "hi", par, float(PWID), float(HI))):
        act(ap, nm, src, "pf", scale=sc, bias=bi)
    act(hL, "hL", p16, "pf g31", fn=F.Identity, scale=g31, bias=g31)
    act(cl, "cl", pg, "pf", fn=F.Identity, scale=16.0, bias=pf_)
    nl, sg, w89, wg, sgx, hl, hu, bl, bu, p58, pM = [col(k) for k in range(36, 47)]
    act(nl, "nl", p5, "pf", scale=-1.0, bias=4.0)
    act(nl, "nl", pg, "pf nl", fn=F.Identity, scale=6.0, bias=nl)
    act(sg, "sg", p5, "pf", scale=-4.0, bias=-1.0)
    act(sg, "sg", pg, "pf sg", fn=F.Identity, scale=2.0, bias=sg)
    act(c2, "c2", pf_, "pf nl", fn=F.Identity, scale=-1.0, bias=nl)
    act(c1, "c1", p8, "pf", fn=F.Identity, scale=-4.0, bias=pi_)
    ts(c1, "c1", c1, "c1", -1.0, -1.0, A.max, A.mult)
    act(c1, "c1", c1, "c1 nl", fn=F.Identity, bias=nl)
    oK, oR, oB8, oF = T.oT[:, 0:24], T.oT[:, 24:36], T.oT[:, 40:44], T.oT[:, 64:72]
    m16 = T.m16[:]
    ts(oR, "oR", T.oRi[:, 0:12], "oRi pf", p16, None, A.add)
    ts(T.G2[:], "G2", T.md16[:], "md16 pf", pg, 2.0, A.is_equal, A.mult)
    ts(T.I16[:], "I16", T.mk[:], "mk", 0.0, None, A.is_equal)
    L2, U2 = T.U2[:, 0:128], T.U2[:, 128:256]
    for ap, nm, h, b, x in ((L2, "L2", hl, bl, (-0.5, 7.5, 0.5, -7.5)), (U2, "U2", hu, bu, (0.5, -0.5, 0.5, 0.5))):
        act(h, nm + "h", p16, "pf", scale=x[0], bias=x[1])
        act(b, nm + "b", p16, "pf", scale=x[2], bias=x[3])
        act(ap, nm, T.mk[:], "mk %sb" % nm, 128, F.Abs, bias=b)
        ts(ap, nm, ap, "%s %sh" % (nm, nm), h, 2.0, A.is_le, A.mult)
    act(T.U2[:, 256:384], "U2n", U2, "U2", 128, half=True, scale=-1.0)
    act(T.cO16[:, 0:BW], "cO16", T.cOw[:], "cOw")
    cp(oK, "oK", T.oKi[:, 0:24], "oKi")
    ts(m16, "m16", T.jm[:], "jm pf", p16, None, A.is_equal)
    act(T.G3[:], "G3", T.bc[:, 0:128], "one", 128, half=True, scale=0.0)
    act(T.G3[:, 3:128:4], "G3", T.G2[:, 3:128:4], "G2", scale=0.5)
    ts(T.pf[:, 32:36], "m4", T.oKi[:, 0:4], "oKi pf", pf_, -float(BIG + K4), A.is_equal, A.mult)
    for j in range(4):
        act(T.sc4[:, j:128:4], "sc4%d" % j, T.bc[:, 0:32], "one m4", scale=col(32 + j), bias=float(K4))
    SC4 = "sc40 sc41 sc42 sc43 "
    ts(T.LP[0:20, :], "LP", T.jm[0:20, :], "jm hL", 1.0, T.pf[0:20, 10:11], A.add, A.is_equal)
    for W, wn, first in ((T.W1, "W1", "S" in SC1), (T.W2, "W2", "S" not in SC1)):
        if first:
            tasks[act(W[:, 0:128], wn + " tab", T.bc[:, 0:128], "one", 128, F.Silu, scale=float(NONE + OFS))]["cost"] += TAB
        else:
            fill(W[:, 0:128], wn, NONE + OFS, 128)
    ts(m3, "m3", pi_, "pf", 3.0, None, A.is_equal)
    act(xm, "xm", m3, "m3", scale=-1.0, bias=1.0)
    act(T.X16[:], "X16", T.X[:], "X", NP)
    for b in range(3):
        fill(blk(T.inj, b), "inj", 0, 128)
    S2, S2a = T.sA[:, 144:188], T.sA[:, 192:236]
    fill(T.R1c[:], "R1c", 0, SW)
    fill(T.R1c[:, 9:SW:22], "R1c", TOP, 4)
    fill(T.R1c[:, 21:SW:22], "R1c", TOP, 4)
    ts(T.sA[:, 48:93], "E1", T.sA[:, 1:46], "sA c2", c2, KV, A.is_equal, A.mult)
    tt(T.S1[:], "S1", T.sA[:, 49:93], T.sA[:, 48:92], "E1", A.subtract, n=88)
    act(sgx, "sgx", xm, "xm sg", scale=sg)
    ts(T.sA[:, 96:140], "E2", T.sA[:, 1:45], "sA c1 sg", c1, sg, A.is_equal, A.mult)
    ts(T.sA[:, 288:332], "E4", T.sA[:, 2:46], "sA c1 sgx", c1, sgx, A.is_equal, A.mult)
    tt(S2a, "S2a", T.sA[:, 96:140], T.sA[:, 288:332], "E2 E4", A.subtract, n=88)
    act(w89, "w89", p8, "pf", scale=-1.0, bias=1.0)
    act(S2, "S2", S2a, "S2a w89", scale=w89)
    fill(T.pt[:, 0:SW], "pt", 0, SW)
    fill(T.pt[:, 0:SW:22], "pt", -2 * TOP, 4)
    fill(T.pt[:, 12:SW:22], "pt", -2 * TOP, 4)
    act(T.pt[:, SW:2 * SW], "pt", T.pt[:, 0:SW], "pt", SW, scale=-1.0)
    act(T.Ib[:], "Ib", T.I16[:], "I16", 128)
    ts(T.tb[:, 0:128], "tb0", T.jm[:], "jm pf", p16, None, A.is_lt)
    act(T.tb[:, 128:256], "tb1", m16, "m16", 128, scale=HOLD)
    mm([((T.o2[:, 0:128], T.Ib[:], blk(T.tb, h), h == 0, h == 1), 128, 0) for h in range(2)], "Ib tb0 tb1", "o2")
    act(T.hk[:, 0:128], "hk", T.o2[:, 0:128], "o2", 128)
    act(T.hk[:, 128:256], "hk2", T.o2[:, 0:128], "o2", 128)
    act(he, "he", T.hk[:, 0:1], "hk", scale=1.0 / HOLD)
    fill(T.hk[:, 0:128:16], "hk", 0, 8)
    ts(f15, "f15", p16, "pf", 14.5, 1.0 / HOLD, A.is_lt, A.max)
    ts(g15, "g15", p16, "pf", 14.5, HOLD, A.is_gt, A.mult)
    ts(g15, "g15", g15, "g15", 1.0, None, A.max)
    act(he2, "he2", he, "he f15", scale=f15)
    act(T.hk[:, 128:256:16], "hk2", T.bc[:, 0:8], "one he2", scale=he2)
    act(wg, "wg", g15, "g15 sg", scale=sg)
    ts(T.sA[:, 240:285], "E3", T.sA[:, 0:45], "sA nl wg", nl, wg, A.is_equal, A.mult)
    tt(T.Ms[:, 0:44], "Ms", T.sA[:, 240:284], T.sA[:, 241:285], "E3", A.subtract, n=88)
    ts(T.Ms[:, 48:56], "Mf", T.oKi[:, 0:8], "oKi pf g15", pg, g15, A.is_equal, A.mult)
    for t, b in (("O", 0), ("O", 1), ("O", 2), ("V", 0)):
        c = QB * b + Q0
        fill(T["q" + t][:, c:c + 128 * GW:GW], "q%s%d" % (t, b), 0, 128)
    m9 = col(47)
    act(m9, "m9", T.m16[:, 9:10], "m16")
    act(cA, "cA", T.m16[:, 8:9], "m16", scale=float(HI))
    act(k8, "k8", T.m16[:, 8:9], "m16", scale=2048.0)
    act(cB, "cBd", T.m16[:, 9:10], "m16 k8", fn=F.Identity, scale=DEAD - 2048.0, bias=k8)
    for a, z in ((0, LO), (HI, PWID + LO), (PWID + HI, 2 * PWID)):
        iota(T.PW[:, a:z], "zP%d" % a, [[0, z - a]], 0, 0, z - a, False)
    fill(T.ND[:, 0:LO], "zN0", 0, LO)
    for k, a, c, cn in ((1, HI, cA, "cA"), (3, PWID + HI, cB, "cBd")):
        act(T.ND[:, a:a + LO], "zN%d" % k, T.bc[:, 0:LO], "one " + cn, scale=c)
    act(cf, "cf", T.m16[:, 8:9], "m16", scale=float(PWID))
    act(T.ND[:, PWID:PWID + LO], "zN2", T.oKi[:, 0:LO], "oKi m9 cf", fn=F.Identity, scale=m9, bias=cf)
    PZ = {"PW": " zP0 zP%d zP%d" % (HI, PWID + HI), "ND": " zN0 zN1 zN2 zN3"}
    iota(T.xq[:, 0:128], "xe", [[16, 8], [0, 4], [1, 4]], 0, -1, 128)
    for f in range(4):
        ts(blk(T.EX, f), "EX%d" % f, T.xq[:, 0:128], "xe", -4.0 * f, None, A.is_equal)
    ts(T.LI[:, 0:140], "LI", T.cL[:, 0:140], "cL cl m3", cl, m3, A.is_equal, A.mult, n=70)
    off = col(48)
    act(off, "off", par, "pf", scale=float(PWID), bias=float(LO - 1))
    dt = NT * (owners[7] - owners[6])
    act(cv, "cv", par, "pf", scale=float(PWID - dt), bias=float(LO - NT * owners[6]))
    for k, a in enumerate([rank] + owners[1:6:2]):
        act(T.cS[:, 2 * k:2 * k + 2], "cS%d" % k, T.pf[:, 6:8], "pf", scale=float(dt - 1), bias=float(HI - LO + NT * (owners[6] - a)))
    fill(T.cD[:, 15:72:8], "cB", -384, 8)
    act(T.zz[:, 0:8], "cQc", T.cQ[:, 0:8 * BW:BW], CQ)
    for n in (8, 16, 32):
        act(T.zz[:, n:2 * n], "cQc", T.zz[:, 0:n], "cQc")
    fill(T.zz[:, 64:128], "RsM", 0, 64)
    fill(T.zz[:, 64:128:8], "RsM", -BIG, 8)
    ts(oB8, "oB8", T.oKi[:, 0:4], "oKi pf", 2.0, p8, A.mult, A.add)
    iota(T.ci[:, 0:8], "ci", [[16, 8]], 0, 1, 8, False)
    iota(T.ci[:, 8:16], "cib", [[-16, 8]], 128, 1, 8, False)
    ts(T.ci[:, 0:16], "ci", T.ci[:, 0:16], "ci cib", 127, None, an)
    cp(T.oT[:, 48:64], "rot", T.ci[:, 0:16], "ci")
    act(T.I2[:, 0:128], "I2", T.I16[:], "I16", 128)
    act(T.I2[:, 128:256], "I2b", T.I16[:], "I16", 128)
    act(T.Gf[:], "Gf", T.G2[:], "G2", 128, scale=0.5)
    act(T.Ip[:], "Ip", T.I2[:, 32:160], "I2 I2b", 128)
    act(p58, "p58", p5, "pf", scale=8.0)
    ts(oF, "oF", T.oKi[:, 0:8], "oKi p58", p58, None, A.add)
    fill(T.vW[:, 128:136], "vW0", 416, 8)
    fill(T.dW[:, 128:136], "dW0", 8192, 8)
    ts(p15, "p15", p16, "pf", 14.5, None, A.is_lt)
    act(pK, "pK", p15, "p15", scale=-float(MID), bias=float(SA - 8192))
    act(pL, "pL", p15, "p15", scale=-float(MID))
    act(pM, "pM", p15, "p15", scale=-float(MID), bias=512.0 * LO - 208.0)
    act(T.I1k[:], "I1k", T.I16[:], "I16", 128, scale=1024.0)

    def steps_rows(src, srcn, k, ext=(), aft=None):
        st, sn, HL, N, t = blk(T.st, k, 32), "st%d" % k, "HL%d" % k, "N%d" % k, 1 - k
        load("Y", "ln%d" % k, [(T[N][8 + h:9 + h, :], T.CC[0:32, 64 * h + 32 * t:64 * h + 32 * t + 32]) for h in range(2)], "CH CL", N + "c")
        to = float(LO - NT * owners[6] if k else -SA)
        ts(T[HL][:, 0:32], HL, src, srcn, to, None, A.add, ext=ext, aft=aft)
        ts(st, sn, src, srcn, to, None, A.add, ext=ext, aft=aft)
        tt(T[HL][:, 32:64], HL + "b", st, T[HL][:, 0:32], sn + " " + HL, A.subtract)
        for h in range(2):
            load("Y", "ln%d" % k, [(T[N][4 * h:4 * h + 4, :], blk(T[HL], h, 32))], HL + "b" * h, N + "b" * h)

    def windows(t, R, Rn, N, banks, on):
        if NDMA[t]:
            c = PWID * t + LO
            load("Y", "ln%d" % (1 - t), [(T[N][10:16, :], T.zb[0:96, :])], "zb", N + "d")
            load("Y", "ld%d" % t, [(T.ND[16 * a:16 * a + 16, c:c + NT], T[N][0:16, :]) for a in range(8)], "%s %sb %sc %sd" % (N, N, N, N),
                 "ND%d0 ND%d1" % (t, t), LAT + 0.6)
        for k, (bk, q) in enumerate(zip(banks, on)):
            if NDMA[t] and k < 2:
                continue
            h, c = k % 2, PWID * t + LO + 512 * (k % 2)
            w, sc, lhs, rhs, ins = (("ND", 1.0, T.m16[0:10, :], T[N], "m16 %s %sb %sc" % (N, N, N)), ("PW", 64.0, T.LP[0:20, :], T.R1, "LP " + Rn))[k // 2]
            for a in (0, 256):
                mm([((T[bk][:, a:a + 256], lhs, rhs[0:10 * (1 + k // 2), 512 * h + a:512 * h + a + 256], True, True), 256, 0)], ins, bk)
            if q == "S":
                act(T[w][:, c:c + 512], "%s%d%d" % (w, t, h), T[bk][:], bk, 512, scale=sc)
            else:
                ts(T[w][:, c:c + 512], "%s%d%d" % (w, t, h), T[bk][:], bk, sc, None, A.mult, n=512)

    c = PWID + LO
    a = load("Y", "lpw", [(T.PW[16 * a:16 * a + 16, c:c + NT], T.planes[:]) for a in range(8)], "", "PW10 PW11", LAT + 1.0,
             *(([("lt", 3 * len(E8))], (sB, 1.5)) if PWA else ()))
    tasks[a]["odeps"].add(wr["X"])
    if sum(NDMA):
        fill(T.zb[:], "zb", 0, 64)
    steps_rows(T.Zn[:], "Zn", 0)
    windows(1, "", "", "N0", ("vK", "vP"), WON0)

    su1, suA, suB, s1c = T.su[:, 0:24], T.su[:, 24:48], T.su[:, 48:56], T.su[:, 64:88]

    def slots(oh, ohn, su, sun):
        M, n7, n8 = 24, 7 * BW, 8 * BW
        mm([((T.rA[:, n7:n8], T.I16[:], T.cO16[:, 0:BW], True, True), M, 0)], "I16 cO16", "rA")
        tt(oh[:], ohn, T.rk[:, 0:32].indirect(oR), T.cQ[:], "rka rkb oR " + CQ, A.is_equal, n8, f=GAT)
        mm([((T.rA[:, 0:n7], L2, oh[:, 0:n7], True, False), n7, 0), ((T.rA[:, 1:n7], U2, oh[:, 0:n7 - 1], False, False), n7, 0),
            ((T.rA[:, M:n7:M], T.U2[:, 256:384], oh[:, M - 1:n7 - 1:M], False, False), 6, 0),
            ((T.rA[:, 0:n7:M], ones, T.cD[0:1, 0:7], False, True), 7, 0)], "L2 U2 U2n one cD " + ohn, "rA")
        sc = T.rA[:, 256:256 + n8]
        scan(sc, "sc", T.Rs[:], T.rA[:, 0:n8], "Rs Rh rA", A.mult, A.add, n8)
        tt(T.z2[:], "z2", sc, oh[:], "sc rA " + ohn, A.mult, n8)
        mm([((T.rB[:, 0:M], T.I16[:], T.z2[:, BW * b:BW * b + M], b == 0, b == 7), M, 0) for b in range(8)], "I16 z2", "rB")
        cp(su, sun, T.rB[:, 0:M], "rB")

    def scatter(q, W, wn, l, src, ins, n):
        if q == "S":
            return act(W[:].indirect(l), wn, src, ins + " tab", n, F.Silu, SCA,
                       alt=[("V", lambda: [V.tensor_copy(W[:].indirect(l), src)], 0.05 + cy * n * SCA)])
        return cp(W[:].indirect(l), wn, src, ins, n, f=SCA)

    def message(W, wn, MB, mn):
        scan(T.sd[:], "sd", T.sc4[:], W[:, 0:128], SC4 + wn, A.add, A.max, 128)
        ts(MB[:, 0:32], mn, T.sd[:, 3:128:4], "sd pK4", pK4, -RND - OFS, A.add, A.add)

    def pack(banks):
        ts(T.inj[:, 0:NP:16], "inj", T.ti[:, 0:24], "ti he", he, None, A.mult)
        for b, bank in enumerate(banks):
            ps = T[bank][:, 256:384]
            scan(blk(T.ex, b), "ex%d" % b, T.hk[:, 0:128], blk(T.inj, b), "hk inj", A.mult, A.add, 128)
            mm([((ps, T.I16[:], blk(T.X16, b), True, False), 128, 0)], "I16 X16", bank)
            mm([((ps, T.G3[:], blk(T.ex, b), False, True), 128, 0)], "G3 ex%d" % b, bank)
            act(blk(T.PK, b), "PK%d" % b, ps, bank, 128, bias=float(OFS))

    def send(buf, ins, sem, w, src, v, dst):
        x = [(d, sem, buf[:, src + v * k:src + v * k + w], buf[:, dst + w * k:dst + w * k + w]) for k, d in enumerate(peers)]
        return remote([[(x[0][0], E8[:4]) + x[0][1:], (x[1][0], E8[4:]) + x[1][1:]], [(x[2][0], E8) + x[2][1:]]], ins)
    ARR = 2 * len(E8)

    def turn(t, b, out, rhs, bank, stop):
        n, c, e = "%s%d" % (t, b), QB * b + Q0, blk(T["e" + t], b)
        scan(e, "e" + n, T["q" + t][:, c:c + 128 * GW:GW], T.hk[:, 128:256], "hk2 q" + n, A.add, A.mult, 128)
        mm([((out, e, rhs, True, stop), 8, 1)], "Ms Mf e" + n, bank)

    def lay(bank, c, a, z):
        mm([((T[bank][:, c:c + z - a], ones, T.pt[0:1, a:z], True, True), z - a, 0)], "one pt", bank)

    def step(t, b, s, X, xn, bK, bP):
        n, c, cP = "%s%d" % (t, b), QB * b, 256 if t == "V" else SW
        pr, pa, w, u = blk(T["pr" + t], b), blk(T["pa" + t], b), blk(T["w" + t], b, 8), blk(T["u" + t], b, SW)
        pK_, pP, c0 = T[bK][:, 1:SW:2], T[bP][:, cP + 1:cP + SW:2], 0 if t == "V" else PWID
        PWn, NDn = [" ".join(x + a + h for a in ("01" if t == "V" else "1") for h in "01") + PZ[x] for x in ("PW", "ND")]
        tt(pr, "pr" + n, T.PW[:, c0:].indirect(w), X, "%s w%s %s" % (PWn, n, xn), A.mult, 128, f=GAT)
        act(pa, "pa" + n, T.ND[:, c0:].indirect(w), "%s w%s" % (NDn, n), 128, f=GAT)
        carry = s and t == "V"
        if carry:
            turn(t, b, pP, T.Ms[:, 0:44], bP, False)
        mm([((pP, pa, S2 if carry else S2a, not carry, True), 44, 0)], ("S2" if carry else "S2a") + " pa" + n, bP)
        mm([((pK_, pr, T.S1[:], True, True), 44, 1)], "S1 pr" + n, bK)
        scan(u, "u" + n, T[bK][:, 0:SW], T.R1c[:], "R1c " + bK, A.add, A.max, SW)
        if s < 2 and t == "O":
            r = blk(T.ra, 3 * s + b, SW)
            scan(r, "r%d%d" % (s, b), T[bP][:, cP:cP + SW], u, "%s u%s" % (bP, n), A.subtract, A.min, SW)
            ts(w, "w" + n, T.ra[:, SW * (3 * s + b) + GW - 1:SW * (3 * s + b + 1):GW], "r%d%d" % (s, b), -float(PWID), float(HI), A.add, A.min)
            return
        scan(T["q" + t][:, c:c + 16 * SW:16], "q" + n, T[bP][:, cP:cP + SW], u, "%s u%s" % (bP, n), A.subtract, A.min, SW)
        if s < 2:
            ts(w, "w" + n, T.qV[:, Q0:16 * SW:16 * GW], "lo hi q" + n, lo, hi, A.max, A.min)

    def own(out, c, on, bias):
        for s in range(3):
            for b in range(3):
                step("O", b, s, blk(T.XT if s == 1 else T.X16, b), "XT" if s == 1 else "X16", "o%d" % b, "o%d" % b)
            if s < 2:
                pl, D, rn = T.ra[:, 3 * SW * s + GW - 1:3 * SW * (s + 1):GW], blk(T.Dd, s, 24), " r%d0 r%d1 r%d2" % (s, s, s)
                ts(D, "D%d" % s, pl, rn, float(PWID), DEAD, A.max, A.min)
                tt(D, "D%d" % s, pl, D, "D%d" % s + rn, A.subtract)
        if bias is not None:
            act(blk(T.Dd, 1, 24), "D1", blk(T.Dd, 1, 24), "D1 pK", fn=F.Identity, bias=bias)
        for b in range(3):
            bk, pl = "o%d" % b, T.qO[:, QB * b + Q0:QB * b + 16 * SW:16 * GW]
            tt(pl, "qO%d" % b, pl, blk(T.Dd, b, 8), "D0 qO%d" % b, A.add)
            turn("O", b, T[bk][:, 192:200], T.Ms[:, 48:56], bk, True)
            tt(blk(out, b + c, 8), on + str(b), T[bk][:, 192:200], blk(T.Dd, 3 + b, 8), bk + " D1", A.add)

    def arrive(MB, mn, sem, sent):
        a = mm([((T.vP[:, 128 + f:256:4], blk(T.EX, f), MB[:, 24:56], True, True), 32, 0) for f in range(4)],
               "EX0 EX1 EX2 EX3 " + mn, "vP", [(sem, ARR)], (sent, FLY))
        b = mm([((T.vL[:, 0:8], T.LI[:, 12 - 4 * c:140 - 4 * c], MB[:, 24 + c:56:4], c == 0, c == 3), 8, 0) for c in range(4)],
               "LI " + mn, "vL", [(sem, ARR)], (sent, FLY))
        tasks[b]["odeps"].add(a)
        act(T.Xv[:], "Xv", T.vP[:, 128:256], "vP xm m3", 128, F.Identity, scale=xm, bias=m3)
        ts(T.wV[:], "wV0", T.vL[:, 0:8], "vL off hi", off, hi, A.add, A.min)

    def visitors(back):
        act(T.Zr[:], "Zr", T.Xv[:].indirect(T.oT[:, 48:56]), "Xv rot", 128, f=GAT)
        for h in range(0, 8, 2):
            mm([((T.vL[:, 128 + 16 * d:144 + 16 * d], T.I2[:, 128 - 16 * d:256 - 16 * d], blk(T.Zr, d, 16), True, True), 16, 0) for d in (h, h + 1)],
               "I2 I2b Zr", "vL")
        act(T.Ur[:], "Ur", T.vL[:, 128:256], "vL", 128)
        act(T.Xw[:], "Xw", T.Ur[:].indirect(T.oT[:, 56:64]), "Ur rot", 128, f=GAT)
        for s in range(3):
            step("V", 0, s, (T.Xw if s == 1 else T.Xv)[:], "Xw" if s == 1 else "Xv", "vK", "vP")
        if back:
            turn("V", 0, T.vL[:, 0:8], T.Ms[:, 48:56], "vL", True)

    ts(T.rk[:, 16:32], "rka", T.L0[:, 0:16], "L0", 10, None, sh)
    ts(T.rk[:, 0:16], "rkb", T.L0[:, 8:24], "L0", 10, None, sh)
    slots(T.oh1, "oh1", su1, "su1")
    ts(T.ti[:, 0:24], "ti", T.L0[:], "L0", 1023, None, an)
    pack(("vL", "o2", "vL"))
    for q, (a, z) in zip(SC1, CUT1):
        scatter(q, T.W1, "W1", T.su[:, a:z], T.PK[:, 16 * a:16 * z], " ".join("PK%d" % b for b in range(a // 8, (z + 7) // 8)) + " su1", 16 * (z - a))
    message(T.W1, "W1", T.MB1, "msg1")
    s1 = send(T.MB1, "msg1", "rq1", 8, 0, 8, 32)
    act(m34, "m34", xm, "m3 xm", fn=F.Identity, scale=-float(OFS), bias=m3)
    act(T.xB[:], "xB", T.W1[:, 0:128], "W1 xm m34", 128, F.Identity, scale=xm, bias=m34)

    load("Y", "ldT", [(T.Yt[0:72, 16 * a:16 * a + 16], T.pts[3 * a:3 * a + 3, :]) for a in range(8)], "HL0b", "Yt")
    act(T.Zr[0:72, :], "Zr", T.Yt[0:72, :], "Yt", 128)
    iota(T.xq[:, 128:256], "xx", [[1, 8], [0, 4], [24, 4]], 0, -1, 128)
    for b in range(3):
        ts(blk(T.Xp, b), "Xp%d" % b, T.xq[:, 128:256], "xx", -8.0 * b, None, A.is_equal)
        mm([((blk(T.rA, b), T.Xp[0:72, 128 * b:128 * b + 128], T.Zr[0:72, :], True, True), 128, 0)], "Zr Xp%d" % b, "rA")
    act(T.XT[:], "XT", T.rA[:, 0:NP], "rA m3", NP, F.Identity, bias=m3)

    arrive(T.MB1, "msg1", "rq1", s1)
    act(T.Lv0[:], "Lv0", T.vL[:, 0:8], "vL")
    steps_rows(T.NP[:], "NP", 1, [("tC", len(E8))], (sC, FLY_T[0]))
    load("Y", "lr1", [(T.R1[16:20, :], T.A2[:])], "", "R1b", LAT, [("tB", len(E8))], (sB, FLY_T[2]))
    load("Y", "lr1", [(T.R1[0:16, :], T.A1[:])], "", "R1", LAT, [("tA", len(E8))], (sA, FLY_T[1]))
    windows(0, "R1", "R1 R1b", "N1", WB, WON)
    lay("vK", 0, 0, SW)
    lay("vP", 256, SW, 2 * SW)
    for b in range(3):
        lay("o%d" % b, 0, 0, 2 * SW)
    act(T.tb[:, 0:128], "tb0", m16, "m16", 128, half=True, scale=-2.0 * BIG)
    act(T.tb[:, 128:256], "tb1", m16, "m16", 128, half=True, scale=float(MID))
    mm([((T.rA[:, 0:128], T.Ib[:], T.tb[:, 0:128], True, False), 128, 0), ((T.rA[:, 1:128], T.Ib[:], T.tb[:, 128:255], False, True), 128, 0)],
       "Ib tb0 tb1", "rA")
    act(T.scC[:, 0:128], "scC", T.rA[:, 0:128], "rA", 128)
    act(T.scC[:, 128:192], "scCb", T.scC[:, 0:64], "scC")

    cj, cd, cr = T.cj[:, 0:24], T.cj[:, 24:48], T.ci[:, 24:32]
    ts(cj, "cj", T.L0[:], "L0", 8192.0 - base, None, A.add)
    ts(cj, "cj", cj, "cj", 8191, None, an)
    ts(T.wO[:], "wO0 wO1 wO2", cj, "cj", float(LO), float(HI), A.add, A.min)
    own(T.Lm, 0, "Lm", None)
    ts(T.rk[:, 16:32], "rka", T.Lm[:, 0:16], "Lm0 Lm1", SA - 511.75, 1.0 / 1024, A.add, A.mult)
    ts(T.rk[:, 0:16], "rkb", T.Lm[:, 8:24], "Lm1 Lm2", SA - 511.75, 1.0 / 1024, A.add, A.mult)
    ts(T.ci[:, 0:24], "ci", T.Lm[:], "Lm0 Lm1 Lm2", 8192.0 - PWID - LO, None, A.add)
    ts(T.ti[:, 0:24], "ti", T.ci[:, 0:24], "ci", 1023, None, an)
    slots(T.ohA, "ohA", suA, "suA")
    pack(("o0", "o1", "o2"))
    for q, (a, z) in zip(SC2, CUT):
        scatter(q, T.W2, "W2", T.su[:, 24 + a:24 + z], T.PK[:, 16 * a:16 * z], " ".join("PK%d" % b for b in range(a // 8, (z + 7) // 8)) + " suA",
                16 * (z - a))

    Cn = T.sm[:, 64:72]
    ts(Cn, "Cn", T.Lv0[:], "Lv0", 3000.0, None, A.is_gt)
    tt(Cn, "Cn", Cn, T.cS[:], "Cn cS0 cS1 cS2 cS3", A.mult)
    act(Cn, "Cn", Cn, "Cn cv", fn=F.Identity, bias=cv)
    visitors(True)
    tt(T.RP1[:, 8:16], "out1", T.vL[:, 0:8], Cn, "vL Cn", A.subtract)
    s2 = send(T.RP1, "out1", "rp1", 2, 10, 2, 2)

    mm([((T.vP[:, 0:64], ones, T.cD[0:1, 8:72], True, False), 64, 0)], "one cB", "vP")
    back = dict(ext=[("rp1", ARR)], aft=(s2, FLY))
    ts(T.rkB[:], "rkB", T.RP1[:, 2:10], "out1", 10, None, sh, **back)
    ts(T.ti[:, 24:32], "tiB", T.RP1[:, 2:10], "out1", 1023, None, an, **back)
    tt(T.ohB[:], "ohB", T.rkB[:].indirect(oB8), T.zz[:, 0:64], "rkB oB8 cQc", A.is_equal, 64, f=GAT)
    mm([((T.vP[:, 8 * d:64], x, T.ohB[:, 0:64 - 8 * d], False, d == 7), 64, 0) for d, x in [(0, T.I1k[:]), (0, L2)] + [(d, T.G2[:]) for d in range(1, 8)]],
       "G2 L2 I1k ohB", "vP")
    scan(T.zz[:, 128:192], "zz", T.zz[:, 64:128], T.vP[:, 0:64], "RsM vP", A.add, A.max)
    ts(suB, "suB", T.zz[:, 135:192:8], "zz", -1.0, 1056.0, A.mult, A.add)
    tt(blk(T.ex, 3), "ex3", T.ti[:, 24:32].indirect(T.oT[:, 0:8]), m16, "tiB oK m16", A.mult, 128, f=GAT)
    mm([((T.vL[:, 256:384], T.I16[:], T.xB[:], True, False), 128, 0)], "I16 xB", "vL")
    mm([((T.vL[:, 256:384], T.G3[:], blk(T.ex, 3), False, True), 128, 0)], "G3 ex3", "vL")
    act(blk(T.PK, 3), "PK3", T.vL[:, 256:384], "vL", 128, bias=float(OFS))
    scatter("S", T.W2, "W2", suB, blk(T.PK, 3), "PK3 suB", 128)
    message(T.W2, "W2", T.MB2, "msg2")
    s3 = send(T.MB2, "msg2", "rq2", 8, 0, 8, 32)

    arrive(T.MB2, "msg2", "rq2", s3)
    visitors(False)
    ts(T.RP2[:, 0:8], "out2", T.qV[:, Q0:16 * SW:16 * GW], "qV0 cv", cv, None, A.subtract)
    s4 = send(T.RP2, "out2", "rp2", 8, 0, 0, 8)

    smA, vB, Yb = T.sm[:, 0:24], T.sm[:, 32:40], T.sm[:, 40:64]
    ts(s1c, "s1c", su1, "su1", 128.0, None, A.min)
    cp(smA, "smA", suA, "suA")
    home = T.oh1[:, 7 * BW:7 * BW + 24]
    ts(cr, "cr", T.RP1[:, 2:10], "rkB", 8192.0 - base, None, A.add)
    ts(cr, "cr", cr, "cr", 8191, None, an)
    act(vB, "vB", cr, "cr", scale=512.0, bias=-640.0)
    tt(vB, "vB", vB, T.zz[:, 135:192:8], "vB zz", A.add)
    tt(T.exv[:], "exv", vB.indirect(T.oT[:, 0:8]), m16, "oK vB m16", A.mult, 128, f=GAT)
    mm([((T.rB[:, 0:128], T.Gf[:], T.exv[:], True, True), 128, 1)], "Gf exv", "rB")
    act(T.vW[:, 0:128], "vW", T.rB[:, 0:128], "rB", 128)
    for b in range(3):
        act(blk(T.gv, b), "gv%d" % b, T.vW[:].indirect(T.su[:, 64 + 8 * b:72 + 8 * b]), "vW vW0 s1c", 128, f=GAT)
        scan(blk(T.sv, b), "sv%d" % b, T.scC[:, 0:128], blk(T.gv, b), "scC gv%d" % b, A.add, A.max, 128)
    ts(cd, "cd", T.ci[:, 0:24], "ci", 8191, None, an)
    tt(T.vO[:], "vO", cd, home, "cd oh1", A.mult)
    act(T.vO[:], "vO", T.vO[:], "vO pM", fn=F.Identity, scale=512.0, bias=pM)
    tt(T.vO[:], "vO", T.vO[:], T.sv[:, 15:NP:16], "vO sv0 sv1 sv2", A.add)
    ts(T.wO[:], "wO0 wO1 wO2", T.vO[:], "vO", 1.0 / 512, float(HI), A.mult, A.min)
    ts(cj, "cj", T.sv[:, 15:NP:16], "sv0 sv1 sv2 pL", pL, None, A.add)
    ts(cd, "cd", cj, "cj", 511, None, an)
    tt(smA, "smA", smA, home, "smA oh1", A.mult)
    tt(smA, "smA", smA, cd, "smA cd", A.subtract)
    ts(T.tau[:], "tau", smA, "smA", 416.0, 128.0, A.add, A.min)
    own(T.sm, 5, "Yb", pK)

    ts(T.RF[:], "RF", T.RP2[:], "out2", 8192.0 - DEAD - SA, None, A.add, ext=[("rp2", ARR)], aft=(s4, FLY))
    act(T.exv[:], "exv", T.RF[:].indirect(oF), "RF oF", 128, f=GAT)
    mm([((T.rB[:, 0:128], T.exv[:], T.Ip[:], True, True), 128, 1)], "Ip exv", "rB")
    act(T.dW[:, 0:128], "dW", T.rB[:, 0:128], "rB", n=128)
    act(T.gv[:, 192:NP], "gv2", T.dW[:].indirect(T.tau[:, 12:24]), "dW dW0 tau", 192, f=GAT)
    act(T.gv[:, 0:192], "gv0", T.dW[:].indirect(T.tau[:, 0:12]), "dW dW0 tau", 192, f=GAT)
    scan(T.sv[:, 0:192], "sv0 sv1", T.scC[:], T.gv[:, 0:192], "scC scCb gv0", A.add, A.max, 192)
    scan(T.sv[:, 192:NP], "sv2", T.scC[:], T.gv[:, 192:NP], "scC scCb gv2", A.add, A.max, 192)
    tt(T.vO[:], "vO", T.sv[:, 15:NP:16], Yb, "sv0 sv2 Yb0 Yb1 Yb2", A.add)
    load("Y", "st", [(T.y[:], T.vO[:])], "vO", "", 0.0)

    order = plan(tasks)
    queue = {"V": V, "S": S, "T": E, "G": g, "Y": g.sync}
    semof = {"V": "sV", "S": "sS", "T": "sT", "G": "sG"}
    done, know, total = {}, {}, {}
    ptr = {q: 0 for q in order}
    known = {q: {} for q in order}
    left = len(tasks)
    while left:
        before = left
        for q in order:
            while ptr[q] < len(order[q]):
                i = order[q][ptr[q]]
                t = tasks[i]
                if any(d not in done for d in t["deps"]):
                    break
                kq = known[q]
                for d in sorted(t["deps"], key=lambda d: (-len(know[d]), -done[d][1])):
                    s, v = done[d]
                    if s is None or kq.get(s, 0) >= v:
                        continue
                    v = max(done[x][1] for x in t["deps"] if done[x][0] == s)
                    if any(done[x][0] not in (s, None) and know[x].get(s, 0) >= v and kq.get(done[x][0], 0) < done[x][1] for x in t["deps"]):
                        continue
                    queue[q].wait_ge(T.sem[s], v)
                    for x in t["deps"]:
                        if done[x][0] == s:
                            for s2, v2 in know[x].items():
                                kq[s2] = max(kq.get(s2, 0), v2)
                    kq[s] = max(kq.get(s, 0), v)
                for s, v in t["ext"]:
                    if kq.get(s, 0) < v:
                        queue[q].wait_ge(T.sem[s], v)
                        kq[s] = v
                ins = ([t["fn"]] if q == t["q"] else [fn for x, fn, c in t["alt"] if x == q])[0]()
                if t["dma"]:
                    for x in ins:
                        x.then_inc(T.sem[t["dma"]], 16)
                    done[i] = (t["dma"], loads[t["dma"]])
                elif not ins:
                    done[i] = (None, 0)
                else:
                    s = semof[q]
                    for x in ins:
                        x.then_inc(T.sem[s], 1)
                    total[s] = total.get(s, 0) + len(ins)
                    done[i] = (s, total[s])
                know[i] = dict(kq)
                if done[i][0] is not None:
                    know[i][done[i][0]] = done[i][1]
                ptr[q] += 1
                left -= 1
        if left == before:
            raise ValueError("the order can't be emitted")
    for s, v in sorted(total.items()):
        g.wait_ge(T.sem[s], v)
    for s, v in loads.items():
        g.wait_ge(T.sem[s], v)
    for s in ("rq1", "rp1", "rq2", "rp2"):
        g.wait_ge(T.sem[s], ARR)
    for s in ("tA", "tB", "tC"):
        g.wait_ge(T.sem[s], len(E8))
    for s, v in nloc.items():
        g.wait_ge(T.sem[s], v)
